import numpy as np
import ml_dtypes


def mxq(x, axis, fmt="e4m3"):
    dtype, down = {"e4m3": (ml_dtypes.float8_e4m3fn, 7), "e5m2": (ml_dtypes.float8_e5m2, 14)}[fmt]
    v = np.moveaxis(np.asarray(x, np.float32).astype(ml_dtypes.bfloat16).astype(np.float64), axis, -1)
    blocks = v.reshape(v.shape[:-1] + (-1, 32))
    amax = np.abs(blocks).max(-1, keepdims=True)
    byte = np.maximum(np.where(amax > 0, np.frexp(amax)[1] - 1 + 127, 0) - down, 1)
    scale = np.exp2(byte - 127.0)
    codes = (blocks / scale).astype(np.float32).astype(dtype).astype(np.float64)
    return np.moveaxis((codes * scale).reshape(v.shape), -1, axis)


WIDE = False


def mx_kscale(k):
    if not WIDE:
        return np.ones(k)
    levels = np.array([10, -10, 5, -5, 0])
    if k % 512:
        return np.exp2(np.random.permutation(np.resize(levels, k // 32))).repeat(32)
    a = np.empty((k // 512, 16))
    for p in range(k // 512):
        a[p, :8] = np.random.permutation(np.resize(levels, 8))
        for g in range(8):
            far = levels[np.abs(levels - a[p, g]) >= 10]
            a[p, g + 8] = far[np.random.randint(len(far))]
    return np.exp2(a.ravel()).repeat(32)


BF16 = ml_dtypes.bfloat16


def bf(x):
    return np.asarray(x, np.float32).astype(BF16)


def f64(x):
    return np.asarray(x).astype(np.float64)


B, S, R, D, G = 2, 512, 4, 512, 16
C = D // G
K = 2 * R + R * R
RD = R * D
M = G * K
ROUNDS = 2


def sigmoid(v):
    return 1.0 / (1.0 + np.exp(-v))


def balance(l):
    q = np.exp(l)
    for _ in range(ROUNDS):
        q = q / np.sum(q, axis=-1, keepdims=True)
        q = q / np.sum(q, axis=-2, keepdims=True)
    return q


def read_streams(pre, xg):
    u = pre[..., 0][..., None] * xg[:, :, 0]
    for r in range(1, xg.shape[2]):
        u = u + pre[..., r][..., None] * xg[:, :, r]
    return u


def mix_streams(q, xg):
    qi = np.transpose(q, (0, 1, 3, 2, 4))
    y = qi[..., 0][..., None] * xg[:, :, 0][:, :, None]
    for j in range(1, xg.shape[2]):
        y = y + qi[..., j][..., None] * xg[:, :, j][:, :, None]
    return y


def draw0():
    s, t = mx_kscale(RD), mx_kscale(D)
    return {
        "x": bf(np.random.standard_normal((B, S, R, D))),
        "gn": bf((1.0 + 0.1 * np.random.standard_normal(RD)) * s),
        "phi": bf(1.5 * np.random.standard_normal((RD, M)) / np.sqrt(RD) / s[:, None]),
        "bm": bf(0.5 * np.random.standard_normal(M)),
        "gf": bf((1.0 + 0.1 * np.random.standard_normal(D)) * t),
        "w": bf(np.random.standard_normal((D, D)) / np.sqrt(D) / t[:, None]),
    }


def core(x, gn, phi, bm, gf, w):
    x = f64(x)
    b, s, r, d = x.shape

    xf = x.reshape(b, s, r * d)
    xn = xf * f64(gn)

    t = (mxq(xn, 2, "e4m3") @ mxq(f64(phi), 0, "e4m3")) + f64(bm)
    t = t.reshape(b, s, G, K)

    pre = sigmoid(t[..., 0:r])
    post = 2.0 * sigmoid(t[..., r:2 * r])
    l = t[..., 2 * r:].reshape(b, s, G, r, r)

    q = balance(l)

    xg = x.reshape(b, s, r, G, C)
    u = read_streams(pre, xg).reshape(b, s, d)

    ug = u * f64(gf)

    h = np.maximum(mxq(ug, 2, "e4m3") @ mxq(f64(w), 0, "e4m3"), 0.0)
    f = h * h
    fg = f.reshape(b, s, G, C)

    mixed = mix_streams(q, xg)
    post_i = np.transpose(post, (0, 1, 3, 2))
    y = mixed + post_i[..., None] * fg[:, :, None]
    return y.reshape(b, s, r, d)


def e4m3fn_bytes(y):
    return np.clip(np.asarray(y, np.float64), -448.0, 448.0).astype(np.float32).astype(ml_dtypes.float8_e4m3fn).view(np.uint8)


def e4m3fn_values(b):
    return np.asarray(b, np.uint8).view(ml_dtypes.float8_e4m3fn).astype(np.float64)


def setup_inputs():
    d = draw0()
    x0 = np.asarray(d['phi']).astype(np.float64)
    s = (np.max(np.abs(x0), axis=(1,), keepdims=True) / 448.0).astype(np.float32)
    out = {}
    for k, v in d.items():
        if k == 'phi':
            out['phi_bytes'] = e4m3fn_bytes(x0 / s.astype(np.float64))
            out['phi_scale'] = s
        else:
            out[k] = v
    return out


def reference(x, gn, phi_bytes, phi_scale, bm, gf, w):
    return core(x, gn, e4m3fn_values(phi_bytes) * phi_scale.astype(np.float64), bm, gf, w)

@@ -1,0 +1,340 @@
+from contextlib import ExitStack
+
+import concourse.mybir as mybir
+from concourse.masks import make_identity
+
+F32 = mybir.dt.float32
+BF16 = mybir.dt.bfloat16
+U32 = mybir.dt.uint32
+U8 = mybir.dt.uint8
+FP8 = mybir.dt.float8_e4m3fn
+FP8X4 = mybir.dt.float8_e4m3fn_x4
+ACT = mybir.ActivationFunctionType
+ALU = mybir.AluOpType
+AX = mybir.AxisListType
+
+P = 128
+T = 4
+R = 4
+D = 512
+G = 16
+C = 32
+KC = 24
+M = G * KC
+TOK = 1024
+NT = TOK // P
+FLOPS = 2 * TOK * R * D * M + 2 * TOK * D * D
+
+SCALAR_PAIRS = ((0, 2), (0, 3), (1, 2), (1, 3), (2, 2), (2, 3), (3, 2), (3, 3))
+
+
+def spread(ap, axis, n):
+    shape = list(ap.shape)
+    shape.insert(axis, n)
+    return ap.unsqueeze(axis).to_broadcast(shape)
+
+
+def tile_groupedmanifoldhyperconnection_kernel(tc, x, gn, phi_bytes, phi_scale, bm, gf, w, out):
+    nc = tc.nc
+    x_rows = x.rearrange("b s r d -> (b s) (r d)")
+    out_rows = out.rearrange("b s r d -> (b s) r d")
+    with ExitStack() as ctx:
+        keep = ctx.enter_context(tc.tile_pool(name="keep", bufs=1))
+        sb = ctx.enter_context(tc.tile_pool(name="sb", bufs=2))
+        ps = ctx.enter_context(tc.psum_pool(name="ps", bufs=1))
+
+        ident = keep.tile([P, P], F32)
+        make_identity(nc, ident[:])
+
+        scale = keep.tile([P, R, T], F32)
+        nc.sync.dma_start(out=scale[:], in_=phi_scale.rearrange("(r p t) o -> p r (t o)", p=P, t=T))
+        phb = keep.tile([P, R, T, M], U8)
+        phv = phi_bytes.rearrange("(r p t) n -> r p t n", p=P, t=T)
+        for r in range(R):
+            nc.sync.dma_start(out=phb[:, r, :, :], in_=phv[r])
+        xs = []
+        gns = keep.tile([P, R, T], BF16)
+        gfs = keep.tile([P, T], BF16)
+        bmz = keep.tile([P, M], BF16)
+        wraw = keep.tile([P, T, D], BF16)
+        nc.gpsimd.memset(bmz[:], 0.0)
+        for n in range(NT):
+            xt = keep.tile([P, R * D], BF16, name="x%d" % n)
+            nc.sync.dma_start(out=xt[:], in_=x_rows[n * P : (n + 1) * P, :])
+            xs.append(xt)
+            if n == 0:
+                nc.sync.dma_start(out=gns[:], in_=gn.rearrange("(r p t) -> p r t", p=P, t=T))
+                nc.sync.dma_start(out=bmz[0:1, :], in_=bm.rearrange("(o n) -> o n", o=1))
+            if n == 1:
+                nc.sync.dma_start(out=wraw[:], in_=w.rearrange("(p t) n -> p t n", t=T))
+                nc.sync.dma_start(out=gfs[:], in_=gf.rearrange("(p t) -> p t", t=T))
+
+        sig = keep.tile([P, 2], F32)
+        nc.gpsimd.memset(sig[0:64, :], 0.5)
+        nc.gpsimd.memset(sig[64:128, :], 1.0)
+
+        phc = keep.tile([P, R, M], U32, align_bytes=64)
+        phs = keep.tile([P, R, M], U8, align_bytes=64)
+        for r in range(R):
+            phw = sb.tile([P, T, M], BF16, name="phw")
+            for t in range(T):
+                src = phb[:, r, t, :].bitcast(FP8)
+                col = scale[:, r, t : t + 1]
+                if t % 2 == 0:
+                    nc.vector.tensor_scalar(phw[:, t, :], src, col, None, op0=ALU.mult)
+                else:
+                    nc.scalar.activation(phw[:, t, :], src, ACT.Copy, scale=col)
+            phg = sb.tile([P, M, T], BF16, name="phg", align_bytes=64)
+            nc.vector.tensor_copy(
+                out=phg[:].rearrange("p (k g) t -> p k g t", g=G),
+                in_=phw[:].rearrange("p t (g k) -> p k g t", g=G),
+            )
+            flat = phg[:].rearrange("p n t -> p (n t)")
+            nc.vector.quantize_mx(out=phc[:, r, 0:128].bitcast(FP8X4), scales=phs[:, r, 0:128], in_=flat[:, 0:512])
+            nc.vector.quantize_mx(out=phc[:, r, 128:384].bitcast(FP8X4), scales=phs[:, r, 128:384], in_=flat[:, 512:1536])
+
+        bmp = keep.tile([P, M], F32)
+        nc.scalar.copy(
+            out=bmp[:].rearrange("p (k g) -> p k g", g=G), in_=bmz[:].rearrange("p (g k) -> p k g", g=G)
+        )
+        bps = ps.tile([P, 3, P], F32, name="ct")
+        for m in range(3):
+            nc.tensor.transpose(bps[:, m, :], bmp[:, m * P : (m + 1) * P], ident[:])
+        bias = keep.tile([P, 3], F32)
+        nc.vector.tensor_copy(out=bias[:], in_=bps[:, :, 0])
+        hbias = keep.tile([P, 1], F32)
+        nc.vector.tensor_scalar(hbias[:], bias[:, 0:1], 0.5, None, op0=ALU.mult)
+
+        wg = keep.tile([P, D, T], BF16, align_bytes=64)
+        nc.scalar.copy(out=wg[:], in_=wraw[:].rearrange("p t n -> p n t"))
+        wc = keep.tile([P, D], U32, align_bytes=64)
+        ws = keep.tile([P, D], U8, align_bytes=64)
+        nc.vector.quantize_mx(out=wc[:].bitcast(FP8X4), scales=ws[:], in_=wg[:].rearrange("p n t -> p (n t)"))
+
+        state = [dict() for n in range(NT)]
+
+        def a_load(n, half):
+            st = state[n]
+            words = xs[n][:].bitcast(F32)
+            if half == 0:
+                st["xn"] = sb.tile([P, R, P, T], BF16, name="xn", align_bytes=64)
+            xn = st["xn"]
+            xp = ps.tile([P, 2, 2, P], F32, name="xp", bufs=2)
+            for rr in range(2):
+                r = 2 * half + rr
+                for u in range(2):
+                    nc.tensor.transpose(xp[:, rr, u, :], words[:, 256 * r + u : 256 * (r + 1) : 2], ident[:])
+            for rr in range(2):
+                r = 2 * half + rr
+                nc.vector.tensor_tensor(
+                    out=xn[:, r, :, :].rearrange("p k (u e) -> p k u e", e=2),
+                    in0=xp[:, rr, :, :].rearrange("p u k -> p (u k)").bitcast(BF16).rearrange(
+                        "p (u k e) -> p k u e", u=2, e=2
+                    ),
+                    in1=spread(gns[:, r, :].rearrange("p (u e) -> p u e", e=2), 1, P),
+                    op=ALU.mult,
+                )
+
+        def a_quant(n):
+            st = state[n]
+            xqc = sb.tile([P, R, P], U32, name="xqc", align_bytes=64)
+            xqs = sb.tile([P, R, P], U8, name="xqs", align_bytes=64)
+            nc.vector.quantize_mx(
+                out=xqc[:].rearrange("p r k -> p (r k)").bitcast(FP8X4),
+                scales=xqs[:].rearrange("p r k -> p (r k)"),
+                in_=st["xn"][:].rearrange("p r k t -> p (r k t)"),
+            )
+            st["xq"] = (xqc, xqs)
+
+        def a_coef(n):
+            st = state[n]
+            xqc, xqs = st["xq"]
+            tt = ps.tile([P, 3, P], F32, name="ct")
+            for m in range(3):
+                for r in range(R):
+                    nc.tensor.matmul_mx(
+                        out=tt[:, m, :],
+                        lhsT=phc[:, r, m * P : (m + 1) * P].bitcast(FP8X4),
+                        lhsT_scale=phs[:, r, m * P : (m + 1) * P],
+                        rhs=xqc[:, r, :].bitcast(FP8X4),
+                        rhs_scale=xqs[:, r, :],
+                        start=(r == 0),
+                        stop=(r == R - 1),
+                    )
+            co = sb.tile([P, 3, P], F32, name="co")
+            for m in (1, 2):
+                nc.scalar.activation(co[:, m, :], tt[:, m, :], ACT.Exp, bias=bias[:, m : m + 1])
+            nc.scalar.activation(co[:, 0, :], tt[:, 0, :], ACT.Tanh, bias=hbias[:], scale=0.5)
+            cs = sb.tile([P, P], F32, name="cs")
+            nc.vector.tensor_scalar(cs[:], co[:, 0, :], sig[:, 0:1], sig[:, 1:2], op0=ALU.mult, op1=ALU.add)
+            ee = ps.tile([P, 2, P], F32, name="ct")
+            for m in (1, 2):
+                nc.tensor.transpose(ee[:, m - 1, :], co[:, m, :], ident[:])
+            st["cs"] = cs
+            st["ee"] = ee
+
+        def s_first(n):
+            st = state[n]
+            ev = st["ee"][:].rearrange("p a (b c g) -> p (a b) c g", b=2, g=G)
+            q1 = sb.tile([P, R, R, G], F32, name="q1")
+            s = sb.tile([P, R, G], F32, name="s1")
+            v = sb.tile([P, R, G], F32, name="v1")
+            nc.vector.tensor_reduce(s[:], ev.rearrange("p i j g -> p i g j"), axis=AX.X, op=ALU.add)
+            nc.vector.reciprocal(v[:], s[:])
+            nc.vector.tensor_tensor(out=q1[:], in0=ev, in1=spread(v[:], 2, R), op=ALU.mult)
+            st["q"] = q1
+
+        def s_step(n, step):
+            st = state[n]
+            cur = st["q"]
+            s = sb.tile([P, R, G], F32, name="s%d" % (step + 2))
+            v = sb.tile([P, R, G], F32, name="v%d" % (step + 2))
+            nxt = sb.tile([P, R, R, G], F32, name="q%d" % (step + 2))
+            order, axis = ("p i j g -> p j g i", 1) if step % 2 == 0 else ("p i j g -> p i g j", 2)
+            nc.vector.tensor_reduce(s[:], cur[:].rearrange(order), axis=AX.X, op=ALU.add)
+            nc.vector.reciprocal(v[:], s[:])
+            nc.gpsimd.tensor_tensor(out=nxt[:], in0=cur[:], in1=spread(v[:], axis, R), op=ALU.mult)
+            st["q"] = nxt
+
+        def u_pp(n):
+            st = state[n]
+            pp = ps.tile([P, P], F32, name="pp")
+            nc.tensor.transpose(pp[:], st["cs"][:], ident[:])
+            st["pp"] = pp
+
+        def u_prod(n):
+            st = state[n]
+            xt = xs[n]
+            pp = st["pp"]
+            up = []
+            for r in range(R):
+                pr = sb.tile([P, T, P], F32, name="pu", bufs=5)
+                nc.vector.tensor_tensor(
+                    out=pr[:].rearrange("p t (g c) -> p t g c", g=G),
+                    in0=xt[:, r * D : (r + 1) * D].rearrange("p (g c t) -> p t g c", g=G, t=T),
+                    in1=spread(spread(pp[:, r * G : (r + 1) * G], 2, 8), 1, T),
+                    op=ALU.mult,
+                )
+                up.append(pr)
+            ut = ps.tile([P, T, P], F32, name="uh")
+            for t in range(T):
+                for r in range(R):
+                    nc.tensor.matmul(
+                        ut[:, t, :], up[r][:, t, :], ident[:], start=(r == 0), stop=(r == R - 1), is_transpose=True
+                    )
+            st["ut"] = ut
+
+        def u_quant(n):
+            st = state[n]
+            ug = sb.tile([P, P, T], BF16, name="ug", align_bytes=64)
+            nc.vector.tensor_tensor(
+                out=ug[:], in0=st["ut"][:].rearrange("p t k -> p k t"), in1=spread(gfs[:], 1, P), op=ALU.mult
+            )
+            ugc = sb.tile([P, P], U32, name="ugc", align_bytes=64)
+            ugs = sb.tile([P, P], U8, name="ugs", align_bytes=64)
+            nc.vector.quantize_mx(out=ugc[:].bitcast(FP8X4), scales=ugs[:], in_=ug[:].rearrange("p k t -> p (k t)"))
+            st["ugq"] = (ugc, ugs)
+
+        def u_h(n):
+            st = state[n]
+            ugc, ugs = st["ugq"]
+            h = ps.tile([P, D], F32, name="uh")
+            nc.tensor.matmul_mx(
+                out=h[:], lhsT=ugc[:].bitcast(FP8X4), lhsT_scale=ugs[:], rhs=wc[:].bitcast(FP8X4), rhs_scale=ws[:],
+                start=True, stop=True,
+            )
+            hr = sb.tile([P, D], F32, name="hr")
+            nc.scalar.activation(hr[:], h[:], ACT.Relu)
+            f = sb.tile([P, D], F32, name="f")
+            nc.scalar.activation(f[:], hr[:], ACT.Square)
+            st["f"] = f
+
+        def u_f(n):
+            st = state[n]
+            pp = st["pp"]
+            fi = []
+            for i in range(R):
+                pf = sb.tile([P, D], F32, name="pf", bufs=10)
+                nc.vector.tensor_tensor(
+                    out=pf[:].rearrange("p (g c) -> p g c", g=G),
+                    in0=st["f"][:].rearrange("p (g c) -> p g c", g=G),
+                    in1=spread(pp[:, (R + i) * G : (R + i + 1) * G], 2, C),
+                    op=ALU.mult,
+                )
+                fi.append(pf)
+            st["fi"] = fi
+
+        def y_prod(n, i):
+            st = state[n]
+            xt = xs[n]
+            q = st["q"]
+            prods = []
+            for j in range(R):
+                pq = sb.tile([P, D], F32, name="pq", bufs=24)
+                xj = xt[:, j * D : (j + 1) * D]
+                if (i, j) in SCALAR_PAIRS:
+                    for g in range(G):
+                        nc.scalar.activation(
+                            pq[:, g * C : (g + 1) * C], xj[:, g * C : (g + 1) * C], ACT.Copy, scale=q[:, i, j, g : g + 1]
+                        )
+                else:
+                    nc.gpsimd.tensor_tensor(
+                        out=pq[:].rearrange("p (g c) -> p g c", g=G),
+                        in0=xj.rearrange("p (g c) -> p g c", g=G),
+                        in1=spread(q[:, i, j, :], 2, C),
+                        op=ALU.mult,
+                    )
+                prods.append(pq)
+            st["prods%d" % i] = prods
+
+        def y_out(n, i):
+            st = state[n]
+            prods = st["prods%d" % i]
+            yt = ps.tile([P, 4, P], F32, name="yy", bufs=3)
+            for b in range(4):
+                for j in range(R):
+                    nc.tensor.matmul(
+                        yt[:, b, :], prods[j][:, b * P : (b + 1) * P], ident[:],
+                        start=(j == 0), stop=(j == R - 1), is_transpose=True,
+                    )
+            ys = sb.tile([P, 4, P], F32, name="ys", bufs=3)
+            nc.scalar.copy(out=ys[:], in_=yt[:])
+            yb = ps.tile([P, 4, P], F32, name="yy", bufs=3)
+            for b in range(4):
+                nc.tensor.transpose(yb[:, b, :], ys[:, b, :], ident[:])
+            yo = sb.tile([P, D], F32, name="yo", bufs=6)
+            nc.vector.tensor_tensor(
+                out=yo[:], in0=yb[:].rearrange("p b k -> p (b k)"), in1=st["fi"][i][:], op=ALU.add
+            )
+            nc.sync.dma_start(out=out_rows[n * P : (n + 1) * P, i, :], in_=yo[:])
+
+        def do(fn, n, *args):
+            if 0 <= n < NT:
+                fn(n, *args)
+
+        for k in range(-2, NT):
+            if k >= 0:
+                y_prod(k, 0)
+            do(u_pp, k + 1)
+            do(u_prod, k + 1)
+            do(a_load, k + 2, 0)
+            if k >= 0:
+                y_prod(k, 1)
+                y_out(k, 0)
+            do(u_quant, k + 1)
+            do(a_load, k + 2, 1)
+            if k >= 0:
+                y_prod(k, 2)
+                y_out(k, 1)
+            do(u_h, k + 1)
+            do(a_quant, k + 2)
+            do(a_coef, k + 2)
+            do(s_first, k + 2)
+            if k >= 0:
+                y_prod(k, 3)
+                y_out(k, 2)
+            do(u_f, k + 1)
+            for step in range(3):
+                do(s_step, k + 2, step)
+            if k >= 0:
+                y_out(k, 3)

@@ -23,9 +23,9 @@ KC = 24
 M = G * KC
 TOK = 1024
 NT = TOK // P
+QUAD = 4
+NQ = G // QUAD
 FLOPS = 2 * TOK * R * D * M + 2 * TOK * D * D
-
-SCALAR_PAIRS = ((0, 2), (0, 3), (1, 2), (1, 3), (2, 2), (2, 3), (3, 2), (3, 3))
 
 
 def spread(ap, axis, n):
@@ -37,105 +37,121 @@ def spread(ap, axis, n):
 def tile_groupedmanifoldhyperconnection_kernel(tc, x, gn, phi_bytes, phi_scale, bm, gf, w, out):
     nc = tc.nc
     x_rows = x.rearrange("b s r d -> (b s) (r d)")
-    out_rows = out.rearrange("b s r d -> (b s) r d")
+    out_view = out.rearrange("b (n tb t) i (q c) -> (b n) i q t tb c", tb=4, t=32, q=NQ)
     with ExitStack() as ctx:
         keep = ctx.enter_context(tc.tile_pool(name="keep", bufs=1))
         sb = ctx.enter_context(tc.tile_pool(name="sb", bufs=2))
         ps = ctx.enter_context(tc.psum_pool(name="ps", bufs=1))
+        ctx.enter_context(tc.manual_schedule())
 
         ident = keep.tile([P, P], F32)
+        bmz = keep.tile([P, M], BF16)
+        nc.gpsimd.memset(bmz[:], 0.0)
         make_identity(nc, ident[:])
 
         scale = keep.tile([P, R, T], F32)
-        nc.sync.dma_start(out=scale[:], in_=phi_scale.rearrange("(r p t) o -> p r (t o)", p=P, t=T))
-        phb = keep.tile([P, R, T, M], U8)
         phv = phi_bytes.rearrange("(r p t) n -> r p t n", p=P, t=T)
-        for r in range(R):
-            nc.sync.dma_start(out=phb[:, r, :, :], in_=phv[r])
-        xs = []
+        phb = [keep.tile([P, T, M], U8, name="phb%d" % r) for r in range(R)]
+        xs = [keep.tile([P, R * D], BF16, name="x%d" % n) for n in range(NT)]
         gns = keep.tile([P, R, T], BF16)
         gfs = keep.tile([P, T], BF16)
-        bmz = keep.tile([P, M], BF16)
         wraw = keep.tile([P, T, D], BF16)
-        nc.gpsimd.memset(bmz[:], 0.0)
-        for n in range(NT):
-            xt = keep.tile([P, R * D], BF16, name="x%d" % n)
-            nc.sync.dma_start(out=xt[:], in_=x_rows[n * P : (n + 1) * P, :])
-            xs.append(xt)
-            if n == 0:
-                nc.sync.dma_start(out=gns[:], in_=gn.rearrange("(r p t) -> p r t", p=P, t=T))
-                nc.sync.dma_start(out=bmz[0:1, :], in_=bm.rearrange("(o n) -> o n", o=1))
-            if n == 1:
-                nc.sync.dma_start(out=wraw[:], in_=w.rearrange("(p t) n -> p t n", t=T))
-                nc.sync.dma_start(out=gfs[:], in_=gf.rearrange("(p t) -> p t", t=T))
 
-        sig = keep.tile([P, 2], F32)
-        nc.gpsimd.memset(sig[0:64, :], 0.5)
-        nc.gpsimd.memset(sig[64:128, :], 1.0)
+        def load_x(n):
+            nc.sync.dma_start(out=xs[n][:], in_=x_rows[n * P : (n + 1) * P, :])
+
+        nc.sync.dma_start(out=scale[:], in_=phi_scale.rearrange("(r p t) o -> p r (t o)", p=P, t=T))
+        nc.sync.dma_start(out=phb[0][:], in_=phv[0])
+        nc.sync.dma_start(out=phb[1][:], in_=phv[1])
+        load_x(0)
+        nc.sync.dma_start(out=gns[:], in_=gn.rearrange("(r p t) -> p r t", p=P, t=T))
+        nc.sync.dma_start(out=phb[2][:], in_=phv[2])
+        nc.sync.dma_start(out=phb[3][:], in_=phv[3])
+        nc.sync.dma_start(out=bmz[0:1, :], in_=bm.rearrange("(o n) -> o n", o=1))
+        load_x(1)
+        nc.sync.dma_start(out=wraw[:], in_=w.rearrange("(p t) n -> p t n", t=T))
+        nc.sync.dma_start(out=gfs[:], in_=gf.rearrange("(p t) -> p t", t=T))
+        for n in range(2, NT):
+            load_x(n)
 
         phc = keep.tile([P, R, M], U32, align_bytes=64)
         phs = keep.tile([P, R, M], U8, align_bytes=64)
-        for r in range(R):
-            phw = sb.tile([P, T, M], BF16, name="phw")
-            for t in range(T):
-                src = phb[:, r, t, :].bitcast(FP8)
-                col = scale[:, r, t : t + 1]
-                if t % 2 == 0:
-                    nc.vector.tensor_scalar(phw[:, t, :], src, col, None, op0=ALU.mult)
-                else:
-                    nc.scalar.activation(phw[:, t, :], src, ACT.Copy, scale=col)
-            phg = sb.tile([P, M, T], BF16, name="phg", align_bytes=64)
-            nc.vector.tensor_copy(
-                out=phg[:].rearrange("p (k g) t -> p k g t", g=G),
-                in_=phw[:].rearrange("p t (g k) -> p k g t", g=G),
-            )
-            flat = phg[:].rearrange("p n t -> p (n t)")
-            nc.vector.quantize_mx(out=phc[:, r, 0:128].bitcast(FP8X4), scales=phs[:, r, 0:128], in_=flat[:, 0:512])
-            nc.vector.quantize_mx(out=phc[:, r, 128:384].bitcast(FP8X4), scales=phs[:, r, 128:384], in_=flat[:, 512:1536])
-
-        bmp = keep.tile([P, M], F32)
-        nc.scalar.copy(
-            out=bmp[:].rearrange("p (k g) -> p k g", g=G), in_=bmz[:].rearrange("p (g k) -> p k g", g=G)
-        )
-        bps = ps.tile([P, 3, P], F32, name="ct")
-        for m in range(3):
-            nc.tensor.transpose(bps[:, m, :], bmp[:, m * P : (m + 1) * P], ident[:])
+        phw = [keep.tile([P, T, M], BF16, name="phw%d" % r) for r in range(R)]
+        phg = [keep.tile([P, M, T], BF16, name="phg%d" % r, align_bytes=64) for r in range(R)]
         bias = keep.tile([P, 3], F32)
-        nc.vector.tensor_copy(out=bias[:], in_=bps[:, :, 0])
         hbias = keep.tile([P, 1], F32)
-        nc.vector.tensor_scalar(hbias[:], bias[:, 0:1], 0.5, None, op0=ALU.mult)
-
+        gfh = keep.tile([P, T], F32)
         wg = keep.tile([P, D, T], BF16, align_bytes=64)
-        nc.scalar.copy(out=wg[:], in_=wraw[:].rearrange("p t n -> p n t"))
         wc = keep.tile([P, D], U32, align_bytes=64)
         ws = keep.tile([P, D], U8, align_bytes=64)
-        nc.vector.quantize_mx(out=wc[:].bitcast(FP8X4), scales=ws[:], in_=wg[:].rearrange("p n t -> p (n t)"))
+
+        def phi_widen(r, t, engine):
+            src = phb[r][:, t, :].bitcast(FP8)
+            col = scale[:, r, t : t + 1]
+            if engine == "vector":
+                nc.vector.tensor_scalar(phw[r][:, t, :], src, col, None, op0=ALU.mult)
+            else:
+                nc.scalar.activation(phw[r][:, t, :], src, ACT.Copy, scale=col)
+
+        def phi_group(r):
+            src = phw[r][:].rearrange("p t (g k) -> p g t k", g=G)
+            for lo, hi, col in ((0, 8, 0), (8, KC, P)):
+                n = hi - lo
+                nc.vector.tensor_copy(
+                    out=phg[r][:, col : col + G * n, :].rearrange("p (g a i) t -> p g a t i", g=G, i=4),
+                    in_=src[:, :, :, lo:hi].rearrange("p g t (a i) -> p g a t i", i=4),
+                )
+
+        def phi_quant(r):
+            nc.vector.quantize_mx(
+                out=phc[:, r, :].bitcast(FP8X4), scales=phs[:, r, :], in_=phg[r][:].rearrange("p n t -> p (n t)")
+            )
+
+        def bias_setup():
+            bmp = keep.tile([P, M], F32)
+            src = bmz[:].rearrange("p (g k) -> p g k", g=G)
+            nc.scalar.copy(out=bmp[:, 0:P].rearrange("p (g k) -> p g k", g=G), in_=src[:, :, 0:8])
+            nc.scalar.copy(out=bmp[:, P:M].rearrange("p (g k) -> p g k", g=G), in_=src[:, :, 8:KC])
+            bps = ps.tile([P, 3, P], F32, name="tt")
+            for m in range(3):
+                nc.tensor.transpose(bps[:, m, :], bmp[:, m * P : (m + 1) * P], ident[:])
+            nc.scalar.copy(out=bias[:], in_=bps[:, :, 0])
+            nc.scalar.activation(hbias[:], bps[:, 0, 0:1], ACT.Copy, scale=0.5)
+
+        def w_group():
+            nc.scalar.copy(
+                out=wg[:].rearrange("p (c i) t -> p c t i", i=4), in_=wraw[:].rearrange("p t (c i) -> p c t i", i=4)
+            )
+            nc.scalar.activation(gfh[:], gfs[:], ACT.Copy, scale=0.5)
+
+        def w_quant():
+            nc.vector.quantize_mx(out=wc[:].bitcast(FP8X4), scales=ws[:], in_=wg[:].rearrange("p n t -> p (n t)"))
 
         state = [dict() for n in range(NT)]
 
-        def a_load(n, half):
-            st = state[n]
+        def x_turn(n, half):
             words = xs[n][:].bitcast(F32)
-            if half == 0:
-                st["xn"] = sb.tile([P, R, P, T], BF16, name="xn", align_bytes=64)
-            xn = st["xn"]
             xp = ps.tile([P, 2, 2, P], F32, name="xp", bufs=2)
             for rr in range(2):
                 r = 2 * half + rr
                 for u in range(2):
                     nc.tensor.transpose(xp[:, rr, u, :], words[:, 256 * r + u : 256 * (r + 1) : 2], ident[:])
-            for rr in range(2):
-                r = 2 * half + rr
-                nc.vector.tensor_tensor(
-                    out=xn[:, r, :, :].rearrange("p k (u e) -> p k u e", e=2),
-                    in0=xp[:, rr, :, :].rearrange("p u k -> p (u k)").bitcast(BF16).rearrange(
-                        "p (u k e) -> p k u e", u=2, e=2
-                    ),
-                    in1=spread(gns[:, r, :].rearrange("p (u e) -> p u e", e=2), 1, P),
-                    op=ALU.mult,
-                )
+            state[n]["xp", half] = xp
 
-        def a_quant(n):
+        def x_gain(n, r):
+            st = state[n]
+            if r == 0:
+                st["xn"] = sb.tile([P, R, P, T], BF16, name="xn", align_bytes=64)
+            nc.vector.tensor_tensor(
+                out=st["xn"][:, r, :, :].rearrange("p k (u e) -> p k u e", e=2),
+                in0=st["xp", r // 2][:, r % 2, :, :].rearrange("p u k -> p (u k)").bitcast(BF16).rearrange(
+                    "p (u k e) -> p k u e", u=2, e=2
+                ),
+                in1=spread(gns[:, r, :].rearrange("p (u e) -> p u e", e=2), 1, P),
+                op=ALU.mult,
+            )
+
+        def x_quant(n):
             st = state[n]
             xqc = sb.tile([P, R, P], U32, name="xqc", align_bytes=64)
             xqs = sb.tile([P, R, P], U8, name="xqs", align_bytes=64)
@@ -146,11 +162,11 @@ def tile_groupedmanifoldhyperconnection_kernel(tc, x, gn, phi_bytes, phi_scale, 
             )
             st["xq"] = (xqc, xqs)
 
-        def a_coef(n):
+        def coef_mm(n):
             st = state[n]
             xqc, xqs = st["xq"]
-            tt = ps.tile([P, 3, P], F32, name="ct")
-            for m in range(3):
+            tt = ps.tile([P, 3, P], F32, name="tt")
+            for m in (1, 2, 0):
                 for r in range(R):
                     nc.tensor.matmul_mx(
                         out=tt[:, m, :],
@@ -161,81 +177,89 @@ def tile_groupedmanifoldhyperconnection_kernel(tc, x, gn, phi_bytes, phi_scale, 
                         start=(r == 0),
                         stop=(r == R - 1),
                     )
+            st["tt"] = tt
+
+        def coef_act(n):
+            st = state[n]
+            tt = st["tt"]
             co = sb.tile([P, 3, P], F32, name="co")
+            th = sb.tile([P, P], F32, name="th")
             for m in (1, 2):
                 nc.scalar.activation(co[:, m, :], tt[:, m, :], ACT.Exp, bias=bias[:, m : m + 1])
-            nc.scalar.activation(co[:, 0, :], tt[:, 0, :], ACT.Tanh, bias=hbias[:], scale=0.5)
-            cs = sb.tile([P, P], F32, name="cs")
-            nc.vector.tensor_scalar(cs[:], co[:, 0, :], sig[:, 0:1], sig[:, 1:2], op0=ALU.mult, op1=ALU.add)
-            ee = ps.tile([P, 2, P], F32, name="ct")
-            for m in (1, 2):
-                nc.tensor.transpose(ee[:, m - 1, :], co[:, m, :], ident[:])
-            st["cs"] = cs
-            st["ee"] = ee
+            nc.scalar.activation(th[:], tt[:, 0, :], ACT.Tanh, bias=hbias[:], scale=0.5)
+            nc.scalar.activation(co[:, 0, :], th[:], ACT.Identity, bias=1.0)
+            st["co"] = co
 
-        def s_first(n):
+        def coef_turn(n):
             st = state[n]
-            ev = st["ee"][:].rearrange("p a (b c g) -> p (a b) c g", b=2, g=G)
-            q1 = sb.tile([P, R, R, G], F32, name="q1")
-            s = sb.tile([P, R, G], F32, name="s1")
-            v = sb.tile([P, R, G], F32, name="v1")
-            nc.vector.tensor_reduce(s[:], ev.rearrange("p i j g -> p i g j"), axis=AX.X, op=ALU.add)
-            nc.vector.reciprocal(v[:], s[:])
-            nc.vector.tensor_tensor(out=q1[:], in0=ev, in1=spread(v[:], 2, R), op=ALU.mult)
-            st["q"] = q1
+            ct = ps.tile([P, 3, P], F32, name="ct", bufs=2)
+            for m in (1, 2, 0):
+                nc.tensor.transpose(ct[:, m, :], st["co"][:, m, :], ident[:])
+            st["e"] = ct[:, 1:3, :].rearrange("p m (g i j) -> p (m g) i j", i=R, j=R)
+            st["gate"] = ct[:, 0, :].rearrange("p (g k) -> p g k", g=G)
 
-        def s_step(n, step):
+        def sink_sum(n):
             st = state[n]
-            cur = st["q"]
-            s = sb.tile([P, R, G], F32, name="s%d" % (step + 2))
-            v = sb.tile([P, R, G], F32, name="v%d" % (step + 2))
-            nxt = sb.tile([P, R, R, G], F32, name="q%d" % (step + 2))
-            order, axis = ("p i j g -> p j g i", 1) if step % 2 == 0 else ("p i j g -> p i g j", 2)
-            nc.vector.tensor_reduce(s[:], cur[:].rearrange(order), axis=AX.X, op=ALU.add)
-            nc.vector.reciprocal(v[:], s[:])
-            nc.gpsimd.tensor_tensor(out=nxt[:], in0=cur[:], in1=spread(v[:], axis, R), op=ALU.mult)
-            st["q"] = nxt
+            s = sb.tile([P, G, R], F32, name="sums")
+            nc.vector.tensor_reduce(s[:], st.get("scaled", st["e"]), axis=AX.X, op=ALU.add)
+            st["sums"] = s
 
-        def u_pp(n):
+        def sink_inv(n):
             st = state[n]
-            pp = ps.tile([P, P], F32, name="pp")
-            nc.tensor.transpose(pp[:], st["cs"][:], ident[:])
-            st["pp"] = pp
+            v = sb.tile([P, G, R], F32, name="factor")
+            nc.vector.reciprocal(v[:], st["sums"][:])
+            st["factor"] = v
 
-        def u_prod(n):
+        def sink_scale(n, by_row):
             st = state[n]
-            xt = xs[n]
-            pp = st["pp"]
-            up = []
-            for r in range(R):
-                pr = sb.tile([P, T, P], F32, name="pu", bufs=5)
-                nc.vector.tensor_tensor(
-                    out=pr[:].rearrange("p t (g c) -> p t g c", g=G),
-                    in0=xt[:, r * D : (r + 1) * D].rearrange("p (g c t) -> p t g c", g=G, t=T),
-                    in1=spread(spread(pp[:, r * G : (r + 1) * G], 2, 8), 1, T),
-                    op=ALU.mult,
-                )
-                up.append(pr)
+            scaled = sb.tile([P, G, R, R], F32, name="scaled")
+            e = st["e"].rearrange("p g i j -> p g j i") if by_row else st["e"]
+            nc.vector.tensor_tensor(out=scaled[:], in0=e, in1=spread(st["factor"][:], 2, R), op=ALU.mult)
+            st["scaled"] = scaled[:]
+
+        def sink_last(n):
+            st = state[n]
+            q = sb.tile([P, G, R, R], F32, name="q")
+            nc.vector.tensor_tensor(out=q[:], in0=st["scaled"], in1=spread(st["factor"][:], 3, R), op=ALU.mult)
+            st["q"] = q
+
+        def pre_prod(n, r):
+            st = state[n]
+            pr = sb.tile([P, T, P], F32, name="pu", bufs=6)
+            nc.vector.tensor_tensor(
+                out=pr[:].rearrange("p t (g c) -> p t g c", g=G),
+                in0=xs[n][:, r * D : (r + 1) * D].rearrange("p (g c t) -> p t g c", g=G, t=T),
+                in1=spread(spread(st["gate"][:, :, r], 2, 8), 1, T),
+                op=ALU.mult,
+            )
+            st["pu", r] = pr
+
+        def u_sum(n):
+            st = state[n]
             ut = ps.tile([P, T, P], F32, name="uh")
             for t in range(T):
                 for r in range(R):
                     nc.tensor.matmul(
-                        ut[:, t, :], up[r][:, t, :], ident[:], start=(r == 0), stop=(r == R - 1), is_transpose=True
+                        ut[:, t, :], st["pu", r][:, t, :], ident[:], start=(r == 0), stop=(r == R - 1), is_transpose=True
                     )
             st["ut"] = ut
 
-        def u_quant(n):
+        def u_gain(n):
             st = state[n]
             ug = sb.tile([P, P, T], BF16, name="ug", align_bytes=64)
             nc.vector.tensor_tensor(
-                out=ug[:], in0=st["ut"][:].rearrange("p t k -> p k t"), in1=spread(gfs[:], 1, P), op=ALU.mult
+                out=ug[:], in0=st["ut"][:].rearrange("p t k -> p k t"), in1=spread(gfh[:], 1, P), op=ALU.mult
             )
+            st["ug"] = ug
+
+        def u_quant(n):
+            st = state[n]
             ugc = sb.tile([P, P], U32, name="ugc", align_bytes=64)
             ugs = sb.tile([P, P], U8, name="ugs", align_bytes=64)
-            nc.vector.quantize_mx(out=ugc[:].bitcast(FP8X4), scales=ugs[:], in_=ug[:].rearrange("p k t -> p (k t)"))
+            nc.vector.quantize_mx(out=ugc[:].bitcast(FP8X4), scales=ugs[:], in_=st["ug"][:].rearrange("p k t -> p (k t)"))
             st["ugq"] = (ugc, ugs)
 
-        def u_h(n):
+        def branch_mm(n):
             st = state[n]
             ugc, ugs = st["ugq"]
             h = ps.tile([P, D], F32, name="uh")
@@ -243,98 +267,156 @@ def tile_groupedmanifoldhyperconnection_kernel(tc, x, gn, phi_bytes, phi_scale, 
                 out=h[:], lhsT=ugc[:].bitcast(FP8X4), lhsT_scale=ugs[:], rhs=wc[:].bitcast(FP8X4), rhs_scale=ws[:],
                 start=True, stop=True,
             )
+            st["h"] = h
+
+        def branch_act(n):
+            st = state[n]
+            post = sb.tile([P, G, R], F32, name="post")
+            nc.scalar.copy(out=post[:], in_=st["gate"][:, :, R : 2 * R])
             hr = sb.tile([P, D], F32, name="hr")
-            nc.scalar.activation(hr[:], h[:], ACT.Relu)
+            nc.scalar.activation(hr[:], st["h"][:], ACT.Relu)
             f = sb.tile([P, D], F32, name="f")
             nc.scalar.activation(f[:], hr[:], ACT.Square)
             st["f"] = f
+            st["post"] = post
 
-        def u_f(n):
+        def term(n, j, quad):
             st = state[n]
-            pp = st["pp"]
-            fi = []
-            for i in range(R):
-                pf = sb.tile([P, D], F32, name="pf", bufs=10)
-                nc.vector.tensor_tensor(
-                    out=pf[:].rearrange("p (g c) -> p g c", g=G),
-                    in0=st["f"][:].rearrange("p (g c) -> p g c", g=G),
-                    in1=spread(pp[:, (R + i) * G : (R + i + 1) * G], 2, C),
-                    op=ALU.mult,
-                )
-                fi.append(pf)
-            st["fi"] = fi
+            gs = slice(QUAD * quad, QUAD * (quad + 1))
+            if j < R:
+                src = xs[n][:, j * D : (j + 1) * D].rearrange("p (g c) -> p g c", g=G)
+                return src[:, gs, :], st["q"][:, gs, j, :]
+            return st["f"][:].rearrange("p (g c) -> p g c", g=G)[:, gs, :], st["post"][:, gs, :]
 
-        def y_prod(n, i):
-            st = state[n]
-            xt = xs[n]
-            q = st["q"]
-            prods = []
-            for j in range(R):
-                pq = sb.tile([P, D], F32, name="pq", bufs=24)
-                xj = xt[:, j * D : (j + 1) * D]
-                if (i, j) in SCALAR_PAIRS:
-                    for g in range(G):
-                        nc.scalar.activation(
-                            pq[:, g * C : (g + 1) * C], xj[:, g * C : (g + 1) * C], ACT.Copy, scale=q[:, i, j, g : g + 1]
-                        )
-                else:
-                    nc.gpsimd.tensor_tensor(
-                        out=pq[:].rearrange("p (g c) -> p g c", g=G),
-                        in0=xj.rearrange("p (g c) -> p g c", g=G),
-                        in1=spread(q[:, i, j, :], 2, C),
-                        op=ALU.mult,
-                    )
-                prods.append(pq)
-            st["prods%d" % i] = prods
+        def prod_scalar(n, j, quad):
+            src, wt = term(n, j, quad)
+            pq = sb.tile([P, QUAD, R, C], F32, name="pq", bufs=20)
+            for g in range(QUAD):
+                for i in range(R):
+                    nc.scalar.activation(pq[:, g, i, :], src[:, g, :], ACT.Copy, scale=wt[:, g, i : i + 1])
+            state[n]["prod", j, quad] = pq[:]
 
-        def y_out(n, i):
+        def prod_gpsimd(n, j, quad, count):
             st = state[n]
-            prods = st["prods%d" % i]
-            yt = ps.tile([P, 4, P], F32, name="yy", bufs=3)
-            for b in range(4):
-                for j in range(R):
-                    nc.tensor.matmul(
-                        yt[:, b, :], prods[j][:, b * P : (b + 1) * P], ident[:],
-                        start=(j == 0), stop=(j == R - 1), is_transpose=True,
-                    )
-            ys = sb.tile([P, 4, P], F32, name="ys", bufs=3)
-            nc.scalar.copy(out=ys[:], in_=yt[:])
-            yb = ps.tile([P, 4, P], F32, name="yy", bufs=3)
-            for b in range(4):
-                nc.tensor.transpose(yb[:, b, :], ys[:, b, :], ident[:])
-            yo = sb.tile([P, D], F32, name="yo", bufs=6)
-            nc.vector.tensor_tensor(
-                out=yo[:], in0=yb[:].rearrange("p b k -> p (b k)"), in1=st["fi"][i][:], op=ALU.add
+            gs = slice(QUAD * quad, QUAD * (quad + count))
+            src = xs[n][:, j * D : (j + 1) * D].rearrange("p (g c) -> p g c", g=G)[:, gs, :]
+            pg = sb.tile([P, 2 * QUAD, R, C], F32, name="pg", bufs=9)
+            nc.gpsimd.tensor_tensor(
+                out=pg[:, 0 : count * QUAD, :, :], in0=spread(src, 2, R), in1=spread(st["q"][:, gs, j, :], 3, C), op=ALU.mult
             )
-            nc.sync.dma_start(out=out_rows[n * P : (n + 1) * P, i, :], in_=yo[:])
+            for a in range(count):
+                st["prod", j, quad + a] = pg[:, a * QUAD : (a + 1) * QUAD, :, :]
+
+        def prod_vector(n, quad):
+            st = state[n]
+            src = term(n, R, quad)[0]
+            pq = sb.tile([P, QUAD, R, C], F32, name="pq", bufs=20)
+            wt = st["gate"][:, QUAD * quad : QUAD * (quad + 1), R : 2 * R]
+            nc.vector.tensor_tensor(out=pq[:], in0=spread(src, 2, R), in1=spread(wt, 3, C), op=ALU.mult)
+            st["prod", R, quad] = pq[:]
+
+        def y_sum(n, quad):
+            st = state[n]
+            yt = ps.tile([P, 4, QUAD, 32], F32, name="yy", bufs=2)
+            for b in range(QUAD):
+                for j in range(R + 1):
+                    nc.tensor.matmul(
+                        yt[:, :, b, :], st["prod", j, quad][:, b, :, :].rearrange("p i c -> p (i c)"), ident[:],
+                        start=(j == 0), stop=(j == R), is_transpose=True,
+                    )
+            st["yt", quad] = yt
+
+        def y_out(n, quad):
+            yo = sb.tile([P, D], F32, name="yo", bufs=6, align_bytes=64)
+            nc.vector.transpose(yo[:], state[n]["yt", quad][:].rearrange("p tb b t -> p (tb b t)"))
+            for i in range(R):
+                nc.sync.dma_start(
+                    out=out_view[n, i, quad], in_=yo[32 * i : 32 * (i + 1), :].rearrange("p (tb c) -> p tb c", tb=4)
+                )
 
         def do(fn, n, *args):
             if 0 <= n < NT:
                 fn(n, *args)
 
-        for k in range(-2, NT):
-            if k >= 0:
-                y_prod(k, 0)
-            do(u_pp, k + 1)
-            do(u_prod, k + 1)
-            do(a_load, k + 2, 0)
-            if k >= 0:
-                y_prod(k, 1)
-                y_out(k, 0)
+        phi_widen(0, 0, "vector")
+        phi_widen(0, 1, "vector")
+        phi_widen(0, 2, "scalar")
+        phi_widen(0, 3, "scalar")
+        for r in range(1, R):
+            for t in range(T):
+                phi_widen(r, t, "scalar")
+        x_turn(0, 0)
+        x_turn(0, 1)
+        phi_group(0)
+        x_gain(0, 0)
+        x_gain(0, 1)
+        phi_quant(0)
+        phi_group(1)
+        x_gain(0, 2)
+        x_gain(0, 3)
+        x_turn(1, 0)
+        x_turn(1, 1)
+        bias_setup()
+        phi_quant(1)
+        phi_group(2)
+        x_quant(0)
+        phi_group(3)
+        phi_quant(2)
+        phi_quant(3)
+
+        for k in range(-1, NT + 1):
+            do(coef_mm, k + 1)
+            do(branch_mm, k)
+            do(prod_gpsimd, k, 0, 0, 2)
+            do(y_out, k - 1, 1)
+            do(coef_act, k + 1)
+            if k == -1:
+                w_group()
+            for r in range(R):
+                do(x_gain, k + 2, r)
+            do(coef_turn, k + 1)
+            do(branch_act, k)
+            do(y_sum, k - 1, 2)
+            do(prod_gpsimd, k, 1, 0, 2)
+            do(sink_sum, k + 1)
+            do(prod_scalar, k, 2, 0)
+            do(pre_prod, k + 1, 0)
+            do(sink_inv, k + 1)
+            do(pre_prod, k + 1, 1)
+            do(sink_scale, k + 1, True)
+            do(y_sum, k - 1, 3)
+            do(prod_scalar, k, 3, 0)
+            do(y_out, k - 1, 2)
+            do(sink_sum, k + 1)
+            do(pre_prod, k + 1, 2)
+            do(prod_scalar, k, R, 0)
+            do(prod_gpsimd, k, 0, 2, 2)
+            do(sink_inv, k + 1)
+            do(pre_prod, k + 1, 3)
+            do(y_sum, k, 0)
+            do(sink_scale, k + 1, False)
+            do(y_out, k - 1, 3)
+            for j in (2, 3, R):
+                do(prod_scalar, k, j, 1)
+            do(u_sum, k + 1)
+            do(prod_gpsimd, k, 1, 2, 2)
+            do(sink_sum, k + 1)
+            do(prod_vector, k, 3)
+            do(sink_inv, k + 1)
+            do(y_sum, k, 1)
+            do(u_gain, k + 1)
+            do(sink_scale, k + 1, True)
+            do(y_out, k, 0)
+            do(x_turn, k + 3, 0)
+            do(x_turn, k + 3, 1)
+            for j in (2, 3, R):
+                do(prod_scalar, k, j, 2)
+            do(prod_gpsimd, k, 2, 3, 1)
+            do(prod_scalar, k, 3, 3)
+            do(sink_sum, k + 1)
+            do(sink_inv, k + 1)
+            if k == -1:
+                w_quant()
+            do(x_quant, k + 2)
             do(u_quant, k + 1)
-            do(a_load, k + 2, 1)
-            if k >= 0:
-                y_prod(k, 2)
-                y_out(k, 1)
-            do(u_h, k + 1)
-            do(a_quant, k + 2)
-            do(a_coef, k + 2)
-            do(s_first, k + 2)
-            if k >= 0:
-                y_prod(k, 3)
-                y_out(k, 2)
-            do(u_f, k + 1)
-            for step in range(3):
-                do(s_step, k + 2, step)
-            if k >= 0:
-                y_out(k, 3)
+            do(sink_last, k + 1)

@@ -25,6 +25,7 @@ TOK = 1024
 NT = TOK // P
 QUAD = 4
 NQ = G // QUAD
+PLAIN_EVERY = 16
 FLOPS = 2 * TOK * R * D * M + 2 * TOK * D * D
 
 
@@ -128,6 +129,12 @@ def tile_groupedmanifoldhyperconnection_kernel(tc, x, gn, phi_bytes, phi_scale, 
             nc.vector.quantize_mx(out=wc[:].bitcast(FP8X4), scales=ws[:], in_=wg[:].rearrange("p n t -> p (n t)"))
 
         state = [dict() for n in range(NT)]
+        passes = []
+
+        def add_turned(dst, src, start, stop):
+            passes.append(0)
+            plain = len(passes) % PLAIN_EVERY == 0
+            nc.tensor.matmul(dst, src, ident[:], start=start, stop=stop, is_transpose=not plain)
 
         def x_turn(n, half):
             words = xs[n][:].bitcast(F32)
@@ -198,30 +205,34 @@ def tile_groupedmanifoldhyperconnection_kernel(tc, x, gn, phi_bytes, phi_scale, 
             st["e"] = ct[:, 1:3, :].rearrange("p m (g i j) -> p (m g) i j", i=R, j=R)
             st["gate"] = ct[:, 0, :].rearrange("p (g k) -> p g k", g=G)
 
-        def sink_sum(n):
+        def sink_sum(n, lo=0, hi=G):
             st = state[n]
-            s = sb.tile([P, G, R], F32, name="sums")
-            nc.vector.tensor_reduce(s[:], st.get("scaled", st["e"]), axis=AX.X, op=ALU.add)
-            st["sums"] = s
+            s = sb.tile([P, hi - lo, R], F32, name="sums", bufs=4)
+            nc.vector.tensor_reduce(s[:], st.get(("scaled", lo), st["e"][:, lo:hi]), axis=AX.X, op=ALU.add)
+            st["sums", lo] = s
 
-        def sink_inv(n):
+        def sink_inv(n, lo=0, hi=G):
             st = state[n]
-            v = sb.tile([P, G, R], F32, name="factor")
-            nc.vector.reciprocal(v[:], st["sums"][:])
-            st["factor"] = v
+            v = sb.tile([P, hi - lo, R], F32, name="factor", bufs=4)
+            nc.vector.reciprocal(v[:], st["sums", lo][:])
+            st["factor", lo] = v
 
-        def sink_scale(n, by_row):
+        def sink_scale(n, by_row, lo=0, hi=G):
             st = state[n]
-            scaled = sb.tile([P, G, R, R], F32, name="scaled")
-            e = st["e"].rearrange("p g i j -> p g j i") if by_row else st["e"]
-            nc.vector.tensor_tensor(out=scaled[:], in0=e, in1=spread(st["factor"][:], 2, R), op=ALU.mult)
-            st["scaled"] = scaled[:]
+            scaled = sb.tile([P, hi - lo, R, R], F32, name="scaled", bufs=4)
+            e = st["e"][:, lo:hi]
+            if by_row:
+                e = e.rearrange("p g i j -> p g j i")
+            nc.vector.tensor_tensor(out=scaled[:], in0=e, in1=spread(st["factor", lo][:], 2, R), op=ALU.mult)
+            st["scaled", lo] = scaled[:]
 
-        def sink_last(n):
+        def sink_last(n, lo=0, hi=G):
             st = state[n]
-            q = sb.tile([P, G, R, R], F32, name="q")
-            nc.vector.tensor_tensor(out=q[:], in0=st["scaled"], in1=spread(st["factor"][:], 3, R), op=ALU.mult)
-            st["q"] = q
+            if lo == 0:
+                st["q"] = sb.tile([P, G, R, R], F32, name="q")
+            nc.vector.tensor_tensor(
+                out=st["q"][:, lo:hi], in0=st["scaled", lo], in1=spread(st["factor", lo][:], 3, R), op=ALU.mult
+            )
 
         def pre_prod(n, r):
             st = state[n]
@@ -239,9 +250,7 @@ def tile_groupedmanifoldhyperconnection_kernel(tc, x, gn, phi_bytes, phi_scale, 
             ut = ps.tile([P, T, P], F32, name="uh")
             for t in range(T):
                 for r in range(R):
-                    nc.tensor.matmul(
-                        ut[:, t, :], st["pu", r][:, t, :], ident[:], start=(r == 0), stop=(r == R - 1), is_transpose=True
-                    )
+                    add_turned(ut[:, t, :], st["pu", r][:, t, :], r == 0, r == R - 1)
             st["ut"] = ut
 
         def u_gain(n):
@@ -290,7 +299,7 @@ def tile_groupedmanifoldhyperconnection_kernel(tc, x, gn, phi_bytes, phi_scale, 
 
         def prod_scalar(n, j, quad):
             src, wt = term(n, j, quad)
-            pq = sb.tile([P, QUAD, R, C], F32, name="pq", bufs=20)
+            pq = sb.tile([P, QUAD, R, C], F32, name="pq", bufs=24)
             for g in range(QUAD):
                 for i in range(R):
                     nc.scalar.activation(pq[:, g, i, :], src[:, g, :], ACT.Copy, scale=wt[:, g, i : i + 1])
@@ -300,9 +309,9 @@ def tile_groupedmanifoldhyperconnection_kernel(tc, x, gn, phi_bytes, phi_scale, 
             st = state[n]
             gs = slice(QUAD * quad, QUAD * (quad + count))
             src = xs[n][:, j * D : (j + 1) * D].rearrange("p (g c) -> p g c", g=G)[:, gs, :]
-            pg = sb.tile([P, 2 * QUAD, R, C], F32, name="pg", bufs=9)
+            pg = sb.tile([P, count * QUAD, R, C], F32, name="pg" if count == 2 else "pq", bufs=8 if count == 2 else 24)
             nc.gpsimd.tensor_tensor(
-                out=pg[:, 0 : count * QUAD, :, :], in0=spread(src, 2, R), in1=spread(st["q"][:, gs, j, :], 3, C), op=ALU.mult
+                out=pg[:], in0=spread(src, 2, R), in1=spread(st["q"][:, gs, j, :], 3, C), op=ALU.mult
             )
             for a in range(count):
                 st["prod", j, quad + a] = pg[:, a * QUAD : (a + 1) * QUAD, :, :]
@@ -310,21 +319,19 @@ def tile_groupedmanifoldhyperconnection_kernel(tc, x, gn, phi_bytes, phi_scale, 
         def prod_vector(n, quad):
             st = state[n]
             src = term(n, R, quad)[0]
-            pq = sb.tile([P, QUAD, R, C], F32, name="pq", bufs=20)
+            pq = sb.tile([P, QUAD, R, C], F32, name="pq", bufs=24)
             wt = st["gate"][:, QUAD * quad : QUAD * (quad + 1), R : 2 * R]
             nc.vector.tensor_tensor(out=pq[:], in0=spread(src, 2, R), in1=spread(wt, 3, C), op=ALU.mult)
             st["prod", R, quad] = pq[:]
 
-        def y_sum(n, quad):
+        def y_sum(n, quad, lo=0, hi=QUAD):
             st = state[n]
-            yt = ps.tile([P, 4, QUAD, 32], F32, name="yy", bufs=2)
-            for b in range(QUAD):
+            if lo == 0:
+                st["yt", quad] = ps.tile([P, 4, QUAD, 32], F32, name="yy", bufs=2)
+            for b in range(lo, hi):
                 for j in range(R + 1):
-                    nc.tensor.matmul(
-                        yt[:, :, b, :], st["prod", j, quad][:, b, :, :].rearrange("p i c -> p (i c)"), ident[:],
-                        start=(j == 0), stop=(j == R), is_transpose=True,
-                    )
-            st["yt", quad] = yt
+                    src = st["prod", j, quad][:, b, :, :].rearrange("p i c -> p (i c)")
+                    add_turned(st["yt", quad][:, :, b, :], src, j == 0, j == R)
 
         def y_out(n, quad):
             yo = sb.tile([P, D], F32, name="yo", bufs=6, align_bytes=64)
@@ -357,6 +364,7 @@ def tile_groupedmanifoldhyperconnection_kernel(tc, x, gn, phi_bytes, phi_scale, 
         x_turn(1, 0)
         x_turn(1, 1)
         bias_setup()
+        w_group()
         phi_quant(1)
         phi_group(2)
         x_quant(0)
@@ -364,59 +372,99 @@ def tile_groupedmanifoldhyperconnection_kernel(tc, x, gn, phi_bytes, phi_scale, 
         phi_quant(2)
         phi_quant(3)
 
-        for k in range(-1, NT + 1):
-            do(coef_mm, k + 1)
+        coef_mm(0)
+        coef_act(0)
+        for r in range(R):
+            x_gain(1, r)
+        coef_turn(0)
+        x_turn(2, 0)
+        x_turn(2, 1)
+        w_quant()
+        x_quant(1)
+        coef_mm(1)
+        halves = ((0, G // 2), (G // 2, G))
+        for by_row in (True, False, True, None):
+            for lo, hi in halves:
+                sink_sum(0, lo, hi)
+            for lo, hi in halves:
+                sink_inv(0, lo, hi)
+            for lo, hi in halves:
+                if by_row is None:
+                    sink_last(0, lo, hi)
+                else:
+                    sink_scale(0, by_row, lo, hi)
+        coef_act(1)
+        coef_turn(1)
+        for r in range(R):
+            pre_prod(0, r)
+        u_sum(0)
+        prod_gpsimd(0, 0, 0, 2)
+        prod_scalar(0, 2, 0)
+        prod_scalar(0, 3, 0)
+        prod_scalar(0, 2, 1)
+        x_gain(2, 0)
+        x_gain(2, 1)
+        u_gain(0)
+        x_gain(2, 2)
+        x_gain(2, 3)
+        u_quant(0)
+
+        for k in range(NT + 1):
+            if k > 0:
+                do(coef_mm, k + 1)
             do(branch_mm, k)
-            do(prod_gpsimd, k, 0, 0, 2)
-            do(y_out, k - 1, 1)
-            do(coef_act, k + 1)
-            if k == -1:
-                w_group()
-            for r in range(R):
-                do(x_gain, k + 2, r)
-            do(coef_turn, k + 1)
+            if k > 0:
+                do(prod_gpsimd, k, 0, 0, 2)
+            do(y_out, k - 1, 0)
+            if k > 0:
+                do(coef_act, k + 1)
+                for r in range(R):
+                    do(x_gain, k + 2, r)
+            do(y_sum, k - 1, 1, 0, 1)
+            if k > 0:
+                do(coef_turn, k + 1)
+            do(y_sum, k - 1, 1, 1, QUAD)
             do(branch_act, k)
             do(y_sum, k - 1, 2)
             do(prod_gpsimd, k, 1, 0, 2)
             do(sink_sum, k + 1)
-            do(prod_scalar, k, 2, 0)
+            if k > 0:
+                do(prod_scalar, k, 2, 0)
             do(pre_prod, k + 1, 0)
             do(sink_inv, k + 1)
             do(pre_prod, k + 1, 1)
             do(sink_scale, k + 1, True)
+            do(y_out, k - 1, 1)
+            do(x_turn, k + 3, 0)
+            do(x_turn, k + 3, 1)
             do(y_sum, k - 1, 3)
-            do(prod_scalar, k, 3, 0)
-            do(y_out, k - 1, 2)
+            if k > 0:
+                do(prod_scalar, k, 3, 0)
             do(sink_sum, k + 1)
             do(pre_prod, k + 1, 2)
             do(prod_scalar, k, R, 0)
             do(prod_gpsimd, k, 0, 2, 2)
             do(sink_inv, k + 1)
             do(pre_prod, k + 1, 3)
-            do(y_sum, k, 0)
-            do(sink_scale, k + 1, False)
-            do(y_out, k - 1, 3)
-            for j in (2, 3, R):
-                do(prod_scalar, k, j, 1)
             do(u_sum, k + 1)
+            do(sink_scale, k + 1, False)
+            do(y_out, k - 1, 2)
+            do(y_sum, k, 0)
+            for j in (2, 3, R) if k > 0 else (3, R):
+                do(prod_scalar, k, j, 1)
             do(prod_gpsimd, k, 1, 2, 2)
             do(sink_sum, k + 1)
             do(prod_vector, k, 3)
             do(sink_inv, k + 1)
-            do(y_sum, k, 1)
-            do(u_gain, k + 1)
+            do(y_out, k - 1, 3)
             do(sink_scale, k + 1, True)
-            do(y_out, k, 0)
-            do(x_turn, k + 3, 0)
-            do(x_turn, k + 3, 1)
+            do(u_gain, k + 1)
             for j in (2, 3, R):
                 do(prod_scalar, k, j, 2)
             do(prod_gpsimd, k, 2, 3, 1)
             do(prod_scalar, k, 3, 3)
             do(sink_sum, k + 1)
             do(sink_inv, k + 1)
-            if k == -1:
-                w_quant()
             do(x_quant, k + 2)
             do(u_quant, k + 1)
             do(sink_last, k + 1)

@@ -199,11 +199,17 @@ def tile_groupedmanifoldhyperconnection_kernel(tc, x, gn, phi_bytes, phi_scale, 
 
         def coef_turn(n):
             st = state[n]
-            ct = ps.tile([P, 3, P], F32, name="ct", bufs=2)
+            ct = ps.tile([P, 4, P], F32, name="ct", bufs=2)
             for m in (1, 2, 0):
                 nc.tensor.transpose(ct[:, m, :], st["co"][:, m, :], ident[:])
             st["e"] = ct[:, 1:3, :].rearrange("p m (g i j) -> p (m g) i j", i=R, j=R)
             st["gate"] = ct[:, 0, :].rearrange("p (g k) -> p g k", g=G)
+            st["spare"] = ct[:, 3, :]
+
+        def q_to_psum(n):
+            st = state[n]
+            upper = st["q"][:, :, 2:R, :].rearrange("p g j i -> p g (j i)")
+            nc.tensor.matmul(st["spare"], ident[:], upper, start=True, stop=True)
 
         def sink_sum(n, lo=0, hi=G):
             st = state[n]
@@ -316,13 +322,17 @@ def tile_groupedmanifoldhyperconnection_kernel(tc, x, gn, phi_bytes, phi_scale, 
             for a in range(count):
                 st["prod", j, quad + a] = pg[:, a * QUAD : (a + 1) * QUAD, :, :]
 
-        def prod_vector(n, quad):
+        def prod_vector(n, j, quad):
             st = state[n]
-            src = term(n, R, quad)[0]
+            src = term(n, j, quad)[0]
             pq = sb.tile([P, QUAD, R, C], F32, name="pq", bufs=24)
-            wt = st["gate"][:, QUAD * quad : QUAD * (quad + 1), R : 2 * R]
+            if j == R:
+                wt = st["gate"][:, :, R : 2 * R]
+            else:
+                wt = st["spare"].rearrange("p (g j i) -> p g j i", j=2, i=R)[:, :, j - 2, :]
+            wt = wt[:, QUAD * quad : QUAD * (quad + 1), :]
             nc.vector.tensor_tensor(out=pq[:], in0=spread(src, 2, R), in1=spread(wt, 3, C), op=ALU.mult)
-            st["prod", R, quad] = pq[:]
+            st["prod", j, quad] = pq[:]
 
         def y_sum(n, quad, lo=0, hi=QUAD):
             st = state[n]
@@ -409,13 +419,18 @@ def tile_groupedmanifoldhyperconnection_kernel(tc, x, gn, phi_bytes, phi_scale, 
         x_gain(2, 3)
         u_quant(0)
 
-        for k in range(NT + 1):
+        for k in range(NT - 1):
             if k > 0:
                 do(coef_mm, k + 1)
             do(branch_mm, k)
+            if k == NT - 2:
+                q_to_psum(k)
             if k > 0:
                 do(prod_gpsimd, k, 0, 0, 2)
             do(y_out, k - 1, 0)
+            if k == NT - 2:
+                prod_vector(k, 2, 3)
+                prod_vector(k, 3, 3)
             if k > 0:
                 do(coef_act, k + 1)
                 for r in range(R):
@@ -454,17 +469,59 @@ def tile_groupedmanifoldhyperconnection_kernel(tc, x, gn, phi_bytes, phi_scale, 
                 do(prod_scalar, k, j, 1)
             do(prod_gpsimd, k, 1, 2, 2)
             do(sink_sum, k + 1)
-            do(prod_vector, k, 3)
+            do(prod_vector, k, R, 3)
             do(sink_inv, k + 1)
             do(y_out, k - 1, 3)
             do(sink_scale, k + 1, True)
             do(u_gain, k + 1)
+            if k == NT - 2:
+                y_sum(k, 1)
+                y_out(k, 0)
             for j in (2, 3, R):
                 do(prod_scalar, k, j, 2)
-            do(prod_gpsimd, k, 2, 3, 1)
-            do(prod_scalar, k, 3, 3)
+            if k < NT - 2:
+                prod_gpsimd(k, 2, 3, 1)
+                prod_gpsimd(k, 3, 3, 1)
             do(sink_sum, k + 1)
             do(sink_inv, k + 1)
             do(x_quant, k + 2)
             do(u_quant, k + 1)
             do(sink_last, k + 1)
+
+        last = NT - 1
+        branch_mm(last)
+        q_to_psum(last)
+        y_out(last - 1, 1)
+        branch_act(last)
+        y_sum(last - 1, 2)
+        prod_gpsimd(last, 0, 0, 1)
+        prod_gpsimd(last, 1, 0, 1)
+        prod_vector(last, 3, 0)
+        prod_vector(last, 2, 0)
+        prod_scalar(last, R, 0)
+        y_sum(last - 1, 3)
+        prod_gpsimd(last, 0, 1, 1)
+        prod_gpsimd(last, 1, 1, 1)
+        prod_vector(last, 3, 1)
+        y_out(last - 1, 2)
+        prod_scalar(last, R, 1)
+        prod_scalar(last, 2, 1)
+        y_sum(last, 0)
+        prod_gpsimd(last, 0, 2, 1)
+        prod_vector(last, 3, 2)
+        prod_vector(last, 2, 2)
+        y_out(last - 1, 3)
+        prod_scalar(last, R, 2)
+        prod_scalar(last, 1, 2)
+        y_sum(last, 1)
+        prod_gpsimd(last, 0, 3, 1)
+        prod_gpsimd(last, 1, 3, 1)
+        prod_vector(last, 3, 3)
+        prod_vector(last, R, 3)
+        prod_scalar(last, 2, 3)
+        y_out(last, 0)
+        y_sum(last, 2)
+        y_out(last, 1)
+        y_sum(last, 3)
+        y_out(last, 2)
+        y_out(last, 3)

@@ -26,6 +26,7 @@ NT = TOK // P
 QUAD = 4
 NQ = G // QUAD
 PLAIN_EVERY = 16
+THIRD_BANK_FROM = 20
 FLOPS = 2 * TOK * R * D * M + 2 * TOK * D * D
 
 
@@ -63,12 +64,12 @@ def tile_groupedmanifoldhyperconnection_kernel(tc, x, gn, phi_bytes, phi_scale, 
 
         nc.sync.dma_start(out=scale[:], in_=phi_scale.rearrange("(r p t) o -> p r (t o)", p=P, t=T))
         nc.sync.dma_start(out=phb[0][:], in_=phv[0])
+        nc.sync.dma_start(out=bmz[0:1, :], in_=bm.rearrange("(o n) -> o n", o=1))
         nc.sync.dma_start(out=phb[1][:], in_=phv[1])
         load_x(0)
         nc.sync.dma_start(out=gns[:], in_=gn.rearrange("(r p t) -> p r t", p=P, t=T))
         nc.sync.dma_start(out=phb[2][:], in_=phv[2])
         nc.sync.dma_start(out=phb[3][:], in_=phv[3])
-        nc.sync.dma_start(out=bmz[0:1, :], in_=bm.rearrange("(o n) -> o n", o=1))
         load_x(1)
         nc.sync.dma_start(out=wraw[:], in_=w.rearrange("(p t) n -> p t n", t=T))
         nc.sync.dma_start(out=gfs[:], in_=gf.rearrange("(p t) -> p t", t=T))
@@ -94,11 +95,12 @@ def tile_groupedmanifoldhyperconnection_kernel(tc, x, gn, phi_bytes, phi_scale, 
             else:
                 nc.scalar.activation(phw[r][:, t, :], src, ACT.Copy, scale=col)
 
-        def phi_group(r):
+        def phi_group(r, engine):
             src = phw[r][:].rearrange("p t (g k) -> p g t k", g=G)
             for lo, hi, col in ((0, 8, 0), (8, KC, P)):
                 n = hi - lo
-                nc.vector.tensor_copy(
+                copy = nc.vector.tensor_copy if engine == "vector" else nc.scalar.copy
+                copy(
                     out=phg[r][:, col : col + G * n, :].rearrange("p (g a i) t -> p g a t i", g=G, i=4),
                     in_=src[:, :, :, lo:hi].rearrange("p g t (a i) -> p g a t i", i=4),
                 )
@@ -108,7 +110,7 @@ def tile_groupedmanifoldhyperconnection_kernel(tc, x, gn, phi_bytes, phi_scale, 
                 out=phc[:, r, :].bitcast(FP8X4), scales=phs[:, r, :], in_=phg[r][:].rearrange("p n t -> p (n t)")
             )
 
-        def bias_setup():
+        def bias_turn():
             bmp = keep.tile([P, M], F32)
             src = bmz[:].rearrange("p (g k) -> p g k", g=G)
             nc.scalar.copy(out=bmp[:, 0:P].rearrange("p (g k) -> p g k", g=G), in_=src[:, :, 0:8])
@@ -116,6 +118,9 @@ def tile_groupedmanifoldhyperconnection_kernel(tc, x, gn, phi_bytes, phi_scale, 
             bps = ps.tile([P, 3, P], F32, name="tt")
             for m in range(3):
                 nc.tensor.transpose(bps[:, m, :], bmp[:, m * P : (m + 1) * P], ident[:])
+            return bps
+
+        def bias_read(bps):
             nc.scalar.copy(out=bias[:], in_=bps[:, :, 0])
             nc.scalar.activation(hbias[:], bps[:, 0, 0:1], ACT.Copy, scale=0.5)
 
@@ -169,47 +174,49 @@ def tile_groupedmanifoldhyperconnection_kernel(tc, x, gn, phi_bytes, phi_scale, 
             )
             st["xq"] = (xqc, xqs)
 
-        def coef_mm(n):
+        def coef_mm(n, lo=0, hi=R):
             st = state[n]
             xqc, xqs = st["xq"]
-            tt = ps.tile([P, 3, P], F32, name="tt")
-            for m in (1, 2, 0):
-                for r in range(R):
+            if lo == 0:
+                st["tt"] = ps.tile([P, 3, P], F32, name="tt")
+            tt = st["tt"]
+            for r in range(lo, hi):
+                for m in range(3):
                     nc.tensor.matmul_mx(
                         out=tt[:, m, :],
                         lhsT=phc[:, r, m * P : (m + 1) * P].bitcast(FP8X4),
                         lhsT_scale=phs[:, r, m * P : (m + 1) * P],
                         rhs=xqc[:, r, :].bitcast(FP8X4),
                         rhs_scale=xqs[:, r, :],
-                        start=(r == 0),
-                        stop=(r == R - 1),
+                        start=(r == 0 and m == 0),
+                        stop=(r == R - 1 and m == 2),
                     )
-            st["tt"] = tt
 
         def coef_act(n):
             st = state[n]
             tt = st["tt"]
             co = sb.tile([P, 3, P], F32, name="co")
             th = sb.tile([P, P], F32, name="th")
-            for m in (1, 2):
-                nc.scalar.activation(co[:, m, :], tt[:, m, :], ACT.Exp, bias=bias[:, m : m + 1])
+            nc.scalar.activation(co[:, 1, :], tt[:, 1, :], ACT.Exp, bias=bias[:, 1:2])
             nc.scalar.activation(th[:], tt[:, 0, :], ACT.Tanh, bias=hbias[:], scale=0.5)
+            nc.scalar.activation(co[:, 2, :], tt[:, 2, :], ACT.Exp, bias=bias[:, 2:3])
             nc.scalar.activation(co[:, 0, :], th[:], ACT.Identity, bias=1.0)
             st["co"] = co
 
         def coef_turn(n):
             st = state[n]
-            ct = ps.tile([P, 4, P], F32, name="ct", bufs=2)
+            ct = ps.tile([P, 3, P], F32, name="ct", bufs=2)
             for m in (1, 2, 0):
                 nc.tensor.transpose(ct[:, m, :], st["co"][:, m, :], ident[:])
             st["e"] = ct[:, 1:3, :].rearrange("p m (g i j) -> p (m g) i j", i=R, j=R)
             st["gate"] = ct[:, 0, :].rearrange("p (g k) -> p g k", g=G)
-            st["spare"] = ct[:, 3, :]
 
-        def q_to_psum(n):
+        def q_to_psum(n, quad):
             st = state[n]
-            upper = st["q"][:, :, 2:R, :].rearrange("p g j i -> p g (j i)")
-            nc.tensor.matmul(st["spare"], ident[:], upper, start=True, stop=True)
+            upper = ps.tile([P, G, 2, R], F32, name="xp", bufs=2)
+            gs = slice(QUAD * quad, G)
+            nc.tensor.matmul(upper[:, gs], ident[:], st["q"][:, gs, 2:R, :], start=True, stop=True)
+            st["upper"] = upper
 
         def sink_sum(n, lo=0, hi=G):
             st = state[n]
@@ -232,11 +239,11 @@ def tile_groupedmanifoldhyperconnection_kernel(tc, x, gn, phi_bytes, phi_scale, 
             nc.vector.tensor_tensor(out=scaled[:], in0=e, in1=spread(st["factor", lo][:], 2, R), op=ALU.mult)
             st["scaled", lo] = scaled[:]
 
-        def sink_last(n, lo=0, hi=G):
+        def sink_last(n, lo=0, hi=G, engine=nc.vector):
             st = state[n]
             if lo == 0:
                 st["q"] = sb.tile([P, G, R, R], F32, name="q")
-            nc.vector.tensor_tensor(
+            engine.tensor_tensor(
                 out=st["q"][:, lo:hi], in0=st["scaled", lo], in1=spread(st["factor", lo][:], 3, R), op=ALU.mult
             )
 
@@ -251,12 +258,25 @@ def tile_groupedmanifoldhyperconnection_kernel(tc, x, gn, phi_bytes, phi_scale, 
             )
             st["pu", r] = pr
 
+        def gate_copy(n):
+            st = state[n]
+            st["pre"] = sb.tile([P, G, R], F32, name="pre")
+            nc.scalar.copy(out=st["pre"][:], in_=st["gate"][:, :, 0:R])
+
+        def pre_prod_scalar(n, r):
+            st = state[n]
+            pr = sb.tile([P, T, P], F32, name="pu", bufs=6)
+            src = xs[n][:, r * D : (r + 1) * D].rearrange("p (g c t) -> p g t c", g=G, t=T)
+            for g in range(G):
+                nc.scalar.activation(pr[:, :, 8 * g : 8 * (g + 1)], src[:, g], ACT.Copy, scale=st["pre"][:, g, r : r + 1])
+            st["pu", r] = pr
+
         def u_sum(n):
             st = state[n]
             ut = ps.tile([P, T, P], F32, name="uh")
-            for t in range(T):
-                for r in range(R):
-                    add_turned(ut[:, t, :], st["pu", r][:, t, :], r == 0, r == R - 1)
+            for r in range(R):
+                for t in range(T):
+                    add_turned(ut[:, t, :], st["pu", r][:, t, :], r == 0 and t == 0, r == R - 1 and t == T - 1)
             st["ut"] = ut
 
         def u_gain(n):
@@ -284,16 +304,17 @@ def tile_groupedmanifoldhyperconnection_kernel(tc, x, gn, phi_bytes, phi_scale, 
             )
             st["h"] = h
 
-        def branch_act(n):
+        def branch_relu(n):
             st = state[n]
-            post = sb.tile([P, G, R], F32, name="post")
-            nc.scalar.copy(out=post[:], in_=st["gate"][:, :, R : 2 * R])
-            hr = sb.tile([P, D], F32, name="hr")
-            nc.scalar.activation(hr[:], st["h"][:], ACT.Relu)
-            f = sb.tile([P, D], F32, name="f")
-            nc.scalar.activation(f[:], hr[:], ACT.Square)
-            st["f"] = f
-            st["post"] = post
+            st["hr"] = sb.tile([P, D], F32, name="hr")
+            nc.scalar.activation(st["hr"][:], st["h"][:], ACT.Relu)
+            st["post"] = sb.tile([P, G, R], F32, name="post")
+            nc.scalar.copy(out=st["post"][:], in_=st["gate"][:, :, R : 2 * R])
+
+        def branch_square(n):
+            st = state[n]
+            st["f"] = sb.tile([P, D], F32, name="f")
+            nc.scalar.activation(st["f"][:], st["hr"][:], ACT.Square)
 
         def term(n, j, quad):
             st = state[n]
@@ -315,7 +336,7 @@ def tile_groupedmanifoldhyperconnection_kernel(tc, x, gn, phi_bytes, phi_scale, 
             st = state[n]
             gs = slice(QUAD * quad, QUAD * (quad + count))
             src = xs[n][:, j * D : (j + 1) * D].rearrange("p (g c) -> p g c", g=G)[:, gs, :]
-            pg = sb.tile([P, count * QUAD, R, C], F32, name="pg" if count == 2 else "pq", bufs=8 if count == 2 else 24)
+            pg = sb.tile([P, count * QUAD, R, C], F32, name="pg%d" % count if count > 1 else "pq", bufs={1: 24, 2: 4, 4: 4}[count])
             nc.gpsimd.tensor_tensor(
                 out=pg[:], in0=spread(src, 2, R), in1=spread(st["q"][:, gs, j, :], 3, C), op=ALU.mult
             )
@@ -329,7 +350,7 @@ def tile_groupedmanifoldhyperconnection_kernel(tc, x, gn, phi_bytes, phi_scale, 
             if j == R:
                 wt = st["gate"][:, :, R : 2 * R]
             else:
-                wt = st["spare"].rearrange("p (g j i) -> p g j i", j=2, i=R)[:, :, j - 2, :]
+                wt = st["upper"][:, :, j - 2, :]
             wt = wt[:, QUAD * quad : QUAD * (quad + 1), :]
             nc.vector.tensor_tensor(out=pq[:], in0=spread(src, 2, R), in1=spread(wt, 3, C), op=ALU.mult)
             st["prod", j, quad] = pq[:]
@@ -337,191 +358,208 @@ def tile_groupedmanifoldhyperconnection_kernel(tc, x, gn, phi_bytes, phi_scale, 
         def y_sum(n, quad, lo=0, hi=QUAD):
             st = state[n]
             if lo == 0:
-                st["yt", quad] = ps.tile([P, 4, QUAD, 32], F32, name="yy", bufs=2)
+                third = NQ * n + quad >= THIRD_BANK_FROM and (NQ * n + quad) % 3 == 0
+                st["yt", quad] = ps.tile([P, 4, QUAD, 32], F32, name="tt" if third else "yy", bufs=1 if third else 2)
             for b in range(lo, hi):
                 for j in range(R + 1):
                     src = st["prod", j, quad][:, b, :, :].rearrange("p i c -> p (i c)")
                     add_turned(st["yt", quad][:, :, b, :], src, j == 0, j == R)
 
         def y_out(n, quad):
-            yo = sb.tile([P, D], F32, name="yo", bufs=6, align_bytes=64)
+            yo = sb.tile([P, D], F32, name="yo", bufs=5, align_bytes=64)
             nc.vector.transpose(yo[:], state[n]["yt", quad][:].rearrange("p tb b t -> p (tb b t)"))
             for i in range(R):
                 nc.sync.dma_start(
                     out=out_view[n, i, quad], in_=yo[32 * i : 32 * (i + 1), :].rearrange("p (tb c) -> p tb c", tb=4)
                 )
 
+        summed = []
+        stored = []
+
+        def next_sum():
+            y_sum(*divmod(len(summed), NQ))
+            summed.append(0)
+
+        def next_out():
+            y_out(*divmod(len(stored), NQ))
+            stored.append(0)
+
         def do(fn, n, *args):
             if 0 <= n < NT:
                 fn(n, *args)
 
-        phi_widen(0, 0, "vector")
-        phi_widen(0, 1, "vector")
-        phi_widen(0, 2, "scalar")
-        phi_widen(0, 3, "scalar")
-        for r in range(1, R):
-            for t in range(T):
-                phi_widen(r, t, "scalar")
+        for t in range(T):
+            phi_widen(0, t, "vector" if t < 2 else "scalar")
         x_turn(0, 0)
         x_turn(0, 1)
-        phi_group(0)
+        for t in range(T):
+            phi_widen(1, t, "scalar")
+        turned_bias = bias_turn()
+        for r in (2, 3):
+            for t in range(T):
+                phi_widen(r, t, "scalar")
+        bias_read(turned_bias)
+        phi_group(0, "vector")
         x_gain(0, 0)
         x_gain(0, 1)
         phi_quant(0)
-        phi_group(1)
         x_gain(0, 2)
         x_gain(0, 3)
         x_turn(1, 0)
         x_turn(1, 1)
-        bias_setup()
-        w_group()
-        phi_quant(1)
-        phi_group(2)
+        phi_group(1, "vector")
         x_quant(0)
-        phi_group(3)
+        phi_quant(1)
+        phi_group(3, "scalar")
+        phi_group(2, "vector")
+        x_gain(1, 0)
         phi_quant(2)
+        x_gain(1, 1)
         phi_quant(3)
-
-        coef_mm(0)
-        coef_act(0)
-        for r in range(R):
-            x_gain(1, r)
-        coef_turn(0)
+        coef_mm(0, 0, R - 1)
         x_turn(2, 0)
+        coef_mm(0, R - 1, R)
+        w_group()
+        coef_act(0)
+        x_gain(1, 2)
+        x_gain(1, 3)
         x_turn(2, 1)
-        w_quant()
+        coef_turn(0)
         x_quant(1)
         coef_mm(1)
-        halves = ((0, G // 2), (G // 2, G))
-        for by_row in (True, False, True, None):
-            for lo, hi in halves:
-                sink_sum(0, lo, hi)
-            for lo, hi in halves:
-                sink_inv(0, lo, hi)
-            for lo, hi in halves:
-                if by_row is None:
-                    sink_last(0, lo, hi)
-                else:
-                    sink_scale(0, by_row, lo, hi)
-        coef_act(1)
-        coef_turn(1)
-        for r in range(R):
-            pre_prod(0, r)
-        u_sum(0)
-        prod_gpsimd(0, 0, 0, 2)
-        prod_scalar(0, 2, 0)
-        prod_scalar(0, 3, 0)
-        prod_scalar(0, 2, 1)
         x_gain(2, 0)
         x_gain(2, 1)
-        u_gain(0)
+        w_quant()
         x_gain(2, 2)
         x_gain(2, 3)
+        x_turn(3, 0)
+        x_turn(3, 1)
+        gate_copy(0)
+        for r in range(R):
+            pre_prod_scalar(0, r)
+        coef_act(1)
+        u_sum(0)
+        coef_turn(1)
+        first, second = (0, G // 2), (G // 2, G)
+        for step, by_row in enumerate((True, False, True)):
+            sink_sum(0, *first)
+            sink_sum(0, *second)
+            if step == 0:
+                x_quant(2)
+            sink_inv(0, *first)
+            sink_inv(0, *second)
+            sink_scale(0, by_row, *first)
+            sink_scale(0, by_row, *second)
+        coef_mm(2)
+        sink_sum(0, *first)
+        sink_sum(0, *second)
+        u_gain(0)
+        sink_inv(0, *first)
+        sink_inv(0, *second)
         u_quant(0)
+        sink_last(0, *first)
+        sink_last(0, *second)
 
         for k in range(NT - 1):
+            late = k >= NT - 3
             if k > 0:
-                do(coef_mm, k + 1)
-            do(branch_mm, k)
-            if k == NT - 2:
-                q_to_psum(k)
+                do(coef_mm, k + 2)
+            branch_mm(k)
+            if late:
+                q_to_psum(k, NQ - 1)
             if k > 0:
-                do(prod_gpsimd, k, 0, 0, 2)
-            do(y_out, k - 1, 0)
+                prod_gpsimd(k, 0, 0, NQ)
+            else:
+                prod_gpsimd(k, 0, 0, 2)
+                prod_gpsimd(k, 1, 0, 2)
+            sink_sum(k + 1)
+            if k > 0:
+                next_out()
             if k == NT - 2:
+                next_sum()
+            prod_scalar(k, 2, 0)
+            prod_scalar(k, 3, 0)
+            branch_relu(k)
+            do(coef_act, k + 2)
+            branch_square(k)
+            if k > 0:
+                next_sum()
+            do(coef_turn, k + 2)
+            if k > 0:
+                next_sum()
+            sink_inv(k + 1)
+            pre_prod(k + 1, 0)
+            sink_scale(k + 1, True)
+            pre_prod(k + 1, 1)
+            sink_sum(k + 1)
+            if k == NT - 2:
+                next_out()
+            pre_prod(k + 1, 2)
+            sink_inv(k + 1)
+            pre_prod(k + 1, 3)
+            u_sum(k + 1)
+            prod_scalar(k, R, 0)
+            if k > 0:
+                prod_gpsimd(k, 1, 0, NQ)
+            else:
+                prod_gpsimd(k, 0, 2, 2)
+                prod_gpsimd(k, 1, 2, 2)
+            sink_scale(k + 1, False)
+            if k > 0:
+                next_out()
+            if k > 0:
+                next_sum()
+            sink_sum(k + 1)
+            do(x_gain, k + 3, 0)
+            do(x_gain, k + 3, 1)
+            if late:
                 prod_vector(k, 2, 3)
-                prod_vector(k, 3, 3)
+            do(x_turn, k + 4, 0)
+            sink_inv(k + 1)
             if k > 0:
-                do(coef_act, k + 1)
-                for r in range(R):
-                    do(x_gain, k + 2, r)
-            do(y_sum, k - 1, 1, 0, 1)
-            if k > 0:
-                do(coef_turn, k + 1)
-            do(y_sum, k - 1, 1, 1, QUAD)
-            do(branch_act, k)
-            do(y_sum, k - 1, 2)
-            do(prod_gpsimd, k, 1, 0, 2)
-            do(sink_sum, k + 1)
-            if k > 0:
-                do(prod_scalar, k, 2, 0)
-            do(pre_prod, k + 1, 0)
-            do(sink_inv, k + 1)
-            do(pre_prod, k + 1, 1)
-            do(sink_scale, k + 1, True)
-            do(y_out, k - 1, 1)
-            do(x_turn, k + 3, 0)
-            do(x_turn, k + 3, 1)
-            do(y_sum, k - 1, 3)
-            if k > 0:
-                do(prod_scalar, k, 3, 0)
-            do(sink_sum, k + 1)
-            do(pre_prod, k + 1, 2)
-            do(prod_scalar, k, R, 0)
-            do(prod_gpsimd, k, 0, 2, 2)
-            do(sink_inv, k + 1)
-            do(pre_prod, k + 1, 3)
-            do(u_sum, k + 1)
-            do(sink_scale, k + 1, False)
-            do(y_out, k - 1, 2)
-            do(y_sum, k, 0)
-            for j in (2, 3, R) if k > 0 else (3, R):
-                do(prod_scalar, k, j, 1)
-            do(prod_gpsimd, k, 1, 2, 2)
-            do(sink_sum, k + 1)
-            do(prod_vector, k, R, 3)
-            do(sink_inv, k + 1)
-            do(y_out, k - 1, 3)
-            do(sink_scale, k + 1, True)
-            do(u_gain, k + 1)
-            if k == NT - 2:
-                y_sum(k, 1)
-                y_out(k, 0)
+                next_out()
             for j in (2, 3, R):
-                do(prod_scalar, k, j, 2)
-            if k < NT - 2:
+                prod_scalar(k, j, 1)
+            next_sum()
+            sink_scale(k + 1, True)
+            do(x_gain, k + 3, 2)
+            do(x_gain, k + 3, 3)
+            if late:
+                prod_vector(k, 3, 3)
+            do(x_turn, k + 4, 1)
+            sink_sum(k + 1)
+            u_gain(k + 1)
+            sink_inv(k + 1)
+            if k > 0:
+                next_out()
+            for j in (2, 3, R):
+                prod_scalar(k, j, 2)
+            if not late:
                 prod_gpsimd(k, 2, 3, 1)
-                prod_gpsimd(k, 3, 3, 1)
-            do(sink_sum, k + 1)
-            do(sink_inv, k + 1)
-            do(x_quant, k + 2)
-            do(u_quant, k + 1)
-            do(sink_last, k + 1)
+                prod_scalar(k, 3, 3)
+            prod_scalar(k, R, 3)
+            do(x_quant, k + 3)
+            u_quant(k + 1)
+            sink_last(k + 1)
 
         last = NT - 1
         branch_mm(last)
-        q_to_psum(last)
-        y_out(last - 1, 1)
-        branch_act(last)
-        y_sum(last - 1, 2)
-        prod_gpsimd(last, 0, 0, 1)
-        prod_gpsimd(last, 1, 0, 1)
-        prod_vector(last, 3, 0)
-        prod_vector(last, 2, 0)
-        prod_scalar(last, R, 0)
-        y_sum(last - 1, 3)
-        prod_gpsimd(last, 0, 1, 1)
-        prod_gpsimd(last, 1, 1, 1)
-        prod_vector(last, 3, 1)
-        y_out(last - 1, 2)
-        prod_scalar(last, R, 1)
-        prod_scalar(last, 2, 1)
-        y_sum(last, 0)
-        prod_gpsimd(last, 0, 2, 1)
-        prod_vector(last, 3, 2)
-        prod_vector(last, 2, 2)
-        y_out(last - 1, 3)
-        prod_scalar(last, R, 2)
+        q_to_psum(last, 0)
+        next_sum()
+        next_out()
+        next_sum()
         prod_scalar(last, 1, 2)
-        y_sum(last, 1)
-        prod_gpsimd(last, 0, 3, 1)
-        prod_gpsimd(last, 1, 3, 1)
-        prod_vector(last, 3, 3)
-        prod_vector(last, R, 3)
-        prod_scalar(last, 2, 3)
-        y_out(last, 0)
-        y_sum(last, 2)
-        y_out(last, 1)
-        y_sum(last, 3)
-        y_out(last, 2)
-        y_out(last, 3)
+        prod_scalar(last, 1, 3)
+        branch_relu(last)
+        branch_square(last)
+        for quad in range(NQ):
+            prod_gpsimd(last, 0, quad, 1)
+            if quad < 2:
+                prod_gpsimd(last, 1, quad, 1)
+            prod_vector(last, 2, quad)
+            prod_vector(last, 3, quad)
+            prod_scalar(last, R, quad)
+            next_out()
+            next_sum()
+        next_out()
+        next_out()

@@ -26,7 +26,9 @@ NT = TOK // P
 QUAD = 4
 NQ = G // QUAD
 PLAIN_EVERY = 16
+PLAIN_UNTIL = 680
 THIRD_BANK_FROM = 20
+SPLIT = 11
 FLOPS = 2 * TOK * R * D * M + 2 * TOK * D * D
 
 
@@ -138,7 +140,7 @@ def tile_groupedmanifoldhyperconnection_kernel(tc, x, gn, phi_bytes, phi_scale, 
 
         def add_turned(dst, src, start, stop):
             passes.append(0)
-            plain = len(passes) % PLAIN_EVERY == 0
+            plain = len(passes) % PLAIN_EVERY == 0 and len(passes) <= PLAIN_UNTIL
             nc.tensor.matmul(dst, src, ident[:], start=start, stop=stop, is_transpose=not plain)
 
         def x_turn(n, half):
@@ -211,10 +213,10 @@ def tile_groupedmanifoldhyperconnection_kernel(tc, x, gn, phi_bytes, phi_scale, 
             st["e"] = ct[:, 1:3, :].rearrange("p m (g i j) -> p (m g) i j", i=R, j=R)
             st["gate"] = ct[:, 0, :].rearrange("p (g k) -> p g k", g=G)
 
-        def q_to_psum(n, quad):
+        def q_to_psum(n, lo):
             st = state[n]
             upper = ps.tile([P, G, 2, R], F32, name="xp", bufs=2)
-            gs = slice(QUAD * quad, G)
+            gs = slice(lo, G)
             nc.tensor.matmul(upper[:, gs], ident[:], st["q"][:, gs, 2:R, :], start=True, stop=True)
             st["upper"] = upper
 
@@ -316,54 +318,41 @@ def tile_groupedmanifoldhyperconnection_kernel(tc, x, gn, phi_bytes, phi_scale, 
             st["f"] = sb.tile([P, D], F32, name="f")
             nc.scalar.activation(st["f"][:], st["hr"][:], ACT.Square)
 
-        def term(n, j, quad):
+        def term(n, j, lo, hi):
             st = state[n]
-            gs = slice(QUAD * quad, QUAD * (quad + 1))
-            if j < R:
-                src = xs[n][:, j * D : (j + 1) * D].rearrange("p (g c) -> p g c", g=G)
-                return src[:, gs, :], st["q"][:, gs, j, :]
-            return st["f"][:].rearrange("p (g c) -> p g c", g=G)[:, gs, :], st["post"][:, gs, :]
+            if ("prod", j) not in st:
+                st["prod", j] = sb.tile([P, G, R, C], F32, name="prod%d" % j)
+            src = xs[n][:, j * D : (j + 1) * D] if j < R else st["f"][:]
+            return st["prod", j][:, lo:hi], src.rearrange("p (g c) -> p g c", g=G)[:, lo:hi]
 
-        def prod_scalar(n, j, quad):
-            src, wt = term(n, j, quad)
-            pq = sb.tile([P, QUAD, R, C], F32, name="pq", bufs=24)
-            for g in range(QUAD):
+        def prod_scalar(n, j, lo, hi):
+            st = state[n]
+            dst, src = term(n, j, lo, hi)
+            wt = st["q"][:, lo:hi, j, :] if j < R else st["post"][:, lo:hi, :]
+            for g in range(hi - lo):
                 for i in range(R):
-                    nc.scalar.activation(pq[:, g, i, :], src[:, g, :], ACT.Copy, scale=wt[:, g, i : i + 1])
-            state[n]["prod", j, quad] = pq[:]
+                    nc.scalar.activation(dst[:, g, i, :], src[:, g, :], ACT.Copy, scale=wt[:, g, i : i + 1])
 
-        def prod_gpsimd(n, j, quad, count):
-            st = state[n]
-            gs = slice(QUAD * quad, QUAD * (quad + count))
-            src = xs[n][:, j * D : (j + 1) * D].rearrange("p (g c) -> p g c", g=G)[:, gs, :]
-            pg = sb.tile([P, count * QUAD, R, C], F32, name="pg%d" % count if count > 1 else "pq", bufs={1: 24, 2: 4, 4: 4}[count])
-            nc.gpsimd.tensor_tensor(
-                out=pg[:], in0=spread(src, 2, R), in1=spread(st["q"][:, gs, j, :], 3, C), op=ALU.mult
-            )
-            for a in range(count):
-                st["prod", j, quad + a] = pg[:, a * QUAD : (a + 1) * QUAD, :, :]
+        def prod_gpsimd(n, j, lo, hi):
+            dst, src = term(n, j, lo, hi)
+            wt = state[n]["q"][:, lo:hi, j, :]
+            nc.gpsimd.tensor_tensor(out=dst, in0=spread(src, 2, R), in1=spread(wt, 3, C), op=ALU.mult)
 
-        def prod_vector(n, j, quad):
+        def prod_vector(n, j, lo, hi):
             st = state[n]
-            src = term(n, j, quad)[0]
-            pq = sb.tile([P, QUAD, R, C], F32, name="pq", bufs=24)
-            if j == R:
-                wt = st["gate"][:, :, R : 2 * R]
-            else:
-                wt = st["upper"][:, :, j - 2, :]
-            wt = wt[:, QUAD * quad : QUAD * (quad + 1), :]
-            nc.vector.tensor_tensor(out=pq[:], in0=spread(src, 2, R), in1=spread(wt, 3, C), op=ALU.mult)
-            st["prod", j, quad] = pq[:]
+            dst, src = term(n, j, lo, hi)
+            wt = st["upper"][:, lo:hi, j - 2, :] if j < R else st["gate"][:, lo:hi, R : 2 * R]
+            nc.vector.tensor_tensor(out=dst, in0=spread(src, 2, R), in1=spread(wt, 3, C), op=ALU.mult)
 
-        def y_sum(n, quad, lo=0, hi=QUAD):
+        def y_sum(n, quad):
             st = state[n]
-            if lo == 0:
-                third = NQ * n + quad >= THIRD_BANK_FROM and (NQ * n + quad) % 3 == 0
-                st["yt", quad] = ps.tile([P, 4, QUAD, 32], F32, name="tt" if third else "yy", bufs=1 if third else 2)
-            for b in range(lo, hi):
+            third = NQ * n + quad >= THIRD_BANK_FROM and (NQ * n + quad) % 3 == 0
+            yt = ps.tile([P, 4, QUAD, 32], F32, name="tt" if third else "yy", bufs=1 if third else 2)
+            for b in range(QUAD):
                 for j in range(R + 1):
-                    src = st["prod", j, quad][:, b, :, :].rearrange("p i c -> p (i c)")
-                    add_turned(st["yt", quad][:, :, b, :], src, j == 0, j == R)
+                    src = st["prod", j][:, QUAD * quad + b].rearrange("p i c -> p (i c)")
+                    add_turned(yt[:, :, b, :], src, j == 0, j == R)
+            st["yt", quad] = yt
 
         def y_out(n, quad):
             yo = sb.tile([P, D], F32, name="yo", bufs=5, align_bytes=64)
@@ -461,31 +450,30 @@ def tile_groupedmanifoldhyperconnection_kernel(tc, x, gn, phi_bytes, phi_scale, 
         sink_last(0, *second)
 
         for k in range(NT - 1):
+            first = k == 0
             late = k >= NT - 3
-            if k > 0:
+            halves = first or k == NT - 2
+            split = G if first else 3 * QUAD if late else SPLIT
+            if not first:
                 do(coef_mm, k + 2)
             branch_mm(k)
             if late:
-                q_to_psum(k, NQ - 1)
-            if k > 0:
-                prod_gpsimd(k, 0, 0, NQ)
+                q_to_psum(k, 3 * QUAD)
+            if halves:
+                prod_gpsimd(k, 0, 0, G // 2)
+                prod_gpsimd(k, 1, 0, G // 2)
             else:
-                prod_gpsimd(k, 0, 0, 2)
-                prod_gpsimd(k, 1, 0, 2)
+                prod_gpsimd(k, 0, 0, G)
             sink_sum(k + 1)
-            if k > 0:
+            if not first:
                 next_out()
-            if k == NT - 2:
-                next_sum()
-            prod_scalar(k, 2, 0)
-            prod_scalar(k, 3, 0)
+            prod_scalar(k, 2, 0, 4)
+            prod_scalar(k, 3, 0, 4)
             branch_relu(k)
             do(coef_act, k + 2)
             branch_square(k)
-            if k > 0:
+            if not first:
                 next_sum()
-            do(coef_turn, k + 2)
-            if k > 0:
                 next_sum()
             sink_inv(k + 1)
             pre_prod(k + 1, 0)
@@ -498,68 +486,74 @@ def tile_groupedmanifoldhyperconnection_kernel(tc, x, gn, phi_bytes, phi_scale, 
             sink_inv(k + 1)
             pre_prod(k + 1, 3)
             u_sum(k + 1)
-            prod_scalar(k, R, 0)
-            if k > 0:
-                prod_gpsimd(k, 1, 0, NQ)
+            prod_scalar(k, R, 0, 4)
+            if halves:
+                prod_gpsimd(k, 0, G // 2, G)
+                prod_gpsimd(k, 1, G // 2, G)
             else:
-                prod_gpsimd(k, 0, 2, 2)
-                prod_gpsimd(k, 1, 2, 2)
+                prod_gpsimd(k, 1, 0, G)
             sink_scale(k + 1, False)
-            if k > 0:
+            if first:
+                prod_vector(k, R, 4, 8)
+            else:
                 next_out()
-            if k > 0:
                 next_sum()
             sink_sum(k + 1)
+            prod_vector(k, R, 12, G)
             do(x_gain, k + 3, 0)
             do(x_gain, k + 3, 1)
-            if late:
-                prod_vector(k, 2, 3)
             do(x_turn, k + 4, 0)
             sink_inv(k + 1)
-            if k > 0:
+            if first:
+                prod_vector(k, R, 8, 12)
+            else:
                 next_out()
-            for j in (2, 3, R):
-                prod_scalar(k, j, 1)
+            do(coef_turn, k + 2)
+            for j in (2, 3) if first else (2, 3, R):
+                prod_scalar(k, j, 4, 8)
             next_sum()
             sink_scale(k + 1, True)
             do(x_gain, k + 3, 2)
             do(x_gain, k + 3, 3)
             if late:
-                prod_vector(k, 3, 3)
+                prod_vector(k, 3, 12, G)
             do(x_turn, k + 4, 1)
             sink_sum(k + 1)
             u_gain(k + 1)
             sink_inv(k + 1)
-            if k > 0:
+            if not first and k < NT - 2:
                 next_out()
-            for j in (2, 3, R):
-                prod_scalar(k, j, 2)
-            if not late:
-                prod_gpsimd(k, 2, 3, 1)
-                prod_scalar(k, 3, 3)
-            prod_scalar(k, R, 3)
+            prod_scalar(k, 2, 8, split)
+            prod_scalar(k, 3, 8, 12)
+            if not first:
+                prod_scalar(k, R, 8, 12)
+                prod_gpsimd(k, 2, split, G)
+            if late:
+                next_sum()
+            else:
+                prod_scalar(k, 3, 12, G)
             do(x_quant, k + 3)
             u_quant(k + 1)
             sink_last(k + 1)
 
         last = NT - 1
-        branch_mm(last)
         q_to_psum(last, 0)
-        next_sum()
+        branch_mm(last)
+        next_out()
         next_out()
         next_sum()
-        prod_scalar(last, 1, 2)
-        prod_scalar(last, 1, 3)
+        prod_scalar(last, 1, 8, G)
         branch_relu(last)
         branch_square(last)
-        for quad in range(NQ):
-            prod_gpsimd(last, 0, quad, 1)
-            if quad < 2:
-                prod_gpsimd(last, 1, quad, 1)
-            prod_vector(last, 2, quad)
-            prod_vector(last, 3, quad)
-            prod_scalar(last, R, quad)
+        for lo in range(0, G, QUAD):
+            hi = lo + QUAD
+            prod_gpsimd(last, 0, lo, hi)
+            if lo < 8:
+                prod_gpsimd(last, 1, lo, hi)
+            prod_vector(last, 2, lo, hi)
             next_out()
+            prod_vector(last, 3, lo, hi)
+            prod_scalar(last, R, lo, hi)
             next_sum()
         next_out()
         next_out()

@@ -25,9 +25,9 @@ TOK = 1024
 NT = TOK // P
 QUAD = 4
 NQ = G // QUAD
-PLAIN_EVERY = 16
+PLAIN_EVERY = 20
 PLAIN_UNTIL = 680
-THIRD_BANK_FROM = 20
+THIRD_BANK_FROM = 24
 SPLIT = 11
 FLOPS = 2 * TOK * R * D * M + 2 * TOK * D * D
 
@@ -457,6 +457,9 @@ def tile_groupedmanifoldhyperconnection_kernel(tc, x, gn, phi_bytes, phi_scale, 
             if not first:
                 do(coef_mm, k + 2)
             branch_mm(k)
+            if not first:
+                do(x_turn, k + 3, 0)
+                do(x_turn, k + 3, 1)
             if late:
                 q_to_psum(k, 3 * QUAD)
             if halves:
@@ -480,7 +483,7 @@ def tile_groupedmanifoldhyperconnection_kernel(tc, x, gn, phi_bytes, phi_scale, 
             sink_scale(k + 1, True)
             pre_prod(k + 1, 1)
             sink_sum(k + 1)
-            if k == NT - 2:
+            if not first:
                 next_out()
             pre_prod(k + 1, 2)
             sink_inv(k + 1)
@@ -491,18 +494,18 @@ def tile_groupedmanifoldhyperconnection_kernel(tc, x, gn, phi_bytes, phi_scale, 
                 prod_gpsimd(k, 0, G // 2, G)
                 prod_gpsimd(k, 1, G // 2, G)
             else:
-                prod_gpsimd(k, 1, 0, G)
+                prod_gpsimd(k, 1, 0, G // 2)
+                prod_gpsimd(k, 1, G // 2, G)
             sink_scale(k + 1, False)
             if first:
                 prod_vector(k, R, 4, 8)
             else:
                 next_out()
-                next_sum()
+            next_sum()
             sink_sum(k + 1)
             prod_vector(k, R, 12, G)
             do(x_gain, k + 3, 0)
             do(x_gain, k + 3, 1)
-            do(x_turn, k + 4, 0)
             sink_inv(k + 1)
             if first:
                 prod_vector(k, R, 8, 12)
@@ -517,20 +520,17 @@ def tile_groupedmanifoldhyperconnection_kernel(tc, x, gn, phi_bytes, phi_scale, 
             do(x_gain, k + 3, 3)
             if late:
                 prod_vector(k, 3, 12, G)
-            do(x_turn, k + 4, 1)
             sink_sum(k + 1)
             u_gain(k + 1)
             sink_inv(k + 1)
-            if not first and k < NT - 2:
-                next_out()
             prod_scalar(k, 2, 8, split)
             prod_scalar(k, 3, 8, 12)
             if not first:
                 prod_scalar(k, R, 8, 12)
                 prod_gpsimd(k, 2, split, G)
-            if late:
+            if k == NT - 2:
                 next_sum()
-            else:
+            if not late:
                 prod_scalar(k, 3, 12, G)
             do(x_quant, k + 3)
             u_quant(k + 1)

@@ -25,10 +25,10 @@ TOK = 1024
 NT = TOK // P
 QUAD = 4
 NQ = G // QUAD
-PLAIN_EVERY = 20
-PLAIN_UNTIL = 680
+PLAIN_EVERY = 16
 THIRD_BANK_FROM = 24
 SPLIT = 11
+VECTOR_FROM = 14
 FLOPS = 2 * TOK * R * D * M + 2 * TOK * D * D
 
 
@@ -140,7 +140,7 @@ def tile_groupedmanifoldhyperconnection_kernel(tc, x, gn, phi_bytes, phi_scale, 
 
         def add_turned(dst, src, start, stop):
             passes.append(0)
-            plain = len(passes) % PLAIN_EVERY == 0 and len(passes) <= PLAIN_UNTIL
+            plain = len(passes) % PLAIN_EVERY == 0
             nc.tensor.matmul(dst, src, ident[:], start=start, stop=stop, is_transpose=not plain)
 
         def x_turn(n, half):
@@ -454,6 +454,7 @@ def tile_groupedmanifoldhyperconnection_kernel(tc, x, gn, phi_bytes, phi_scale, 
             late = k >= NT - 3
             halves = first or k == NT - 2
             split = G if first else 3 * QUAD if late else SPLIT
+            post_from = 3 * QUAD if first or late else VECTOR_FROM
             if not first:
                 do(coef_mm, k + 2)
             branch_mm(k)
@@ -503,7 +504,8 @@ def tile_groupedmanifoldhyperconnection_kernel(tc, x, gn, phi_bytes, phi_scale, 
                 next_out()
             next_sum()
             sink_sum(k + 1)
-            prod_vector(k, R, 12, G)
+            if post_from < G:
+                prod_vector(k, R, post_from, G)
             do(x_gain, k + 3, 0)
             do(x_gain, k + 3, 1)
             sink_inv(k + 1)
@@ -532,6 +534,7 @@ def tile_groupedmanifoldhyperconnection_kernel(tc, x, gn, phi_bytes, phi_scale, 
                 next_sum()
             if not late:
                 prod_scalar(k, 3, 12, G)
+                prod_scalar(k, R, 12, post_from)
             do(x_quant, k + 3)
             u_quant(k + 1)
             sink_last(k + 1)

@@ -27,8 +27,7 @@ QUAD = 4
 NQ = G // QUAD
 PLAIN_EVERY = 16
 THIRD_BANK_FROM = 24
-SPLIT = 11
-VECTOR_FROM = 14
+SPLIT = 13
 FLOPS = 2 * TOK * R * D * M + 2 * TOK * D * D
 
 
@@ -454,7 +453,6 @@ def tile_groupedmanifoldhyperconnection_kernel(tc, x, gn, phi_bytes, phi_scale, 
             late = k >= NT - 3
             halves = first or k == NT - 2
             split = G if first else 3 * QUAD if late else SPLIT
-            post_from = 3 * QUAD if first or late else VECTOR_FROM
             if not first:
                 do(coef_mm, k + 2)
             branch_mm(k)
@@ -504,10 +502,11 @@ def tile_groupedmanifoldhyperconnection_kernel(tc, x, gn, phi_bytes, phi_scale, 
                 next_out()
             next_sum()
             sink_sum(k + 1)
-            if post_from < G:
-                prod_vector(k, R, post_from, G)
+            prod_vector(k, R, 12, G)
             do(x_gain, k + 3, 0)
             do(x_gain, k + 3, 1)
+            if late:
+                prod_vector(k, 2, 12, G)
             sink_inv(k + 1)
             if first:
                 prod_vector(k, R, 8, 12)
@@ -529,12 +528,12 @@ def tile_groupedmanifoldhyperconnection_kernel(tc, x, gn, phi_bytes, phi_scale, 
             prod_scalar(k, 3, 8, 12)
             if not first:
                 prod_scalar(k, R, 8, 12)
+            if not first and not late:
                 prod_gpsimd(k, 2, split, G)
             if k == NT - 2:
                 next_sum()
             if not late:
                 prod_scalar(k, 3, 12, G)
-                prod_scalar(k, R, 12, post_from)
             do(x_quant, k + 3)
             u_quant(k + 1)
             sink_last(k + 1)

@@ -25,9 +25,10 @@ TOK = 1024
 NT = TOK // P
 QUAD = 4
 NQ = G // QUAD
-PLAIN_EVERY = 16
+PLAIN_QUADS = (0, 2)
+PLAIN_GROUP = 3
 THIRD_BANK_FROM = 24
-SPLIT = 13
+SPLIT = 12
 FLOPS = 2 * TOK * R * D * M + 2 * TOK * D * D
 
 
@@ -135,11 +136,8 @@ def tile_groupedmanifoldhyperconnection_kernel(tc, x, gn, phi_bytes, phi_scale, 
             nc.vector.quantize_mx(out=wc[:].bitcast(FP8X4), scales=ws[:], in_=wg[:].rearrange("p n t -> p (n t)"))
 
         state = [dict() for n in range(NT)]
-        passes = []
 
-        def add_turned(dst, src, start, stop):
-            passes.append(0)
-            plain = len(passes) % PLAIN_EVERY == 0
+        def add_turned(dst, src, start, stop, plain=False):
             nc.tensor.matmul(dst, src, ident[:], start=start, stop=stop, is_transpose=not plain)
 
         def x_turn(n, half):
@@ -350,7 +348,8 @@ def tile_groupedmanifoldhyperconnection_kernel(tc, x, gn, phi_bytes, phi_scale, 
             for b in range(QUAD):
                 for j in range(R + 1):
                     src = st["prod", j][:, QUAD * quad + b].rearrange("p i c -> p (i c)")
-                    add_turned(yt[:, :, b, :], src, j == 0, j == R)
+                    plain = quad in PLAIN_QUADS and b == PLAIN_GROUP and j < 2
+                    add_turned(yt[:, :, b, :], src, j == 0, j == R, plain)
             st["yt", quad] = yt
 
         def y_out(n, quad):

@@ -19,17 +19,23 @@ R = 4
 D = 512
 G = 16
 C = 32
-KC = 24
+GATES = 2 * R
+KC = GATES + R * R
 M = G * KC
+MT = M // P
 TOK = 1024
 NT = TOK // P
+TB = P // C
 QUAD = 4
 NQ = G // QUAD
-PLAIN_QUADS = (0, 2)
-PLAIN_GROUP = 3
-THIRD_BANK_FROM = 24
-SPLIT = 12
+HALF = G // 2
+BRANCH = R
 FLOPS = 2 * TOK * R * D * M + 2 * TOK * D * D
+
+PLAIN_QUADS = (0, 2)
+PLAIN_TERMS = 2
+LATE_PLAIN_QUADS = (0,)
+THIRD_BANK_FROM = NQ * (NT - 2)
 
 
 def spread(ap, axis, n):
@@ -38,10 +44,14 @@ def spread(ap, axis, n):
     return ap.unsqueeze(axis).to_broadcast(shape)
 
 
+def quad(a):
+    return QUAD * a, QUAD * (a + 1)
+
+
 def tile_groupedmanifoldhyperconnection_kernel(tc, x, gn, phi_bytes, phi_scale, bm, gf, w, out):
     nc = tc.nc
     x_rows = x.rearrange("b s r d -> (b s) (r d)")
-    out_view = out.rearrange("b (n tb t) i (q c) -> (b n) i q t tb c", tb=4, t=32, q=NQ)
+    out_view = out.rearrange("b (n tb t) i (q c) -> (b n) i q t tb c", tb=TB, t=C, q=NQ)
     with ExitStack() as ctx:
         keep = ctx.enter_context(tc.tile_pool(name="keep", bufs=1))
         sb = ctx.enter_context(tc.tile_pool(name="sb", bufs=2))
@@ -49,185 +59,177 @@ def tile_groupedmanifoldhyperconnection_kernel(tc, x, gn, phi_bytes, phi_scale, 
         ctx.enter_context(tc.manual_schedule())
 
         ident = keep.tile([P, P], F32)
-        bmz = keep.tile([P, M], BF16)
-        nc.gpsimd.memset(bmz[:], 0.0)
+        bm_row = keep.tile([P, M], BF16)
+        nc.gpsimd.memset(bm_row[:], 0.0)
         make_identity(nc, ident[:])
 
         scale = keep.tile([P, R, T], F32)
-        phv = phi_bytes.rearrange("(r p t) n -> r p t n", p=P, t=T)
-        phb = [keep.tile([P, T, M], U8, name="phb%d" % r) for r in range(R)]
+        phi_view = phi_bytes.rearrange("(r p t) n -> r p t n", p=P, t=T)
+        phi_raw = [keep.tile([P, T, M], U8, name="phb%d" % r) for r in range(R)]
         xs = [keep.tile([P, R * D], BF16, name="x%d" % n) for n in range(NT)]
-        gns = keep.tile([P, R, T], BF16)
-        gfs = keep.tile([P, T], BF16)
-        wraw = keep.tile([P, T, D], BF16)
+        gn_k = keep.tile([P, R, T], BF16)
+        gf_k = keep.tile([P, T], BF16)
+        w_raw = keep.tile([P, T, D], BF16)
 
         def load_x(n):
             nc.sync.dma_start(out=xs[n][:], in_=x_rows[n * P : (n + 1) * P, :])
 
         nc.sync.dma_start(out=scale[:], in_=phi_scale.rearrange("(r p t) o -> p r (t o)", p=P, t=T))
-        nc.sync.dma_start(out=phb[0][:], in_=phv[0])
-        nc.sync.dma_start(out=bmz[0:1, :], in_=bm.rearrange("(o n) -> o n", o=1))
-        nc.sync.dma_start(out=phb[1][:], in_=phv[1])
+        nc.sync.dma_start(out=phi_raw[0][:], in_=phi_view[0])
+        nc.sync.dma_start(out=bm_row[0:1, :], in_=bm.rearrange("(o n) -> o n", o=1))
+        nc.sync.dma_start(out=phi_raw[1][:], in_=phi_view[1])
         load_x(0)
-        nc.sync.dma_start(out=gns[:], in_=gn.rearrange("(r p t) -> p r t", p=P, t=T))
-        nc.sync.dma_start(out=phb[2][:], in_=phv[2])
-        nc.sync.dma_start(out=phb[3][:], in_=phv[3])
+        nc.sync.dma_start(out=gn_k[:], in_=gn.rearrange("(r p t) -> p r t", p=P, t=T))
+        nc.sync.dma_start(out=phi_raw[2][:], in_=phi_view[2])
+        nc.sync.dma_start(out=phi_raw[3][:], in_=phi_view[3])
         load_x(1)
-        nc.sync.dma_start(out=wraw[:], in_=w.rearrange("(p t) n -> p t n", t=T))
-        nc.sync.dma_start(out=gfs[:], in_=gf.rearrange("(p t) -> p t", t=T))
+        nc.sync.dma_start(out=w_raw[:], in_=w.rearrange("(p t) n -> p t n", t=T))
+        nc.sync.dma_start(out=gf_k[:], in_=gf.rearrange("(p t) -> p t", t=T))
         for n in range(2, NT):
             load_x(n)
 
-        phc = keep.tile([P, R, M], U32, align_bytes=64)
-        phs = keep.tile([P, R, M], U8, align_bytes=64)
-        phw = [keep.tile([P, T, M], BF16, name="phw%d" % r) for r in range(R)]
-        phg = [keep.tile([P, M, T], BF16, name="phg%d" % r, align_bytes=64) for r in range(R)]
-        bias = keep.tile([P, 3], F32)
-        hbias = keep.tile([P, 1], F32)
-        gfh = keep.tile([P, T], F32)
-        wg = keep.tile([P, D, T], BF16, align_bytes=64)
-        wc = keep.tile([P, D], U32, align_bytes=64)
-        ws = keep.tile([P, D], U8, align_bytes=64)
+        phi_codes = keep.tile([P, R, M], U32, align_bytes=64)
+        phi_scales = keep.tile([P, R, M], U8, align_bytes=64)
+        phi_wide = [keep.tile([P, T, M], BF16, name="phw%d" % r) for r in range(R)]
+        phi_words = [keep.tile([P, M, T], BF16, name="phg%d" % r, align_bytes=64) for r in range(R)]
+        bias = keep.tile([P, MT], F32)
+        half_bias = keep.tile([P, 1], F32)
+        half_gf = keep.tile([P, T], F32)
+        w_words = keep.tile([P, D, T], BF16, align_bytes=64)
+        w_codes = keep.tile([P, D], U32, align_bytes=64)
+        w_scales = keep.tile([P, D], U8, align_bytes=64)
 
-        def phi_widen(r, t, engine):
-            src = phb[r][:, t, :].bitcast(FP8)
-            col = scale[:, r, t : t + 1]
-            if engine == "vector":
-                nc.vector.tensor_scalar(phw[r][:, t, :], src, col, None, op0=ALU.mult)
-            else:
-                nc.scalar.activation(phw[r][:, t, :], src, ACT.Copy, scale=col)
 
-        def phi_group(r, engine):
-            src = phw[r][:].rearrange("p t (g k) -> p g t k", g=G)
-            for lo, hi, col in ((0, 8, 0), (8, KC, P)):
-                n = hi - lo
-                copy = nc.vector.tensor_copy if engine == "vector" else nc.scalar.copy
+        def phi_widen_vector(r, t):
+            src = phi_raw[r][:, t, :].bitcast(FP8)
+            nc.vector.tensor_scalar(phi_wide[r][:, t, :], src, scale[:, r, t : t + 1], None, op0=ALU.mult)
+
+        def phi_widen_scalar(r, t):
+            src = phi_raw[r][:, t, :].bitcast(FP8)
+            nc.scalar.activation(phi_wide[r][:, t, :], src, ACT.Copy, scale=scale[:, r, t : t + 1])
+
+        def phi_group(r, copy):
+            src = phi_wide[r][:].rearrange("p t (g k) -> p g t k", g=G)
+            for lo, hi, col in ((0, GATES, 0), (GATES, KC, P)):
                 copy(
-                    out=phg[r][:, col : col + G * n, :].rearrange("p (g a i) t -> p g a t i", g=G, i=4),
+                    out=phi_words[r][:, col : col + G * (hi - lo), :].rearrange("p (g a i) t -> p g a t i", g=G, i=4),
                     in_=src[:, :, :, lo:hi].rearrange("p g t (a i) -> p g a t i", i=4),
                 )
 
         def phi_quant(r):
             nc.vector.quantize_mx(
-                out=phc[:, r, :].bitcast(FP8X4), scales=phs[:, r, :], in_=phg[r][:].rearrange("p n t -> p (n t)")
+                out=phi_codes[:, r, :].bitcast(FP8X4),
+                scales=phi_scales[:, r, :],
+                in_=phi_words[r][:].rearrange("p n t -> p (n t)"),
             )
 
         def bias_turn():
-            bmp = keep.tile([P, M], F32)
-            src = bmz[:].rearrange("p (g k) -> p g k", g=G)
-            nc.scalar.copy(out=bmp[:, 0:P].rearrange("p (g k) -> p g k", g=G), in_=src[:, :, 0:8])
-            nc.scalar.copy(out=bmp[:, P:M].rearrange("p (g k) -> p g k", g=G), in_=src[:, :, 8:KC])
-            bps = ps.tile([P, 3, P], F32, name="tt")
-            for m in range(3):
-                nc.tensor.transpose(bps[:, m, :], bmp[:, m * P : (m + 1) * P], ident[:])
-            return bps
+            ordered = keep.tile([P, M], F32)
+            src = bm_row[:].rearrange("p (g k) -> p g k", g=G)
+            nc.scalar.copy(out=ordered[:, 0:P].rearrange("p (g k) -> p g k", g=G), in_=src[:, :, 0:GATES])
+            nc.scalar.copy(out=ordered[:, P:M].rearrange("p (g k) -> p g k", g=G), in_=src[:, :, GATES:KC])
+            turned = ps.tile([P, MT, P], F32, name="tt")
+            for m in range(MT):
+                nc.tensor.transpose(turned[:, m, :], ordered[:, m * P : (m + 1) * P], ident[:])
+            return turned
 
-        def bias_read(bps):
-            nc.scalar.copy(out=bias[:], in_=bps[:, :, 0])
-            nc.scalar.activation(hbias[:], bps[:, 0, 0:1], ACT.Copy, scale=0.5)
+        def bias_read(turned):
+            nc.scalar.copy(out=bias[:], in_=turned[:, :, 0])
+            nc.scalar.activation(half_bias[:], turned[:, 0, 0:1], ACT.Copy, scale=0.5)
 
         def w_group():
             nc.scalar.copy(
-                out=wg[:].rearrange("p (c i) t -> p c t i", i=4), in_=wraw[:].rearrange("p t (c i) -> p c t i", i=4)
+                out=w_words[:].rearrange("p (c i) t -> p c t i", i=4), in_=w_raw[:].rearrange("p t (c i) -> p c t i", i=4)
             )
-            nc.scalar.activation(gfh[:], gfs[:], ACT.Copy, scale=0.5)
+            nc.scalar.activation(half_gf[:], gf_k[:], ACT.Copy, scale=0.5)
 
         def w_quant():
-            nc.vector.quantize_mx(out=wc[:].bitcast(FP8X4), scales=ws[:], in_=wg[:].rearrange("p n t -> p (n t)"))
+            nc.vector.quantize_mx(
+                out=w_codes[:].bitcast(FP8X4), scales=w_scales[:], in_=w_words[:].rearrange("p n t -> p (n t)")
+            )
+
 
         state = [dict() for n in range(NT)]
 
-        def add_turned(dst, src, start, stop, plain=False):
+        def add_turned(dst, src, start, stop, plain):
             nc.tensor.matmul(dst, src, ident[:], start=start, stop=stop, is_transpose=not plain)
 
-        def x_turn(n, half):
+        def x_turn(n, pair):
             words = xs[n][:].bitcast(F32)
             xp = ps.tile([P, 2, 2, P], F32, name="xp", bufs=2)
             for rr in range(2):
-                r = 2 * half + rr
+                r = 2 * pair + rr
                 for u in range(2):
                     nc.tensor.transpose(xp[:, rr, u, :], words[:, 256 * r + u : 256 * (r + 1) : 2], ident[:])
-            state[n]["xp", half] = xp
+            state[n]["xp", pair] = xp
 
         def x_gain(n, r):
             st = state[n]
             if r == 0:
                 st["xn"] = sb.tile([P, R, P, T], BF16, name="xn", align_bytes=64)
+            turned = st["xp", r // 2][:, r % 2, :, :].rearrange("p u s -> p (u s)").bitcast(BF16)
             nc.vector.tensor_tensor(
-                out=st["xn"][:, r, :, :].rearrange("p k (u e) -> p k u e", e=2),
-                in0=st["xp", r // 2][:, r % 2, :, :].rearrange("p u k -> p (u k)").bitcast(BF16).rearrange(
-                    "p (u k e) -> p k u e", u=2, e=2
-                ),
-                in1=spread(gns[:, r, :].rearrange("p (u e) -> p u e", e=2), 1, P),
+                out=st["xn"][:, r, :, :].rearrange("p s (u e) -> p s u e", e=2),
+                in0=turned.rearrange("p (u s e) -> p s u e", u=2, e=2),
+                in1=spread(gn_k[:, r, :].rearrange("p (u e) -> p u e", e=2), 1, P),
                 op=ALU.mult,
             )
 
         def x_quant(n):
             st = state[n]
-            xqc = sb.tile([P, R, P], U32, name="xqc", align_bytes=64)
-            xqs = sb.tile([P, R, P], U8, name="xqs", align_bytes=64)
+            st["x_codes"] = sb.tile([P, R, P], U32, name="xqc", align_bytes=64)
+            st["x_scales"] = sb.tile([P, R, P], U8, name="xqs", align_bytes=64)
             nc.vector.quantize_mx(
-                out=xqc[:].rearrange("p r k -> p (r k)").bitcast(FP8X4),
-                scales=xqs[:].rearrange("p r k -> p (r k)"),
-                in_=st["xn"][:].rearrange("p r k t -> p (r k t)"),
+                out=st["x_codes"][:].rearrange("p r s -> p (r s)").bitcast(FP8X4),
+                scales=st["x_scales"][:].rearrange("p r s -> p (r s)"),
+                in_=st["xn"][:].rearrange("p r s t -> p (r s t)"),
             )
-            st["xq"] = (xqc, xqs)
 
         def coef_mm(n, lo=0, hi=R):
             st = state[n]
-            xqc, xqs = st["xq"]
             if lo == 0:
-                st["tt"] = ps.tile([P, 3, P], F32, name="tt")
-            tt = st["tt"]
+                st["tt"] = ps.tile([P, MT, P], F32, name="tt")
             for r in range(lo, hi):
-                for m in range(3):
+                for m in range(MT):
                     nc.tensor.matmul_mx(
-                        out=tt[:, m, :],
-                        lhsT=phc[:, r, m * P : (m + 1) * P].bitcast(FP8X4),
-                        lhsT_scale=phs[:, r, m * P : (m + 1) * P],
-                        rhs=xqc[:, r, :].bitcast(FP8X4),
-                        rhs_scale=xqs[:, r, :],
+                        out=st["tt"][:, m, :],
+                        lhsT=phi_codes[:, r, m * P : (m + 1) * P].bitcast(FP8X4),
+                        lhsT_scale=phi_scales[:, r, m * P : (m + 1) * P],
+                        rhs=st["x_codes"][:, r, :].bitcast(FP8X4),
+                        rhs_scale=st["x_scales"][:, r, :],
                         start=(r == 0 and m == 0),
-                        stop=(r == R - 1 and m == 2),
+                        stop=(r == R - 1 and m == MT - 1),
                     )
 
         def coef_act(n):
             st = state[n]
             tt = st["tt"]
-            co = sb.tile([P, 3, P], F32, name="co")
+            st["co"] = sb.tile([P, MT, P], F32, name="co")
             th = sb.tile([P, P], F32, name="th")
-            nc.scalar.activation(co[:, 1, :], tt[:, 1, :], ACT.Exp, bias=bias[:, 1:2])
-            nc.scalar.activation(th[:], tt[:, 0, :], ACT.Tanh, bias=hbias[:], scale=0.5)
-            nc.scalar.activation(co[:, 2, :], tt[:, 2, :], ACT.Exp, bias=bias[:, 2:3])
-            nc.scalar.activation(co[:, 0, :], th[:], ACT.Identity, bias=1.0)
-            st["co"] = co
+            nc.scalar.activation(st["co"][:, 1, :], tt[:, 1, :], ACT.Exp, bias=bias[:, 1:2])
+            nc.scalar.activation(th[:], tt[:, 0, :], ACT.Tanh, bias=half_bias[:], scale=0.5)
+            nc.scalar.activation(st["co"][:, 2, :], tt[:, 2, :], ACT.Exp, bias=bias[:, 2:3])
+            nc.scalar.activation(st["co"][:, 0, :], th[:], ACT.Identity, bias=1.0)
 
         def coef_turn(n):
             st = state[n]
-            ct = ps.tile([P, 3, P], F32, name="ct", bufs=2)
+            ct = ps.tile([P, MT, P], F32, name="ct", bufs=2)
             for m in (1, 2, 0):
                 nc.tensor.transpose(ct[:, m, :], st["co"][:, m, :], ident[:])
-            st["e"] = ct[:, 1:3, :].rearrange("p m (g i j) -> p (m g) i j", i=R, j=R)
+            st["e"] = ct[:, 1:MT, :].rearrange("p m (g i j) -> p (m g) i j", i=R, j=R)
             st["gate"] = ct[:, 0, :].rearrange("p (g k) -> p g k", g=G)
 
-        def q_to_psum(n, lo):
-            st = state[n]
-            upper = ps.tile([P, G, 2, R], F32, name="xp", bufs=2)
-            gs = slice(lo, G)
-            nc.tensor.matmul(upper[:, gs], ident[:], st["q"][:, gs, 2:R, :], start=True, stop=True)
-            st["upper"] = upper
 
         def sink_sum(n, lo=0, hi=G):
             st = state[n]
-            s = sb.tile([P, hi - lo, R], F32, name="sums", bufs=4)
-            nc.vector.tensor_reduce(s[:], st.get(("scaled", lo), st["e"][:, lo:hi]), axis=AX.X, op=ALU.add)
-            st["sums", lo] = s
+            sums = sb.tile([P, hi - lo, R], F32, name="sums", bufs=4)
+            nc.vector.tensor_reduce(sums[:], st.get(("scaled", lo), st["e"][:, lo:hi]), axis=AX.X, op=ALU.add)
+            st["sums", lo] = sums
 
         def sink_inv(n, lo=0, hi=G):
             st = state[n]
-            v = sb.tile([P, hi - lo, R], F32, name="factor", bufs=4)
-            nc.vector.reciprocal(v[:], st["sums", lo][:])
-            st["factor", lo] = v
+            st["factor", lo] = sb.tile([P, hi - lo, R], F32, name="factor", bufs=4)
+            nc.vector.reciprocal(st["factor", lo][:], st["sums", lo][:])
 
         def sink_scale(n, by_row, lo=0, hi=G):
             st = state[n]
@@ -238,82 +240,91 @@ def tile_groupedmanifoldhyperconnection_kernel(tc, x, gn, phi_bytes, phi_scale, 
             nc.vector.tensor_tensor(out=scaled[:], in0=e, in1=spread(st["factor", lo][:], 2, R), op=ALU.mult)
             st["scaled", lo] = scaled[:]
 
-        def sink_last(n, lo=0, hi=G, engine=nc.vector):
+        def sink_last(n, lo=0, hi=G):
             st = state[n]
             if lo == 0:
                 st["q"] = sb.tile([P, G, R, R], F32, name="q")
-            engine.tensor_tensor(
+            nc.vector.tensor_tensor(
                 out=st["q"][:, lo:hi], in0=st["scaled", lo], in1=spread(st["factor", lo][:], 3, R), op=ALU.mult
             )
 
-        def pre_prod(n, r):
+        def q_to_psum(n, lo):
             st = state[n]
-            pr = sb.tile([P, T, P], F32, name="pu", bufs=6)
+            st["q_upper"] = ps.tile([P, G, 2, R], F32, name="xp", bufs=2)
+            nc.tensor.matmul(st["q_upper"][:, lo:G], ident[:], st["q"][:, lo:G, 2:R, :], start=True, stop=True)
+
+
+        def pre_prod_vector(n, r):
+            st = state[n]
+            st["pu", r] = sb.tile([P, T, P], F32, name="pu", bufs=6)
             nc.vector.tensor_tensor(
-                out=pr[:].rearrange("p t (g c) -> p t g c", g=G),
+                out=st["pu", r][:].rearrange("p t (g c) -> p t g c", g=G),
                 in0=xs[n][:, r * D : (r + 1) * D].rearrange("p (g c t) -> p t g c", g=G, t=T),
-                in1=spread(spread(st["gate"][:, :, r], 2, 8), 1, T),
+                in1=spread(spread(st["gate"][:, :, r], 2, C // T), 1, T),
                 op=ALU.mult,
             )
-            st["pu", r] = pr
 
-        def gate_copy(n):
+        def pre_copy(n):
             st = state[n]
             st["pre"] = sb.tile([P, G, R], F32, name="pre")
             nc.scalar.copy(out=st["pre"][:], in_=st["gate"][:, :, 0:R])
 
         def pre_prod_scalar(n, r):
             st = state[n]
-            pr = sb.tile([P, T, P], F32, name="pu", bufs=6)
+            st["pu", r] = sb.tile([P, T, P], F32, name="pu", bufs=6)
             src = xs[n][:, r * D : (r + 1) * D].rearrange("p (g c t) -> p g t c", g=G, t=T)
+            dst = st["pu", r][:].rearrange("p t (g c) -> p g t c", g=G)
             for g in range(G):
-                nc.scalar.activation(pr[:, :, 8 * g : 8 * (g + 1)], src[:, g], ACT.Copy, scale=st["pre"][:, g, r : r + 1])
-            st["pu", r] = pr
+                nc.scalar.activation(dst[:, g], src[:, g], ACT.Copy, scale=st["pre"][:, g, r : r + 1])
 
         def u_sum(n):
             st = state[n]
-            ut = ps.tile([P, T, P], F32, name="uh")
+            st["ut"] = ps.tile([P, T, P], F32, name="uh")
             for r in range(R):
                 for t in range(T):
-                    add_turned(ut[:, t, :], st["pu", r][:, t, :], r == 0 and t == 0, r == R - 1 and t == T - 1)
-            st["ut"] = ut
+                    first_pass, last_pass = r == 0 and t == 0, r == R - 1 and t == T - 1
+                    add_turned(st["ut"][:, t, :], st["pu", r][:, t, :], first_pass, last_pass, False)
 
         def u_gain(n):
             st = state[n]
-            ug = sb.tile([P, P, T], BF16, name="ug", align_bytes=64)
+            st["ug"] = sb.tile([P, P, T], BF16, name="ug", align_bytes=64)
             nc.vector.tensor_tensor(
-                out=ug[:], in0=st["ut"][:].rearrange("p t k -> p k t"), in1=spread(gfh[:], 1, P), op=ALU.mult
+                out=st["ug"][:], in0=st["ut"][:].rearrange("p t s -> p s t"), in1=spread(half_gf[:], 1, P), op=ALU.mult
             )
-            st["ug"] = ug
 
         def u_quant(n):
             st = state[n]
-            ugc = sb.tile([P, P], U32, name="ugc", align_bytes=64)
-            ugs = sb.tile([P, P], U8, name="ugs", align_bytes=64)
-            nc.vector.quantize_mx(out=ugc[:].bitcast(FP8X4), scales=ugs[:], in_=st["ug"][:].rearrange("p k t -> p (k t)"))
-            st["ugq"] = (ugc, ugs)
+            st["u_codes"] = sb.tile([P, P], U32, name="ugc", align_bytes=64)
+            st["u_scales"] = sb.tile([P, P], U8, name="ugs", align_bytes=64)
+            nc.vector.quantize_mx(
+                out=st["u_codes"][:].bitcast(FP8X4), scales=st["u_scales"][:], in_=st["ug"][:].rearrange("p s t -> p (s t)")
+            )
 
         def branch_mm(n):
             st = state[n]
-            ugc, ugs = st["ugq"]
-            h = ps.tile([P, D], F32, name="uh")
+            st["h"] = ps.tile([P, D], F32, name="uh")
             nc.tensor.matmul_mx(
-                out=h[:], lhsT=ugc[:].bitcast(FP8X4), lhsT_scale=ugs[:], rhs=wc[:].bitcast(FP8X4), rhs_scale=ws[:],
-                start=True, stop=True,
+                out=st["h"][:],
+                lhsT=st["u_codes"][:].bitcast(FP8X4),
+                lhsT_scale=st["u_scales"][:],
+                rhs=w_codes[:].bitcast(FP8X4),
+                rhs_scale=w_scales[:],
+                start=True,
+                stop=True,
             )
-            st["h"] = h
 
         def branch_relu(n):
             st = state[n]
             st["hr"] = sb.tile([P, D], F32, name="hr")
             nc.scalar.activation(st["hr"][:], st["h"][:], ACT.Relu)
             st["post"] = sb.tile([P, G, R], F32, name="post")
-            nc.scalar.copy(out=st["post"][:], in_=st["gate"][:, :, R : 2 * R])
+            nc.scalar.copy(out=st["post"][:], in_=st["gate"][:, :, R:GATES])
 
         def branch_square(n):
             st = state[n]
             st["f"] = sb.tile([P, D], F32, name="f")
             nc.scalar.activation(st["f"][:], st["hr"][:], ACT.Square)
+
 
         def term(n, j, lo, hi):
             st = state[n]
@@ -325,39 +336,40 @@ def tile_groupedmanifoldhyperconnection_kernel(tc, x, gn, phi_bytes, phi_scale, 
         def prod_scalar(n, j, lo, hi):
             st = state[n]
             dst, src = term(n, j, lo, hi)
-            wt = st["q"][:, lo:hi, j, :] if j < R else st["post"][:, lo:hi, :]
+            weight = st["q"][:, lo:hi, j, :] if j < R else st["post"][:, lo:hi, :]
             for g in range(hi - lo):
                 for i in range(R):
-                    nc.scalar.activation(dst[:, g, i, :], src[:, g, :], ACT.Copy, scale=wt[:, g, i : i + 1])
+                    nc.scalar.activation(dst[:, g, i, :], src[:, g, :], ACT.Copy, scale=weight[:, g, i : i + 1])
 
         def prod_gpsimd(n, j, lo, hi):
             dst, src = term(n, j, lo, hi)
-            wt = state[n]["q"][:, lo:hi, j, :]
-            nc.gpsimd.tensor_tensor(out=dst, in0=spread(src, 2, R), in1=spread(wt, 3, C), op=ALU.mult)
+            weight = state[n]["q"][:, lo:hi, j, :]
+            nc.gpsimd.tensor_tensor(out=dst, in0=spread(src, 2, R), in1=spread(weight, 3, C), op=ALU.mult)
 
         def prod_vector(n, j, lo, hi):
             st = state[n]
             dst, src = term(n, j, lo, hi)
-            wt = st["upper"][:, lo:hi, j - 2, :] if j < R else st["gate"][:, lo:hi, R : 2 * R]
-            nc.vector.tensor_tensor(out=dst, in0=spread(src, 2, R), in1=spread(wt, 3, C), op=ALU.mult)
+            weight = st["q_upper"][:, lo:hi, j - 2, :] if j < R else st["gate"][:, lo:hi, R:GATES]
+            nc.vector.tensor_tensor(out=dst, in0=spread(src, 2, R), in1=spread(weight, 3, C), op=ALU.mult)
 
-        def y_sum(n, quad):
+        def y_sum(n, a):
             st = state[n]
-            third = NQ * n + quad >= THIRD_BANK_FROM and (NQ * n + quad) % 3 == 0
-            yt = ps.tile([P, 4, QUAD, 32], F32, name="tt" if third else "yy", bufs=1 if third else 2)
+            bank = NQ * n + a
+            plain_quads = PLAIN_QUADS if n < NT - 2 else LATE_PLAIN_QUADS
+            third = bank >= THIRD_BANK_FROM and bank % 3 == 0
+            st["yt", a] = ps.tile([P, TB, QUAD, C], F32, name="tt" if third else "yy", bufs=1 if third else 2)
             for b in range(QUAD):
-                for j in range(R + 1):
-                    src = st["prod", j][:, QUAD * quad + b].rearrange("p i c -> p (i c)")
-                    plain = quad in PLAIN_QUADS and b == PLAIN_GROUP and j < 2
-                    add_turned(yt[:, :, b, :], src, j == 0, j == R, plain)
-            st["yt", quad] = yt
+                for j in range(BRANCH + 1):
+                    src = st["prod", j][:, QUAD * a + b].rearrange("p i c -> p (i c)")
+                    plain = a in plain_quads and b == QUAD - 1 and j < PLAIN_TERMS
+                    add_turned(st["yt", a][:, :, b, :], src, j == 0, j == BRANCH, plain)
 
-        def y_out(n, quad):
+        def y_out(n, a):
             yo = sb.tile([P, D], F32, name="yo", bufs=5, align_bytes=64)
-            nc.vector.transpose(yo[:], state[n]["yt", quad][:].rearrange("p tb b t -> p (tb b t)"))
+            nc.vector.transpose(yo[:], state[n]["yt", a][:].rearrange("p tb b t -> p (tb b t)"))
             for i in range(R):
                 nc.sync.dma_start(
-                    out=out_view[n, i, quad], in_=yo[32 * i : 32 * (i + 1), :].rearrange("p (tb c) -> p tb c", tb=4)
+                    out=out_view[n, i, a], in_=yo[C * i : C * (i + 1), :].rearrange("p (tb c) -> p tb c", tb=TB)
                 )
 
         summed = []
@@ -365,28 +377,30 @@ def tile_groupedmanifoldhyperconnection_kernel(tc, x, gn, phi_bytes, phi_scale, 
 
         def next_sum():
             y_sum(*divmod(len(summed), NQ))
-            summed.append(0)
+            summed.append(True)
 
         def next_out():
             y_out(*divmod(len(stored), NQ))
-            stored.append(0)
+            stored.append(True)
 
-        def do(fn, n, *args):
-            if 0 <= n < NT:
-                fn(n, *args)
+        def if_tile(step, n, *args):
+            if n < NT:
+                step(n, *args)
 
-        for t in range(T):
-            phi_widen(0, t, "vector" if t < 2 else "scalar")
+        phi_widen_vector(0, 0)
+        phi_widen_vector(0, 1)
+        phi_widen_scalar(0, 2)
+        phi_widen_scalar(0, 3)
         x_turn(0, 0)
         x_turn(0, 1)
         for t in range(T):
-            phi_widen(1, t, "scalar")
+            phi_widen_scalar(1, t)
         turned_bias = bias_turn()
         for r in (2, 3):
             for t in range(T):
-                phi_widen(r, t, "scalar")
+                phi_widen_scalar(r, t)
         bias_read(turned_bias)
-        phi_group(0, "vector")
+        phi_group(0, nc.vector.tensor_copy)
         x_gain(0, 0)
         x_gain(0, 1)
         phi_quant(0)
@@ -394,11 +408,11 @@ def tile_groupedmanifoldhyperconnection_kernel(tc, x, gn, phi_bytes, phi_scale, 
         x_gain(0, 3)
         x_turn(1, 0)
         x_turn(1, 1)
-        phi_group(1, "vector")
+        phi_group(1, nc.vector.tensor_copy)
         x_quant(0)
         phi_quant(1)
-        phi_group(3, "scalar")
-        phi_group(2, "vector")
+        phi_group(3, nc.scalar.copy)
+        phi_group(2, nc.vector.tensor_copy)
         x_gain(1, 0)
         phi_quant(2)
         x_gain(1, 1)
@@ -421,119 +435,120 @@ def tile_groupedmanifoldhyperconnection_kernel(tc, x, gn, phi_bytes, phi_scale, 
         x_gain(2, 3)
         x_turn(3, 0)
         x_turn(3, 1)
-        gate_copy(0)
+        pre_copy(0)
         for r in range(R):
             pre_prod_scalar(0, r)
         coef_act(1)
         u_sum(0)
         coef_turn(1)
-        first, second = (0, G // 2), (G // 2, G)
+        low, high = (0, HALF), (HALF, G)
         for step, by_row in enumerate((True, False, True)):
-            sink_sum(0, *first)
-            sink_sum(0, *second)
+            sink_sum(0, *low)
+            sink_sum(0, *high)
             if step == 0:
                 x_quant(2)
-            sink_inv(0, *first)
-            sink_inv(0, *second)
-            sink_scale(0, by_row, *first)
-            sink_scale(0, by_row, *second)
+            sink_inv(0, *low)
+            sink_inv(0, *high)
+            sink_scale(0, by_row, *low)
+            sink_scale(0, by_row, *high)
         coef_mm(2)
-        sink_sum(0, *first)
-        sink_sum(0, *second)
+        sink_sum(0, *low)
+        sink_sum(0, *high)
         u_gain(0)
-        sink_inv(0, *first)
-        sink_inv(0, *second)
+        sink_inv(0, *low)
+        sink_inv(0, *high)
         u_quant(0)
-        sink_last(0, *first)
-        sink_last(0, *second)
+        sink_last(0, *low)
+        sink_last(0, *high)
 
         for k in range(NT - 1):
             first = k == 0
-            late = k >= NT - 3
-            halves = first or k == NT - 2
-            split = G if first else 3 * QUAD if late else SPLIT
+            late = k + 3 >= NT
+            before_last = k == NT - 2
+            halves = first or before_last
             if not first:
-                do(coef_mm, k + 2)
+                if_tile(coef_mm, k + 2)
             branch_mm(k)
             if not first:
-                do(x_turn, k + 3, 0)
-                do(x_turn, k + 3, 1)
+                if_tile(x_turn, k + 3, 0)
+                if_tile(x_turn, k + 3, 1)
             if late:
-                q_to_psum(k, 3 * QUAD)
+                q_to_psum(k, quad(3)[0])
             if halves:
-                prod_gpsimd(k, 0, 0, G // 2)
-                prod_gpsimd(k, 1, 0, G // 2)
+                prod_gpsimd(k, 0, *low)
+                prod_gpsimd(k, 1, *low)
             else:
                 prod_gpsimd(k, 0, 0, G)
             sink_sum(k + 1)
             if not first:
                 next_out()
-            prod_scalar(k, 2, 0, 4)
-            prod_scalar(k, 3, 0, 4)
+            prod_scalar(k, 2, *quad(0))
+            prod_scalar(k, 3, *quad(0))
             branch_relu(k)
-            do(coef_act, k + 2)
+            if_tile(coef_act, k + 2)
             branch_square(k)
             if not first:
                 next_sum()
                 next_sum()
             sink_inv(k + 1)
-            pre_prod(k + 1, 0)
+            pre_prod_vector(k + 1, 0)
             sink_scale(k + 1, True)
-            pre_prod(k + 1, 1)
+            pre_prod_vector(k + 1, 1)
             sink_sum(k + 1)
             if not first:
                 next_out()
-            pre_prod(k + 1, 2)
+            pre_prod_vector(k + 1, 2)
             sink_inv(k + 1)
-            pre_prod(k + 1, 3)
+            pre_prod_vector(k + 1, 3)
             u_sum(k + 1)
-            prod_scalar(k, R, 0, 4)
+            prod_scalar(k, BRANCH, *quad(0))
             if halves:
-                prod_gpsimd(k, 0, G // 2, G)
-                prod_gpsimd(k, 1, G // 2, G)
+                prod_gpsimd(k, 0, *high)
             else:
-                prod_gpsimd(k, 1, 0, G // 2)
-                prod_gpsimd(k, 1, G // 2, G)
+                prod_gpsimd(k, 1, *low)
+            prod_gpsimd(k, 1, *high)
             sink_scale(k + 1, False)
             if first:
-                prod_vector(k, R, 4, 8)
+                prod_vector(k, BRANCH, *quad(1))
             else:
                 next_out()
             next_sum()
             sink_sum(k + 1)
-            prod_vector(k, R, 12, G)
-            do(x_gain, k + 3, 0)
-            do(x_gain, k + 3, 1)
+            prod_vector(k, BRANCH, *quad(3))
+            if_tile(x_gain, k + 3, 0)
+            if_tile(x_gain, k + 3, 1)
             if late:
-                prod_vector(k, 2, 12, G)
+                prod_vector(k, 2, *quad(3))
             sink_inv(k + 1)
             if first:
-                prod_vector(k, R, 8, 12)
+                prod_vector(k, BRANCH, *quad(2))
             else:
                 next_out()
-            do(coef_turn, k + 2)
-            for j in (2, 3) if first else (2, 3, R):
-                prod_scalar(k, j, 4, 8)
+            if_tile(coef_turn, k + 2)
+            prod_scalar(k, 2, *quad(1))
+            prod_scalar(k, 3, *quad(1))
+            if not first:
+                prod_scalar(k, BRANCH, *quad(1))
             next_sum()
             sink_scale(k + 1, True)
-            do(x_gain, k + 3, 2)
-            do(x_gain, k + 3, 3)
+            if_tile(x_gain, k + 3, 2)
+            if_tile(x_gain, k + 3, 3)
             if late:
-                prod_vector(k, 3, 12, G)
+                prod_vector(k, 3, *quad(3))
             sink_sum(k + 1)
             u_gain(k + 1)
             sink_inv(k + 1)
-            prod_scalar(k, 2, 8, split)
-            prod_scalar(k, 3, 8, 12)
+            prod_scalar(k, 2, *(high if first else quad(2)))
+            prod_scalar(k, 3, *quad(2))
             if not first:
-                prod_scalar(k, R, 8, 12)
+                prod_scalar(k, BRANCH, *quad(2))
             if not first and not late:
-                prod_gpsimd(k, 2, split, G)
-            if k == NT - 2:
+                prod_gpsimd(k, 2, *quad(3))
+            if before_last:
                 next_sum()
             if not late:
-                prod_scalar(k, 3, 12, G)
-            do(x_quant, k + 3)
+                prod_scalar(k, 3, *quad(3))
+            if_tile(x_quant, k + 3)
             u_quant(k + 1)
             sink_last(k + 1)
 
@@ -543,18 +558,17 @@ def tile_groupedmanifoldhyperconnection_kernel(tc, x, gn, phi_bytes, phi_scale, 
         next_out()
         next_out()
         next_sum()
-        prod_scalar(last, 1, 8, G)
+        prod_scalar(last, 1, *high)
         branch_relu(last)
         branch_square(last)
-        for lo in range(0, G, QUAD):
-            hi = lo + QUAD
-            prod_gpsimd(last, 0, lo, hi)
-            if lo < 8:
-                prod_gpsimd(last, 1, lo, hi)
-            prod_vector(last, 2, lo, hi)
+        for a in range(NQ):
+            prod_gpsimd(last, 0, *quad(a))
+            if a < NQ // 2:
+                prod_gpsimd(last, 1, *quad(a))
+            prod_vector(last, 2, *quad(a))
             next_out()
-            prod_vector(last, 3, lo, hi)
-            prod_scalar(last, R, lo, hi)
+            prod_vector(last, 3, *quad(a))
+            prod_scalar(last, BRANCH, *quad(a))
             next_sum()
         next_out()
         next_out()

@@ -34,7 +34,7 @@ FLOPS = 2 * TOK * R * D * M + 2 * TOK * D * D
 
 PLAIN_QUADS = (0, 2)
 PLAIN_TERMS = 2
-LATE_PLAIN_QUADS = (0,)
+LAST_PLAIN_BANK = NQ * (NT - 2)
 THIRD_BANK_FROM = NQ * (NT - 2)
 
 
@@ -355,13 +355,13 @@ def tile_groupedmanifoldhyperconnection_kernel(tc, x, gn, phi_bytes, phi_scale, 
         def y_sum(n, a):
             st = state[n]
             bank = NQ * n + a
-            plain_quads = PLAIN_QUADS if n < NT - 2 else LATE_PLAIN_QUADS
             third = bank >= THIRD_BANK_FROM and bank % 3 == 0
+            paired = a in PLAIN_QUADS and bank <= LAST_PLAIN_BANK
             st["yt", a] = ps.tile([P, TB, QUAD, C], F32, name="tt" if third else "yy", bufs=1 if third else 2)
             for b in range(QUAD):
                 for j in range(BRANCH + 1):
                     src = st["prod", j][:, QUAD * a + b].rearrange("p i c -> p (i c)")
-                    plain = a in plain_quads and b == QUAD - 1 and j < PLAIN_TERMS
+                    plain = paired and b == QUAD - 1 and j < PLAIN_TERMS
                     add_turned(st["yt", a][:, :, b, :], src, j == 0, j == BRANCH, plain)
 
         def y_out(n, a):
@@ -401,16 +401,14 @@ def tile_groupedmanifoldhyperconnection_kernel(tc, x, gn, phi_bytes, phi_scale, 
                 phi_widen_scalar(r, t)
         bias_read(turned_bias)
         phi_group(0, nc.vector.tensor_copy)
-        x_gain(0, 0)
-        x_gain(0, 1)
         phi_quant(0)
-        x_gain(0, 2)
-        x_gain(0, 3)
+        phi_group(1, nc.vector.tensor_copy)
+        for r in range(R):
+            x_gain(0, r)
         x_turn(1, 0)
         x_turn(1, 1)
-        phi_group(1, nc.vector.tensor_copy)
-        x_quant(0)
         phi_quant(1)
+        x_quant(0)
         phi_group(3, nc.scalar.copy)
         phi_group(2, nc.vector.tensor_copy)
         x_gain(1, 0)

@@ -32,10 +32,8 @@ HALF = G // 2
 BRANCH = R
 FLOPS = 2 * TOK * R * D * M + 2 * TOK * D * D
 
-PLAIN_QUADS = (0, 2)
-PLAIN_TERMS = 2
-LAST_PLAIN_BANK = NQ * (NT - 2)
-THIRD_BANK_FROM = NQ * (NT - 2)
+BANKS = {"xp": 2, "tt": 1, "yy": 2, "uh": 1, "ct": 2}
+XN_BUFS = 3
 
 
 def spread(ap, axis, n):
@@ -61,6 +59,8 @@ def tile_groupedmanifoldhyperconnection_kernel(tc, x, gn, phi_bytes, phi_scale, 
         ident = keep.tile([P, P], F32)
         bm_row = keep.tile([P, M], BF16)
         nc.gpsimd.memset(bm_row[:], 0.0)
+        ones = keep.tile([P, 2], BF16)
+        nc.gpsimd.memset(ones[:], 1.0)
         make_identity(nc, ident[:])
 
         scale = keep.tile([P, R, T], F32)
@@ -76,12 +76,14 @@ def tile_groupedmanifoldhyperconnection_kernel(tc, x, gn, phi_bytes, phi_scale, 
 
         nc.sync.dma_start(out=scale[:], in_=phi_scale.rearrange("(r p t) o -> p r (t o)", p=P, t=T))
         nc.sync.dma_start(out=phi_raw[0][:], in_=phi_view[0])
-        nc.sync.dma_start(out=bm_row[0:1, :], in_=bm.rearrange("(o n) -> o n", o=1))
         nc.sync.dma_start(out=phi_raw[1][:], in_=phi_view[1])
         load_x(0)
         nc.sync.dma_start(out=gn_k[:], in_=gn.rearrange("(r p t) -> p r t", p=P, t=T))
         nc.sync.dma_start(out=phi_raw[2][:], in_=phi_view[2])
         nc.sync.dma_start(out=phi_raw[3][:], in_=phi_view[3])
+        bm_groups = bm.rearrange("(o g k) -> o g k", o=1, g=G)
+        nc.sync.dma_start(out=bm_row[0:1, 0:P].rearrange("p (g k) -> p g k", g=G), in_=bm_groups[:, :, 0:GATES])
+        nc.sync.dma_start(out=bm_row[0:1, P:M].rearrange("p (g k) -> p g k", g=G), in_=bm_groups[:, :, GATES:KC])
         load_x(1)
         nc.sync.dma_start(out=w_raw[:], in_=w.rearrange("(p t) n -> p t n", t=T))
         nc.sync.dma_start(out=gf_k[:], in_=gf.rearrange("(p t) -> p t", t=T))
@@ -100,6 +102,8 @@ def tile_groupedmanifoldhyperconnection_kernel(tc, x, gn, phi_bytes, phi_scale, 
         w_scales = keep.tile([P, D], U8, align_bytes=64)
 
 
+        once = dict()
+
         def phi_widen_vector(r, t):
             src = phi_raw[r][:, t, :].bitcast(FP8)
             nc.vector.tensor_scalar(phi_wide[r][:, t, :], src, scale[:, r, t : t + 1], None, op0=ALU.mult)
@@ -108,8 +112,9 @@ def tile_groupedmanifoldhyperconnection_kernel(tc, x, gn, phi_bytes, phi_scale, 
             src = phi_raw[r][:, t, :].bitcast(FP8)
             nc.scalar.activation(phi_wide[r][:, t, :], src, ACT.Copy, scale=scale[:, r, t : t + 1])
 
-        def phi_group(r, copy):
+        def phi_group(r, engine):
             src = phi_wide[r][:].rearrange("p t (g k) -> p g t k", g=G)
+            copy = nc.vector.tensor_copy if engine == "vector" else nc.scalar.copy
             for lo, hi, col in ((0, GATES, 0), (GATES, KC, P)):
                 copy(
                     out=phi_words[r][:, col : col + G * (hi - lo), :].rearrange("p (g a i) t -> p g a t i", g=G, i=4),
@@ -124,28 +129,31 @@ def tile_groupedmanifoldhyperconnection_kernel(tc, x, gn, phi_bytes, phi_scale, 
             )
 
         def bias_turn():
-            ordered = keep.tile([P, M], F32)
-            src = bm_row[:].rearrange("p (g k) -> p g k", g=G)
-            nc.scalar.copy(out=ordered[:, 0:P].rearrange("p (g k) -> p g k", g=G), in_=src[:, :, 0:GATES])
-            nc.scalar.copy(out=ordered[:, P:M].rearrange("p (g k) -> p g k", g=G), in_=src[:, :, GATES:KC])
-            turned = ps.tile([P, MT, P], F32, name="tt")
+            once["bias"] = ps.tile([P, MT, 2], F32, name="uh")
             for m in range(MT):
-                nc.tensor.transpose(turned[:, m, :], ordered[:, m * P : (m + 1) * P], ident[:])
-            return turned
+                nc.tensor.matmul(once["bias"][:, m, :], bm_row[:, m * P : (m + 1) * P], ones[:], start=True, stop=True)
 
-        def bias_read(turned):
-            nc.scalar.copy(out=bias[:], in_=turned[:, :, 0])
-            nc.scalar.activation(half_bias[:], turned[:, 0, 0:1], ACT.Copy, scale=0.5)
+        def bias_read():
+            nc.scalar.copy(out=bias[:], in_=once["bias"][:, :, 0])
+            nc.scalar.activation(half_bias[:], once["bias"][:, 0, 0:1], ACT.Copy, scale=0.5)
 
-        def w_group():
-            nc.scalar.copy(
-                out=w_words[:].rearrange("p (c i) t -> p c t i", i=4), in_=w_raw[:].rearrange("p t (c i) -> p c t i", i=4)
+        def w_group(half):
+            cols = slice(half * D // 2, (half + 1) * D // 2)
+            copy = nc.vector.tensor_copy if half else nc.scalar.copy
+            copy(
+                out=w_words[:, cols, :].rearrange("p (c i) t -> p c t i", i=4),
+                in_=w_raw[:, :, cols].rearrange("p t (c i) -> p c t i", i=4),
             )
+
+        def gf_half():
             nc.scalar.activation(half_gf[:], gf_k[:], ACT.Copy, scale=0.5)
 
-        def w_quant():
+        def w_quant(half):
+            cols = slice(half * D // 2, (half + 1) * D // 2)
             nc.vector.quantize_mx(
-                out=w_codes[:].bitcast(FP8X4), scales=w_scales[:], in_=w_words[:].rearrange("p n t -> p (n t)")
+                out=w_codes[:, cols].bitcast(FP8X4),
+                scales=w_scales[:, cols],
+                in_=w_words[:, cols, :].rearrange("p n t -> p (n t)"),
             )
 
 
@@ -166,7 +174,7 @@ def tile_groupedmanifoldhyperconnection_kernel(tc, x, gn, phi_bytes, phi_scale, 
         def x_gain(n, r):
             st = state[n]
             if r == 0:
-                st["xn"] = sb.tile([P, R, P, T], BF16, name="xn", align_bytes=64)
+                st["xn"] = sb.tile([P, R, P, T], BF16, name="xn", bufs=XN_BUFS, align_bytes=64)
             turned = st["xp", r // 2][:, r % 2, :, :].rearrange("p u s -> p (u s)").bitcast(BF16)
             nc.vector.tensor_tensor(
                 out=st["xn"][:, r, :, :].rearrange("p s (u e) -> p s u e", e=2),
@@ -177,18 +185,18 @@ def tile_groupedmanifoldhyperconnection_kernel(tc, x, gn, phi_bytes, phi_scale, 
 
         def x_quant(n):
             st = state[n]
-            st["x_codes"] = sb.tile([P, R, P], U32, name="xqc", align_bytes=64)
-            st["x_scales"] = sb.tile([P, R, P], U8, name="xqs", align_bytes=64)
+            st["x_codes"] = sb.tile([P, R, P], U32, name="xqc", bufs=3, align_bytes=64)
+            st["x_scales"] = sb.tile([P, R, P], U8, name="xqs", bufs=3, align_bytes=64)
             nc.vector.quantize_mx(
                 out=st["x_codes"][:].rearrange("p r s -> p (r s)").bitcast(FP8X4),
                 scales=st["x_scales"][:].rearrange("p r s -> p (r s)"),
                 in_=st["xn"][:].rearrange("p r s t -> p (r s t)"),
             )
 
-        def coef_mm(n, lo=0, hi=R):
+        def coef_mm(n, bank, lo, hi):
             st = state[n]
             if lo == 0:
-                st["tt"] = ps.tile([P, MT, P], F32, name="tt")
+                st["tt"] = ps.tile([P, MT, P], F32, name=bank, bufs=BANKS[bank])
             for r in range(lo, hi):
                 for m in range(MT):
                     nc.tensor.matmul_mx(
@@ -204,7 +212,7 @@ def tile_groupedmanifoldhyperconnection_kernel(tc, x, gn, phi_bytes, phi_scale, 
         def coef_act(n):
             st = state[n]
             tt = st["tt"]
-            st["co"] = sb.tile([P, MT, P], F32, name="co")
+            st["co"] = sb.tile([P, MT, P], F32, name="co", bufs=3)
             th = sb.tile([P, P], F32, name="th")
             nc.scalar.activation(st["co"][:, 1, :], tt[:, 1, :], ACT.Exp, bias=bias[:, 1:2])
             nc.scalar.activation(th[:], tt[:, 0, :], ACT.Tanh, bias=half_bias[:], scale=0.5)
@@ -217,30 +225,41 @@ def tile_groupedmanifoldhyperconnection_kernel(tc, x, gn, phi_bytes, phi_scale, 
             for m in (1, 2, 0):
                 nc.tensor.transpose(ct[:, m, :], st["co"][:, m, :], ident[:])
             st["e"] = ct[:, 1:MT, :].rearrange("p m (g i j) -> p (m g) i j", i=R, j=R)
+            st["q_psum"] = ct[:, 1:MT, :].rearrange("p m (g j i) -> p (m g) j i", i=R, j=R)
             st["gate"] = ct[:, 0, :].rearrange("p (g k) -> p g k", g=G)
 
 
-        def sink_sum(n, lo=0, hi=G):
+        def sink_sum(n, step, lo, hi):
             st = state[n]
             sums = sb.tile([P, hi - lo, R], F32, name="sums", bufs=4)
             nc.vector.tensor_reduce(sums[:], st.get(("scaled", lo), st["e"][:, lo:hi]), axis=AX.X, op=ALU.add)
             st["sums", lo] = sums
 
-        def sink_inv(n, lo=0, hi=G):
+        def sink_inv_vector(n, step, lo, hi):
             st = state[n]
             st["factor", lo] = sb.tile([P, hi - lo, R], F32, name="factor", bufs=4)
             nc.vector.reciprocal(st["factor", lo][:], st["sums", lo][:])
 
-        def sink_scale(n, by_row, lo=0, hi=G):
+        def sink_root(n, step, lo, hi):
+            st = state[n]
+            st["root", lo] = sb.tile([P, hi - lo, R], F32, name="root")
+            nc.scalar.activation(st["root", lo][:], st["sums", lo][:], ACT.Abs_reciprocal_sqrt)
+
+        def sink_inv_scalar(n, step, lo, hi):
+            st = state[n]
+            st["factor", lo] = sb.tile([P, hi - lo, R], F32, name="factor", bufs=4)
+            nc.scalar.activation(st["factor", lo][:], st["root", lo][:], ACT.Square)
+
+        def sink_scale(n, step, lo, hi):
             st = state[n]
             scaled = sb.tile([P, hi - lo, R, R], F32, name="scaled", bufs=4)
             e = st["e"][:, lo:hi]
-            if by_row:
+            if step % 2 == 0:
                 e = e.rearrange("p g i j -> p g j i")
             nc.vector.tensor_tensor(out=scaled[:], in0=e, in1=spread(st["factor", lo][:], 2, R), op=ALU.mult)
             st["scaled", lo] = scaled[:]
 
-        def sink_last(n, lo=0, hi=G):
+        def sink_last(n, lo, hi):
             st = state[n]
             if lo == 0:
                 st["q"] = sb.tile([P, G, R, R], F32, name="q")
@@ -248,10 +267,9 @@ def tile_groupedmanifoldhyperconnection_kernel(tc, x, gn, phi_bytes, phi_scale, 
                 out=st["q"][:, lo:hi], in0=st["scaled", lo], in1=spread(st["factor", lo][:], 3, R), op=ALU.mult
             )
 
-        def q_to_psum(n, lo):
+        def q_to_psum(n):
             st = state[n]
-            st["q_upper"] = ps.tile([P, G, 2, R], F32, name="xp", bufs=2)
-            nc.tensor.matmul(st["q_upper"][:, lo:G], ident[:], st["q"][:, lo:G, 2:R, :], start=True, stop=True)
+            nc.tensor.matmul(st["q_psum"], ident[:], st["q"][:], start=True, stop=True)
 
 
         def pre_prod_vector(n, r):
@@ -264,10 +282,26 @@ def tile_groupedmanifoldhyperconnection_kernel(tc, x, gn, phi_bytes, phi_scale, 
                 op=ALU.mult,
             )
 
-        def pre_copy(n):
+        def gate_copy(n):
             st = state[n]
-            st["pre"] = sb.tile([P, G, R], F32, name="pre")
-            nc.scalar.copy(out=st["pre"][:], in_=st["gate"][:, :, 0:R])
+            st["gate_sb"] = sb.tile([P, G, GATES], F32, name="gate")
+            nc.vector.tensor_copy(out=st["gate_sb"][:], in_=st["gate"])
+
+        def post_copy(n):
+            st = state[n]
+            st["gate_sb"] = sb.tile([P, G, GATES], F32, name="gate")
+            nc.scalar.copy(out=st["gate_sb"][:, :, R:GATES], in_=st["gate"][:, :, R:GATES])
+
+        def pre_prod_gpsimd(n, r):
+            st = state[n]
+            tile = sb.tile([P, P, T], F32, name="pu", bufs=6)
+            st["pu", r] = tile[:].rearrange("p c t -> p t c")
+            nc.gpsimd.tensor_tensor(
+                out=tile[:].rearrange("p (g c) t -> p g (c t)", g=G),
+                in0=xs[n][:, r * D : (r + 1) * D].rearrange("p (g c) -> p g c", g=G),
+                in1=spread(st["gate_sb"][:, :, r], 2, C),
+                op=ALU.mult,
+            )
 
         def pre_prod_scalar(n, r):
             st = state[n]
@@ -275,15 +309,15 @@ def tile_groupedmanifoldhyperconnection_kernel(tc, x, gn, phi_bytes, phi_scale, 
             src = xs[n][:, r * D : (r + 1) * D].rearrange("p (g c t) -> p g t c", g=G, t=T)
             dst = st["pu", r][:].rearrange("p t (g c) -> p g t c", g=G)
             for g in range(G):
-                nc.scalar.activation(dst[:, g], src[:, g], ACT.Copy, scale=st["pre"][:, g, r : r + 1])
+                nc.scalar.activation(dst[:, g], src[:, g], ACT.Copy, scale=st["gate_sb"][:, g, r : r + 1])
 
-        def u_sum(n):
+        def u_sum(n, plain):
             st = state[n]
             st["ut"] = ps.tile([P, T, P], F32, name="uh")
             for r in range(R):
                 for t in range(T):
                     first_pass, last_pass = r == 0 and t == 0, r == R - 1 and t == T - 1
-                    add_turned(st["ut"][:, t, :], st["pu", r][:, t, :], first_pass, last_pass, False)
+                    add_turned(st["ut"][:, t, :], st["pu", r][:, t, :], first_pass, last_pass, r == 0 and t < plain)
 
         def u_gain(n):
             st = state[n]
@@ -317,8 +351,6 @@ def tile_groupedmanifoldhyperconnection_kernel(tc, x, gn, phi_bytes, phi_scale, 
             st = state[n]
             st["hr"] = sb.tile([P, D], F32, name="hr")
             nc.scalar.activation(st["hr"][:], st["h"][:], ACT.Relu)
-            st["post"] = sb.tile([P, G, R], F32, name="post")
-            nc.scalar.copy(out=st["post"][:], in_=st["gate"][:, :, R:GATES])
 
         def branch_square(n):
             st = state[n]
@@ -336,7 +368,7 @@ def tile_groupedmanifoldhyperconnection_kernel(tc, x, gn, phi_bytes, phi_scale, 
         def prod_scalar(n, j, lo, hi):
             st = state[n]
             dst, src = term(n, j, lo, hi)
-            weight = st["q"][:, lo:hi, j, :] if j < R else st["post"][:, lo:hi, :]
+            weight = st["q"][:, lo:hi, j, :] if j < R else st["gate_sb"][:, lo:hi, R:GATES]
             for g in range(hi - lo):
                 for i in range(R):
                     nc.scalar.activation(dst[:, g, i, :], src[:, g, :], ACT.Copy, scale=weight[:, g, i : i + 1])
@@ -349,20 +381,17 @@ def tile_groupedmanifoldhyperconnection_kernel(tc, x, gn, phi_bytes, phi_scale, 
         def prod_vector(n, j, lo, hi):
             st = state[n]
             dst, src = term(n, j, lo, hi)
-            weight = st["q_upper"][:, lo:hi, j - 2, :] if j < R else st["gate"][:, lo:hi, R:GATES]
+            weight = st["q_psum"][:, lo:hi, j, :] if j < R else st["gate"][:, lo:hi, R:GATES]
             nc.vector.tensor_tensor(out=dst, in0=spread(src, 2, R), in1=spread(weight, 3, C), op=ALU.mult)
 
-        def y_sum(n, a):
+        def y_sum(n, a, bank, terms, plain):
             st = state[n]
-            bank = NQ * n + a
-            third = bank >= THIRD_BANK_FROM and bank % 3 == 0
-            paired = a in PLAIN_QUADS and bank <= LAST_PLAIN_BANK
-            st["yt", a] = ps.tile([P, TB, QUAD, C], F32, name="tt" if third else "yy", bufs=1 if third else 2)
-            for b in range(QUAD):
-                for j in range(BRANCH + 1):
+            st["yt", a] = ps.tile([P, TB, QUAD, C], F32, name=bank, bufs=BANKS[bank])
+            for j in terms:
+                for b in range(QUAD):
                     src = st["prod", j][:, QUAD * a + b].rearrange("p i c -> p (i c)")
-                    plain = paired and b == QUAD - 1 and j < PLAIN_TERMS
-                    add_turned(st["yt", a][:, :, b, :], src, j == 0, j == BRANCH, plain)
+                    first_pass, last_pass = j == terms[0] and b == 0, j == terms[-1] and b == QUAD - 1
+                    add_turned(st["yt", a][:, :, b, :], src, first_pass, last_pass, j == terms[0] and b < plain)
 
         def y_out(n, a):
             yo = sb.tile([P, D], F32, name="yo", bufs=5, align_bytes=64)
@@ -372,201 +401,269 @@ def tile_groupedmanifoldhyperconnection_kernel(tc, x, gn, phi_bytes, phi_scale, 
                     out=out_view[n, i, a], in_=yo[C * i : C * (i + 1), :].rearrange("p (tb c) -> p tb c", tb=TB)
                 )
 
-        summed = []
-        stored = []
+        PAIRS = [0,(0,),(0,),(0,2,0,0,0),(2,0,2,0,0),(2,0,2,0,0),(2,0,2,0,0)]
+        LAG = [0,0,0,2,2,2,2,1]
+        OUT = [0,0,0,3,3,3,3,3]
+        low, high, every = (0, HALF), (HALF, G), (0, G)
+        tensor, vector, scalar, gpsimd = [], [], [], []
 
-        def next_sum():
-            y_sum(*divmod(len(summed), NQ))
-            summed.append(True)
+        def chain(n, fill, own_inverses, parts=(every,)):
+            out = []
+            for step in range(4):
+                out.extend((sink_sum, n, step) + part for part in parts)
+                out.extend(fill[2 * step])
+                if step in own_inverses:
+                    out.extend((sink_inv_vector, n, step) + part for part in parts)
+                    out.extend(fill[2 * step + 1][:1])
+                if step < 3:
+                    out.extend((sink_scale, n, step) + part for part in parts)
+                out.extend(fill[2 * step + 1][1 if step in own_inverses else 0 :])
+            return out
 
-        def next_out():
-            y_out(*divmod(len(stored), NQ))
-            stored.append(True)
+        def gains(n, *streams):
+            return [(x_gain, n, r) for r in streams]
 
-        def if_tile(step, n, *args):
-            if n < NT:
-                step(n, *args)
+        def pres(n, *streams):
+            return [(pre_prod_vector, n, r) for r in streams]
 
-        phi_widen_vector(0, 0)
-        phi_widen_vector(0, 1)
-        phi_widen_scalar(0, 2)
-        phi_widen_scalar(0, 3)
-        x_turn(0, 0)
-        x_turn(0, 1)
-        for t in range(T):
-            phi_widen_scalar(1, t)
-        turned_bias = bias_turn()
-        for r in (2, 3):
-            for t in range(T):
-                phi_widen_scalar(r, t)
-        bias_read(turned_bias)
-        phi_group(0, nc.vector.tensor_copy)
-        phi_quant(0)
-        phi_group(1, nc.vector.tensor_copy)
-        for r in range(R):
-            x_gain(0, r)
-        x_turn(1, 0)
-        x_turn(1, 1)
-        phi_quant(1)
-        x_quant(0)
-        phi_group(3, nc.scalar.copy)
-        phi_group(2, nc.vector.tensor_copy)
-        x_gain(1, 0)
-        phi_quant(2)
-        x_gain(1, 1)
-        phi_quant(3)
-        coef_mm(0, 0, R - 1)
-        x_turn(2, 0)
-        coef_mm(0, R - 1, R)
-        w_group()
-        coef_act(0)
-        x_gain(1, 2)
-        x_gain(1, 3)
-        x_turn(2, 1)
-        coef_turn(0)
-        x_quant(1)
-        coef_mm(1)
-        x_gain(2, 0)
-        x_gain(2, 1)
-        w_quant()
-        x_gain(2, 2)
-        x_gain(2, 3)
-        x_turn(3, 0)
-        x_turn(3, 1)
-        pre_copy(0)
-        for r in range(R):
-            pre_prod_scalar(0, r)
-        coef_act(1)
-        u_sum(0)
-        coef_turn(1)
-        low, high = (0, HALF), (HALF, G)
-        for step, by_row in enumerate((True, False, True)):
-            sink_sum(0, *low)
-            sink_sum(0, *high)
-            if step == 0:
-                x_quant(2)
-            sink_inv(0, *low)
-            sink_inv(0, *high)
-            sink_scale(0, by_row, *low)
-            sink_scale(0, by_row, *high)
-        coef_mm(2)
-        sink_sum(0, *low)
-        sink_sum(0, *high)
-        u_gain(0)
-        sink_inv(0, *low)
-        sink_inv(0, *high)
-        u_quant(0)
-        sink_last(0, *low)
-        sink_last(0, *high)
+        def vq(n, j, a):
+            return (prod_vector, n, j) + quad(a)
 
-        for k in range(NT - 1):
-            first = k == 0
-            late = k + 3 >= NT
-            before_last = k == NT - 2
-            halves = first or before_last
-            if not first:
-                if_tile(coef_mm, k + 2)
-            branch_mm(k)
-            if not first:
-                if_tile(x_turn, k + 3, 0)
-                if_tile(x_turn, k + 3, 1)
-            if late:
-                q_to_psum(k, quad(3)[0])
-            if halves:
-                prod_gpsimd(k, 0, *low)
-                prod_gpsimd(k, 1, *low)
+        def sq(n, j, a):
+            return [(prod_scalar, n, j, g, g + 1) for g in range(*quad(a))]
+
+        def deal(work, *marks):
+            out = []
+            for m, entry in enumerate(work + [None]):
+                out.extend(step for place, step in marks if min(place, len(work)) == m)
+                out.extend([entry] if entry else [])
+            return out
+
+        def inv(n, step, place, parts=(every,)):
+            return [(place, (sink_root, n, step) + part) for part in parts] + [(place + 1, (sink_inv_scalar, n, step) + part) for part in parts]
+
+        def relu(n, place):
+            return [(place, (branch_relu, n)), (place + 1, (branch_square, n))]
+
+        TERMS = (0, 1, 2, 3, BRANCH)
+
+        def ys(n, a, pair=0, bank="yy", terms=TERMS):
+            return (y_sum, n, a, bank, terms, pair)
+
+        def g_halves(n):
+            return [(prod_gpsimd, n, 0) + low, (prod_gpsimd, n, 1) + low, (prod_gpsimd, n, 0) + high, (prod_gpsimd, n, 1) + high]
+
+        def gq(n, j, a):
+            return (prod_gpsimd, n, j) + quad(a)
+
+        U1 = 3
+        SPLIT = 9
+        def br(k, *quads):
+            return [vq(k, BRANCH, a) for a in quads]
+
+        def mm(n, bank):
+            return (coef_mm, n, bank, 0, R)
+
+        def turns(n):
+            return [(x_turn, n, 0), (x_turn, n, 1)]
+
+        def terms(k, *pairs):
+            return [s for j, a in pairs for s in sq(k, j, a)]
+
+        both = [(j, a) for a in range(NQ) for j in (2, 3)]
+
+        halves = (low, high)
+        vector += [(phi_widen_vector, 0, 0), (phi_widen_vector, 0, 1), (phi_group, 0, "vector")]
+        vector += [(phi_quant, 0), (phi_group, 1, "vector")] + gains(0, 0, 1, 2, 3) + [(phi_quant, 1), (x_quant, 0)]
+        vector += [(phi_group, 2, "vector")] + gains(1, 0) + [(phi_quant, 2)] + gains(1, 1, 2) + [(phi_quant, 3)]
+        vector += gains(1, 3) + [(w_group, 1), (x_quant, 1), (w_quant, 0), (w_quant, 1), (gate_copy, 0)]
+        own = (0, 1, 2, 3)
+        vector += chain(0, [gains(2, 0, 1, 2, 3), [(x_quant, 2)], [], [], [], [], [(u_gain, 0)], []], own, halves)
+        vector += [(u_quant, 0), (sink_last, 0) + low, (sink_last, 0) + high]
+        scalar += [(phi_widen_scalar, 0, 2), (phi_widen_scalar, 0, 3)]
+        scalar += [(phi_widen_scalar, r, t) for r in (1, 2, 3) for t in range(T)]
+        scalar += [(phi_group, 3, "scalar"), (bias_read,), (w_group, 0), (coef_act, 0), (gf_half,)]
+        scalar += [(pre_prod_scalar, 0, r) for r in range(R)] + [(coef_act, 1)]
+        tensor += turns(0) + turns(1) + [(bias_turn,), (coef_mm, 0, "tt", 0, 3), (coef_mm, 0, "tt", 3, 4)] + turns(2)
+        tensor += [(coef_turn, 0), mm(1, "tt")] + turns(3) + [(u_sum, 0, 0), (coef_turn, 1), mm(2, "tt")]
+
+        def bank(n, a, plain=0):
+            index = NQ * n + a
+            return ys(n, a, plain, "xp" if index >= 10 and index % 2 == 1 else "yy")
+
+        def vqs(k, *pairs):
+            return [vq(k, j, a) for j, a in pairs]
+
+        def out(index):
+            return [(y_out,) + divmod(index, NQ)] if index >= 0 else []
+
+        def prep(m, *streams):
+            return gains(m, *streams) if m < NT else []
+
+        branches = [(BRANCH, a) for a in range(NQ)]
+        vector += chain(
+            1,
+            [prep(3, 0, 1), prep(3, 2, 3), pres(1, 0, 1), pres(1, 2, 3), prep(4, 0, 1), prep(4, 2, 3),
+             [(u_gain, 1)] + out(0) + prep(5, 0, 1), prep(5, 2, 3)], own)
+        vector += [(x_quant, 3), (x_quant, 4), (x_quant, 5), (u_quant, 1), (sink_last, 1) + every]
+        scalar += terms(0, (2, 0), (3, 0)) + [(branch_relu, 0), (coef_act, 2), (branch_square, 0)]
+        scalar += terms(0, (BRANCH, 0), (2, 1), (3, 1), (BRANCH, 1), (2, 2), (3, 2), (BRANCH, 2), (3, 3), (BRANCH, 3))
+        gpsimd += g_halves(0) + [gq(0, 2, 3)]
+        tensor += [(branch_mm, 0)] + turns(4) + [(u_sum, 1, U1), bank(0, 0, 2)] + turns(5) + [(coef_turn, 2), bank(0, 1)]
+        for k in (1, 2):
+            n = k + 1
+            o = [out(NQ * k - 3 + b) for b in range(NQ)]
+            vector += chain(
+                n,
+                [o[0], pres(n, 0, 1), pres(n, 2), pres(n, 3) + o[1], [(prod_vector, k, BRANCH, SPLIT, G)] + prep(k + 5, 0, 1), o[2] + [(u_gain, n)],
+                 prep(k + 5, 2, 3), o[3]], own)
+            vector += [(x_quant, k + 5), (u_quant, n), (sink_last, n) + every]
+            scalar += [(post_copy, k)] + terms(k, (2, 0), (3, 0)) + [(branch_relu, k), (coef_act, 2 * k + 1), (branch_square, k)]
+            scalar += terms(k, (BRANCH, 0), (2, 1), (3, 1), (BRANCH, 1), (2, 2)) + [(coef_act, 2 * k + 2)] + terms(k, (3, 2))
+            scalar += terms(k, (BRANCH, 2))[: SPLIT - HALF] + terms(k, (3, 3))
+            gpsimd += [(prod_gpsimd, k, 0) + every, (prod_gpsimd, k, 1) + low, (prod_gpsimd, k, 1) + high, gq(k, 2, 3)]
+            tensor += [mm(2 * k + 1, "tt"), (branch_mm, k), (x_turn, k + 5, 0), bank(k - 1, 2, PAIRS[k][0]), bank(k - 1, 3), (u_sum, n, 0)]
+            tensor += [mm(2 * k + 2, "tt"), (x_turn, k + 5, 1), bank(k, 0), (coef_turn, k + 2), bank(k, 1)]
+        for k in range(3, NT - 1):
+            n = k + 1
+            lag = LAG[k]
+            o = [out(NQ * k - OUT[k] + b) for b in range(OUT[k] + NQ - OUT[k + 1])] + [[]]
+            mine = (0, 1) if k == 3 else ()
+            vector += chain(
+                n,
+                [o[0], pres(n, 0, 1), pres(n, 2), pres(n, 3) + br(k, 0), o[1] + br(k, 1), br(k, 2),
+                 o[2] + br(k, 3) + [(u_gain, n)] + o[3] + o[4], []] if k == 3 else
+                [o[0] + pres(n, 0), pres(n, 1), pres(n, 2, 3), br(k, 0), o[1] + br(k, 1), br(k, 2),
+                 o[2] + br(k, 3) + [(u_gain, n)] + o[3] + o[4], []], mine)
+            vector += [(u_quant, n), (sink_last, n) + every]
+            work = terms(k, *both)
+            if k == 3:
+                scalar += work[:5] + [(branch_relu, k), (coef_act, 7), (branch_square, k)] + deal(work[5:-4], *inv(n, 2, 4) + inv(n, 3, 11))
             else:
-                prod_gpsimd(k, 0, 0, G)
-            sink_sum(k + 1)
-            if not first:
-                next_out()
-            prod_scalar(k, 2, *quad(0))
-            prod_scalar(k, 3, *quad(0))
-            branch_relu(k)
-            if_tile(coef_act, k + 2)
-            branch_square(k)
-            if not first:
-                next_sum()
-                next_sum()
-            sink_inv(k + 1)
-            pre_prod_vector(k + 1, 0)
-            sink_scale(k + 1, True)
-            pre_prod_vector(k + 1, 1)
-            sink_sum(k + 1)
-            if not first:
-                next_out()
-            pre_prod_vector(k + 1, 2)
-            sink_inv(k + 1)
-            pre_prod_vector(k + 1, 3)
-            u_sum(k + 1)
-            prod_scalar(k, BRANCH, *quad(0))
-            if halves:
-                prod_gpsimd(k, 0, *high)
+                scalar += deal(work, *inv(n, 0, 1) + relu(k, 3) + inv(n, 1, 6) + inv(n, 2, 14) + inv(n, 3, 22) + [(24, (post_copy, n))] * (n == NT - 1))
+            if k == 3:
+                gpsimd += g_halves(k) + [gq(k, 3, 3)]
             else:
-                prod_gpsimd(k, 1, *low)
-            prod_gpsimd(k, 1, *high)
-            sink_scale(k + 1, False)
-            if first:
-                prod_vector(k, BRANCH, *quad(1))
-            else:
-                next_out()
-            next_sum()
-            sink_sum(k + 1)
-            prod_vector(k, BRANCH, *quad(3))
-            if_tile(x_gain, k + 3, 0)
-            if_tile(x_gain, k + 3, 1)
-            if late:
-                prod_vector(k, 2, *quad(3))
-            sink_inv(k + 1)
-            if first:
-                prod_vector(k, BRANCH, *quad(2))
-            else:
-                next_out()
-            if_tile(coef_turn, k + 2)
-            prod_scalar(k, 2, *quad(1))
-            prod_scalar(k, 3, *quad(1))
-            if not first:
-                prod_scalar(k, BRANCH, *quad(1))
-            next_sum()
-            sink_scale(k + 1, True)
-            if_tile(x_gain, k + 3, 2)
-            if_tile(x_gain, k + 3, 3)
-            if late:
-                prod_vector(k, 3, *quad(3))
-            sink_sum(k + 1)
-            u_gain(k + 1)
-            sink_inv(k + 1)
-            prod_scalar(k, 2, *(high if first else quad(2)))
-            prod_scalar(k, 3, *quad(2))
-            if not first:
-                prod_scalar(k, BRANCH, *quad(2))
-            if not first and not late:
-                prod_gpsimd(k, 2, *quad(3))
-            if before_last:
-                next_sum()
-            if not late:
-                prod_scalar(k, 3, *quad(3))
-            if_tile(x_quant, k + 3)
-            u_quant(k + 1)
-            sink_last(k + 1)
+                gpsimd += g_halves(k)[:2] + ([gq(k, 0, 2), gq(k, 1, 2), gq(k, 0, 3), gq(k, 1, 3)] if k == NT - 2 else g_halves(k)[2:])
+            banks = [bank(*divmod(b, NQ), PAIRS[k][i]) for i, b in enumerate(range(NQ * k - lag, NQ * n - LAG[n]))]
+            tensor += [mm(7, "tt")] * (k == 3) + [(branch_mm, k)] + banks[:lag] + [(u_sum, n, 0)] + banks[lag : lag + 1]
+            tensor += banks[lag + 1 : lag + 2] + [(coef_turn, k + 2)] * (k + 2 < NT) + banks[lag + 2 :]
 
-        last = NT - 1
-        q_to_psum(last, 0)
-        branch_mm(last)
-        next_out()
-        next_out()
-        next_sum()
-        prod_scalar(last, 1, *high)
-        branch_relu(last)
-        branch_square(last)
-        for a in range(NQ):
-            prod_gpsimd(last, 0, *quad(a))
-            if a < NQ // 2:
-                prod_gpsimd(last, 1, *quad(a))
-            prod_vector(last, 2, *quad(a))
-            next_out()
-            prod_vector(last, 3, *quad(a))
-            prod_scalar(last, BRANCH, *quad(a))
-            next_sum()
-        next_out()
-        next_out()
+        k = NT - 1
+        tensor += [(branch_mm, k), (q_to_psum, k)] + [bank(*divmod(b, NQ)) for b in range(NQ * k - LAG[k], NQ * NT)]
+        o = [s for b in range(NQ * k - OUT[k], NQ * NT) for s in out(b)]
+        vector += o[:-6] + [vq(k, 2, 0), vq(k, 3, 0), o[-6], vq(k, 2, 1), vq(k, 3, 1), o[-5]]
+        vector += [vq(k, 2, 2), vq(k, 3, 2), vq(k, 2, 3), o[-4], vq(k, 3, 3)] + o[-3:]
+        work = terms(k, (1, 1), (BRANCH, 0), (BRANCH, 1), (1, 3), (BRANCH, 2), (BRANCH, 3))
+        scalar += deal(work, *relu(k, 2))
+        gpsimd += [gq(k, 0, 0), gq(k, 1, 0), gq(k, 0, 1), gq(k, 0, 2), gq(k, 1, 2), gq(k, 0, 3)]
+
+        queues = (tensor, vector, scalar, gpsimd)
+        steps = [s for queue in queues for s in queue]
+        products = (prod_vector, prod_scalar, prod_gpsimd)
+
+        def find(fns, *args):
+            return [s for s in steps if s[0] in fns and s[1 : 1 + len(args)] == args]
+
+        def bank_readers(s):
+            fn = s[0]
+            if fn is x_turn:
+                return "xp", gains(s[1], 2 * s[2], 2 * s[2] + 1)
+            if fn is coef_mm and s[3] == 0:
+                return s[2], [(coef_act, s[1])]
+            if fn is bias_turn:
+                return "uh", [(bias_read,)]
+            if fn is y_sum:
+                return s[3], [(y_out, s[1], s[2])]
+            if fn is u_sum:
+                return "uh", [(u_gain, s[1])]
+            if fn is branch_mm:
+                return "uh", [(branch_relu, s[1])]
+            if fn is coef_turn:
+                return "ct", find((prod_vector, pre_prod_vector, sink_scale, gate_copy, post_copy), s[1])
+            return None, []
+
+        before = dict()
+        held = dict()
+        for s in tensor:
+            tag, readers = bank_readers(s)
+            if tag:
+                held.setdefault(tag, []).append(readers)
+                before[s] = held[tag][-1 - BANKS[tag]] if len(held[tag]) > BANKS[tag] else []
+
+        def needs(s):
+            fn, n = s[0], s[1] if len(s) > 1 else 0
+            if fn is phi_group:
+                return find((phi_widen_vector, phi_widen_scalar), n)
+            if fn is phi_quant:
+                return find((phi_group,), n)
+            if fn is bias_read:
+                return [(bias_turn,)]
+            if fn is w_quant:
+                return [(w_group, n)]
+            if fn is x_gain:
+                return [(x_turn, n, s[2] // 2)] + find((x_quant,), n - XN_BUFS)
+            if fn is x_quant:
+                return find((coef_mm,), n - 3)
+            if fn is coef_mm:
+                return [(x_quant, n)] + [(phi_quant, r) for r in range(s[3], s[4])]
+            if fn is coef_act:
+                return find((coef_mm,), n) + find((coef_turn,), n - 3) + [(bias_read,)]
+            if fn is coef_turn:
+                return [(coef_act, n)]
+            if fn in (gate_copy, post_copy):
+                return [(coef_turn, n)] + find((prod_scalar,), n - 2, BRANCH) + find((sink_scale,), n) * (fn is post_copy)
+            if fn is sink_sum or fn is pre_prod_vector:
+                return [(coef_turn, n)] + (find((u_sum,), n - 1 - (s[2] < 2)) if fn is pre_prod_vector else [])
+            if fn is sink_root:
+                return [(sink_sum,) + s[1:]]
+            if fn is sink_scale:
+                return find((sink_inv_scalar,), *s[1:])
+            if fn is sink_last:
+                return find((sink_inv_scalar,), n, 3) + find(products + (q_to_psum,), n - 2)
+            if fn is q_to_psum:
+                return find((sink_last, post_copy), n)
+            if fn in (pre_prod_scalar, pre_prod_gpsimd):
+                return [(gate_copy, n)] + find((u_sum,), n - 1 - (s[2] < 2))
+            if fn is u_sum:
+                return find((pre_prod_vector, pre_prod_scalar, pre_prod_gpsimd), n)
+            if fn is u_gain:
+                return find((u_sum,), n) + [(gf_half,)]
+            if fn is branch_mm:
+                return [(u_quant, n), (w_quant, 0), (w_quant, 1)]
+            if fn is branch_relu:
+                return [(branch_mm, n)]
+            if fn is branch_square:
+                return find(products, n - 2, BRANCH)
+            if fn in products:
+                source = [(branch_square, n)] if s[2] == BRANCH else find((sink_last,), n)
+                if fn is prod_vector:
+                    source = source + find((q_to_psum, post_copy), n)
+                if fn is prod_scalar and s[2] == BRANCH:
+                    source = source + find((gate_copy, post_copy), n)
+                return source + find((y_sum,), n - 2)
+            if fn is y_sum:
+                lo, hi = quad(s[2])
+                return [t for t in find(products, n) if t[3] < hi and t[4] > lo]
+            if fn is y_out:
+                return find((y_sum,), n, s[2])
+            return []
+
+        def weave():
+            done = set()
+            pos = [0] * len(queues)
+            while len(done) < len(steps):
+                count = len(done)
+                for e, queue in enumerate(queues):
+                    while pos[e] < len(queue) and all(t in done for t in needs(queue[pos[e]]) + before.get(queue[pos[e]], [])):
+                        s = queue[pos[e]]
+                        s[0](*s[1:])
+                        done.add(s)
+                        pos[e] = pos[e] + 1
+                assert len(done) > count, [(q[p][0], q[p][1:]) for q, p in zip(queues, pos) if p < len(q)]
+
+        assert len(set(steps)) == len(steps)
+        for n in range(NT):
+            for j in range(BRANCH + 1):
+                assert sum(s[4] - s[3] for s in find(products, n, j)) == G, (n, j)
+        weave()

@@ -401,7 +401,7 @@ def tile_groupedmanifoldhyperconnection_kernel(tc, x, gn, phi_bytes, phi_scale, 
                     out=out_view[n, i, a], in_=yo[C * i : C * (i + 1), :].rearrange("p (tb c) -> p tb c", tb=TB)
                 )
 
-        PAIRS = [0,(0,),(0,),(0,2,0,0,0),(2,0,2,0,0),(2,0,2,0,0),(2,0,2,0,0)]
+        PAIRS = [0,(2,),(2,),(0,0,2,0,0),(2,0,2,0,0),(2,0,2,0,0),(2,0,2,0,0)]
         LAG = [0,0,0,2,2,2,2,1]
         OUT = [0,0,0,3,3,3,3,3]
         low, high, every = (0, HALF), (HALF, G), (0, G)
@@ -445,7 +445,7 @@ def tile_groupedmanifoldhyperconnection_kernel(tc, x, gn, phi_bytes, phi_scale, 
         def relu(n, place):
             return [(place, (branch_relu, n)), (place + 1, (branch_square, n))]
 
-        TERMS = (0, 1, 2, 3, BRANCH)
+        TERMS = (0, 2, 3, BRANCH, 1)
 
         def ys(n, a, pair=0, bank="yy", terms=TERMS):
             return (y_sum, n, a, bank, terms, pair)
@@ -489,7 +489,10 @@ def tile_groupedmanifoldhyperconnection_kernel(tc, x, gn, phi_bytes, phi_scale, 
 
         def bank(n, a, plain=0):
             index = NQ * n + a
-            return ys(n, a, plain, "xp" if index >= 10 and index % 2 == 1 else "yy")
+            return ys(n, a, plain, "xp" if index >= 10 and index % 2 == 1 else "yy", TERMS if index < NQ * NT - 2 else (2, 3, 1, 0, BRANCH))
+
+        def g_whole(k):
+            return [(prod_gpsimd, k, 0) + every, (prod_gpsimd, k, 1) + low, (prod_gpsimd, k, 1) + high]
 
         def vqs(k, *pairs):
             return [vq(k, j, a) for j, a in pairs]
@@ -532,7 +535,7 @@ def tile_groupedmanifoldhyperconnection_kernel(tc, x, gn, phi_bytes, phi_scale, 
             vector += chain(
                 n,
                 [o[0], pres(n, 0, 1), pres(n, 2), pres(n, 3) + br(k, 0), o[1] + br(k, 1), br(k, 2),
-                 o[2] + br(k, 3) + [(u_gain, n)] + o[3] + o[4], []] if k == 3 else
+                 o[2] + br(k, 3) + vqs(k, (3, 3)) + [(u_gain, n)] + o[3] + o[4], []] if k == 3 else
                 [o[0] + pres(n, 0), pres(n, 1), pres(n, 2, 3), br(k, 0), o[1] + br(k, 1), br(k, 2),
                  o[2] + br(k, 3) + [(u_gain, n)] + o[3] + o[4], []], mine)
             vector += [(u_quant, n), (sink_last, n) + every]
@@ -542,21 +545,20 @@ def tile_groupedmanifoldhyperconnection_kernel(tc, x, gn, phi_bytes, phi_scale, 
             else:
                 scalar += deal(work, *inv(n, 0, 1) + relu(k, 3) + inv(n, 1, 6) + inv(n, 2, 14) + inv(n, 3, 22) + [(24, (post_copy, n))] * (n == NT - 1))
             if k == 3:
-                gpsimd += g_halves(k) + [gq(k, 3, 3)]
+                gpsimd += g_whole(k)
             else:
-                gpsimd += g_halves(k)[:2] + ([gq(k, 0, 2), gq(k, 1, 2), gq(k, 0, 3), gq(k, 1, 3)] if k == NT - 2 else g_halves(k)[2:])
+                gpsimd += g_halves(k) if k == NT - 2 else g_whole(k)
             banks = [bank(*divmod(b, NQ), PAIRS[k][i]) for i, b in enumerate(range(NQ * k - lag, NQ * n - LAG[n]))]
-            tensor += [mm(7, "tt")] * (k == 3) + [(branch_mm, k)] + banks[:lag] + [(u_sum, n, 0)] + banks[lag : lag + 1]
+            tensor += [mm(7, "tt")] * (k == 3) + [(branch_mm, k)] + [(q_to_psum, k)] * (k == 3) + banks[:lag] + [(u_sum, n, 0)] + banks[lag : lag + 1]
             tensor += banks[lag + 1 : lag + 2] + [(coef_turn, k + 2)] * (k + 2 < NT) + banks[lag + 2 :]
 
         k = NT - 1
         tensor += [(branch_mm, k), (q_to_psum, k)] + [bank(*divmod(b, NQ)) for b in range(NQ * k - LAG[k], NQ * NT)]
         o = [s for b in range(NQ * k - OUT[k], NQ * NT) for s in out(b)]
-        vector += o[:-6] + [vq(k, 2, 0), vq(k, 3, 0), o[-6], vq(k, 2, 1), vq(k, 3, 1), o[-5]]
-        vector += [vq(k, 2, 2), vq(k, 3, 2), vq(k, 2, 3), o[-4], vq(k, 3, 3)] + o[-3:]
-        work = terms(k, (1, 1), (BRANCH, 0), (BRANCH, 1), (1, 3), (BRANCH, 2), (BRANCH, 3))
+        vector += o[:-5] + vqs(k, (2, 0), (3, 0), (2, 1), (3, 1)) + [o[-5]] + vqs(k, (2, 2), (3, 2), (1, 3), (2, 3), (3, 3)) + o[-4:]
+        work = terms(k, (1, 1), (BRANCH, 0), (BRANCH, 1), (1, 2), (BRANCH, 2), (BRANCH, 3))
         scalar += deal(work, *relu(k, 2))
-        gpsimd += [gq(k, 0, 0), gq(k, 1, 0), gq(k, 0, 1), gq(k, 0, 2), gq(k, 1, 2), gq(k, 0, 3)]
+        gpsimd += [(prod_gpsimd, k, 0) + low, gq(k, 1, 0), (prod_gpsimd, k, 0) + high]
 
         queues = (tensor, vector, scalar, gpsimd)
         steps = [s for queue in queues for s in queue]

@@ -401,7 +401,7 @@ def tile_groupedmanifoldhyperconnection_kernel(tc, x, gn, phi_bytes, phi_scale, 
                     out=out_view[n, i, a], in_=yo[C * i : C * (i + 1), :].rearrange("p (tb c) -> p tb c", tb=TB)
                 )
 
-        PAIRS = [0,(2,),(2,),(0,0,2,0,0),(2,0,2,0,0),(2,0,2,0,0),(2,0,2,0,0)]
+        PAIRS = [0,(0,),(0,),(0,0,0,0,0),(2,0,0,0,0),(2,0,0,0,0),(2,0,0,0,0)]
         LAG = [0,0,0,2,2,2,2,1]
         OUT = [0,0,0,3,3,3,3,3]
         low, high, every = (0, HALF), (HALF, G), (0, G)

@@ -34,6 +34,7 @@ FLOPS = 2 * TOK * R * D * M + 2 * TOK * D * D
 
 BANKS = {"xp": 2, "tt": 1, "yy": 2, "uh": 1, "ct": 2}
 XN_BUFS = 3
+THIRD_TURN = 5
 
 
 def spread(ap, axis, n):
@@ -77,9 +78,9 @@ def tile_groupedmanifoldhyperconnection_kernel(tc, x, gn, phi_bytes, phi_scale, 
         nc.sync.dma_start(out=scale[:], in_=phi_scale.rearrange("(r p t) o -> p r (t o)", p=P, t=T))
         nc.sync.dma_start(out=phi_raw[0][:], in_=phi_view[0])
         nc.sync.dma_start(out=phi_raw[1][:], in_=phi_view[1])
+        nc.sync.dma_start(out=phi_raw[2][:], in_=phi_view[2])
         load_x(0)
         nc.sync.dma_start(out=gn_k[:], in_=gn.rearrange("(r p t) -> p r t", p=P, t=T))
-        nc.sync.dma_start(out=phi_raw[2][:], in_=phi_view[2])
         nc.sync.dma_start(out=phi_raw[3][:], in_=phi_view[3])
         bm_groups = bm.rearrange("(o g k) -> o g k", o=1, g=G)
         nc.sync.dma_start(out=bm_row[0:1, 0:P].rearrange("p (g k) -> p g k", g=G), in_=bm_groups[:, :, 0:GATES])
@@ -92,7 +93,7 @@ def tile_groupedmanifoldhyperconnection_kernel(tc, x, gn, phi_bytes, phi_scale, 
 
         phi_codes = keep.tile([P, R, M], U32, align_bytes=64)
         phi_scales = keep.tile([P, R, M], U8, align_bytes=64)
-        phi_wide = [keep.tile([P, T, M], BF16, name="phw%d" % r) for r in range(R)]
+        phi_wide = [sb.tile([P, T, M], BF16, name="prod%d" % r) for r in range(R)]
         phi_words = [keep.tile([P, M, T], BF16, name="phg%d" % r, align_bytes=64) for r in range(R)]
         bias = keep.tile([P, MT], F32)
         half_bias = keep.tile([P, 1], F32)
@@ -171,17 +172,19 @@ def tile_groupedmanifoldhyperconnection_kernel(tc, x, gn, phi_bytes, phi_scale, 
                     nc.tensor.transpose(xp[:, rr, u, :], words[:, 256 * r + u : 256 * (r + 1) : 2], ident[:])
             state[n]["xp", pair] = xp
 
-        def x_gain(n, r):
+        def x_gain(n, pair):
             st = state[n]
-            if r == 0:
+            if pair == 0:
                 st["xn"] = sb.tile([P, R, P, T], BF16, name="xn", bufs=XN_BUFS, align_bytes=64)
-            turned = st["xp", r // 2][:, r % 2, :, :].rearrange("p u s -> p (u s)").bitcast(BF16)
-            nc.vector.tensor_tensor(
-                out=st["xn"][:, r, :, :].rearrange("p s (u e) -> p s u e", e=2),
-                in0=turned.rearrange("p (u s e) -> p s u e", u=2, e=2),
-                in1=spread(gn_k[:, r, :].rearrange("p (u e) -> p u e", e=2), 1, P),
-                op=ALU.mult,
-            )
+            for rr in range(2):
+                r = 2 * pair + rr
+                turned = st["xp", pair][:, rr, :, :].rearrange("p u s -> p (u s)").bitcast(BF16)
+                nc.vector.tensor_tensor(
+                    out=st["xn"][:, r, :, :].rearrange("p s (u e) -> p s u e", e=2),
+                    in0=turned.rearrange("p (u s e) -> p s u e", u=2, e=2),
+                    in1=spread(gn_k[:, r, :].rearrange("p (u e) -> p u e", e=2), 1, P),
+                    op=ALU.mult,
+                )
 
         def x_quant(n):
             st = state[n]
@@ -221,7 +224,8 @@ def tile_groupedmanifoldhyperconnection_kernel(tc, x, gn, phi_bytes, phi_scale, 
 
         def coef_turn(n):
             st = state[n]
-            ct = ps.tile([P, MT, P], F32, name="ct", bufs=2)
+            bank = "tt" if n == THIRD_TURN else "ct"
+            ct = ps.tile([P, MT, P], F32, name=bank, bufs=BANKS[bank])
             for m in (1, 2, 0):
                 nc.tensor.transpose(ct[:, m, :], st["co"][:, m, :], ident[:])
             st["e"] = ct[:, 1:MT, :].rearrange("p m (g i j) -> p (m g) i j", i=R, j=R)
@@ -274,7 +278,7 @@ def tile_groupedmanifoldhyperconnection_kernel(tc, x, gn, phi_bytes, phi_scale, 
 
         def pre_prod_vector(n, r):
             st = state[n]
-            st["pu", r] = sb.tile([P, T, P], F32, name="pu", bufs=6)
+            st["pu", r] = sb.tile([P, T, P], F32, name="pu", bufs=8)
             nc.vector.tensor_tensor(
                 out=st["pu", r][:].rearrange("p t (g c) -> p t g c", g=G),
                 in0=xs[n][:, r * D : (r + 1) * D].rearrange("p (g c t) -> p t g c", g=G, t=T),
@@ -294,7 +298,7 @@ def tile_groupedmanifoldhyperconnection_kernel(tc, x, gn, phi_bytes, phi_scale, 
 
         def pre_prod_gpsimd(n, r):
             st = state[n]
-            tile = sb.tile([P, P, T], F32, name="pu", bufs=6)
+            tile = sb.tile([P, P, T], F32, name="pu", bufs=8)
             st["pu", r] = tile[:].rearrange("p c t -> p t c")
             nc.gpsimd.tensor_tensor(
                 out=tile[:].rearrange("p (g c) t -> p g (c t)", g=G),
@@ -305,19 +309,20 @@ def tile_groupedmanifoldhyperconnection_kernel(tc, x, gn, phi_bytes, phi_scale, 
 
         def pre_prod_scalar(n, r):
             st = state[n]
-            st["pu", r] = sb.tile([P, T, P], F32, name="pu", bufs=6)
+            st["pu", r] = sb.tile([P, T, P], F32, name="pu", bufs=8)
             src = xs[n][:, r * D : (r + 1) * D].rearrange("p (g c t) -> p g t c", g=G, t=T)
             dst = st["pu", r][:].rearrange("p t (g c) -> p g t c", g=G)
             for g in range(G):
                 nc.scalar.activation(dst[:, g], src[:, g], ACT.Copy, scale=st["gate_sb"][:, g, r : r + 1])
 
-        def u_sum(n, plain):
+        def u_sum(n, plain, streams, start, stop):
             st = state[n]
-            st["ut"] = ps.tile([P, T, P], F32, name="uh")
-            for r in range(R):
-                for t in range(T):
-                    first_pass, last_pass = r == 0 and t == 0, r == R - 1 and t == T - 1
-                    add_turned(st["ut"][:, t, :], st["pu", r][:, t, :], first_pass, last_pass, r == 0 and t < plain)
+            if start:
+                st["ut"] = ps.tile([P, T, P], F32, name="uh")
+            passes = [(r, t) for t in range(T) for r in streams]
+            for m, (r, t) in enumerate(passes):
+                first_pass, last_pass = start and m == 0, stop and m == len(passes) - 1
+                add_turned(st["ut"][:, t, :], st["pu", r][:, t, :], first_pass, last_pass, m < plain)
 
         def u_gain(n):
             st = state[n]
@@ -387,11 +392,11 @@ def tile_groupedmanifoldhyperconnection_kernel(tc, x, gn, phi_bytes, phi_scale, 
         def y_sum(n, a, bank, terms, plain):
             st = state[n]
             st["yt", a] = ps.tile([P, TB, QUAD, C], F32, name=bank, bufs=BANKS[bank])
-            for j in terms:
-                for b in range(QUAD):
-                    src = st["prod", j][:, QUAD * a + b].rearrange("p i c -> p (i c)")
-                    first_pass, last_pass = j == terms[0] and b == 0, j == terms[-1] and b == QUAD - 1
-                    add_turned(st["yt", a][:, :, b, :], src, first_pass, last_pass, j == terms[0] and b < plain)
+            early, late = terms
+            passes = [(b, j) for b in range(QUAD) for j in early] + [(b, j) for j in late for b in range(QUAD)]
+            for m, (b, j) in enumerate(passes):
+                src = st["prod", j][:, QUAD * a + b].rearrange("p i c -> p (i c)")
+                add_turned(st["yt", a][:, :, b, :], src, m == 0, m == len(passes) - 1, m < plain)
 
         def y_out(n, a):
             yo = sb.tile([P, D], F32, name="yo", bufs=5, align_bytes=64)
@@ -401,9 +406,9 @@ def tile_groupedmanifoldhyperconnection_kernel(tc, x, gn, phi_bytes, phi_scale, 
                     out=out_view[n, i, a], in_=yo[C * i : C * (i + 1), :].rearrange("p (tb c) -> p tb c", tb=TB)
                 )
 
-        PAIRS = [0,(0,),(0,),(0,0,0,0,0),(2,0,0,0,0),(2,0,0,0,0),(2,0,0,0,0)]
-        LAG = [0,0,0,2,2,2,2,1]
-        OUT = [0,0,0,3,3,3,3,3]
+        PAIRS = [0, 0, 0, (0, 2, 0, 0), (2, 0, 0, 0, 0), (2, 0, 0, 0), (2, 0, 0, 0, 0)]
+        LAG = [0, 1, 1, 1, 2, 2, 2, 1]
+        OUT = [0, 0, 0, 3, 3, 3, 3, 3]
         low, high, every = (0, HALF), (HALF, G), (0, G)
         tensor, vector, scalar, gpsimd = [], [], [], []
 
@@ -445,7 +450,7 @@ def tile_groupedmanifoldhyperconnection_kernel(tc, x, gn, phi_bytes, phi_scale, 
         def relu(n, place):
             return [(place, (branch_relu, n)), (place + 1, (branch_square, n))]
 
-        TERMS = (0, 2, 3, BRANCH, 1)
+        TERMS = ((0, 2, 3, BRANCH), (1,))
 
         def ys(n, a, pair=0, bank="yy", terms=TERMS):
             return (y_sum, n, a, bank, terms, pair)
@@ -457,7 +462,13 @@ def tile_groupedmanifoldhyperconnection_kernel(tc, x, gn, phi_bytes, phi_scale, 
             return (prod_gpsimd, n, j) + quad(a)
 
         U1 = 3
-        SPLIT = 9
+        SPLIT = 12
+        GSPLIT = 11
+        MARK = (1, 3, 5, 14, 22)
+        G3 = 12
+        PRE1 = 4
+        CUTS = [0, 0, 0, (0, 8, 16), (0, 8, 16), (0, 8, 16), (0, 8, 16)]
+        LATE = (0, 2)
         def br(k, *quads):
             return [vq(k, BRANCH, a) for a in quads]
 
@@ -473,23 +484,24 @@ def tile_groupedmanifoldhyperconnection_kernel(tc, x, gn, phi_bytes, phi_scale, 
         both = [(j, a) for a in range(NQ) for j in (2, 3)]
 
         halves = (low, high)
-        vector += [(phi_widen_vector, 0, 0), (phi_widen_vector, 0, 1), (phi_group, 0, "vector")]
-        vector += [(phi_quant, 0), (phi_group, 1, "vector")] + gains(0, 0, 1, 2, 3) + [(phi_quant, 1), (x_quant, 0)]
-        vector += [(phi_group, 2, "vector")] + gains(1, 0) + [(phi_quant, 2)] + gains(1, 1, 2) + [(phi_quant, 3)]
-        vector += gains(1, 3) + [(w_group, 1), (x_quant, 1), (w_quant, 0), (w_quant, 1), (gate_copy, 0)]
         own = (0, 1, 2, 3)
-        vector += chain(0, [gains(2, 0, 1, 2, 3), [(x_quant, 2)], [], [], [], [], [(u_gain, 0)], []], own, halves)
+        vector += [(phi_widen_vector, 0, t) for t in range(T)] + [(phi_group, 0, "vector"), (phi_quant, 0), (phi_group, 1, "vector")]
+        vector += gains(0, 0) + [(phi_quant, 1)] + gains(0, 1) + [(phi_group, 2, "vector"), (x_quant, 0), (phi_quant, 2)]
+        vector += gains(1, 0) + [(phi_quant, 3)] + gains(1, 1)
+        vector += [(w_group, 1), (x_quant, 1), (w_quant, 0), (w_quant, 1), (gate_copy, 0)]
+        vector += chain(0, [gains(2, 0), [], gains(2, 1), [], [(gate_copy, 1), (x_quant, 2)], [], [(u_gain, 0)], []], own, halves)
         vector += [(u_quant, 0), (sink_last, 0) + low, (sink_last, 0) + high]
-        scalar += [(phi_widen_scalar, 0, 2), (phi_widen_scalar, 0, 3)]
         scalar += [(phi_widen_scalar, r, t) for r in (1, 2, 3) for t in range(T)]
         scalar += [(phi_group, 3, "scalar"), (bias_read,), (w_group, 0), (coef_act, 0), (gf_half,)]
-        scalar += [(pre_prod_scalar, 0, r) for r in range(R)] + [(coef_act, 1)]
-        tensor += turns(0) + turns(1) + [(bias_turn,), (coef_mm, 0, "tt", 0, 3), (coef_mm, 0, "tt", 3, 4)] + turns(2)
-        tensor += [(coef_turn, 0), mm(1, "tt")] + turns(3) + [(u_sum, 0, 0), (coef_turn, 1), mm(2, "tt")]
+        scalar += [(pre_prod_scalar, 0, 0), (coef_act, 1), (pre_prod_scalar, 0, 1)] + [(pre_prod_scalar, 1, r) for r in range(PRE1)]
+        gpsimd += [(pre_prod_gpsimd, 0, 2), (pre_prod_gpsimd, 0, 3)]
+        tensor += turns(0) + turns(1) + [(bias_turn,), (coef_mm, 0, "tt", 0, 3), (coef_mm, 0, "tt", 3, 4), (x_turn, 2, 0)]
+        tensor += [(coef_turn, 0), mm(1, "tt"), (x_turn, 2, 1), (u_sum, 0, 0, (0, 2), True, False), (coef_turn, 1), (u_sum, 0, 0, (1, 3), False, True)]
+        tensor += turns(3) + [mm(2, "tt")]
 
         def bank(n, a, plain=0):
             index = NQ * n + a
-            return ys(n, a, plain, "xp" if index >= 10 and index % 2 == 1 else "yy", TERMS if index < NQ * NT - 2 else (2, 3, 1, 0, BRANCH))
+            return ys(n, a, plain, "xp" if index >= 10 and index % 2 == 1 else "yy", TERMS if a in LATE else ((0, 2, 3, BRANCH, 1), ()))
 
         def g_whole(k):
             return [(prod_gpsimd, k, 0) + every, (prod_gpsimd, k, 1) + low, (prod_gpsimd, k, 1) + high]
@@ -506,27 +518,26 @@ def tile_groupedmanifoldhyperconnection_kernel(tc, x, gn, phi_bytes, phi_scale, 
         branches = [(BRANCH, a) for a in range(NQ)]
         vector += chain(
             1,
-            [prep(3, 0, 1), prep(3, 2, 3), pres(1, 0, 1), pres(1, 2, 3), prep(4, 0, 1), prep(4, 2, 3),
-             [(u_gain, 1)] + out(0) + prep(5, 0, 1), prep(5, 2, 3)], own)
-        vector += [(x_quant, 3), (x_quant, 4), (x_quant, 5), (u_quant, 1), (sink_last, 1) + every]
-        scalar += terms(0, (2, 0), (3, 0)) + [(branch_relu, 0), (coef_act, 2), (branch_square, 0)]
-        scalar += terms(0, (BRANCH, 0), (2, 1), (3, 1), (BRANCH, 1), (2, 2), (3, 2), (BRANCH, 2), (3, 3), (BRANCH, 3))
-        gpsimd += g_halves(0) + [gq(0, 2, 3)]
-        tensor += [(branch_mm, 0)] + turns(4) + [(u_sum, 1, U1), bank(0, 0, 2)] + turns(5) + [(coef_turn, 2), bank(0, 1)]
+            [prep(3, 0, 1), [], prep(4, 0), [], prep(4, 1) + br(0, 2), [], [(u_gain, 1)] + prep(5, 0, 1), out(0)], own, halves)
+        vector += [(x_quant, 3), (x_quant, 4), (x_quant, 5), (u_quant, 1), (sink_last, 1) + low, (sink_last, 1) + high]
+        scalar += terms(0, (2, 0)) + [(branch_relu, 0)] + terms(0, (3, 0))[:1] + [(branch_square, 0)] + terms(0, (3, 0))[1:]
+        scalar += terms(0, (BRANCH, 0)) + [(coef_act, 2)] + terms(0, (2, 1), (3, 1), (BRANCH, 1), (2, 2), (3, 2), (2, 3), (3, 3), (BRANCH, 3))
+        gpsimd += g_halves(0)
+        tensor += [(branch_mm, 0)] + turns(4) + [(u_sum, 1, U1, own, True, True)] + turns(5) + [bank(0, 0, 2)] + [(coef_turn, 2), bank(0, 1), bank(0, 2)]
         for k in (1, 2):
             n = k + 1
             o = [out(NQ * k - 3 + b) for b in range(NQ)]
             vector += chain(
                 n,
-                [o[0], pres(n, 0, 1), pres(n, 2), pres(n, 3) + o[1], [(prod_vector, k, BRANCH, SPLIT, G)] + prep(k + 5, 0, 1), o[2] + [(u_gain, n)],
-                 prep(k + 5, 2, 3), o[3]], own)
+                [o[0], pres(n, 0, 1), pres(n, 2), pres(n, 3) + o[1], [(prod_vector, k, BRANCH, HALF, SPLIT)] + o[2], prep(k + 5, 0) + [(u_gain, n)],
+                 o[3], prep(k + 5, 1)], own)
             vector += [(x_quant, k + 5), (u_quant, n), (sink_last, n) + every]
-            scalar += [(post_copy, k)] + terms(k, (2, 0), (3, 0)) + [(branch_relu, k), (coef_act, 2 * k + 1), (branch_square, k)]
-            scalar += terms(k, (BRANCH, 0), (2, 1), (3, 1), (BRANCH, 1), (2, 2)) + [(coef_act, 2 * k + 2)] + terms(k, (3, 2))
-            scalar += terms(k, (BRANCH, 2))[: SPLIT - HALF] + terms(k, (3, 3))
-            gpsimd += [(prod_gpsimd, k, 0) + every, (prod_gpsimd, k, 1) + low, (prod_gpsimd, k, 1) + high, gq(k, 2, 3)]
-            tensor += [mm(2 * k + 1, "tt"), (branch_mm, k), (x_turn, k + 5, 0), bank(k - 1, 2, PAIRS[k][0]), bank(k - 1, 3), (u_sum, n, 0)]
-            tensor += [mm(2 * k + 2, "tt"), (x_turn, k + 5, 1), bank(k, 0), (coef_turn, k + 2), bank(k, 1)]
+            scalar += [(post_copy, k)] + terms(k, (2, 0)) + [(coef_act, 2 * k + 1), (branch_relu, k)] + terms(k, (3, 0))[:1] + [(branch_square, k)]
+            scalar += terms(k, (3, 0))[1:] + terms(k, (BRANCH, 0), (2, 1), (3, 1), (BRANCH, 1)) + [(coef_act, 2 * k + 2)]
+            scalar += terms(k, (2, 2))[: GSPLIT - HALF] + terms(k, (3, 2)) + terms(k, (3, 3)) + terms(k, (BRANCH, 2), (BRANCH, 3))[SPLIT - HALF :]
+            gpsimd += g_whole(k) + [(prod_gpsimd, k, 2, GSPLIT, G)]
+            tensor += [mm(2 * k + 1, "tt"), (branch_mm, k), (x_turn, k + 5, 0), bank(k - 1, 3)]
+            tensor += [mm(2 * k + 2, "tt"), (x_turn, k + 5, 1), (u_sum, n, 0, own, True, True), bank(k, 0), (coef_turn, k + 2), bank(k, 1)] + [bank(k, 2)] * (LAG[n] == 1)
         for k in range(3, NT - 1):
             n = k + 1
             lag = LAG[k]
@@ -534,23 +545,20 @@ def tile_groupedmanifoldhyperconnection_kernel(tc, x, gn, phi_bytes, phi_scale, 
             mine = (0, 1) if k == 3 else ()
             vector += chain(
                 n,
-                [o[0], pres(n, 0, 1), pres(n, 2), pres(n, 3) + br(k, 0), o[1] + br(k, 1), br(k, 2),
-                 o[2] + br(k, 3) + vqs(k, (3, 3)) + [(u_gain, n)] + o[3] + o[4], []] if k == 3 else
-                [o[0] + pres(n, 0), pres(n, 1), pres(n, 2, 3), br(k, 0), o[1] + br(k, 1), br(k, 2),
+                [pres(n, 0), pres(n, 1, 2), pres(n, 3), o[0] + br(k, 0), br(k, 1) + o[1] + br(k, 2), o[2],
+                 br(k, 3) + [(u_gain, n)] + o[3] + o[4], []] if k == 3 else
+                [pres(n, 0, 1), pres(n, 2), pres(n, 3) + o[0], br(k, 0), br(k, 1) + o[1], br(k, 2),
                  o[2] + br(k, 3) + [(u_gain, n)] + o[3] + o[4], []], mine)
             vector += [(u_quant, n), (sink_last, n) + every]
             work = terms(k, *both)
             if k == 3:
-                scalar += work[:5] + [(branch_relu, k), (coef_act, 7), (branch_square, k)] + deal(work[5:-4], *inv(n, 2, 4) + inv(n, 3, 11))
+                scalar += work[:5] + [(branch_relu, k), (coef_act, 7), (branch_square, k)] + deal(work[5 : G3 - G], *inv(n, 2, 7) + inv(n, 3, 14))
             else:
-                scalar += deal(work, *inv(n, 0, 1) + relu(k, 3) + inv(n, 1, 6) + inv(n, 2, 14) + inv(n, 3, 22) + [(24, (post_copy, n))] * (n == NT - 1))
-            if k == 3:
-                gpsimd += g_whole(k)
-            else:
-                gpsimd += g_halves(k) if k == NT - 2 else g_whole(k)
+                scalar += deal(work, *inv(n, 0, MARK[0]) + relu(k, MARK[1]) + inv(n, 1, MARK[2]) + inv(n, 2, MARK[3]) + inv(n, 3, MARK[4]) + [(24, (post_copy, n))] * (n == NT - 1))
+            cuts = CUTS[k]
+            gpsimd += [(prod_gpsimd, k, j, lo, hi) for lo, hi in zip(cuts, cuts[1:]) for j in (0, 1)] + [(prod_gpsimd, k, 3, G3, G)] * (k == 3)
             banks = [bank(*divmod(b, NQ), PAIRS[k][i]) for i, b in enumerate(range(NQ * k - lag, NQ * n - LAG[n]))]
-            tensor += [mm(7, "tt")] * (k == 3) + [(branch_mm, k)] + [(q_to_psum, k)] * (k == 3) + banks[:lag] + [(u_sum, n, 0)] + banks[lag : lag + 1]
-            tensor += banks[lag + 1 : lag + 2] + [(coef_turn, k + 2)] * (k + 2 < NT) + banks[lag + 2 :]
+            tensor += [mm(7, "tt")] * (k == 3) + [(branch_mm, k)] + banks[:lag] + [(coef_turn, k + 2)] * (k + 2 < NT) + [(u_sum, n, 0, own, True, True)] + banks[lag:]
 
         k = NT - 1
         tensor += [(branch_mm, k), (q_to_psum, k)] + [bank(*divmod(b, NQ)) for b in range(NQ * k - LAG[k], NQ * NT)]
@@ -570,19 +578,19 @@ def tile_groupedmanifoldhyperconnection_kernel(tc, x, gn, phi_bytes, phi_scale, 
         def bank_readers(s):
             fn = s[0]
             if fn is x_turn:
-                return "xp", gains(s[1], 2 * s[2], 2 * s[2] + 1)
+                return "xp", gains(s[1], s[2])
             if fn is coef_mm and s[3] == 0:
                 return s[2], [(coef_act, s[1])]
             if fn is bias_turn:
                 return "uh", [(bias_read,)]
             if fn is y_sum:
                 return s[3], [(y_out, s[1], s[2])]
-            if fn is u_sum:
+            if fn is u_sum and s[4]:
                 return "uh", [(u_gain, s[1])]
             if fn is branch_mm:
                 return "uh", [(branch_relu, s[1])]
             if fn is coef_turn:
-                return "ct", find((prod_vector, pre_prod_vector, sink_scale, gate_copy, post_copy), s[1])
+                return "tt" if s[1] == THIRD_TURN else "ct", find((prod_vector, pre_prod_vector, sink_scale, gate_copy, post_copy), s[1])
             return None, []
 
         before = dict()
@@ -604,7 +612,7 @@ def tile_groupedmanifoldhyperconnection_kernel(tc, x, gn, phi_bytes, phi_scale, 
             if fn is w_quant:
                 return [(w_group, n)]
             if fn is x_gain:
-                return [(x_turn, n, s[2] // 2)] + find((x_quant,), n - XN_BUFS)
+                return [(x_turn, n, s[2])] + find((x_quant,), n - XN_BUFS)
             if fn is x_quant:
                 return find((coef_mm,), n - 3)
             if fn is coef_mm:
@@ -616,7 +624,7 @@ def tile_groupedmanifoldhyperconnection_kernel(tc, x, gn, phi_bytes, phi_scale, 
             if fn in (gate_copy, post_copy):
                 return [(coef_turn, n)] + find((prod_scalar,), n - 2, BRANCH) + find((sink_scale,), n) * (fn is post_copy)
             if fn is sink_sum or fn is pre_prod_vector:
-                return [(coef_turn, n)] + (find((u_sum,), n - 1 - (s[2] < 2)) if fn is pre_prod_vector else [])
+                return [(coef_turn, n)] + (find((u_sum,), n - 2) if fn is pre_prod_vector else [])
             if fn is sink_root:
                 return [(sink_sum,) + s[1:]]
             if fn is sink_scale:
@@ -626,9 +634,9 @@ def tile_groupedmanifoldhyperconnection_kernel(tc, x, gn, phi_bytes, phi_scale, 
             if fn is q_to_psum:
                 return find((sink_last, post_copy), n)
             if fn in (pre_prod_scalar, pre_prod_gpsimd):
-                return [(gate_copy, n)] + find((u_sum,), n - 1 - (s[2] < 2))
+                return [(gate_copy, n)] + find((u_sum,), n - 2)
             if fn is u_sum:
-                return find((pre_prod_vector, pre_prod_scalar, pre_prod_gpsimd), n)
+                return [t for r in s[3] for t in find((pre_prod_vector, pre_prod_scalar, pre_prod_gpsimd), n, r)]
             if fn is u_gain:
                 return find((u_sum,), n) + [(gf_half,)]
             if fn is branch_mm:

@@ -34,7 +34,9 @@ FLOPS = 2 * TOK * R * D * M + 2 * TOK * D * D
 
 BANKS = {"xp": 2, "tt": 1, "yy": 2, "uh": 1, "ct": 2}
 XN_BUFS = 3
-THIRD_TURN = 5
+TERMS = (0, 2, 3, BRANCH, 1)
+CO_BUFS = 4
+THIRD_TURNS = (4, 7)
 
 
 def spread(ap, axis, n):
@@ -51,6 +53,7 @@ def tile_groupedmanifoldhyperconnection_kernel(tc, x, gn, phi_bytes, phi_scale, 
     nc = tc.nc
     x_rows = x.rearrange("b s r d -> (b s) (r d)")
     out_view = out.rearrange("b (n tb t) i (q c) -> (b n) i q t tb c", tb=TB, t=C, q=NQ)
+    out_rows = out.rearrange("b s i (q c) -> (b s) i q c", q=NQ)
     with ExitStack() as ctx:
         keep = ctx.enter_context(tc.tile_pool(name="keep", bufs=1))
         sb = ctx.enter_context(tc.tile_pool(name="sb", bufs=2))
@@ -215,7 +218,7 @@ def tile_groupedmanifoldhyperconnection_kernel(tc, x, gn, phi_bytes, phi_scale, 
         def coef_act(n):
             st = state[n]
             tt = st["tt"]
-            st["co"] = sb.tile([P, MT, P], F32, name="co", bufs=3)
+            st["co"] = sb.tile([P, MT, P], F32, name="co", bufs=CO_BUFS)
             th = sb.tile([P, P], F32, name="th")
             nc.scalar.activation(st["co"][:, 1, :], tt[:, 1, :], ACT.Exp, bias=bias[:, 1:2])
             nc.scalar.activation(th[:], tt[:, 0, :], ACT.Tanh, bias=half_bias[:], scale=0.5)
@@ -224,7 +227,7 @@ def tile_groupedmanifoldhyperconnection_kernel(tc, x, gn, phi_bytes, phi_scale, 
 
         def coef_turn(n):
             st = state[n]
-            bank = "tt" if n == THIRD_TURN else "ct"
+            bank = "tt" if n in THIRD_TURNS else "ct"
             ct = ps.tile([P, MT, P], F32, name=bank, bufs=BANKS[bank])
             for m in (1, 2, 0):
                 nc.tensor.transpose(ct[:, m, :], st["co"][:, m, :], ident[:])
@@ -265,7 +268,7 @@ def tile_groupedmanifoldhyperconnection_kernel(tc, x, gn, phi_bytes, phi_scale, 
 
         def sink_last(n, lo, hi):
             st = state[n]
-            if lo == 0:
+            if "q" not in st:
                 st["q"] = sb.tile([P, G, R, R], F32, name="q")
             nc.vector.tensor_tensor(
                 out=st["q"][:, lo:hi], in0=st["scaled", lo], in1=spread(st["factor", lo][:], 3, R), op=ALU.mult
@@ -276,36 +279,32 @@ def tile_groupedmanifoldhyperconnection_kernel(tc, x, gn, phi_bytes, phi_scale, 
             nc.tensor.matmul(st["q_psum"], ident[:], st["q"][:], start=True, stop=True)
 
 
-        def pre_prod_vector(n, r):
+        def pre_prod(n, r, multiply, gate):
             st = state[n]
             st["pu", r] = sb.tile([P, T, P], F32, name="pu", bufs=8)
-            nc.vector.tensor_tensor(
+            multiply(
                 out=st["pu", r][:].rearrange("p t (g c) -> p t g c", g=G),
                 in0=xs[n][:, r * D : (r + 1) * D].rearrange("p (g c t) -> p t g c", g=G, t=T),
-                in1=spread(spread(st["gate"][:, :, r], 2, C // T), 1, T),
+                in1=spread(spread(gate[:, :, r], 2, C // T), 1, T),
                 op=ALU.mult,
             )
+
+        def pre_prod_vector(n, r):
+            pre_prod(n, r, nc.vector.tensor_tensor, state[n]["gate"])
+
+        def pre_prod_gpsimd(n, r):
+            pre_prod(n, r, nc.gpsimd.tensor_tensor, state[n]["gate_sb"])
 
         def gate_copy(n):
             st = state[n]
             st["gate_sb"] = sb.tile([P, G, GATES], F32, name="gate")
-            nc.vector.tensor_copy(out=st["gate_sb"][:], in_=st["gate"])
+            copy = nc.scalar.copy if n else nc.vector.tensor_copy
+            copy(out=st["gate_sb"][:], in_=st["gate"])
 
         def post_copy(n):
             st = state[n]
             st["gate_sb"] = sb.tile([P, G, GATES], F32, name="gate")
             nc.scalar.copy(out=st["gate_sb"][:, :, R:GATES], in_=st["gate"][:, :, R:GATES])
-
-        def pre_prod_gpsimd(n, r):
-            st = state[n]
-            tile = sb.tile([P, P, T], F32, name="pu", bufs=8)
-            st["pu", r] = tile[:].rearrange("p c t -> p t c")
-            nc.gpsimd.tensor_tensor(
-                out=tile[:].rearrange("p (g c) t -> p g (c t)", g=G),
-                in0=xs[n][:, r * D : (r + 1) * D].rearrange("p (g c) -> p g c", g=G),
-                in1=spread(st["gate_sb"][:, :, r], 2, C),
-                op=ALU.mult,
-            )
 
         def pre_prod_scalar(n, r):
             st = state[n]
@@ -319,7 +318,7 @@ def tile_groupedmanifoldhyperconnection_kernel(tc, x, gn, phi_bytes, phi_scale, 
             st = state[n]
             if start:
                 st["ut"] = ps.tile([P, T, P], F32, name="uh")
-            passes = [(r, t) for t in range(T) for r in streams]
+            passes = [(r, t) for r in streams for t in range(T)]
             for m, (r, t) in enumerate(passes):
                 first_pass, last_pass = start and m == 0, stop and m == len(passes) - 1
                 add_turned(st["ut"][:, t, :], st["pu", r][:, t, :], first_pass, last_pass, m < plain)
@@ -380,7 +379,7 @@ def tile_groupedmanifoldhyperconnection_kernel(tc, x, gn, phi_bytes, phi_scale, 
 
         def prod_gpsimd(n, j, lo, hi):
             dst, src = term(n, j, lo, hi)
-            weight = state[n]["q"][:, lo:hi, j, :]
+            weight = state[n]["q"][:, lo:hi, j, :] if j < R else state[n]["gate_sb"][:, lo:hi, R:GATES]
             nc.gpsimd.tensor_tensor(out=dst, in0=spread(src, 2, R), in1=spread(weight, 3, C), op=ALU.mult)
 
         def prod_vector(n, j, lo, hi):
@@ -389,14 +388,15 @@ def tile_groupedmanifoldhyperconnection_kernel(tc, x, gn, phi_bytes, phi_scale, 
             weight = st["q_psum"][:, lo:hi, j, :] if j < R else st["gate"][:, lo:hi, R:GATES]
             nc.vector.tensor_tensor(out=dst, in0=spread(src, 2, R), in1=spread(weight, 3, C), op=ALU.mult)
 
-        def y_sum(n, a, bank, terms, plain):
+        def y_sum(n, a, bank, lo, hi, plain):
             st = state[n]
-            st["yt", a] = ps.tile([P, TB, QUAD, C], F32, name=bank, bufs=BANKS[bank])
-            early, late = terms
-            passes = [(b, j) for b in range(QUAD) for j in early] + [(b, j) for j in late for b in range(QUAD)]
-            for m, (b, j) in enumerate(passes):
-                src = st["prod", j][:, QUAD * a + b].rearrange("p i c -> p (i c)")
-                add_turned(st["yt", a][:, :, b, :], src, m == 0, m == len(passes) - 1, m < plain)
+            if lo == 0:
+                st["yt", a] = ps.tile([P, TB, QUAD, C], F32, name=bank, bufs=BANKS[bank])
+            for m in range(lo, hi):
+                for b in range(QUAD):
+                    src = st["prod", TERMS[m]][:, QUAD * a + b].rearrange("p i c -> p (i c)")
+                    first_pass, last_pass = m == 0 and b == 0, m == BRANCH and b == QUAD - 1
+                    add_turned(st["yt", a][:, :, b, :], src, first_pass, last_pass, m == lo and b < plain)
 
         def y_out(n, a):
             yo = sb.tile([P, D], F32, name="yo", bufs=5, align_bytes=64)
@@ -406,9 +406,24 @@ def tile_groupedmanifoldhyperconnection_kernel(tc, x, gn, phi_bytes, phi_scale, 
                     out=out_view[n, i, a], in_=yo[C * i : C * (i + 1), :].rearrange("p (tb c) -> p tb c", tb=TB)
                 )
 
-        PAIRS = [0, 0, 0, (0, 2, 0, 0), (2, 0, 0, 0, 0), (2, 0, 0, 0), (2, 0, 0, 0, 0)]
-        LAG = [0, 1, 1, 1, 2, 2, 2, 1]
-        OUT = [0, 0, 0, 3, 3, 3, 3, 3]
+        def y_add(n, a, into, other, engine):
+            lo, hi = quad(a)
+            dst = state[n]["prod", into][:, lo:hi].rearrange("p g i c -> p (g i c)")
+            src = state[n]["prod", other][:, lo:hi].rearrange("p g i c -> p (g i c)")
+            add = nc.vector.tensor_tensor if engine == "vector" else nc.gpsimd.tensor_tensor
+            add(out=dst, in0=dst, in1=src, op=ALU.add)
+
+        def y_add_out(n, a, one, other):
+            lo, hi = quad(a)
+            yo = sb.tile([P, R, QUAD, C], F32, name="yo", bufs=5, align_bytes=64)
+            nc.vector.tensor_tensor(
+                out=yo[:],
+                in0=state[n]["prod", one][:, lo:hi].rearrange("p g i c -> p i g c"),
+                in1=state[n]["prod", other][:, lo:hi].rearrange("p g i c -> p i g c"),
+                op=ALU.add,
+            )
+            nc.sync.dma_start(out=out_rows[n * P : (n + 1) * P, :, a, :], in_=yo[:].rearrange("p i b c -> p i (b c)"))
+
         low, high, every = (0, HALF), (HALF, G), (0, G)
         tensor, vector, scalar, gpsimd = [], [], [], []
 
@@ -450,25 +465,12 @@ def tile_groupedmanifoldhyperconnection_kernel(tc, x, gn, phi_bytes, phi_scale, 
         def relu(n, place):
             return [(place, (branch_relu, n)), (place + 1, (branch_square, n))]
 
-        TERMS = ((0, 2, 3, BRANCH), (1,))
-
-        def ys(n, a, pair=0, bank="yy", terms=TERMS):
-            return (y_sum, n, a, bank, terms, pair)
-
         def g_halves(n):
             return [(prod_gpsimd, n, 0) + low, (prod_gpsimd, n, 1) + low, (prod_gpsimd, n, 0) + high, (prod_gpsimd, n, 1) + high]
 
         def gq(n, j, a):
             return (prod_gpsimd, n, j) + quad(a)
 
-        U1 = 3
-        SPLIT = 12
-        GSPLIT = 11
-        MARK = (1, 3, 5, 14, 22)
-        G3 = 12
-        PRE1 = 4
-        CUTS = [0, 0, 0, (0, 8, 16), (0, 8, 16), (0, 8, 16), (0, 8, 16)]
-        LATE = (0, 2)
         def br(k, *quads):
             return [vq(k, BRANCH, a) for a in quads]
 
@@ -483,90 +485,116 @@ def tile_groupedmanifoldhyperconnection_kernel(tc, x, gn, phi_bytes, phi_scale, 
 
         both = [(j, a) for a in range(NQ) for j in (2, 3)]
 
+
+        U1 = 3
+        V1 = 16
+        G1 = 9
+        U0 = 0
+        PRE1 = 4
+        XP_FROM = 7
+        G2 = 12
+        V3 = 15
+        G3 = 15
+        MARK = (1, 3, 5, 13, 21)
+        QP = (2, 3, 4, 5, 6)
+        V2 = 8
+        M2 = (0, 8)
+        A7 = 5
+        OWN3 = (0, 1)
+        PAIR = {0: 2}
+        CUT = 2
+
         halves = (low, high)
         own = (0, 1, 2, 3)
         vector += [(phi_widen_vector, 0, t) for t in range(T)] + [(phi_group, 0, "vector"), (phi_quant, 0), (phi_group, 1, "vector")]
         vector += gains(0, 0) + [(phi_quant, 1)] + gains(0, 1) + [(phi_group, 2, "vector"), (x_quant, 0), (phi_quant, 2)]
         vector += gains(1, 0) + [(phi_quant, 3)] + gains(1, 1)
         vector += [(w_group, 1), (x_quant, 1), (w_quant, 0), (w_quant, 1), (gate_copy, 0)]
-        vector += chain(0, [gains(2, 0), [], gains(2, 1), [], [(gate_copy, 1), (x_quant, 2)], [], [(u_gain, 0)], []], own, halves)
-        vector += [(u_quant, 0), (sink_last, 0) + low, (sink_last, 0) + high]
+        vector += chain(0, [gains(2, 0), [], gains(2, 1), [], [(x_quant, 2)], [], [(u_gain, 0)], []], own, halves)
+        vector += [(sink_last, 0) + high, (sink_last, 0) + low, (u_quant, 0)]
         scalar += [(phi_widen_scalar, r, t) for r in (1, 2, 3) for t in range(T)]
         scalar += [(phi_group, 3, "scalar"), (bias_read,), (w_group, 0), (coef_act, 0), (gf_half,)]
-        scalar += [(pre_prod_scalar, 0, 0), (coef_act, 1), (pre_prod_scalar, 0, 1)] + [(pre_prod_scalar, 1, r) for r in range(PRE1)]
-        gpsimd += [(pre_prod_gpsimd, 0, 2), (pre_prod_gpsimd, 0, 3)]
+        scalar += [(pre_prod_scalar, 0, 0), (coef_act, 1), (pre_prod_scalar, 0, 1), (gate_copy, 1)] + [(pre_prod_scalar, 1, r) for r in range(PRE1)]
+        gpsimd += [(pre_prod_gpsimd, 0, 2), (pre_prod_gpsimd, 0, 3)] + [(pre_prod_gpsimd, 1, r) for r in range(PRE1, R)]
         tensor += turns(0) + turns(1) + [(bias_turn,), (coef_mm, 0, "tt", 0, 3), (coef_mm, 0, "tt", 3, 4), (x_turn, 2, 0)]
-        tensor += [(coef_turn, 0), mm(1, "tt"), (x_turn, 2, 1), (u_sum, 0, 0, (0, 2), True, False), (coef_turn, 1), (u_sum, 0, 0, (1, 3), False, True)]
+        tensor += [(coef_turn, 0), mm(1, "tt"), (x_turn, 2, 1), (coef_turn, 1), (u_sum, 0, U0, (0, 2), True, False), (u_sum, 0, U0, (1, 3), False, True)]
         tensor += turns(3) + [mm(2, "tt")]
 
-        def bank(n, a, plain=0):
-            index = NQ * n + a
-            return ys(n, a, plain, "xp" if index >= 10 and index % 2 == 1 else "yy", TERMS if a in LATE else ((0, 2, 3, BRANCH, 1), ()))
-
-        def g_whole(k):
-            return [(prod_gpsimd, k, 0) + every, (prod_gpsimd, k, 1) + low, (prod_gpsimd, k, 1) + high]
+        def bank(index, lo=0, hi=BRANCH + 1):
+            n, a = divmod(index, NQ)
+            return (y_sum, n, a, "xp" if index >= XP_FROM and index % 2 == 1 else "yy", lo, hi, PAIR.get(index, 0) * (lo == 0))
 
         def vqs(k, *pairs):
             return [vq(k, j, a) for j, a in pairs]
 
         def out(index):
-            return [(y_out,) + divmod(index, NQ)] if index >= 0 else []
+            return [(y_out,) + divmod(index, NQ)]
 
-        def prep(m, *streams):
-            return gains(m, *streams) if m < NT else []
+        def usum(n, plain=0):
+            return (u_sum, n, plain, own, True, True)
 
-        branches = [(BRANCH, a) for a in range(NQ)]
+        def sgroups(k, j, lo, hi):
+            return [(prod_scalar, k, j, g, g + 1) for g in range(lo, hi)]
+
+        def burst(n):
+            return [(sink_last, n) + every, (u_quant, n)]
+
         vector += chain(
             1,
-            [prep(3, 0, 1), [], prep(4, 0), [], prep(4, 1) + br(0, 2), [], [(u_gain, 1)] + prep(5, 0, 1), out(0)], own, halves)
-        vector += [(x_quant, 3), (x_quant, 4), (x_quant, 5), (u_quant, 1), (sink_last, 1) + low, (sink_last, 1) + high]
+            [gains(3, 0, 1), [], gains(4, 0), [], gains(4, 1), [], [(u_gain, 1)] + gains(5, 0, 1), out(0)], own, halves)
+        vector += [(x_quant, 3), (x_quant, 4), (x_quant, 5), (sink_last, 1) + high, (sink_last, 1) + low, (u_quant, 1)]
         scalar += terms(0, (2, 0)) + [(branch_relu, 0)] + terms(0, (3, 0))[:1] + [(branch_square, 0)] + terms(0, (3, 0))[1:]
-        scalar += terms(0, (BRANCH, 0)) + [(coef_act, 2)] + terms(0, (2, 1), (3, 1), (BRANCH, 1), (2, 2), (3, 2), (2, 3), (3, 3), (BRANCH, 3))
+        scalar += terms(0, (BRANCH, 0)) + [(coef_act, 2)] + terms(0, (2, 1), (3, 1), (BRANCH, 1), (2, 2), (3, 2), (BRANCH, 2), (2, 3), (3, 3), (BRANCH, 3))
         gpsimd += g_halves(0)
-        tensor += [(branch_mm, 0)] + turns(4) + [(u_sum, 1, U1, own, True, True)] + turns(5) + [bank(0, 0, 2)] + [(coef_turn, 2), bank(0, 1), bank(0, 2)]
-        for k in (1, 2):
+        tensor += [(branch_mm, 0)] + turns(4) + [usum(1, U1)] + turns(5) + [bank(0), (coef_turn, 2), bank(1), bank(2)]
+
+        vector += chain(
+            2,
+            [out(1), pres(2, 0, 1), pres(2, 2), pres(2, 3) + gains(6, 0), gains(6, 1) + out(2), out(3) + [(u_gain, 2)],
+             gains(7, 0) + [(prod_vector, 1, BRANCH, V1, G)] * (V1 < G), gains(7, 1) + out(4)], own)
+        vector += [(x_quant, 6), (x_quant, 7)] + burst(2)
+        scalar += [(post_copy, 1)] + terms(1, (2, 0)) + [(coef_act, 3), (branch_relu, 1)] + terms(1, (3, 0))[:1] + [(branch_square, 1)]
+        scalar += terms(1, (3, 0))[1:] + terms(1, (BRANCH, 0), (2, 1)) + [(coef_act, 4)] + terms(1, (3, 1), (BRANCH, 1), (3, 2))
+        scalar += terms(1, (BRANCH, 2)) + [(coef_act, 5)] + sgroups(1, 2, HALF, G1) + terms(1, (3, 3)) + sgroups(1, BRANCH, 12, V1)
+        gpsimd += [(prod_gpsimd, 1, 0) + every, (prod_gpsimd, 1, 1) + low, (prod_gpsimd, 1, 1) + high, (prod_gpsimd, 1, 2, G1, G)]
+        tensor += [mm(3, "tt"), (branch_mm, 1)] + turns(6) + [bank(3), mm(4, "tt"), usum(2), (x_turn, 7, 0), bank(4), (x_turn, 7, 1)]
+        tensor += [mm(5, "tt"), (coef_turn, 3), bank(5)]
+
+        vector += chain(
+            3,
+            [pres(3, 0), pres(3, 1, 2), pres(3, 3), out(5) + br(2, 0), [(prod_vector, 2, 3, 0, V2)] + br(2, 1) + out(6) + br(2, 2), out(7),
+             br(2, 3) + [(u_gain, 3)] + out(8), []], OWN3)
+        vector += burst(3)
+        work = sgroups(2, 2, 0, G2) + sgroups(2, 3, V2, G)
+        scalar += [(coef_act, 6), (branch_relu, 2)] + work[:1] + [(branch_square, 2)] + work[1:A7] + [(coef_act, 7)]
+        scalar += deal(work[A7:], *inv(3, 2, M2[0]) + inv(3, 3, M2[1]))
+        gpsimd += [(prod_gpsimd, 2, 0) + every, (prod_gpsimd, 2, 1) + low, (prod_gpsimd, 2, 1) + high, (prod_gpsimd, 2, 2, G2, G)]
+        tensor += [mm(6, "tt"), (branch_mm, 2), (q_to_psum, 2), bank(6), mm(7, "tt"), bank(7), usum(3), (coef_turn, 4), bank(8), bank(9)]
+
+        for k in range(3, NT - 1):
             n = k + 1
             o = [out(NQ * k - 3 + b) for b in range(NQ)]
             vector += chain(
                 n,
-                [o[0], pres(n, 0, 1), pres(n, 2), pres(n, 3) + o[1], [(prod_vector, k, BRANCH, HALF, SPLIT)] + o[2], prep(k + 5, 0) + [(u_gain, n)],
-                 o[3], prep(k + 5, 1)], own)
-            vector += [(x_quant, k + 5), (u_quant, n), (sink_last, n) + every]
-            scalar += [(post_copy, k)] + terms(k, (2, 0)) + [(coef_act, 2 * k + 1), (branch_relu, k)] + terms(k, (3, 0))[:1] + [(branch_square, k)]
-            scalar += terms(k, (3, 0))[1:] + terms(k, (BRANCH, 0), (2, 1), (3, 1), (BRANCH, 1)) + [(coef_act, 2 * k + 2)]
-            scalar += terms(k, (2, 2))[: GSPLIT - HALF] + terms(k, (3, 2)) + terms(k, (3, 3)) + terms(k, (BRANCH, 2), (BRANCH, 3))[SPLIT - HALF :]
-            gpsimd += g_whole(k) + [(prod_gpsimd, k, 2, GSPLIT, G)]
-            tensor += [mm(2 * k + 1, "tt"), (branch_mm, k), (x_turn, k + 5, 0), bank(k - 1, 3)]
-            tensor += [mm(2 * k + 2, "tt"), (x_turn, k + 5, 1), (u_sum, n, 0, own, True, True), bank(k, 0), (coef_turn, k + 2), bank(k, 1)] + [bank(k, 2)] * (LAG[n] == 1)
-        for k in range(3, NT - 1):
-            n = k + 1
-            lag = LAG[k]
-            o = [out(NQ * k - OUT[k] + b) for b in range(OUT[k] + NQ - OUT[k + 1])] + [[]]
-            mine = (0, 1) if k == 3 else ()
-            vector += chain(
-                n,
-                [pres(n, 0), pres(n, 1, 2), pres(n, 3), o[0] + br(k, 0), br(k, 1) + o[1] + br(k, 2), o[2],
-                 br(k, 3) + [(u_gain, n)] + o[3] + o[4], []] if k == 3 else
                 [pres(n, 0, 1), pres(n, 2), pres(n, 3) + o[0], br(k, 0), br(k, 1) + o[1], br(k, 2),
-                 o[2] + br(k, 3) + [(u_gain, n)] + o[3] + o[4], []], mine)
-            vector += [(u_quant, n), (sink_last, n) + every]
-            work = terms(k, *both)
-            if k == 3:
-                scalar += work[:5] + [(branch_relu, k), (coef_act, 7), (branch_square, k)] + deal(work[5 : G3 - G], *inv(n, 2, 7) + inv(n, 3, 14))
-            else:
-                scalar += deal(work, *inv(n, 0, MARK[0]) + relu(k, MARK[1]) + inv(n, 1, MARK[2]) + inv(n, 2, MARK[3]) + inv(n, 3, MARK[4]) + [(24, (post_copy, n))] * (n == NT - 1))
-            cuts = CUTS[k]
-            gpsimd += [(prod_gpsimd, k, j, lo, hi) for lo, hi in zip(cuts, cuts[1:]) for j in (0, 1)] + [(prod_gpsimd, k, 3, G3, G)] * (k == 3)
-            banks = [bank(*divmod(b, NQ), PAIRS[k][i]) for i, b in enumerate(range(NQ * k - lag, NQ * n - LAG[n]))]
-            tensor += [mm(7, "tt")] * (k == 3) + [(branch_mm, k)] + banks[:lag] + [(coef_turn, k + 2)] * (k + 2 < NT) + [(u_sum, n, 0, own, True, True)] + banks[lag:]
+                 o[2] + br(k, 3) + [(prod_vector, k, 3, V3, G)] * (V3 < G) + [(u_gain, n)] + o[3], []], ())
+            vector += burst(n)
+            work = terms(k, (2, 0), (3, 0), (2, 1), (3, 1), (2, 2), (2, 3)) + sgroups(k, 3, HALF, V3) + sgroups(k, 1, G3, G)
+            scalar += deal(work, *inv(n, 0, MARK[0]) + relu(k, MARK[1]) + inv(n, 1, MARK[2]) + inv(n, 2, MARK[3]) + inv(n, 3, MARK[4]) + [(24, (post_copy, n))] * (n == NT - 1))
+            gpsimd += [(prod_gpsimd, k, 0) + low, (prod_gpsimd, k, 1) + low, (prod_gpsimd, k, 0) + high, (prod_gpsimd, k, 1, HALF, G3)]
+            first = NQ * k - 2
+            tensor += [(branch_mm, k)] + [(q_to_psum, k)] * (k in QP) + [bank(first), bank(first + 1)] + [(coef_turn, k + 2)] * (k + 2 < NT)
+            tensor += [usum(n), bank(first + 2), bank(first + 3)] + [bank(first + 4, 0, CUT)] * (k == NT - 2)
 
         k = NT - 1
-        tensor += [(branch_mm, k), (q_to_psum, k)] + [bank(*divmod(b, NQ)) for b in range(NQ * k - LAG[k], NQ * NT)]
-        o = [s for b in range(NQ * k - OUT[k], NQ * NT) for s in out(b)]
-        vector += o[:-5] + vqs(k, (2, 0), (3, 0), (2, 1), (3, 1)) + [o[-5]] + vqs(k, (2, 2), (3, 2), (1, 3), (2, 3), (3, 3)) + o[-4:]
+        last = NQ - 1
+        tensor += [(q_to_psum, k), (branch_mm, k), bank(NQ * k - 2, CUT)] + [bank(b) for b in range(NQ * k - 1, NQ * NT - 1)]
+        o = [out(b)[0] for b in range(NQ * k - 3, NQ * NT - 1)]
+        vector += o[:1] + vqs(k, (2, 0), (3, 0), (2, 1)) + [o[1]] + vqs(k, (3, 1), (2, 2)) + [o[2]] + vqs(k, (3, 2), (2, 3), (3, 3)) + [o[3]]
+        vector += [(y_add, k, last, 2, 3, "vector"), (y_add, k, last, 0, 1, "vector"), (y_add, k, last, 2, BRANCH, "vector"), o[4], (y_add_out, k, last, 0, 2), o[5]]
         work = terms(k, (1, 1), (BRANCH, 0), (BRANCH, 1), (1, 2), (BRANCH, 2), (BRANCH, 3))
         scalar += deal(work, *relu(k, 2))
-        gpsimd += [(prod_gpsimd, k, 0) + low, gq(k, 1, 0), (prod_gpsimd, k, 0) + high]
+        gpsimd += [(prod_gpsimd, k, 0) + low, gq(k, 1, 0), (prod_gpsimd, k, 0) + high, gq(k, 1, last)]
 
         queues = (tensor, vector, scalar, gpsimd)
         steps = [s for queue in queues for s in queue]
@@ -583,14 +611,14 @@ def tile_groupedmanifoldhyperconnection_kernel(tc, x, gn, phi_bytes, phi_scale, 
                 return s[2], [(coef_act, s[1])]
             if fn is bias_turn:
                 return "uh", [(bias_read,)]
-            if fn is y_sum:
+            if fn is y_sum and s[4] == 0:
                 return s[3], [(y_out, s[1], s[2])]
             if fn is u_sum and s[4]:
                 return "uh", [(u_gain, s[1])]
             if fn is branch_mm:
                 return "uh", [(branch_relu, s[1])]
             if fn is coef_turn:
-                return "tt" if s[1] == THIRD_TURN else "ct", find((prod_vector, pre_prod_vector, sink_scale, gate_copy, post_copy), s[1])
+                return "tt" if s[1] in THIRD_TURNS else "ct", find((prod_vector, pre_prod_vector, sink_scale, gate_copy, post_copy), s[1])
             return None, []
 
         before = dict()
@@ -618,13 +646,13 @@ def tile_groupedmanifoldhyperconnection_kernel(tc, x, gn, phi_bytes, phi_scale, 
             if fn is coef_mm:
                 return [(x_quant, n)] + [(phi_quant, r) for r in range(s[3], s[4])]
             if fn is coef_act:
-                return find((coef_mm,), n) + find((coef_turn,), n - 3) + [(bias_read,)]
+                return find((coef_mm,), n) + find((coef_turn,), n - CO_BUFS) + [(bias_read,)]
             if fn is coef_turn:
                 return [(coef_act, n)]
             if fn in (gate_copy, post_copy):
-                return [(coef_turn, n)] + find((prod_scalar,), n - 2, BRANCH) + find((sink_scale,), n) * (fn is post_copy)
+                return [(coef_turn, n)] + find((prod_scalar, prod_gpsimd), n - 2, BRANCH) + find((sink_scale,), n) * (fn is post_copy)
             if fn is sink_sum or fn is pre_prod_vector:
-                return [(coef_turn, n)] + (find((u_sum,), n - 2) if fn is pre_prod_vector else [])
+                return [(coef_turn, n)] + find((gate_copy,), n) + (find((u_sum,), n - 2) if fn is pre_prod_vector else [])
             if fn is sink_root:
                 return [(sink_sum,) + s[1:]]
             if fn is sink_scale:
@@ -649,12 +677,16 @@ def tile_groupedmanifoldhyperconnection_kernel(tc, x, gn, phi_bytes, phi_scale, 
                 source = [(branch_square, n)] if s[2] == BRANCH else find((sink_last,), n)
                 if fn is prod_vector:
                     source = source + find((q_to_psum, post_copy), n)
-                if fn is prod_scalar and s[2] == BRANCH:
+                if fn is not prod_vector and s[2] == BRANCH:
                     source = source + find((gate_copy, post_copy), n)
                 return source + find((y_sum,), n - 2)
             if fn is y_sum:
                 lo, hi = quad(s[2])
-                return [t for t in find(products, n) if t[3] < hi and t[4] > lo]
+                return [t for t in find(products, n) if t[2] in TERMS[s[4] : s[5]] and t[3] < hi and t[4] > lo]
+            if fn in (y_add, y_add_out):
+                lo, hi = quad(s[2])
+                sums = [t for t in find((y_add,), n, s[2]) if t[3] in s[3:5] and (fn is y_add_out or t[4] < s[4] and t != s)]
+                return [t for t in find(products, n) if t[2] in s[3:5] and t[3] < hi and t[4] > lo] + sums
             if fn is y_out:
                 return find((y_sum,), n, s[2])
             return []

@@ -274,9 +274,9 @@ def tile_groupedmanifoldhyperconnection_kernel(tc, x, gn, phi_bytes, phi_scale, 
                 out=st["q"][:, lo:hi], in0=st["scaled", lo], in1=spread(st["factor", lo][:], 3, R), op=ALU.mult
             )
 
-        def q_to_psum(n):
+        def q_to_psum(n, lo, hi):
             st = state[n]
-            nc.tensor.matmul(st["q_psum"], ident[:], st["q"][:], start=True, stop=True)
+            nc.tensor.matmul(st["q_psum"][:, lo:hi], ident[:], st["q"][:, lo:hi], start=True, stop=True)
 
 
         def pre_prod(n, r, multiply, gate):
@@ -321,7 +321,7 @@ def tile_groupedmanifoldhyperconnection_kernel(tc, x, gn, phi_bytes, phi_scale, 
             passes = [(r, t) for r in streams for t in range(T)]
             for m, (r, t) in enumerate(passes):
                 first_pass, last_pass = start and m == 0, stop and m == len(passes) - 1
-                add_turned(st["ut"][:, t, :], st["pu", r][:, t, :], first_pass, last_pass, m < plain)
+                add_turned(st["ut"][:, t, :], st["pu", r][:, t, :], first_pass, last_pass, m < plain[0] or m >= len(passes) - plain[1])
 
         def u_gain(n):
             st = state[n]
@@ -394,9 +394,10 @@ def tile_groupedmanifoldhyperconnection_kernel(tc, x, gn, phi_bytes, phi_scale, 
                 st["yt", a] = ps.tile([P, TB, QUAD, C], F32, name=bank, bufs=BANKS[bank])
             for m in range(lo, hi):
                 for b in range(QUAD):
-                    src = st["prod", TERMS[m]][:, QUAD * a + b].rearrange("p i c -> p (i c)")
+                    g = QUAD - 1 - b
+                    src = st["prod", TERMS[m]][:, QUAD * a + g].rearrange("p i c -> p (i c)")
                     first_pass, last_pass = m == 0 and b == 0, m == BRANCH and b == QUAD - 1
-                    add_turned(st["yt", a][:, :, b, :], src, first_pass, last_pass, m == lo and b < plain)
+                    add_turned(st["yt", a][:, :, g, :], src, first_pass, last_pass, (m == 0 and b < plain[0]) or (m == BRANCH and b >= QUAD - plain[1]))
 
         def y_out(n, a):
             yo = sb.tile([P, D], F32, name="yo", bufs=5, align_bytes=64)
@@ -486,10 +487,12 @@ def tile_groupedmanifoldhyperconnection_kernel(tc, x, gn, phi_bytes, phi_scale, 
         both = [(j, a) for a in range(NQ) for j in (2, 3)]
 
 
-        U1 = 3
+        U1 = (3, 0)
         V1 = 16
         G1 = 9
-        U0 = 0
+        U0 = (0, 0)
+        UK = (0, 0)
+        UORD = (3, 2, 1, 0)
         PRE1 = 4
         XP_FROM = 7
         G2 = 12
@@ -501,7 +504,7 @@ def tile_groupedmanifoldhyperconnection_kernel(tc, x, gn, phi_bytes, phi_scale, 
         M2 = (0, 8)
         A7 = 5
         OWN3 = (0, 1)
-        PAIR = {0: 2}
+        PAIR = {0: (2, 0)}
         CUT = 2
 
         halves = (low, high)
@@ -522,7 +525,7 @@ def tile_groupedmanifoldhyperconnection_kernel(tc, x, gn, phi_bytes, phi_scale, 
 
         def bank(index, lo=0, hi=BRANCH + 1):
             n, a = divmod(index, NQ)
-            return (y_sum, n, a, "xp" if index >= XP_FROM and index % 2 == 1 else "yy", lo, hi, PAIR.get(index, 0) * (lo == 0))
+            return (y_sum, n, a, "xp" if index >= XP_FROM and index % 2 == 1 else "yy", lo, hi, PAIR.get(index, (0, 0)))
 
         def vqs(k, *pairs):
             return [vq(k, j, a) for j, a in pairs]
@@ -530,8 +533,8 @@ def tile_groupedmanifoldhyperconnection_kernel(tc, x, gn, phi_bytes, phi_scale, 
         def out(index):
             return [(y_out,) + divmod(index, NQ)]
 
-        def usum(n, plain=0):
-            return (u_sum, n, plain, own, True, True)
+        def usum(n, plain=(0, 0)):
+            return (u_sum, n, plain, UORD, True, True)
 
         def sgroups(k, j, lo, hi):
             return [(prod_scalar, k, j, g, g + 1) for g in range(lo, hi)]
@@ -551,7 +554,7 @@ def tile_groupedmanifoldhyperconnection_kernel(tc, x, gn, phi_bytes, phi_scale, 
         vector += chain(
             2,
             [out(1), pres(2, 0, 1), pres(2, 2), pres(2, 3) + gains(6, 0), gains(6, 1) + out(2), out(3) + [(u_gain, 2)],
-             gains(7, 0) + [(prod_vector, 1, BRANCH, V1, G)] * (V1 < G), gains(7, 1) + out(4)], own)
+             gains(7, 0), gains(7, 1) + out(4)], own)
         vector += [(x_quant, 6), (x_quant, 7)] + burst(2)
         scalar += [(post_copy, 1)] + terms(1, (2, 0)) + [(coef_act, 3), (branch_relu, 1)] + terms(1, (3, 0))[:1] + [(branch_square, 1)]
         scalar += terms(1, (3, 0))[1:] + terms(1, (BRANCH, 0), (2, 1)) + [(coef_act, 4)] + terms(1, (3, 1), (BRANCH, 1), (3, 2))
@@ -569,7 +572,7 @@ def tile_groupedmanifoldhyperconnection_kernel(tc, x, gn, phi_bytes, phi_scale, 
         scalar += [(coef_act, 6), (branch_relu, 2)] + work[:1] + [(branch_square, 2)] + work[1:A7] + [(coef_act, 7)]
         scalar += deal(work[A7:], *inv(3, 2, M2[0]) + inv(3, 3, M2[1]))
         gpsimd += [(prod_gpsimd, 2, 0) + every, (prod_gpsimd, 2, 1) + low, (prod_gpsimd, 2, 1) + high, (prod_gpsimd, 2, 2, G2, G)]
-        tensor += [mm(6, "tt"), (branch_mm, 2), (q_to_psum, 2), bank(6), mm(7, "tt"), bank(7), usum(3), (coef_turn, 4), bank(8), bank(9)]
+        tensor += [mm(6, "tt"), (branch_mm, 2), (q_to_psum, 2) + low, bank(6), mm(7, "tt"), bank(7), usum(3), (coef_turn, 4), bank(8), bank(9)]
 
         for k in range(3, NT - 1):
             n = k + 1
@@ -583,12 +586,12 @@ def tile_groupedmanifoldhyperconnection_kernel(tc, x, gn, phi_bytes, phi_scale, 
             scalar += deal(work, *inv(n, 0, MARK[0]) + relu(k, MARK[1]) + inv(n, 1, MARK[2]) + inv(n, 2, MARK[3]) + inv(n, 3, MARK[4]) + [(24, (post_copy, n))] * (n == NT - 1))
             gpsimd += [(prod_gpsimd, k, 0) + low, (prod_gpsimd, k, 1) + low, (prod_gpsimd, k, 0) + high, (prod_gpsimd, k, 1, HALF, G3)]
             first = NQ * k - 2
-            tensor += [(branch_mm, k)] + [(q_to_psum, k)] * (k in QP) + [bank(first), bank(first + 1)] + [(coef_turn, k + 2)] * (k + 2 < NT)
-            tensor += [usum(n), bank(first + 2), bank(first + 3)] + [bank(first + 4, 0, CUT)] * (k == NT - 2)
+            tensor += [(branch_mm, k)] + [(q_to_psum, k) + high] * (k in QP) + [bank(first), bank(first + 1)] + [(coef_turn, k + 2)] * (k + 2 < NT)
+            tensor += [usum(n, UK), bank(first + 2), bank(first + 3)] + [bank(first + 4, 0, CUT)] * (k == NT - 2)
 
         k = NT - 1
         last = NQ - 1
-        tensor += [(q_to_psum, k), (branch_mm, k), bank(NQ * k - 2, CUT)] + [bank(b) for b in range(NQ * k - 1, NQ * NT - 1)]
+        tensor += [(q_to_psum, k) + every, (branch_mm, k), bank(NQ * k - 2, CUT)] + [bank(b) for b in range(NQ * k - 1, NQ * NT - 1)]
         o = [out(b)[0] for b in range(NQ * k - 3, NQ * NT - 1)]
         vector += o[:1] + vqs(k, (2, 0), (3, 0), (2, 1)) + [o[1]] + vqs(k, (3, 1), (2, 2)) + [o[2]] + vqs(k, (3, 2), (2, 3), (3, 3)) + [o[3]]
         vector += [(y_add, k, last, 2, 3, "vector"), (y_add, k, last, 0, 1, "vector"), (y_add, k, last, 2, BRANCH, "vector"), o[4], (y_add_out, k, last, 0, 2), o[5]]

@@ -20,7 +20,8 @@ D = 512
 G = 16
 C = 32
 GATES = 2 * R
-KC = GATES + R * R
+LOGITS = R * R
+KC = GATES + LOGITS
 M = G * KC
 MT = M // P
 TOK = 1024
@@ -28,15 +29,49 @@ NT = TOK // P
 TB = P // C
 QUAD = 4
 NQ = G // QUAD
-HALF = G // 2
 BRANCH = R
+HALF = G // 2
+U_BATCHES = ((0, 4), (4, 8))
+X_BATCHES = ((0, 1), (1, 2), (2, 4), (4, 6), (6, 7), (7, 8))
+OWN_GATES = 4
+LATE_PRE = (4, 1)
 FLOPS = 2 * TOK * R * D * M + 2 * TOK * D * D
 
-BANKS = {"xp": 2, "tt": 1, "yy": 2, "uh": 1, "ct": 2}
-XN_BUFS = 3
-TERMS = (0, 2, 3, BRANCH, 1)
-CO_BUFS = 4
-THIRD_TURNS = (4, 7)
+BANKS = {"four": 4, "b0": 1, "b1": 1, "b2": 1, "b3": 1}
+KINDS = {
+    "wide": ([P, T, M], BF16, "yo", 4),
+    "bias_ps": ([P, MT, 2], F32, "b2", 1),
+    "warm": ([P, 2, P], F32, "b0", 1),
+    "gate_words": ([P, R, P, T], BF16, "late", 7),
+    "logit_words": ([P, 2, 2 * P, T], BF16, "late", 7),
+    "w_words": ([P, D, T], BF16, "late", 7),
+    "xp": ([P, 2, 2, P], F32, "four", 4),
+    "xn": ([P, R, 0, T], BF16, "xn", 2),
+    "xc": ([P, R, 0], U32, "xc", 3),
+    "xs": ([P, R, 0], U8, "xs", 3),
+    "tg": ([P, 0], F32, "b0", 1),
+    "tl": ([P, 2, 0], F32, "b1", 1),
+    "th": ([P, 0], F32, "th", 2),
+    "th1": ([P, 0], F32, "th1", 1),
+    "gt": ([P, 0], F32, "b2", 1),
+    "gate": ([P, 0], F32, "gate", len(X_BATCHES)),
+    "co": ([P, 2, 0], F32, "co", len(X_BATCHES)),
+    "ct": ([P, 2 * P], F32, "b0", 1),
+    "qp": ([P, 2 * P], F32, "b3", 1),
+    "sums": ([P, G, R], F32, "sums", 3),
+    "root": ([P, G, R], F32, "root", 2),
+    "factor": ([P, G, R], F32, "factor", 3),
+    "scaled": ([P, G, R, R], F32, "scaled", 3),
+    "q": ([P, R, G, R], F32, "q", 3),
+    "pu": ([P, T, 2, P], F32, "prod", 3),
+    "ut": ([P, T, P], F32, "four", 4),
+    "h": ([P, D], F32, "four", 4),
+    "hr": ([P, D], F32, "hr", 1),
+    "f": ([P, D], F32, "f", 2),
+    "prod": ([P, HALF, R, C], F32, "prod", 3),
+    "yt": ([P, TB, QUAD, C], F32, "four", 4),
+    "yo": ([P, D], F32, "yo", 4),
+}
 
 
 def spread(ap, axis, n):
@@ -45,8 +80,27 @@ def spread(ap, axis, n):
     return ap.unsqueeze(axis).to_broadcast(shape)
 
 
-def quad(a):
-    return QUAD * a, QUAD * (a + 1)
+def tag_of(key):
+    tag = KINDS[key[0]][2]
+    if key[0] == "ct":
+        return ("b0", "b1")[key[1] % 2] if key[1] else "b3"
+    if key[0] == "qp":
+        return ("b3", "b2")[key[1] % 2]
+    if key in (("tl", 1), ("xp", 2, 1)):
+        return "b3"
+    if key in (("tl", 4), ("tl", 5), ("gt", 5)):
+        return "four"
+    if key == ("xp", 2, 0):
+        return "b1"
+    if key[0] == "pu" and key[1:] >= LATE_PRE:
+        return "late"
+    if key[0] == "pu":
+        return "prod%d" % ((2 * key[1] + key[2]) % (BRANCH + 1))
+    return "prod%d" % key[2] if tag == "prod" else tag
+
+
+def bufs_of(key):
+    return 7 if tag_of(key) == "late" else BANKS.get(tag_of(key), KINDS[key[0]][3])
 
 
 def tile_groupedmanifoldhyperconnection_kernel(tc, x, gn, phi_bytes, phi_scale, bm, gf, w, out):
@@ -75,276 +129,272 @@ def tile_groupedmanifoldhyperconnection_kernel(tc, x, gn, phi_bytes, phi_scale, 
         gf_k = keep.tile([P, T], BF16)
         w_raw = keep.tile([P, T, D], BF16)
 
-        def load_x(n):
-            nc.sync.dma_start(out=xs[n][:], in_=x_rows[n * P : (n + 1) * P, :])
+        def load_x(n, lo, hi):
+            nc.sync.dma_start(out=xs[n][:, lo * D : hi * D], in_=x_rows[n * P : (n + 1) * P, lo * D : hi * D])
 
         nc.sync.dma_start(out=scale[:], in_=phi_scale.rearrange("(r p t) o -> p r (t o)", p=P, t=T))
-        nc.sync.dma_start(out=phi_raw[0][:], in_=phi_view[0])
-        nc.sync.dma_start(out=phi_raw[1][:], in_=phi_view[1])
-        nc.sync.dma_start(out=phi_raw[2][:], in_=phi_view[2])
-        load_x(0)
+        for r in range(R):
+            nc.sync.dma_start(out=phi_raw[r][:], in_=phi_view[r])
+        load_x(0, 0, 2)
         nc.sync.dma_start(out=gn_k[:], in_=gn.rearrange("(r p t) -> p r t", p=P, t=T))
-        nc.sync.dma_start(out=phi_raw[3][:], in_=phi_view[3])
+        load_x(0, 2, 4)
+        load_x(1, 0, R)
         bm_groups = bm.rearrange("(o g k) -> o g k", o=1, g=G)
         nc.sync.dma_start(out=bm_row[0:1, 0:P].rearrange("p (g k) -> p g k", g=G), in_=bm_groups[:, :, 0:GATES])
         nc.sync.dma_start(out=bm_row[0:1, P:M].rearrange("p (g k) -> p g k", g=G), in_=bm_groups[:, :, GATES:KC])
-        load_x(1)
+        load_x(2, 0, R)
+        load_x(3, 0, R)
         nc.sync.dma_start(out=w_raw[:], in_=w.rearrange("(p t) n -> p t n", t=T))
         nc.sync.dma_start(out=gf_k[:], in_=gf.rearrange("(p t) -> p t", t=T))
-        for n in range(2, NT):
-            load_x(n)
+        for n in range(4, NT):
+            load_x(n, 0, R)
 
-        phi_codes = keep.tile([P, R, M], U32, align_bytes=64)
-        phi_scales = keep.tile([P, R, M], U8, align_bytes=64)
-        phi_wide = [sb.tile([P, T, M], BF16, name="prod%d" % r) for r in range(R)]
-        phi_words = [keep.tile([P, M, T], BF16, name="phg%d" % r, align_bytes=64) for r in range(R)]
+        gate_codes = keep.tile([P, R, P], U32, align_bytes=64)
+        gate_scales = keep.tile([P, R, P], U8, align_bytes=64)
+        logit_codes = keep.tile([P, R, 2 * P], U32, align_bytes=64)
+        logit_scales = keep.tile([P, R, 2 * P], U8, align_bytes=64)
         bias = keep.tile([P, MT], F32)
         half_bias = keep.tile([P, 1], F32)
         half_gf = keep.tile([P, T], F32)
-        w_words = keep.tile([P, D, T], BF16, align_bytes=64)
         w_codes = keep.tile([P, D], U32, align_bytes=64)
         w_scales = keep.tile([P, D], U8, align_bytes=64)
+        u_words = [keep.tile([P, hi - lo, P, T], BF16, name="uw%d" % lo, align_bytes=64) for lo, hi in U_BATCHES]
+        u_codes = [keep.tile([P, hi - lo, P], U32, name="uc%d" % lo, align_bytes=64) for lo, hi in U_BATCHES]
+        u_scales = [keep.tile([P, hi - lo, P], U8, name="us%d" % lo, align_bytes=64) for lo, hi in U_BATCHES]
+        batch_of = {n: (b, n - lo) for b, (lo, hi) in enumerate(U_BATCHES) for n in range(lo, hi)}
 
+        xb_of = {n: (b, n - lo) for b, (lo, hi) in enumerate(X_BATCHES) for n in range(lo, hi)}
 
-        once = dict()
+        tiles = dict()
 
-        def phi_widen_vector(r, t):
-            src = phi_raw[r][:, t, :].bitcast(FP8)
-            nc.vector.tensor_scalar(phi_wide[r][:, t, :], src, scale[:, r, t : t + 1], None, op0=ALU.mult)
+        def value(*key):
+            if key not in tiles:
+                shape, dtype, tag, bufs = KINDS[key[0]]
+                if 0 in shape:
+                    lo, hi = X_BATCHES[key[1]]
+                    shape = [size or (hi - lo) * P for size in shape]
+                if tag in BANKS:
+                    tiles[key] = ps.tile(shape, dtype, name=tag_of(key), bufs=bufs_of(key))
+                else:
+                    tiles[key] = sb.tile(shape, dtype, name=tag_of(key), bufs=bufs_of(key), align_bytes=64)
+            return tiles[key]
 
-        def phi_widen_scalar(r, t):
-            src = phi_raw[r][:, t, :].bitcast(FP8)
-            nc.scalar.activation(phi_wide[r][:, t, :], src, ACT.Copy, scale=scale[:, r, t : t + 1])
+        def turn(dst, src, start, stop, plain):
+            nc.tensor.matmul(dst, src, ident[:], start=start, stop=stop, is_transpose=not plain)
 
-        def phi_group(r, engine):
-            src = phi_wide[r][:].rearrange("p t (g k) -> p g t k", g=G)
+        def warm(m, width):
+            nc.tensor.matmul(value("warm")[:, 0:width], ident[:], spread(ident[:], 1, width), start=True, stop=True)
+
+        def phi_widen(r, engine, lo, hi):
+            for t in range(lo, hi):
+                src = phi_raw[r][:, t, :].bitcast(FP8)
+                if engine == "vector":
+                    nc.vector.tensor_scalar(value("wide", r)[:, t, :], src, scale[:, r, t : t + 1], None, op0=ALU.mult)
+                else:
+                    nc.scalar.activation(value("wide", r)[:, t, :], src, ACT.Copy, scale=scale[:, r, t : t + 1])
+
+        def phi_group(r, logits, engine):
+            lo, hi = (GATES, KC) if logits else (0, GATES)
+            dst = value("logit_words", r // 2)[:, r % 2] if logits else value("gate_words")[:, r]
+            src = value("wide", r)[:].rearrange("p t (g k) -> p g t k", g=G)[:, :, :, lo:hi]
             copy = nc.vector.tensor_copy if engine == "vector" else nc.scalar.copy
-            for lo, hi, col in ((0, GATES, 0), (GATES, KC, P)):
-                copy(
-                    out=phi_words[r][:, col : col + G * (hi - lo), :].rearrange("p (g a i) t -> p g a t i", g=G, i=4),
-                    in_=src[:, :, :, lo:hi].rearrange("p g t (a i) -> p g a t i", i=4),
-                )
+            copy(out=dst.rearrange("p (g a i) t -> p g a t i", g=G, i=4), in_=src.rearrange("p g t (a i) -> p g a t i", i=4))
 
-        def phi_quant(r):
+        def gate_quant():
             nc.vector.quantize_mx(
-                out=phi_codes[:, r, :].bitcast(FP8X4),
-                scales=phi_scales[:, r, :],
-                in_=phi_words[r][:].rearrange("p n t -> p (n t)"),
+                out=gate_codes[:].rearrange("p r n -> p (r n)").bitcast(FP8X4),
+                scales=gate_scales[:].rearrange("p r n -> p (r n)"),
+                in_=value("gate_words")[:].rearrange("p r n t -> p (r n t)"),
+            )
+
+        def logit_quant(h):
+            nc.vector.quantize_mx(
+                out=logit_codes[:, 2 * h : 2 * h + 2].rearrange("p r n -> p (r n)").bitcast(FP8X4),
+                scales=logit_scales[:, 2 * h : 2 * h + 2].rearrange("p r n -> p (r n)"),
+                in_=value("logit_words", h)[:].rearrange("p r n t -> p (r n t)"),
             )
 
         def bias_turn():
-            once["bias"] = ps.tile([P, MT, 2], F32, name="uh")
             for m in range(MT):
-                nc.tensor.matmul(once["bias"][:, m, :], bm_row[:, m * P : (m + 1) * P], ones[:], start=True, stop=True)
+                nc.tensor.matmul(value("bias_ps")[:, m, :], bm_row[:, m * P : (m + 1) * P], ones[:], start=True, stop=True)
 
         def bias_read():
-            nc.scalar.copy(out=bias[:], in_=once["bias"][:, :, 0])
-            nc.scalar.activation(half_bias[:], once["bias"][:, 0, 0:1], ACT.Copy, scale=0.5)
+            nc.scalar.copy(out=bias[:], in_=value("bias_ps")[:, :, 0])
+            nc.scalar.activation(half_bias[:], value("bias_ps")[:, 0, 0:1], ACT.Copy, scale=0.5)
 
-        def w_group(half):
+        def w_group(half, engine):
             cols = slice(half * D // 2, (half + 1) * D // 2)
-            copy = nc.vector.tensor_copy if half else nc.scalar.copy
+            copy = nc.vector.tensor_copy if engine == "vector" else nc.scalar.copy
             copy(
-                out=w_words[:, cols, :].rearrange("p (c i) t -> p c t i", i=4),
+                out=value("w_words")[:, cols, :].rearrange("p (c i) t -> p c t i", i=4),
                 in_=w_raw[:, :, cols].rearrange("p t (c i) -> p c t i", i=4),
             )
 
         def gf_half():
             nc.scalar.activation(half_gf[:], gf_k[:], ACT.Copy, scale=0.5)
 
-        def w_quant(half):
-            cols = slice(half * D // 2, (half + 1) * D // 2)
-            nc.vector.quantize_mx(
-                out=w_codes[:, cols].bitcast(FP8X4),
-                scales=w_scales[:, cols],
-                in_=w_words[:, cols, :].rearrange("p n t -> p (n t)"),
-            )
-
-
-        state = [dict() for n in range(NT)]
-
-        def add_turned(dst, src, start, stop, plain):
-            nc.tensor.matmul(dst, src, ident[:], start=start, stop=stop, is_transpose=not plain)
+        def w_quant():
+            nc.vector.quantize_mx(out=w_codes[:].bitcast(FP8X4), scales=w_scales[:], in_=value("w_words")[:].rearrange("p n t -> p (n t)"))
 
         def x_turn(n, pair):
             words = xs[n][:].bitcast(F32)
-            xp = ps.tile([P, 2, 2, P], F32, name="xp", bufs=2)
             for rr in range(2):
                 r = 2 * pair + rr
                 for u in range(2):
-                    nc.tensor.transpose(xp[:, rr, u, :], words[:, 256 * r + u : 256 * (r + 1) : 2], ident[:])
-            state[n]["xp", pair] = xp
+                    nc.tensor.transpose(value("xp", n, pair)[:, u, rr, :], words[:, 256 * r + u : 256 * (r + 1) : 2], ident[:])
 
         def x_gain(n, pair):
-            st = state[n]
-            if pair == 0:
-                st["xn"] = sb.tile([P, R, P, T], BF16, name="xn", bufs=XN_BUFS, align_bytes=64)
-            for rr in range(2):
-                r = 2 * pair + rr
-                turned = st["xp", pair][:, rr, :, :].rearrange("p u s -> p (u s)").bitcast(BF16)
-                nc.vector.tensor_tensor(
-                    out=st["xn"][:, r, :, :].rearrange("p s (u e) -> p s u e", e=2),
-                    in0=turned.rearrange("p (u s e) -> p s u e", u=2, e=2),
-                    in1=spread(gn_k[:, r, :].rearrange("p (u e) -> p u e", e=2), 1, P),
-                    op=ALU.mult,
-                )
-
-        def x_quant(n):
-            st = state[n]
-            st["x_codes"] = sb.tile([P, R, P], U32, name="xqc", bufs=3, align_bytes=64)
-            st["x_scales"] = sb.tile([P, R, P], U8, name="xqs", bufs=3, align_bytes=64)
-            nc.vector.quantize_mx(
-                out=st["x_codes"][:].rearrange("p r s -> p (r s)").bitcast(FP8X4),
-                scales=st["x_scales"][:].rearrange("p r s -> p (r s)"),
-                in_=st["xn"][:].rearrange("p r s t -> p (r s t)"),
-            )
-
-        def coef_mm(n, bank, lo, hi):
-            st = state[n]
-            if lo == 0:
-                st["tt"] = ps.tile([P, MT, P], F32, name=bank, bufs=BANKS[bank])
-            for r in range(lo, hi):
-                for m in range(MT):
-                    nc.tensor.matmul_mx(
-                        out=st["tt"][:, m, :],
-                        lhsT=phi_codes[:, r, m * P : (m + 1) * P].bitcast(FP8X4),
-                        lhsT_scale=phi_scales[:, r, m * P : (m + 1) * P],
-                        rhs=st["x_codes"][:, r, :].bitcast(FP8X4),
-                        rhs_scale=st["x_scales"][:, r, :],
-                        start=(r == 0 and m == 0),
-                        stop=(r == R - 1 and m == MT - 1),
-                    )
-
-        def coef_act(n):
-            st = state[n]
-            tt = st["tt"]
-            st["co"] = sb.tile([P, MT, P], F32, name="co", bufs=CO_BUFS)
-            th = sb.tile([P, P], F32, name="th")
-            nc.scalar.activation(st["co"][:, 1, :], tt[:, 1, :], ACT.Exp, bias=bias[:, 1:2])
-            nc.scalar.activation(th[:], tt[:, 0, :], ACT.Tanh, bias=half_bias[:], scale=0.5)
-            nc.scalar.activation(st["co"][:, 2, :], tt[:, 2, :], ACT.Exp, bias=bias[:, 2:3])
-            nc.scalar.activation(st["co"][:, 0, :], th[:], ACT.Identity, bias=1.0)
-
-        def coef_turn(n):
-            st = state[n]
-            bank = "tt" if n in THIRD_TURNS else "ct"
-            ct = ps.tile([P, MT, P], F32, name=bank, bufs=BANKS[bank])
-            for m in (1, 2, 0):
-                nc.tensor.transpose(ct[:, m, :], st["co"][:, m, :], ident[:])
-            st["e"] = ct[:, 1:MT, :].rearrange("p m (g i j) -> p (m g) i j", i=R, j=R)
-            st["q_psum"] = ct[:, 1:MT, :].rearrange("p m (g j i) -> p (m g) j i", i=R, j=R)
-            st["gate"] = ct[:, 0, :].rearrange("p (g k) -> p g k", g=G)
-
-
-        def sink_sum(n, step, lo, hi):
-            st = state[n]
-            sums = sb.tile([P, hi - lo, R], F32, name="sums", bufs=4)
-            nc.vector.tensor_reduce(sums[:], st.get(("scaled", lo), st["e"][:, lo:hi]), axis=AX.X, op=ALU.add)
-            st["sums", lo] = sums
-
-        def sink_inv_vector(n, step, lo, hi):
-            st = state[n]
-            st["factor", lo] = sb.tile([P, hi - lo, R], F32, name="factor", bufs=4)
-            nc.vector.reciprocal(st["factor", lo][:], st["sums", lo][:])
-
-        def sink_root(n, step, lo, hi):
-            st = state[n]
-            st["root", lo] = sb.tile([P, hi - lo, R], F32, name="root")
-            nc.scalar.activation(st["root", lo][:], st["sums", lo][:], ACT.Abs_reciprocal_sqrt)
-
-        def sink_inv_scalar(n, step, lo, hi):
-            st = state[n]
-            st["factor", lo] = sb.tile([P, hi - lo, R], F32, name="factor", bufs=4)
-            nc.scalar.activation(st["factor", lo][:], st["root", lo][:], ACT.Square)
-
-        def sink_scale(n, step, lo, hi):
-            st = state[n]
-            scaled = sb.tile([P, hi - lo, R, R], F32, name="scaled", bufs=4)
-            e = st["e"][:, lo:hi]
-            if step % 2 == 0:
-                e = e.rearrange("p g i j -> p g j i")
-            nc.vector.tensor_tensor(out=scaled[:], in0=e, in1=spread(st["factor", lo][:], 2, R), op=ALU.mult)
-            st["scaled", lo] = scaled[:]
-
-        def sink_last(n, lo, hi):
-            st = state[n]
-            if "q" not in st:
-                st["q"] = sb.tile([P, G, R, R], F32, name="q")
+            b, m = xb_of[n]
+            turned = value("xp", n, pair)[:].rearrange("p u r s -> p (u r s)").bitcast(BF16)
+            dst = value("xn", b)[:, 2 * pair : 2 * pair + 2, m * P : (m + 1) * P, :]
             nc.vector.tensor_tensor(
-                out=st["q"][:, lo:hi], in0=st["scaled", lo], in1=spread(st["factor", lo][:], 3, R), op=ALU.mult
-            )
-
-        def q_to_psum(n, lo, hi):
-            st = state[n]
-            nc.tensor.matmul(st["q_psum"][:, lo:hi], ident[:], st["q"][:, lo:hi], start=True, stop=True)
-
-
-        def pre_prod(n, r, multiply, gate):
-            st = state[n]
-            st["pu", r] = sb.tile([P, T, P], F32, name="pu", bufs=8)
-            multiply(
-                out=st["pu", r][:].rearrange("p t (g c) -> p t g c", g=G),
-                in0=xs[n][:, r * D : (r + 1) * D].rearrange("p (g c t) -> p t g c", g=G, t=T),
-                in1=spread(spread(gate[:, :, r], 2, C // T), 1, T),
+                out=dst.rearrange("p r s (u e) -> p r s u e", e=2),
+                in0=turned.rearrange("p (u r s e) -> p r s u e", u=2, r=2, e=2),
+                in1=spread(gn_k[:, 2 * pair : 2 * pair + 2, :].rearrange("p r (u e) -> p r u e", e=2), 2, P),
                 op=ALU.mult,
             )
 
-        def pre_prod_vector(n, r):
-            pre_prod(n, r, nc.vector.tensor_tensor, state[n]["gate"])
-
-        def pre_prod_gpsimd(n, r):
-            pre_prod(n, r, nc.gpsimd.tensor_tensor, state[n]["gate_sb"])
-
-        def gate_copy(n):
-            st = state[n]
-            st["gate_sb"] = sb.tile([P, G, GATES], F32, name="gate")
-            copy = nc.scalar.copy if n else nc.vector.tensor_copy
-            copy(out=st["gate_sb"][:], in_=st["gate"])
-
-        def post_copy(n):
-            st = state[n]
-            st["gate_sb"] = sb.tile([P, G, GATES], F32, name="gate")
-            nc.scalar.copy(out=st["gate_sb"][:, :, R:GATES], in_=st["gate"][:, :, R:GATES])
-
-        def pre_prod_scalar(n, r):
-            st = state[n]
-            st["pu", r] = sb.tile([P, T, P], F32, name="pu", bufs=8)
-            src = xs[n][:, r * D : (r + 1) * D].rearrange("p (g c t) -> p g t c", g=G, t=T)
-            dst = st["pu", r][:].rearrange("p t (g c) -> p g t c", g=G)
-            for g in range(G):
-                nc.scalar.activation(dst[:, g], src[:, g], ACT.Copy, scale=st["gate_sb"][:, g, r : r + 1])
-
-        def u_sum(n, plain, streams, start, stop):
-            st = state[n]
-            if start:
-                st["ut"] = ps.tile([P, T, P], F32, name="uh")
-            passes = [(r, t) for r in streams for t in range(T)]
-            for m, (r, t) in enumerate(passes):
-                first_pass, last_pass = start and m == 0, stop and m == len(passes) - 1
-                add_turned(st["ut"][:, t, :], st["pu", r][:, t, :], first_pass, last_pass, m < plain[0] or m >= len(passes) - plain[1])
-
-        def u_gain(n):
-            st = state[n]
-            st["ug"] = sb.tile([P, P, T], BF16, name="ug", align_bytes=64)
-            nc.vector.tensor_tensor(
-                out=st["ug"][:], in0=st["ut"][:].rearrange("p t s -> p s t"), in1=spread(half_gf[:], 1, P), op=ALU.mult
+        def x_quant(b):
+            nc.vector.quantize_mx(
+                out=value("xc", b)[:].rearrange("p r s -> p (r s)").bitcast(FP8X4),
+                scales=value("xs", b)[:].rearrange("p r s -> p (r s)"),
+                in_=value("xn", b)[:].rearrange("p r s t -> p (r s t)"),
             )
 
-        def u_quant(n):
-            st = state[n]
-            st["u_codes"] = sb.tile([P, P], U32, name="ugc", align_bytes=64)
-            st["u_scales"] = sb.tile([P, P], U8, name="ugs", align_bytes=64)
+        def coef_pass(b, dst, codes, scales, r, start, stop):
+            nc.tensor.matmul_mx(
+                out=dst,
+                lhsT=codes.bitcast(FP8X4),
+                lhsT_scale=scales,
+                rhs=value("xc", b)[:, r, :].bitcast(FP8X4),
+                rhs_scale=value("xs", b)[:, r, :],
+                start=start,
+                stop=stop,
+            )
+
+        def gate_mm(b):
+            for r in range(R):
+                coef_pass(b, value("tg", b)[:], gate_codes[:, r, :], gate_scales[:, r, :], r, r == 0, r == R - 1)
+
+        def logit_mm(b, lo, hi):
+            for r in range(lo, hi):
+                for m in range(2):
+                    cols = slice(m * P, (m + 1) * P)
+                    first, last = r == 0 and m == 0, r == R - 1 and m == 1
+                    coef_pass(b, value("tl", b)[:, m, :], logit_codes[:, r, cols], logit_scales[:, r, cols], r, first, last)
+
+        def gate_tanh(b):
+            nc.scalar.activation(value("th", b)[:], value("tg", b)[:], ACT.Tanh, bias=half_bias[:], scale=0.5)
+
+        def gate_one(b):
+            nc.scalar.activation(value("th1", b)[:], value("th", b)[:], ACT.Identity, bias=1.0)
+
+        def gate_turn(b, plain):
+            lo, hi = X_BATCHES[b]
+            for m in range(hi - lo):
+                cols = slice(m * P, (m + 1) * P)
+                turn(value("gt", b)[:, cols], value("th1" if b == OWN_GATES else "th", b)[:, cols], True, True, plain)
+
+        def gate_copy(b, engine):
+            dst = value("gate", b)[:].rearrange("p (m k g) -> p m k g", k=GATES, g=G)
+            src = value("gt", b)[:].rearrange("p (m g k) -> p m k g", k=GATES, g=G)
+            if b == OWN_GATES:
+                nc.vector.tensor_copy(out=dst, in_=src)
+            elif engine == "vector":
+                nc.vector.tensor_scalar(dst, src, 1.0, None, op0=ALU.add)
+            else:
+                nc.scalar.activation(dst, src, ACT.Identity, bias=1.0)
+
+        def gates_of(n, engine):
+            b, m = xb_of[n]
+            if engine == "vector":
+                return value("gt", b)[:, m * P : (m + 1) * P].rearrange("p (g k) -> p k g", k=GATES)
+            return value("gate", b)[:, m * P : (m + 1) * P].rearrange("p (k g) -> p k g", k=GATES)
+
+        def logit_exp(b):
+            for m in range(2):
+                nc.scalar.activation(value("co", b)[:, m, :], value("tl", b)[:, m, :], ACT.Exp, bias=bias[:, 1 + m : 2 + m])
+
+        def e_turn(n, plain):
+            b, k = xb_of[n]
+            for m in range(2):
+                turn(value("ct", n)[:, m * P : (m + 1) * P], value("co", b)[:, m, k * P : (k + 1) * P], True, True, m >= 2 - plain)
+
+        def e_of(n):
+            return value("ct", n)[:].rearrange("p (g i j) -> p g i j", i=R, j=R)
+
+        def sink_sum(n, step):
+            src = value("scaled", n, step - 1)[:] if step else e_of(n)
+            nc.vector.tensor_reduce(value("sums", n, step)[:], src, axis=AX.X, op=ALU.add)
+
+        def sink_root(n, step):
+            nc.scalar.activation(value("root", n, step)[:], value("sums", n, step)[:], ACT.Abs_reciprocal_sqrt)
+
+        def sink_inv(n, step):
+            nc.scalar.activation(value("factor", n, step)[:], value("root", n, step)[:], ACT.Square)
+
+        def sink_recip(n, step):
+            nc.vector.reciprocal(value("factor", n, step)[:], value("sums", n, step)[:])
+
+        def sink_scale(n, step):
+            e = e_of(n).rearrange("p g i j -> p g j i") if step % 2 == 0 else e_of(n)
+            factor = spread(value("factor", n, step)[:], 2, R)
+            nc.vector.tensor_tensor(out=value("scaled", n, step)[:], in0=e, in1=factor, op=ALU.mult)
+
+        def sink_last(n):
+            nc.gpsimd.tensor_tensor(
+                out=value("q", n)[:].rearrange("p j g i -> p g j i"),
+                in0=value("scaled", n, 2)[:],
+                in1=spread(value("factor", n, 3)[:], 3, R),
+                op=ALU.mult,
+            )
+
+        def q_to_psum(n, lo, hi):
+            q = value("q", n)[:].rearrange("p j g i -> p (j g i)")
+            cols = slice(lo * R, hi * R)
+            nc.tensor.matmul(value("qp", n)[:, cols], ident[:], q[:, cols], start=True, stop=True)
+
+        def pre_prod(n, pair, lo, hi, engine):
+            src = xs[n][:, 2 * pair * D : (2 * pair + 2) * D].rearrange("p (a c t) -> p t a c", a=2 * G, t=T)
+            dst = value("pu", n, pair)[:].rearrange("p t r (g c) -> p t (r g) c", g=G)
+            gate = gates_of(n, engine)[:, 2 * pair : 2 * pair + 2, :]
+            if engine == "gpsimd":
+                weights = spread(spread(gate.rearrange("p r g -> p (r g)")[:, lo:hi], 2, C // T), 1, T)
+                nc.gpsimd.tensor_tensor(out=dst[:, :, lo:hi], in0=src[:, :, lo:hi], in1=weights, op=ALU.mult)
+            elif engine == "vector":
+                weights = spread(spread(gate[:, lo // G, :], 2, C // T), 1, T)
+                nc.vector.tensor_tensor(out=dst[:, :, lo:hi], in0=src[:, :, lo:hi], in1=weights, op=ALU.mult)
+            else:
+                for a in range(lo, hi):
+                    nc.scalar.activation(dst[:, :, a], src[:, :, a], ACT.Copy, scale=gate[:, a // G, a % G : a % G + 1])
+
+        def u_sum(n, plain):
+            for r in range(R):
+                for t in range(T):
+                    first, last = r == 0 and t == 0, r == R - 1 and t == T - 1
+                    src = value("pu", n, r // 2)[:, t, r % 2, :]
+                    turn(value("ut", n)[:, t, :], src, first, last, T * r + t < plain[0] or T * r + t >= R * T - plain[1])
+
+        def u_gain(n):
+            nc.vector.tensor_tensor(
+                out=u_words[batch_of[n][0]][:, batch_of[n][1]],
+                in0=value("ut", n)[:].rearrange("p t s -> p s t"),
+                in1=spread(half_gf[:], 1, P),
+                op=ALU.mult,
+            )
+
+        def u_quant(b):
             nc.vector.quantize_mx(
-                out=st["u_codes"][:].bitcast(FP8X4), scales=st["u_scales"][:], in_=st["ug"][:].rearrange("p s t -> p (s t)")
+                out=u_codes[b][:].rearrange("p n s -> p (n s)").bitcast(FP8X4),
+                scales=u_scales[b][:].rearrange("p n s -> p (n s)"),
+                in_=u_words[b][:].rearrange("p n s t -> p (n s t)"),
             )
 
         def branch_mm(n):
-            st = state[n]
-            st["h"] = ps.tile([P, D], F32, name="uh")
             nc.tensor.matmul_mx(
-                out=st["h"][:],
-                lhsT=st["u_codes"][:].bitcast(FP8X4),
-                lhsT_scale=st["u_scales"][:],
+                out=value("h", n)[:],
+                lhsT=u_codes[batch_of[n][0]][:, batch_of[n][1]].bitcast(FP8X4),
+                lhsT_scale=u_scales[batch_of[n][0]][:, batch_of[n][1]],
                 rhs=w_codes[:].bitcast(FP8X4),
                 rhs_scale=w_scales[:],
                 start=True,
@@ -352,363 +402,253 @@ def tile_groupedmanifoldhyperconnection_kernel(tc, x, gn, phi_bytes, phi_scale, 
             )
 
         def branch_relu(n):
-            st = state[n]
-            st["hr"] = sb.tile([P, D], F32, name="hr")
-            nc.scalar.activation(st["hr"][:], st["h"][:], ACT.Relu)
+            nc.scalar.activation(value("hr", n)[:], value("h", n)[:], ACT.Relu)
 
         def branch_square(n):
-            st = state[n]
-            st["f"] = sb.tile([P, D], F32, name="f")
-            nc.scalar.activation(st["f"][:], st["hr"][:], ACT.Square)
-
+            nc.scalar.activation(value("f", n)[:], value("hr", n)[:], ACT.Square)
 
         def term(n, j, lo, hi):
-            st = state[n]
-            if ("prod", j) not in st:
-                st["prod", j] = sb.tile([P, G, R, C], F32, name="prod%d" % j)
-            src = xs[n][:, j * D : (j + 1) * D] if j < R else st["f"][:]
-            return st["prod", j][:, lo:hi], src.rearrange("p (g c) -> p g c", g=G)[:, lo:hi]
+            return value("prod", n, j, lo // HALF)[:, lo % HALF : lo % HALF + hi - lo]
 
-        def prod_scalar(n, j, lo, hi):
-            st = state[n]
-            dst, src = term(n, j, lo, hi)
-            weight = st["q"][:, lo:hi, j, :] if j < R else st["gate_sb"][:, lo:hi, R:GATES]
-            for g in range(hi - lo):
-                for i in range(R):
-                    nc.scalar.activation(dst[:, g, i, :], src[:, g, :], ACT.Copy, scale=weight[:, g, i : i + 1])
+        def product(n, j, lo, hi, engine):
+            src = xs[n][:, j * D : (j + 1) * D] if j < R else value("f", n)[:]
+            src = src.rearrange("p (g c) -> p g c", g=G)[:, lo:hi]
+            dst = term(n, j, lo, hi)
+            if engine == "vector":
+                weight = value("qp", n)[:].rearrange("p (j g i) -> p j g i", j=R, i=R)[:, j, lo:hi, :]
+            elif j < R:
+                weight = value("q", n)[:, j, lo:hi, :]
+            else:
+                weight = gates_of(n, engine)[:, R:GATES, lo:hi].rearrange("p i g -> p g i")
+            if engine == "scalar":
+                for g in range(hi - lo):
+                    for i in range(R):
+                        nc.scalar.activation(dst[:, g, i, :], src[:, g, :], ACT.Copy, scale=weight[:, g, i : i + 1])
+            else:
+                multiply = nc.vector.tensor_tensor if engine == "vector" else nc.gpsimd.tensor_tensor
+                multiply(out=dst, in0=spread(src, 2, R), in1=spread(weight, 3, C), op=ALU.mult)
 
-        def prod_gpsimd(n, j, lo, hi):
-            dst, src = term(n, j, lo, hi)
-            weight = state[n]["q"][:, lo:hi, j, :] if j < R else state[n]["gate_sb"][:, lo:hi, R:GATES]
-            nc.gpsimd.tensor_tensor(out=dst, in0=spread(src, 2, R), in1=spread(weight, 3, C), op=ALU.mult)
-
-        def prod_vector(n, j, lo, hi):
-            st = state[n]
-            dst, src = term(n, j, lo, hi)
-            weight = st["q_psum"][:, lo:hi, j, :] if j < R else st["gate"][:, lo:hi, R:GATES]
-            nc.vector.tensor_tensor(out=dst, in0=spread(src, 2, R), in1=spread(weight, 3, C), op=ALU.mult)
-
-        def y_sum(n, a, bank, lo, hi, plain):
-            st = state[n]
-            if lo == 0:
-                st["yt", a] = ps.tile([P, TB, QUAD, C], F32, name=bank, bufs=BANKS[bank])
-            for m in range(lo, hi):
+        def y_sum(n, a, order, plain):
+            for m, j in enumerate(order):
                 for b in range(QUAD):
                     g = QUAD - 1 - b
-                    src = st["prod", TERMS[m]][:, QUAD * a + g].rearrange("p i c -> p (i c)")
-                    first_pass, last_pass = m == 0 and b == 0, m == BRANCH and b == QUAD - 1
-                    add_turned(st["yt", a][:, :, g, :], src, first_pass, last_pass, (m == 0 and b < plain[0]) or (m == BRANCH and b >= QUAD - plain[1]))
+                    src = term(n, j, QUAD * a, QUAD * (a + 1))[:, g].rearrange("p i c -> p (i c)")
+                    first, last = m == 0 and b == 0, m == BRANCH and b == QUAD - 1
+                    turn(value("yt", n, a)[:, :, g, :], src, first, last, QUAD * m + b < plain[0] or QUAD * m + b >= QUAD * (BRANCH + 1) - plain[1])
 
         def y_out(n, a):
-            yo = sb.tile([P, D], F32, name="yo", bufs=5, align_bytes=64)
-            nc.vector.transpose(yo[:], state[n]["yt", a][:].rearrange("p tb b t -> p (tb b t)"))
+            yo = value("yo", n, a)
+            nc.vector.transpose(yo[:], value("yt", n, a)[:].rearrange("p tb b t -> p (tb b t)"))
             for i in range(R):
                 nc.sync.dma_start(
                     out=out_view[n, i, a], in_=yo[C * i : C * (i + 1), :].rearrange("p (tb c) -> p tb c", tb=TB)
                 )
 
-        def y_add(n, a, into, other, engine):
-            lo, hi = quad(a)
-            dst = state[n]["prod", into][:, lo:hi].rearrange("p g i c -> p (g i c)")
-            src = state[n]["prod", other][:, lo:hi].rearrange("p g i c -> p (g i c)")
-            add = nc.vector.tensor_tensor if engine == "vector" else nc.gpsimd.tensor_tensor
-            add(out=dst, in0=dst, in1=src, op=ALU.add)
+        def y_add(n, a, into, other):
+            dst = term(n, into, QUAD * a, QUAD * (a + 1)).rearrange("p g i c -> p (g i c)")
+            src = term(n, other, QUAD * a, QUAD * (a + 1)).rearrange("p g i c -> p (g i c)")
+            nc.gpsimd.tensor_tensor(out=dst, in0=dst, in1=src, op=ALU.add)
 
         def y_add_out(n, a, one, other):
-            lo, hi = quad(a)
-            yo = sb.tile([P, R, QUAD, C], F32, name="yo", bufs=5, align_bytes=64)
-            nc.vector.tensor_tensor(
-                out=yo[:],
-                in0=state[n]["prod", one][:, lo:hi].rearrange("p g i c -> p i g c"),
-                in1=state[n]["prod", other][:, lo:hi].rearrange("p g i c -> p i g c"),
+            yo = value("yo", n, a)[:].rearrange("p (i g c) -> p i g c", i=R, g=QUAD)
+            nc.gpsimd.tensor_tensor(
+                out=yo,
+                in0=term(n, one, QUAD * a, QUAD * (a + 1)).rearrange("p g i c -> p i g c"),
+                in1=term(n, other, QUAD * a, QUAD * (a + 1)).rearrange("p g i c -> p i g c"),
                 op=ALU.add,
             )
-            nc.sync.dma_start(out=out_rows[n * P : (n + 1) * P, :, a, :], in_=yo[:].rearrange("p i b c -> p i (b c)"))
 
-        low, high, every = (0, HALF), (HALF, G), (0, G)
+        def y_store(n, a):
+            yo = value("yo", n, a)[:].rearrange("p (i c) -> p i c", i=R)
+            nc.sync.dma_start(out=out_rows[n * P : (n + 1) * P, :, a, :], in_=yo)
+
+        def parts(n, terms, quad):
+            return [("part", n, j, quad) for j in terms] + [("held", "prod", n, j, quad // 2) for j in terms]
+
+        def uses(fn, n=0, *a):
+            xb = xb_of[n][0]
+            table = {
+                warm: lambda: ([], [("warm",)]),
+                phi_widen: lambda: ([], [("wide", n)]),
+                phi_group: lambda: ([("wide", n)], [("logit_words", n // 2) if a[0] else ("gate_words",)]),
+                gate_quant: lambda: ([("gate_words",)], [("gate_codes",)]),
+                logit_quant: lambda: ([("logit_words", n)], [("logit_codes", n)]),
+                bias_turn: lambda: ([], [("bias_ps",)]),
+                bias_read: lambda: ([("bias_ps",)], [("bias",)]),
+                w_group: lambda: ([], [("w_words",)]),
+                gf_half: lambda: ([], [("half_gf",)]),
+                w_quant: lambda: ([("w_words",)], [("w_codes",)]),
+                x_turn: lambda: ([], [("xp", n, a[0])]),
+                x_gain: lambda: ([("xp", n, a[0])], [("xn", xb)]),
+                x_quant: lambda: ([("xn", n)], [("xc", n), ("xs", n)]),
+                gate_mm: lambda: ([("xc", n), ("xs", n), ("gate_codes",)], [("tg", n)]),
+                logit_mm: lambda: ([("xc", n), ("xs", n)] + [("logit_codes", r // 2) for r in range(*a)], [("tl", n)]),
+                gate_tanh: lambda: ([("tg", n), ("bias",)], [("th", n)]),
+                gate_one: lambda: ([("th", n)], [("th1", n)]),
+                gate_turn: lambda: ([("th1" if n == OWN_GATES else "th", n)], [("gt", n)]),
+                gate_copy: lambda: ([("gt", n)], [("gate", n)]),
+                logit_exp: lambda: ([("tl", n), ("bias",)], [("co", n)]),
+                e_turn: lambda: ([("co", xb)], [("ct", n)]),
+                sink_sum: lambda: ([("scaled", n, a[0] - 1) if a[0] else ("ct", n)], [("sums", n, a[0])]),
+                sink_root: lambda: ([("sums", n, a[0])], [("root", n, a[0])]),
+                sink_inv: lambda: ([("root", n, a[0])], [("factor", n, a[0])]),
+                sink_recip: lambda: ([("sums", n, a[0])], [("factor", n, a[0])]),
+                sink_scale: lambda: ([("ct", n), ("factor", n, a[0])], [("scaled", n, a[0])]),
+                sink_last: lambda: ([("scaled", n, 2), ("factor", n, 3)], [("q", n)]),
+                q_to_psum: lambda: ([("q", n)], [("qp", n)]),
+                pre_prod: lambda: ([("gt" if a[3] == "vector" else "gate", xb)], [("pu", n, a[0])]),
+                u_sum: lambda: ([("pu", n, pair) for pair in range(2)], [("ut", n)]),
+                u_gain: lambda: ([("ut", n), ("half_gf",)], [("u_words", batch_of[n][0])]),
+                u_quant: lambda: ([("u_words", n)], [("u_codes", n)]),
+                branch_mm: lambda: ([("u_codes", batch_of[n][0]), ("w_codes",)], [("h", n)]),
+                branch_relu: lambda: ([("h", n)], [("hr", n)]),
+                branch_square: lambda: ([("hr", n)], [("f", n)]),
+                product: lambda: (
+                    [("f", n), ("gate", xb)] if a[0] == BRANCH else [("qp", n)] if a[3] == "vector" else [("q", n)],
+                    [("prod", n, a[0], a[1] // HALF)] + [("part", n, a[0], quad) for quad in range(a[1] // QUAD, (a[2] - 1) // QUAD + 1)],
+                ),
+                y_sum: lambda: (parts(n, range(BRANCH + 1), a[0]), [("yt", n, a[0])]),
+                y_add: lambda: (parts(n, a[1:3], a[0]), [("added", n, a[0])]),
+                y_add_out: lambda: (parts(n, a[1:3], a[0]) + [("added", n, a[0])], [("yo", n, a[0])]),
+                y_store: lambda: ([("yo", n, a[0])], []),
+                y_out: lambda: ([("yt", n, a[0])], [("yo", n, a[0])]),
+            }
+            return table[fn]()
+
+        V, S, GP = "vector", "scalar", "gpsimd"
         tensor, vector, scalar, gpsimd = [], [], [], []
+        ORDER = (2, 3, BRANCH, 0, 1)
 
-        def chain(n, fill, own_inverses, parts=(every,)):
-            out = []
-            for step in range(4):
-                out.extend((sink_sum, n, step) + part for part in parts)
-                out.extend(fill[2 * step])
-                if step in own_inverses:
-                    out.extend((sink_inv_vector, n, step) + part for part in parts)
-                    out.extend(fill[2 * step + 1][:1])
-                if step < 3:
-                    out.extend((sink_scale, n, step) + part for part in parts)
-                out.extend(fill[2 * step + 1][1 if step in own_inverses else 0 :])
-            return out
+        def turns(*ns):
+            return [(x_turn, n, pair) for n in ns for pair in range(2)]
 
-        def gains(n, *streams):
-            return [(x_gain, n, r) for r in streams]
+        def gains(*ns):
+            return [(x_gain, n, pair) for n in ns for pair in range(2)]
 
-        def pres(n, *streams):
-            return [(pre_prod_vector, n, r) for r in streams]
+        def pre_g(n, pair, lo=0, hi=2 * G):
+            return (pre_prod, n, pair, lo, hi, GP)
 
-        def vq(n, j, a):
-            return (prod_vector, n, j) + quad(a)
+        def pre_v(n, pair, r):
+            return (pre_prod, n, pair, r * G, (r + 1) * G, V)
 
-        def sq(n, j, a):
-            return [(prod_scalar, n, j, g, g + 1) for g in range(*quad(a))]
-
-        def deal(work, *marks):
-            out = []
-            for m, entry in enumerate(work + [None]):
-                out.extend(step for place, step in marks if min(place, len(work)) == m)
-                out.extend([entry] if entry else [])
-            return out
-
-        def inv(n, step, place, parts=(every,)):
-            return [(place, (sink_root, n, step) + part) for part in parts] + [(place + 1, (sink_inv_scalar, n, step) + part) for part in parts]
-
-        def relu(n, place):
-            return [(place, (branch_relu, n)), (place + 1, (branch_square, n))]
-
-        def g_halves(n):
-            return [(prod_gpsimd, n, 0) + low, (prod_gpsimd, n, 1) + low, (prod_gpsimd, n, 0) + high, (prod_gpsimd, n, 1) + high]
-
-        def gq(n, j, a):
-            return (prod_gpsimd, n, j) + quad(a)
-
-        def br(k, *quads):
-            return [vq(k, BRANCH, a) for a in quads]
-
-        def mm(n, bank):
-            return (coef_mm, n, bank, 0, R)
-
-        def turns(n):
-            return [(x_turn, n, 0), (x_turn, n, 1)]
-
-        def terms(k, *pairs):
-            return [s for j, a in pairs for s in sq(k, j, a)]
-
-        both = [(j, a) for a in range(NQ) for j in (2, 3)]
-
-
-        U1 = (3, 0)
-        V1 = 16
-        G1 = 9
-        U0 = (0, 0)
-        UK = (0, 0)
-        UORD = (3, 2, 1, 0)
-        PRE1 = 4
-        XP_FROM = 7
-        G2 = 12
-        V3 = 15
-        G3 = 15
-        MARK = (1, 3, 5, 13, 21)
-        QP = (2, 3, 4, 5, 6)
-        V2 = 8
-        M2 = (0, 8)
-        A7 = 5
-        OWN3 = (0, 1)
-        PAIR = {0: (2, 0)}
-        CUT = 2
-
-        halves = (low, high)
-        own = (0, 1, 2, 3)
-        vector += [(phi_widen_vector, 0, t) for t in range(T)] + [(phi_group, 0, "vector"), (phi_quant, 0), (phi_group, 1, "vector")]
-        vector += gains(0, 0) + [(phi_quant, 1)] + gains(0, 1) + [(phi_group, 2, "vector"), (x_quant, 0), (phi_quant, 2)]
-        vector += gains(1, 0) + [(phi_quant, 3)] + gains(1, 1)
-        vector += [(w_group, 1), (x_quant, 1), (w_quant, 0), (w_quant, 1), (gate_copy, 0)]
-        vector += chain(0, [gains(2, 0), [], gains(2, 1), [], [(x_quant, 2)], [], [(u_gain, 0)], []], own, halves)
-        vector += [(sink_last, 0) + high, (sink_last, 0) + low, (u_quant, 0)]
-        scalar += [(phi_widen_scalar, r, t) for r in (1, 2, 3) for t in range(T)]
-        scalar += [(phi_group, 3, "scalar"), (bias_read,), (w_group, 0), (coef_act, 0), (gf_half,)]
-        scalar += [(pre_prod_scalar, 0, 0), (coef_act, 1), (pre_prod_scalar, 0, 1), (gate_copy, 1)] + [(pre_prod_scalar, 1, r) for r in range(PRE1)]
-        gpsimd += [(pre_prod_gpsimd, 0, 2), (pre_prod_gpsimd, 0, 3)] + [(pre_prod_gpsimd, 1, r) for r in range(PRE1, R)]
-        tensor += turns(0) + turns(1) + [(bias_turn,), (coef_mm, 0, "tt", 0, 3), (coef_mm, 0, "tt", 3, 4), (x_turn, 2, 0)]
-        tensor += [(coef_turn, 0), mm(1, "tt"), (x_turn, 2, 1), (coef_turn, 1), (u_sum, 0, U0, (0, 2), True, False), (u_sum, 0, U0, (1, 3), False, True)]
-        tensor += turns(3) + [mm(2, "tt")]
-
-        def bank(index, lo=0, hi=BRANCH + 1):
-            n, a = divmod(index, NQ)
-            return (y_sum, n, a, "xp" if index >= XP_FROM and index % 2 == 1 else "yy", lo, hi, PAIR.get(index, (0, 0)))
-
-        def vqs(k, *pairs):
-            return [vq(k, j, a) for j, a in pairs]
-
-        def out(index):
-            return [(y_out,) + divmod(index, NQ)]
+        def pre_s(n, pair, lo=0, hi=2 * G):
+            return [(pre_prod, n, pair, a, min(a + QUAD, hi), S) for a in range(lo, hi, QUAD)]
 
         def usum(n, plain=(0, 0)):
-            return (u_sum, n, plain, UORD, True, True)
+            return (u_sum, n, plain)
 
-        def sgroups(k, j, lo, hi):
-            return [(prod_scalar, k, j, g, g + 1) for g in range(lo, hi)]
+        def unit(n, j, lo, hi, engine):
+            return (product, n, j, lo, hi, engine)
 
-        def burst(n):
-            return [(sink_last, n) + every, (u_quant, n)]
+        def unit_s(n, j, lo, hi):
+            return [unit(n, j, g, g + 1, S) for g in range(lo, hi)]
 
-        vector += chain(
-            1,
-            [gains(3, 0, 1), [], gains(4, 0), [], gains(4, 1), [], [(u_gain, 1)] + gains(5, 0, 1), out(0)], own, halves)
-        vector += [(x_quant, 3), (x_quant, 4), (x_quant, 5), (sink_last, 1) + high, (sink_last, 1) + low, (u_quant, 1)]
-        scalar += terms(0, (2, 0)) + [(branch_relu, 0)] + terms(0, (3, 0))[:1] + [(branch_square, 0)] + terms(0, (3, 0))[1:]
-        scalar += terms(0, (BRANCH, 0)) + [(coef_act, 2)] + terms(0, (2, 1), (3, 1), (BRANCH, 1), (2, 2), (3, 2), (BRANCH, 2), (2, 3), (3, 3), (BRANCH, 3))
-        gpsimd += g_halves(0)
-        tensor += [(branch_mm, 0)] + turns(4) + [usum(1, U1)] + turns(5) + [bank(0), (coef_turn, 2), bank(1), bank(2)]
+        def deal(work, *marks):
+            merged = []
+            for m, entry in enumerate(work + [None]):
+                merged.extend(step for place, step in marks if min(place, len(work)) == m)
+                merged.extend([entry] if entry else [])
+            return merged
 
-        vector += chain(
-            2,
-            [out(1), pres(2, 0, 1), pres(2, 2), pres(2, 3) + gains(6, 0), gains(6, 1) + out(2), out(3) + [(u_gain, 2)],
-             gains(7, 0), gains(7, 1) + out(4)], own)
-        vector += [(x_quant, 6), (x_quant, 7)] + burst(2)
-        scalar += [(post_copy, 1)] + terms(1, (2, 0)) + [(coef_act, 3), (branch_relu, 1)] + terms(1, (3, 0))[:1] + [(branch_square, 1)]
-        scalar += terms(1, (3, 0))[1:] + terms(1, (BRANCH, 0), (2, 1)) + [(coef_act, 4)] + terms(1, (3, 1), (BRANCH, 1), (3, 2))
-        scalar += terms(1, (BRANCH, 2)) + [(coef_act, 5)] + sgroups(1, 2, HALF, G1) + terms(1, (3, 3)) + sgroups(1, BRANCH, 12, V1)
-        gpsimd += [(prod_gpsimd, 1, 0) + every, (prod_gpsimd, 1, 1) + low, (prod_gpsimd, 1, 1) + high, (prod_gpsimd, 1, 2, G1, G)]
-        tensor += [mm(3, "tt"), (branch_mm, 1)] + turns(6) + [bank(3), mm(4, "tt"), usum(2), (x_turn, 7, 0), bank(4), (x_turn, 7, 1)]
-        tensor += [mm(5, "tt"), (coef_turn, 3), bank(5)]
+        def inverse(n, step, place):
+            return [(place, (sink_root, n, step)), (place + 1, (sink_inv, n, step))]
 
-        vector += chain(
-            3,
-            [pres(3, 0), pres(3, 1, 2), pres(3, 3), out(5) + br(2, 0), [(prod_vector, 2, 3, 0, V2)] + br(2, 1) + out(6) + br(2, 2), out(7),
-             br(2, 3) + [(u_gain, 3)] + out(8), []], OWN3)
-        vector += burst(3)
-        work = sgroups(2, 2, 0, G2) + sgroups(2, 3, V2, G)
-        scalar += [(coef_act, 6), (branch_relu, 2)] + work[:1] + [(branch_square, 2)] + work[1:A7] + [(coef_act, 7)]
-        scalar += deal(work[A7:], *inv(3, 2, M2[0]) + inv(3, 3, M2[1]))
-        gpsimd += [(prod_gpsimd, 2, 0) + every, (prod_gpsimd, 2, 1) + low, (prod_gpsimd, 2, 1) + high, (prod_gpsimd, 2, 2, G2, G)]
-        tensor += [mm(6, "tt"), (branch_mm, 2), (q_to_psum, 2) + low, bank(6), mm(7, "tt"), bank(7), usum(3), (coef_turn, 4), bank(8), bank(9)]
+        def when(n, *steps):
+            return list(steps) if 0 <= n < NT else []
 
-        for k in range(3, NT - 1):
-            n = k + 1
-            o = [out(NQ * k - 3 + b) for b in range(NQ)]
-            vector += chain(
-                n,
-                [pres(n, 0, 1), pres(n, 2), pres(n, 3) + o[0], br(k, 0), br(k, 1) + o[1], br(k, 2),
-                 o[2] + br(k, 3) + [(prod_vector, k, 3, V3, G)] * (V3 < G) + [(u_gain, n)] + o[3], []], ())
-            vector += burst(n)
-            work = terms(k, (2, 0), (3, 0), (2, 1), (3, 1), (2, 2), (2, 3)) + sgroups(k, 3, HALF, V3) + sgroups(k, 1, G3, G)
-            scalar += deal(work, *inv(n, 0, MARK[0]) + relu(k, MARK[1]) + inv(n, 1, MARK[2]) + inv(n, 2, MARK[3]) + inv(n, 3, MARK[4]) + [(24, (post_copy, n))] * (n == NT - 1))
-            gpsimd += [(prod_gpsimd, k, 0) + low, (prod_gpsimd, k, 1) + low, (prod_gpsimd, k, 0) + high, (prod_gpsimd, k, 1, HALF, G3)]
-            first = NQ * k - 2
-            tensor += [(branch_mm, k)] + [(q_to_psum, k) + high] * (k in QP) + [bank(first), bank(first + 1)] + [(coef_turn, k + 2)] * (k + 2 < NT)
-            tensor += [usum(n, UK), bank(first + 2), bank(first + 3)] + [bank(first + 4, 0, CUT)] * (k == NT - 2)
+        G_LAST = [10, 10] + [12] * (NT - 4) + [9]
+        V_FROM = [13, 13] + [G] * (NT - 3)
+        V_LOW = [HALF] + [QUAD] * (NT - 3) + [HALF]
+        Q_COLS = [(G, 4 * G)] * 2 + [(2 * G, 4 * G)] * (NT - 3) + [(0, 4 * G)]
+        M0, M1, M2, RELU, SQUARE = 4, 11, 21, 2, 9
+        QUANT_AT = 2
+        WARM = [(warm, m, 2) for m in range(5)]
+        PAIR = {(0, 0): (0, 0)}
+        EXTRA_T = {1: [usum(7)]}
+        EXTRA_V = {(0, 0): [(u_gain, 4)], (0, 1): [(u_gain, 5)], (0, 2): [(u_gain, 6)], (2, 1): [(u_gain, 7)]}
+        EXTRA_S = {0: pre_s(7, 0, 0, G), 1: pre_s(7, 1, 0, G)}
+        EXTRA_G = {0: [pre_g(7, 0, G)], 1: [pre_g(7, 1, G)]}
+        tensor += WARM[0:3] + turns(0) + WARM[3:4] + turns(1) + [(bias_turn,)] + WARM[4:5] + turns(2)
+        tensor += [(gate_mm, 0)] + turns(3) + [(gate_turn, 0, True), (gate_mm, 1)] + turns(4)
+        tensor += [(gate_turn, 1, True), (logit_mm, 0, 0, R), (logit_mm, 1, 0, R)] + turns(5) + [(e_turn, 0, 0), (gate_mm, 2), (logit_mm, 2, 0, R)]
+        tensor += turns(6) + [(gate_turn, 2, False)] + turns(7) + [(gate_mm, 3), (logit_mm, 3, 0, R), (gate_turn, 3, False)]
+        tensor += [(gate_mm, 4), (logit_mm, 4, 0, R), (gate_mm, 5), (logit_mm, 5, 0, R), (e_turn, 1, 0), (gate_turn, 4, False), usum(0), (gate_turn, 5, False), usum(1)]
+        tensor += [(e_turn, 2, 0), usum(2), usum(3), usum(4), (branch_mm, 0), (q_to_psum, 0) + Q_COLS[0], (branch_mm, 1), usum(5), usum(6)]
+
+        vector += [(phi_widen, 1, V, 0, T), (phi_widen, 3, V, 0, T), (phi_group, 0, False, V), (phi_group, 1, False, V), (phi_group, 3, False, V)]
+        vector += [(x_gain, 0, 0), (phi_group, 2, False, V), (x_gain, 0, 1), (gate_quant,), (x_quant, 0)]
+        vector += gains(1) + [(logit_quant, 0), (x_quant, 1)] + gains(2) + [(logit_quant, 1), (gate_copy, 0, V)]
+        vector += gains(3) + [(x_quant, 2), (gate_copy, 1, V)] + gains(4, 5) + [(sink_sum, 0, 0), (x_quant, 3), (sink_recip, 0, 0), (gate_copy, 2, V)]
+        vector += gains(6) + [(x_gain, 7, 0), (sink_scale, 0, 0), (x_gain, 7, 1), (x_quant, 4), (x_quant, 5), (w_quant,), (sink_sum, 0, 1), (gate_copy, 3, V)]
+        vector += [(sink_recip, 0, 1), (sink_scale, 0, 1), (sink_sum, 1, 0), (sink_sum, 0, 2), pre_v(6, 0, 0), (u_gain, 0), pre_v(6, 0, 1), (sink_scale, 0, 2), (sink_scale, 1, 0)]
+        vector += [(u_gain, 1), (sink_sum, 1, 1), (gate_copy, 5, V), (u_gain, 2), (sink_scale, 1, 1), (gate_copy, 4, V), (sink_sum, 1, 2), (u_gain, 3), (sink_sum, 0, 3), (u_quant, 0)]
+        vector += [pre_v(6, 1, 0), pre_v(6, 1, 1)]
+
+        scalar += [(phi_widen, 0, S, 0, T), (phi_widen, 2, S, 0, T)] + [(phi_group, r, True, S) for r in range(R)]
+        scalar += [(bias_read,), (gate_tanh, 0), (w_group, 0, S), (gate_tanh, 1), (gf_half,)] + pre_s(0, 0, G) + [(w_group, 1, S), (logit_exp, 0), (logit_exp, 1)]
+        scalar += pre_s(0, 1, 0, G) + [(gate_tanh, 2)] + pre_s(0, 1, G) + [(logit_exp, 2)] + pre_s(1, 1) + [(gate_tanh, 3)] + pre_s(2, 1, 0, G)
+        scalar += [(logit_exp, 3)] + pre_s(2, 1, G) + [(gate_tanh, 4), (logit_exp, 4), (gate_tanh, 5), (gate_one, 4), (logit_exp, 5)]
+        work = pre_s(3, 1) + pre_s(4, 1) + pre_s(5, 1, G)
+        scalar += deal(work, *inverse(0, 2, 0) + inverse(1, 0, 1) + inverse(1, 1, 7) + inverse(1, 2, 14) + inverse(0, 3, 16) + [(19, (branch_relu, 0)), (20, (branch_square, 0))])
+
+        gpsimd += [pre_g(0, 0, 0, G), pre_g(1, 0), pre_g(2, 0), pre_g(4, 0), pre_g(3, 0), pre_g(5, 0), pre_g(5, 1, 0, G), (sink_last, 0)]
+
+        for k in range(NT - 1):
+            near, far = k + 1, k + 2
+            banks = [(y_sum, k, a, ORDER, PAIR.get((k, a), (0, 0))) for a in range(NQ)]
+            tensor += banks[:1] + when(k + 3, (e_turn, k + 3, 1)) + [(q_to_psum, near) + Q_COLS[near]] + when(far, (branch_mm, far)) + banks[1:2] + EXTRA_T.get(k, []) + banks[2:]
+            back = [when(k - 1, (y_out, k - 1, a)) + EXTRA_V.get((k, a), []) for a in range(NQ)]
+            last_sum = [(sink_sum, near, 3)]
+            vector += [(sink_scale, near, 2)] + back[0] + when(far, (sink_sum, far, 0)) + last_sum * (k != QUANT_AT) + [unit(k, 2, 0, HALF, V)]
+            vector += when(far, (sink_scale, far, 0)) + [unit(k, 3, 0, V_LOW[k], V)] + when(far, (sink_sum, far, 1)) + back[1] + (last_sum + [(u_quant, 1)]) * (k == QUANT_AT) + [unit(k, 2, HALF, G, V)]
+            vector += when(far, (sink_scale, far, 1)) + back[2] + when(far, (sink_sum, far, 2)) + [unit(k, 3, HALF, G, V)] + [unit(k, 1, V_FROM[k], G, V)] * (V_FROM[k] < G) + back[3]
+            work = unit_s(k, BRANCH, 0, HALF) + unit_s(k, 3, V_LOW[k], HALF) + unit_s(k, BRANCH, HALF, G) + unit_s(k, 1, G_LAST[k], V_FROM[k]) + EXTRA_S.get(k, [])
+            marks = when(far, *inverse(far, 0, M0)) + inverse(near, 3, M0 + 2 if k != QUANT_AT else M1 + 2) + [(RELU, (branch_relu, near)), (SQUARE, (branch_square, near))]
+            marks = marks + when(far, *inverse(far, 1, M1) + inverse(far, 2, M2))
+            scalar += deal(work, *marks)
+            gpsimd += [unit(k, 0, 0, HALF, GP), unit(k, 1, 0, HALF, GP), (sink_last, near), unit(k, 0, HALF, G, GP)]
+            gpsimd += [unit(k, 1, HALF, G_LAST[k], GP)] * (G_LAST[k] > HALF) + EXTRA_G.get(k, [])
 
         k = NT - 1
-        last = NQ - 1
-        tensor += [(q_to_psum, k) + every, (branch_mm, k), bank(NQ * k - 2, CUT)] + [bank(b) for b in range(NQ * k - 1, NQ * NT - 1)]
-        o = [out(b)[0] for b in range(NQ * k - 3, NQ * NT - 1)]
-        vector += o[:1] + vqs(k, (2, 0), (3, 0), (2, 1)) + [o[1]] + vqs(k, (3, 1), (2, 2)) + [o[2]] + vqs(k, (3, 2), (2, 3), (3, 3)) + [o[3]]
-        vector += [(y_add, k, last, 2, 3, "vector"), (y_add, k, last, 0, 1, "vector"), (y_add, k, last, 2, BRANCH, "vector"), o[4], (y_add_out, k, last, 0, 2), o[5]]
-        work = terms(k, (1, 1), (BRANCH, 0), (BRANCH, 1), (1, 2), (BRANCH, 2), (BRANCH, 3))
-        scalar += deal(work, *relu(k, 2))
-        gpsimd += [(prod_gpsimd, k, 0) + low, gq(k, 1, 0), (prod_gpsimd, k, 0) + high, gq(k, 1, last)]
+        tensor += [(y_sum, k, a, (2, 3, 0, BRANCH, 1), (0, 0)) for a in range(NQ - 1)]
+        vector += [unit(k, j, 12, G, V) for j in (2, 3, 0)] + [(y_out, k - 1, 0)] + [unit(k, j, 0, 4, V) for j in (2, 3)] + [(y_out, k - 1, 1), unit(k, 0, 0, 4, V), (y_out, k - 1, 2)]
+        vector += [unit(k, j, 4, 8, V) for j in (2, 3, 0)] + [(y_out, k - 1, 3)] + [unit(k, j, 8, 12, V) for j in (2, 3)] + [(y_store, k, 3), (y_out, k, 0), (y_out, k, 1), (y_out, k, 2)]
+        scalar += [s for j, a in ((BRANCH, 3), (BRANCH, 0), (1, 0), (BRANCH, 1), (1, 1), (BRANCH, 2), (0, 2)) for s in unit_s(k, j, QUAD * a, QUAD * a + QUAD)]
+        gpsimd += [unit(k, 1, 12, G, GP), (y_add, k, 3, 2, 3), (y_add, k, 3, 0, 1), (y_add, k, 3, 2, BRANCH), (y_add_out, k, 3, 0, 2), unit(k, 1, 8, 12, GP)]
 
         queues = (tensor, vector, scalar, gpsimd)
         steps = [s for queue in queues for s in queue]
-        products = (prod_vector, prod_scalar, prod_gpsimd)
-
-        def find(fns, *args):
-            return [s for s in steps if s[0] in fns and s[1 : 1 + len(args)] == args]
-
-        def bank_readers(s):
-            fn = s[0]
-            if fn is x_turn:
-                return "xp", gains(s[1], s[2])
-            if fn is coef_mm and s[3] == 0:
-                return s[2], [(coef_act, s[1])]
-            if fn is bias_turn:
-                return "uh", [(bias_read,)]
-            if fn is y_sum and s[4] == 0:
-                return s[3], [(y_out, s[1], s[2])]
-            if fn is u_sum and s[4]:
-                return "uh", [(u_gain, s[1])]
-            if fn is branch_mm:
-                return "uh", [(branch_relu, s[1])]
-            if fn is coef_turn:
-                return "tt" if s[1] in THIRD_TURNS else "ct", find((prod_vector, pre_prod_vector, sink_scale, gate_copy, post_copy), s[1])
-            return None, []
-
-        before = dict()
-        held = dict()
-        for s in tensor:
-            tag, readers = bank_readers(s)
-            if tag:
-                held.setdefault(tag, []).append(readers)
-                before[s] = held[tag][-1 - BANKS[tag]] if len(held[tag]) > BANKS[tag] else []
-
-        def needs(s):
-            fn, n = s[0], s[1] if len(s) > 1 else 0
-            if fn is phi_group:
-                return find((phi_widen_vector, phi_widen_scalar), n)
-            if fn is phi_quant:
-                return find((phi_group,), n)
-            if fn is bias_read:
-                return [(bias_turn,)]
-            if fn is w_quant:
-                return [(w_group, n)]
-            if fn is x_gain:
-                return [(x_turn, n, s[2])] + find((x_quant,), n - XN_BUFS)
-            if fn is x_quant:
-                return find((coef_mm,), n - 3)
-            if fn is coef_mm:
-                return [(x_quant, n)] + [(phi_quant, r) for r in range(s[3], s[4])]
-            if fn is coef_act:
-                return find((coef_mm,), n) + find((coef_turn,), n - CO_BUFS) + [(bias_read,)]
-            if fn is coef_turn:
-                return [(coef_act, n)]
-            if fn in (gate_copy, post_copy):
-                return [(coef_turn, n)] + find((prod_scalar, prod_gpsimd), n - 2, BRANCH) + find((sink_scale,), n) * (fn is post_copy)
-            if fn is sink_sum or fn is pre_prod_vector:
-                return [(coef_turn, n)] + find((gate_copy,), n) + (find((u_sum,), n - 2) if fn is pre_prod_vector else [])
-            if fn is sink_root:
-                return [(sink_sum,) + s[1:]]
-            if fn is sink_scale:
-                return find((sink_inv_scalar,), *s[1:])
-            if fn is sink_last:
-                return find((sink_inv_scalar,), n, 3) + find(products + (q_to_psum,), n - 2)
-            if fn is q_to_psum:
-                return find((sink_last, post_copy), n)
-            if fn in (pre_prod_scalar, pre_prod_gpsimd):
-                return [(gate_copy, n)] + find((u_sum,), n - 2)
-            if fn is u_sum:
-                return [t for r in s[3] for t in find((pre_prod_vector, pre_prod_scalar, pre_prod_gpsimd), n, r)]
-            if fn is u_gain:
-                return find((u_sum,), n) + [(gf_half,)]
-            if fn is branch_mm:
-                return [(u_quant, n), (w_quant, 0), (w_quant, 1)]
-            if fn is branch_relu:
-                return [(branch_mm, n)]
-            if fn is branch_square:
-                return find(products, n - 2, BRANCH)
-            if fn in products:
-                source = [(branch_square, n)] if s[2] == BRANCH else find((sink_last,), n)
-                if fn is prod_vector:
-                    source = source + find((q_to_psum, post_copy), n)
-                if fn is not prod_vector and s[2] == BRANCH:
-                    source = source + find((gate_copy, post_copy), n)
-                return source + find((y_sum,), n - 2)
-            if fn is y_sum:
-                lo, hi = quad(s[2])
-                return [t for t in find(products, n) if t[2] in TERMS[s[4] : s[5]] and t[3] < hi and t[4] > lo]
-            if fn in (y_add, y_add_out):
-                lo, hi = quad(s[2])
-                sums = [t for t in find((y_add,), n, s[2]) if t[3] in s[3:5] and (fn is y_add_out or t[4] < s[4] and t != s)]
-                return [t for t in find(products, n) if t[2] in s[3:5] and t[3] < hi and t[4] > lo] + sums
-            if fn is y_out:
-                return find((y_sum,), n, s[2])
-            return []
-
-        def weave():
-            done = set()
-            pos = [0] * len(queues)
-            while len(done) < len(steps):
-                count = len(done)
-                for e, queue in enumerate(queues):
-                    while pos[e] < len(queue) and all(t in done for t in needs(queue[pos[e]]) + before.get(queue[pos[e]], [])):
-                        s = queue[pos[e]]
-                        s[0](*s[1:])
-                        done.add(s)
-                        pos[e] = pos[e] + 1
-                assert len(done) > count, [(q[p][0], q[p][1:]) for q, p in zip(queues, pos) if p < len(q)]
-
         assert len(set(steps)) == len(steps)
-        for n in range(NT):
-            for j in range(BRANCH + 1):
-                assert sum(s[4] - s[3] for s in find(products, n, j)) == G, (n, j)
-        weave()
+        writers, users = dict(), dict()
+        for s in steps:
+            reads, writes = uses(*s)
+            for key in writes:
+                writers.setdefault(key, []).append(s)
+            for key in reads + writes:
+                users.setdefault(key[1:] if key[0] == "held" else key, []).append(s)
+        done, taken = set(), dict()
+
+        def ready(s):
+            reads, writes = uses(*s)
+            if not all(t in done for key in reads for t in writers.get(key, [])):
+                return False
+            for key in writes:
+                if key[0] in KINDS and key not in tiles:
+                    older, bufs = taken.setdefault(tag_of(key), []), bufs_of(key)
+                    if len(older) >= bufs and not all(t in done for t in users[older[-bufs]]):
+                        return False
+            return True
+
+        pos = [0] * len(queues)
+        while len(done) < len(steps):
+            count = len(done)
+            for e, queue in enumerate(queues):
+                if pos[e] < len(queue) and ready(queue[pos[e]]):
+                    s = queue[pos[e]]
+                    for key in uses(*s)[1]:
+                        if key[0] in KINDS and key not in tiles:
+                            taken[tag_of(key)].append(key)
+                    s[0](*s[1:])
+                    done.add(s)
+                    pos[e] = pos[e] + 1
+            assert len(done) > count, [(q[p][0], q[p][1:]) for q, p in zip(queues, pos) if p < len(q)]

@@ -34,6 +34,7 @@ HALF = G // 2
 U_BATCHES = ((0, 4), (4, 8))
 X_BATCHES = ((0, 1), (1, 2), (2, 4), (4, 6), (6, 7), (7, 8))
 OWN_GATES = 4
+WHOLE = 2
 LATE_PRE = (4, 1)
 FLOPS = 2 * TOK * R * D * M + 2 * TOK * D * D
 
@@ -69,6 +70,8 @@ KINDS = {
     "hr": ([P, D], F32, "hr", 1),
     "f": ([P, D], F32, "f", 2),
     "prod": ([P, HALF, R, C], F32, "prod", 3),
+    "whole": ([P, G, R, C], F32, "whole", 2),
+    "w_raw": ([P, T, D], BF16, "whole", 2),
     "yt": ([P, TB, QUAD, C], F32, "four", 4),
     "yo": ([P, D], F32, "yo", 4),
 }
@@ -95,7 +98,9 @@ def tag_of(key):
     if key[0] == "pu" and key[1:] >= LATE_PRE:
         return "late"
     if key[0] == "pu":
-        return "prod%d" % ((2 * key[1] + key[2]) % (BRANCH + 1))
+        return "prod%d" % (2 + (2 * key[1] + key[2]) % 3)
+    if tag == "whole":
+        return "whole%d" % (key[2] if key[1:] else 0)
     return "prod%d" % key[2] if tag == "prod" else tag
 
 
@@ -114,11 +119,27 @@ def tile_groupedmanifoldhyperconnection_kernel(tc, x, gn, phi_bytes, phi_scale, 
         ps = ctx.enter_context(tc.psum_pool(name="ps", bufs=1))
         ctx.enter_context(tc.manual_schedule())
 
+        xb_of = {n: (b, n - lo) for b, (lo, hi) in enumerate(X_BATCHES) for n in range(lo, hi)}
+
+        tiles = dict()
+
+        def value(*key):
+            if key not in tiles:
+                shape, dtype, tag, bufs = KINDS[key[0]]
+                if 0 in shape:
+                    lo, hi = X_BATCHES[key[1]]
+                    shape = [size or (hi - lo) * P for size in shape]
+                if tag in BANKS:
+                    tiles[key] = ps.tile(shape, dtype, name=tag_of(key), bufs=bufs_of(key))
+                else:
+                    tiles[key] = sb.tile(shape, dtype, name=tag_of(key), bufs=bufs_of(key), align_bytes=64)
+            return tiles[key]
+
         ident = keep.tile([P, P], F32)
         bm_row = keep.tile([P, M], BF16)
-        nc.gpsimd.memset(bm_row[:], 0.0)
+        nc.vector.memset(bm_row[:], 0.0)
         ones = keep.tile([P, 2], BF16)
-        nc.gpsimd.memset(ones[:], 1.0)
+        nc.vector.memset(ones[:], 1.0)
         make_identity(nc, ident[:])
 
         scale = keep.tile([P, R, T], F32)
@@ -127,7 +148,6 @@ def tile_groupedmanifoldhyperconnection_kernel(tc, x, gn, phi_bytes, phi_scale, 
         xs = [keep.tile([P, R * D], BF16, name="x%d" % n) for n in range(NT)]
         gn_k = keep.tile([P, R, T], BF16)
         gf_k = keep.tile([P, T], BF16)
-        w_raw = keep.tile([P, T, D], BF16)
 
         def load_x(n, lo, hi):
             nc.sync.dma_start(out=xs[n][:, lo * D : hi * D], in_=x_rows[n * P : (n + 1) * P, lo * D : hi * D])
@@ -144,7 +164,7 @@ def tile_groupedmanifoldhyperconnection_kernel(tc, x, gn, phi_bytes, phi_scale, 
         nc.sync.dma_start(out=bm_row[0:1, P:M].rearrange("p (g k) -> p g k", g=G), in_=bm_groups[:, :, GATES:KC])
         load_x(2, 0, R)
         load_x(3, 0, R)
-        nc.sync.dma_start(out=w_raw[:], in_=w.rearrange("(p t) n -> p t n", t=T))
+        nc.sync.dma_start(out=value("w_raw")[:], in_=w.rearrange("(p t) n -> p t n", t=T))
         nc.sync.dma_start(out=gf_k[:], in_=gf.rearrange("(p t) -> p t", t=T))
         for n in range(4, NT):
             load_x(n, 0, R)
@@ -162,22 +182,6 @@ def tile_groupedmanifoldhyperconnection_kernel(tc, x, gn, phi_bytes, phi_scale, 
         u_codes = [keep.tile([P, hi - lo, P], U32, name="uc%d" % lo, align_bytes=64) for lo, hi in U_BATCHES]
         u_scales = [keep.tile([P, hi - lo, P], U8, name="us%d" % lo, align_bytes=64) for lo, hi in U_BATCHES]
         batch_of = {n: (b, n - lo) for b, (lo, hi) in enumerate(U_BATCHES) for n in range(lo, hi)}
-
-        xb_of = {n: (b, n - lo) for b, (lo, hi) in enumerate(X_BATCHES) for n in range(lo, hi)}
-
-        tiles = dict()
-
-        def value(*key):
-            if key not in tiles:
-                shape, dtype, tag, bufs = KINDS[key[0]]
-                if 0 in shape:
-                    lo, hi = X_BATCHES[key[1]]
-                    shape = [size or (hi - lo) * P for size in shape]
-                if tag in BANKS:
-                    tiles[key] = ps.tile(shape, dtype, name=tag_of(key), bufs=bufs_of(key))
-                else:
-                    tiles[key] = sb.tile(shape, dtype, name=tag_of(key), bufs=bufs_of(key), align_bytes=64)
-            return tiles[key]
 
         def turn(dst, src, start, stop, plain):
             nc.tensor.matmul(dst, src, ident[:], start=start, stop=stop, is_transpose=not plain)
@@ -227,7 +231,7 @@ def tile_groupedmanifoldhyperconnection_kernel(tc, x, gn, phi_bytes, phi_scale, 
             copy = nc.vector.tensor_copy if engine == "vector" else nc.scalar.copy
             copy(
                 out=value("w_words")[:, cols, :].rearrange("p (c i) t -> p c t i", i=4),
-                in_=w_raw[:, :, cols].rearrange("p t (c i) -> p c t i", i=4),
+                in_=value("w_raw")[:, :, cols].rearrange("p t (c i) -> p c t i", i=4),
             )
 
         def gf_half():
@@ -408,6 +412,8 @@ def tile_groupedmanifoldhyperconnection_kernel(tc, x, gn, phi_bytes, phi_scale, 
             nc.scalar.activation(value("f", n)[:], value("hr", n)[:], ACT.Square)
 
         def term(n, j, lo, hi):
+            if j < WHOLE:
+                return value("whole", n, j)[:, lo:hi]
             return value("prod", n, j, lo // HALF)[:, lo % HALF : lo % HALF + hi - lo]
 
         def product(n, j, lo, hi, engine):
@@ -444,14 +450,15 @@ def tile_groupedmanifoldhyperconnection_kernel(tc, x, gn, phi_bytes, phi_scale, 
                     out=out_view[n, i, a], in_=yo[C * i : C * (i + 1), :].rearrange("p (tb c) -> p tb c", tb=TB)
                 )
 
-        def y_add(n, a, into, other):
+        def y_add(n, a, into, other, engine):
             dst = term(n, into, QUAD * a, QUAD * (a + 1)).rearrange("p g i c -> p (g i c)")
             src = term(n, other, QUAD * a, QUAD * (a + 1)).rearrange("p g i c -> p (g i c)")
-            nc.gpsimd.tensor_tensor(out=dst, in0=dst, in1=src, op=ALU.add)
+            add = nc.vector.tensor_tensor if engine == "vector" else nc.gpsimd.tensor_tensor
+            add(out=dst, in0=dst, in1=src, op=ALU.add)
 
         def y_add_out(n, a, one, other):
             yo = value("yo", n, a)[:].rearrange("p (i g c) -> p i g c", i=R, g=QUAD)
-            nc.gpsimd.tensor_tensor(
+            nc.vector.tensor_tensor(
                 out=yo,
                 in0=term(n, one, QUAD * a, QUAD * (a + 1)).rearrange("p g i c -> p i g c"),
                 in1=term(n, other, QUAD * a, QUAD * (a + 1)).rearrange("p g i c -> p i g c"),
@@ -462,8 +469,11 @@ def tile_groupedmanifoldhyperconnection_kernel(tc, x, gn, phi_bytes, phi_scale, 
             yo = value("yo", n, a)[:].rearrange("p (i c) -> p i c", i=R)
             nc.sync.dma_start(out=out_rows[n * P : (n + 1) * P, :, a, :], in_=yo)
 
+        def home(n, j, group):
+            return ("whole", n, j) if j < WHOLE else ("prod", n, j, group // HALF)
+
         def parts(n, terms, quad):
-            return [("part", n, j, quad) for j in terms] + [("held", "prod", n, j, quad // 2) for j in terms]
+            return [("part", n, j, quad) for j in terms] + [("held",) + home(n, j, QUAD * quad) for j in terms]
 
         def uses(fn, n=0, *a):
             xb = xb_of[n][0]
@@ -475,7 +485,7 @@ def tile_groupedmanifoldhyperconnection_kernel(tc, x, gn, phi_bytes, phi_scale, 
                 logit_quant: lambda: ([("logit_words", n)], [("logit_codes", n)]),
                 bias_turn: lambda: ([], [("bias_ps",)]),
                 bias_read: lambda: ([("bias_ps",)], [("bias",)]),
-                w_group: lambda: ([], [("w_words",)]),
+                w_group: lambda: ([("w_raw",)], [("w_words",)]),
                 gf_half: lambda: ([], [("half_gf",)]),
                 w_quant: lambda: ([("w_words",)], [("w_codes",)]),
                 x_turn: lambda: ([], [("xp", n, a[0])]),
@@ -505,7 +515,7 @@ def tile_groupedmanifoldhyperconnection_kernel(tc, x, gn, phi_bytes, phi_scale, 
                 branch_square: lambda: ([("hr", n)], [("f", n)]),
                 product: lambda: (
                     [("f", n), ("gate", xb)] if a[0] == BRANCH else [("qp", n)] if a[3] == "vector" else [("q", n)],
-                    [("prod", n, a[0], a[1] // HALF)] + [("part", n, a[0], quad) for quad in range(a[1] // QUAD, (a[2] - 1) // QUAD + 1)],
+                    [home(n, a[0], a[1])] + [("part", n, a[0], quad) for quad in range(a[1] // QUAD, (a[2] - 1) // QUAD + 1)],
                 ),
                 y_sum: lambda: (parts(n, range(BRANCH + 1), a[0]), [("yt", n, a[0])]),
                 y_add: lambda: (parts(n, a[1:3], a[0]), [("added", n, a[0])]),
@@ -556,42 +566,41 @@ def tile_groupedmanifoldhyperconnection_kernel(tc, x, gn, phi_bytes, phi_scale, 
         def when(n, *steps):
             return list(steps) if 0 <= n < NT else []
 
-        G_LAST = [10, 10] + [12] * (NT - 4) + [9]
-        V_FROM = [13, 13] + [G] * (NT - 3)
-        V_LOW = [HALF] + [QUAD] * (NT - 3) + [HALF]
-        Q_COLS = [(G, 4 * G)] * 2 + [(2 * G, 4 * G)] * (NT - 3) + [(0, 4 * G)]
-        M0, M1, M2, RELU, SQUARE = 4, 11, 21, 2, 9
-        QUANT_AT = 2
+        G_FROM = [G, 4] + [HALF] * (NT - 3)
+        V_LOW = [HALF, HALF] + [6] * (NT - 4) + [HALF]
+        Q_COLS = [(G + HALF, 4 * G)] + [(2 * G, 4 * G)] * (NT - 1)
+        M0, M1, M2, RELU, SQUARE = 4, 12, 22, 2, 9
+        QUANT_AT = {2: 1}
         WARM = [(warm, m, 2) for m in range(5)]
-        PAIR = {(0, 0): (0, 0)}
-        EXTRA_T = {1: [usum(7)]}
-        EXTRA_V = {(0, 0): [(u_gain, 4)], (0, 1): [(u_gain, 5)], (0, 2): [(u_gain, 6)], (2, 1): [(u_gain, 7)]}
-        EXTRA_S = {0: pre_s(7, 0, 0, G), 1: pre_s(7, 1, 0, G)}
-        EXTRA_G = {0: [pre_g(7, 0, G)], 1: [pre_g(7, 1, G)]}
+        PAIR = {(0, 0): (2, 0)}
+        EXTRA_T = {0: [usum(5)], 1: [usum(7)]}
+        EXTRA_V = {(0, 0): [(u_gain, 4)], (0, 1): [(u_gain, 6)], (0, 3): [unit(0, 1, HALF, G, V)], (1, 1): [(u_gain, 5)]}
+        EXTRA_S = {1: pre_s(7, 1)}
+        EXTRA_G = {0: [pre_g(7, 0)]}
         tensor += WARM[0:3] + turns(0) + WARM[3:4] + turns(1) + [(bias_turn,)] + WARM[4:5] + turns(2)
         tensor += [(gate_mm, 0)] + turns(3) + [(gate_turn, 0, True), (gate_mm, 1)] + turns(4)
         tensor += [(gate_turn, 1, True), (logit_mm, 0, 0, R), (logit_mm, 1, 0, R)] + turns(5) + [(e_turn, 0, 0), (gate_mm, 2), (logit_mm, 2, 0, R)]
-        tensor += turns(6) + [(gate_turn, 2, False)] + turns(7) + [(gate_mm, 3), (logit_mm, 3, 0, R), (gate_turn, 3, False)]
-        tensor += [(gate_mm, 4), (logit_mm, 4, 0, R), (gate_mm, 5), (logit_mm, 5, 0, R), (e_turn, 1, 0), (gate_turn, 4, False), usum(0), (gate_turn, 5, False), usum(1)]
-        tensor += [(e_turn, 2, 0), usum(2), usum(3), usum(4), (branch_mm, 0), (q_to_psum, 0) + Q_COLS[0], (branch_mm, 1), usum(5), usum(6)]
+        tensor += turns(6) + [(gate_turn, 2, False)] + turns(7) + [(gate_mm, 3), (logit_mm, 3, 0, R), (gate_turn, 3, False), usum(0)]
+        tensor += [(gate_mm, 4), (logit_mm, 4, 0, R), (gate_mm, 5), (logit_mm, 5, 0, R), (e_turn, 1, 0), (gate_turn, 4, False), (gate_turn, 5, False), usum(1)]
+        tensor += [(e_turn, 2, 0), usum(2), usum(3, (2, 0)), usum(4), (branch_mm, 0), (q_to_psum, 0) + Q_COLS[0], (branch_mm, 1), usum(6)]
 
         vector += [(phi_widen, 1, V, 0, T), (phi_widen, 3, V, 0, T), (phi_group, 0, False, V), (phi_group, 1, False, V), (phi_group, 3, False, V)]
         vector += [(x_gain, 0, 0), (phi_group, 2, False, V), (x_gain, 0, 1), (gate_quant,), (x_quant, 0)]
         vector += gains(1) + [(logit_quant, 0), (x_quant, 1)] + gains(2) + [(logit_quant, 1), (gate_copy, 0, V)]
         vector += gains(3) + [(x_quant, 2), (gate_copy, 1, V)] + gains(4, 5) + [(sink_sum, 0, 0), (x_quant, 3), (sink_recip, 0, 0), (gate_copy, 2, V)]
         vector += gains(6) + [(x_gain, 7, 0), (sink_scale, 0, 0), (x_gain, 7, 1), (x_quant, 4), (x_quant, 5), (w_quant,), (sink_sum, 0, 1), (gate_copy, 3, V)]
-        vector += [(sink_recip, 0, 1), (sink_scale, 0, 1), (sink_sum, 1, 0), (sink_sum, 0, 2), pre_v(6, 0, 0), (u_gain, 0), pre_v(6, 0, 1), (sink_scale, 0, 2), (sink_scale, 1, 0)]
-        vector += [(u_gain, 1), (sink_sum, 1, 1), (gate_copy, 5, V), (u_gain, 2), (sink_scale, 1, 1), (gate_copy, 4, V), (sink_sum, 1, 2), (u_gain, 3), (sink_sum, 0, 3), (u_quant, 0)]
-        vector += [pre_v(6, 1, 0), pre_v(6, 1, 1)]
+        vector += [(sink_recip, 0, 1), (u_gain, 0), (sink_scale, 0, 1), (sink_sum, 1, 0), (sink_sum, 0, 2), pre_v(6, 0, 0), (gate_copy, 5, V), pre_v(6, 0, 1), (sink_scale, 0, 2), (sink_scale, 1, 0)]
+        vector += [(u_gain, 1), (sink_sum, 1, 1), (u_gain, 2), (sink_scale, 1, 1), (gate_copy, 4, V), (sink_sum, 1, 2), pre_v(6, 1, 0), (u_gain, 3), (sink_sum, 0, 3), (u_quant, 0)]
+        vector += [pre_v(6, 1, 1)]
 
         scalar += [(phi_widen, 0, S, 0, T), (phi_widen, 2, S, 0, T)] + [(phi_group, r, True, S) for r in range(R)]
         scalar += [(bias_read,), (gate_tanh, 0), (w_group, 0, S), (gate_tanh, 1), (gf_half,)] + pre_s(0, 0, G) + [(w_group, 1, S), (logit_exp, 0), (logit_exp, 1)]
         scalar += pre_s(0, 1, 0, G) + [(gate_tanh, 2)] + pre_s(0, 1, G) + [(logit_exp, 2)] + pre_s(1, 1) + [(gate_tanh, 3)] + pre_s(2, 1, 0, G)
         scalar += [(logit_exp, 3)] + pre_s(2, 1, G) + [(gate_tanh, 4), (logit_exp, 4), (gate_tanh, 5), (gate_one, 4), (logit_exp, 5)]
-        work = pre_s(3, 1) + pre_s(4, 1) + pre_s(5, 1, G)
-        scalar += deal(work, *inverse(0, 2, 0) + inverse(1, 0, 1) + inverse(1, 1, 7) + inverse(1, 2, 14) + inverse(0, 3, 16) + [(19, (branch_relu, 0)), (20, (branch_square, 0))])
+        work = pre_s(3, 1) + pre_s(4, 1) + pre_s(5, 1)
+        scalar += deal(work, *inverse(0, 2, 0) + inverse(1, 0, 1) + inverse(1, 1, 7) + inverse(1, 2, 14) + inverse(0, 3, 17))
 
-        gpsimd += [pre_g(0, 0, 0, G), pre_g(1, 0), pre_g(2, 0), pre_g(4, 0), pre_g(3, 0), pre_g(5, 0), pre_g(5, 1, 0, G), (sink_last, 0)]
+        gpsimd += [pre_g(0, 0, 0, G), pre_g(1, 0), pre_g(2, 0), pre_g(4, 0), pre_g(3, 0), pre_g(5, 0), (sink_last, 0)]
 
         for k in range(NT - 1):
             near, far = k + 1, k + 2
@@ -599,22 +608,25 @@ def tile_groupedmanifoldhyperconnection_kernel(tc, x, gn, phi_bytes, phi_scale, 
             tensor += banks[:1] + when(k + 3, (e_turn, k + 3, 1)) + [(q_to_psum, near) + Q_COLS[near]] + when(far, (branch_mm, far)) + banks[1:2] + EXTRA_T.get(k, []) + banks[2:]
             back = [when(k - 1, (y_out, k - 1, a)) + EXTRA_V.get((k, a), []) for a in range(NQ)]
             last_sum = [(sink_sum, near, 3)]
-            vector += [(sink_scale, near, 2)] + back[0] + when(far, (sink_sum, far, 0)) + last_sum * (k != QUANT_AT) + [unit(k, 2, 0, HALF, V)]
-            vector += when(far, (sink_scale, far, 0)) + [unit(k, 3, 0, V_LOW[k], V)] + when(far, (sink_sum, far, 1)) + back[1] + (last_sum + [(u_quant, 1)]) * (k == QUANT_AT) + [unit(k, 2, HALF, G, V)]
-            vector += when(far, (sink_scale, far, 1)) + back[2] + when(far, (sink_sum, far, 2)) + [unit(k, 3, HALF, G, V)] + [unit(k, 1, V_FROM[k], G, V)] * (V_FROM[k] < G) + back[3]
-            work = unit_s(k, BRANCH, 0, HALF) + unit_s(k, 3, V_LOW[k], HALF) + unit_s(k, BRANCH, HALF, G) + unit_s(k, 1, G_LAST[k], V_FROM[k]) + EXTRA_S.get(k, [])
-            marks = when(far, *inverse(far, 0, M0)) + inverse(near, 3, M0 + 2 if k != QUANT_AT else M1 + 2) + [(RELU, (branch_relu, near)), (SQUARE, (branch_square, near))]
+            vector += [(sink_scale, near, 2)] + back[0] + when(far, (sink_sum, far, 0)) + last_sum * (k not in QUANT_AT) + [unit(k, 2, 0, HALF, V)]
+            vector += when(far, (sink_scale, far, 0)) + [unit(k, 3, 0, V_LOW[k], V)] + when(far, (sink_sum, far, 1)) + back[1] + ([(u_gain, NT - 1)] + last_sum + [(u_quant, 1)]) * (k in QUANT_AT) + [unit(k, 2, HALF, G, V)]
+            vector += when(far, (sink_scale, far, 1)) + back[2] + when(far, (sink_sum, far, 2)) + [unit(k, 3, HALF, G, V)] + back[3]
+            work = unit_s(k, 1, 0, QUAD) + unit_s(k, BRANCH, 0, HALF) + unit_s(k, 1, QUAD, min(G_FROM[k], HALF))
+            work = work + unit_s(k, 3, V_LOW[k], HALF) + unit_s(k, BRANCH, HALF, G) + EXTRA_S.get(k, [])
+            marks = when(far, *inverse(far, 0, M0)) + inverse(near, 3, M0 + 2 if k not in QUANT_AT else M1 + 3) + [(RELU if k else SQUARE, (branch_relu, near)), (SQUARE if k else 2 * SQUARE, (branch_square, near))]
+            marks = [(1, (branch_relu, 0)), (2, (branch_square, 0))] * (k == 0) + marks
             marks = marks + when(far, *inverse(far, 1, M1) + inverse(far, 2, M2))
             scalar += deal(work, *marks)
-            gpsimd += [unit(k, 0, 0, HALF, GP), unit(k, 1, 0, HALF, GP), (sink_last, near), unit(k, 0, HALF, G, GP)]
-            gpsimd += [unit(k, 1, HALF, G_LAST[k], GP)] * (G_LAST[k] > HALF) + EXTRA_G.get(k, [])
+            second = [unit(k, 1, G_FROM[k], G, GP)] * (G_FROM[k] < G)
+            gpsimd += [unit(k, 0, 0, G, GP)] + second * (k in QUANT_AT) + [(sink_last, near)] + second * (k not in QUANT_AT) + EXTRA_G.get(k, [])
 
-        k = NT - 1
-        tensor += [(y_sum, k, a, (2, 3, 0, BRANCH, 1), (0, 0)) for a in range(NQ - 1)]
-        vector += [unit(k, j, 12, G, V) for j in (2, 3, 0)] + [(y_out, k - 1, 0)] + [unit(k, j, 0, 4, V) for j in (2, 3)] + [(y_out, k - 1, 1), unit(k, 0, 0, 4, V), (y_out, k - 1, 2)]
-        vector += [unit(k, j, 4, 8, V) for j in (2, 3, 0)] + [(y_out, k - 1, 3)] + [unit(k, j, 8, 12, V) for j in (2, 3)] + [(y_store, k, 3), (y_out, k, 0), (y_out, k, 1), (y_out, k, 2)]
-        scalar += [s for j, a in ((BRANCH, 3), (BRANCH, 0), (1, 0), (BRANCH, 1), (1, 1), (BRANCH, 2), (0, 2)) for s in unit_s(k, j, QUAD * a, QUAD * a + QUAD)]
-        gpsimd += [unit(k, 1, 12, G, GP), (y_add, k, 3, 2, 3), (y_add, k, 3, 0, 1), (y_add, k, 3, 2, BRANCH), (y_add_out, k, 3, 0, 2), unit(k, 1, 8, 12, GP)]
+        k, last = NT - 1, NQ - 1
+        tensor += [(y_sum, k, a, ORDER, (0, 0)) for a in range(last)]
+        outs = [(y_out, k - 1, a) for a in range(NQ)] + [(y_out, k, a) for a in range(last)]
+        vector += [unit(k, 2, 0, HALF, V), outs[0], unit(k, 3, 0, HALF, V), outs[1], unit(k, 2, HALF, G, V), outs[2], unit(k, 3, HALF, G, V), outs[3]]
+        vector += [outs[4], (y_add, k, last, 2, 3, V), outs[5], (y_add, k, last, 2, BRANCH, V), (y_add_out, k, last, 0, 2), (y_store, k, last), outs[6]]
+        scalar += [s for a in range(NQ) for j in (BRANCH, 1)[: 1 + (a < last)] for s in unit_s(k, j, QUAD * a, QUAD * a + QUAD)]
+        gpsimd += [unit(k, 0, 0, HALF, GP), unit(k, 0, HALF, G, GP), unit(k, 1, QUAD * last, G, GP), (y_add, k, last, 0, 1, GP)]
 
         queues = (tensor, vector, scalar, gpsimd)
         steps = [s for queue in queues for s in queue]
@@ -626,7 +638,7 @@ def tile_groupedmanifoldhyperconnection_kernel(tc, x, gn, phi_bytes, phi_scale, 
                 writers.setdefault(key, []).append(s)
             for key in reads + writes:
                 users.setdefault(key[1:] if key[0] == "held" else key, []).append(s)
-        done, taken = set(), dict()
+        done, taken = set(), {"whole0": [("w_raw",)]}
 
         def ready(s):
             reads, writes = uses(*s)

@@ -41,7 +41,7 @@ FLOPS = 2 * TOK * R * D * M + 2 * TOK * D * D
 BANKS = {"four": 4, "b0": 1, "b1": 1, "b2": 1, "b3": 1}
 KINDS = {
     "wide": ([P, T, M], BF16, "yo", 4),
-    "bias_ps": ([P, MT, 2], F32, "b2", 1),
+    "bias_ps": ([P, MT + T, 2], F32, "b2", 1),
     "warm": ([P, 2, P], F32, "b0", 1),
     "gate_words": ([P, R, P, T], BF16, "late", 7),
     "logit_words": ([P, 2, 2 * P, T], BF16, "late", 7),
@@ -136,7 +136,7 @@ def tile_groupedmanifoldhyperconnection_kernel(tc, x, gn, phi_bytes, phi_scale, 
             return tiles[key]
 
         ident = keep.tile([P, P], F32)
-        bm_row = keep.tile([P, M], BF16)
+        bm_row = keep.tile([P, M + D], BF16)
         nc.vector.memset(bm_row[:], 0.0)
         ones = keep.tile([P, 2], BF16)
         nc.vector.memset(ones[:], 1.0)
@@ -147,7 +147,6 @@ def tile_groupedmanifoldhyperconnection_kernel(tc, x, gn, phi_bytes, phi_scale, 
         phi_raw = [keep.tile([P, T, M], U8, name="phb%d" % r) for r in range(R)]
         xs = [keep.tile([P, R * D], BF16, name="x%d" % n) for n in range(NT)]
         gn_k = keep.tile([P, R, T], BF16)
-        gf_k = keep.tile([P, T], BF16)
 
         def load_x(n, lo, hi):
             nc.sync.dma_start(out=xs[n][:, lo * D : hi * D], in_=x_rows[n * P : (n + 1) * P, lo * D : hi * D])
@@ -162,10 +161,13 @@ def tile_groupedmanifoldhyperconnection_kernel(tc, x, gn, phi_bytes, phi_scale, 
         bm_groups = bm.rearrange("(o g k) -> o g k", o=1, g=G)
         nc.sync.dma_start(out=bm_row[0:1, 0:P].rearrange("p (g k) -> p g k", g=G), in_=bm_groups[:, :, 0:GATES])
         nc.sync.dma_start(out=bm_row[0:1, P:M].rearrange("p (g k) -> p g k", g=G), in_=bm_groups[:, :, GATES:KC])
+        gf_dst = bm_row[0:1, M : M + D].rearrange("p (t g c) -> p t g c", t=T, g=G)
+        nc.sync.dma_start(out=gf_dst, in_=gf.rearrange("(o g t c) -> o t g c", o=1, g=G, t=T))
         load_x(2, 0, R)
         load_x(3, 0, R)
-        nc.sync.dma_start(out=value("w_raw")[:], in_=w.rearrange("(p t) n -> p t n", t=T))
-        nc.sync.dma_start(out=gf_k[:], in_=gf.rearrange("(p t) -> p t", t=T))
+        w_rows = w.rearrange("(g t c) n -> t g c n", g=G, t=T)
+        for t in range(T):
+            nc.sync.dma_start(out=value("w_raw")[:, t, :], in_=w_rows[t])
         for n in range(4, NT):
             load_x(n, 0, R)
 
@@ -219,11 +221,11 @@ def tile_groupedmanifoldhyperconnection_kernel(tc, x, gn, phi_bytes, phi_scale, 
             )
 
         def bias_turn():
-            for m in range(MT):
+            for m in range(MT + T):
                 nc.tensor.matmul(value("bias_ps")[:, m, :], bm_row[:, m * P : (m + 1) * P], ones[:], start=True, stop=True)
 
         def bias_read():
-            nc.scalar.copy(out=bias[:], in_=value("bias_ps")[:, :, 0])
+            nc.scalar.copy(out=bias[:], in_=value("bias_ps")[:, 0:MT, 0])
             nc.scalar.activation(half_bias[:], value("bias_ps")[:, 0, 0:1], ACT.Copy, scale=0.5)
 
         def w_group(half, engine):
@@ -235,7 +237,7 @@ def tile_groupedmanifoldhyperconnection_kernel(tc, x, gn, phi_bytes, phi_scale, 
             )
 
         def gf_half():
-            nc.scalar.activation(half_gf[:], gf_k[:], ACT.Copy, scale=0.5)
+            nc.scalar.activation(half_gf[:], value("bias_ps")[:, MT:, 0], ACT.Copy, scale=0.5)
 
         def w_quant():
             nc.vector.quantize_mx(out=w_codes[:].bitcast(FP8X4), scales=w_scales[:], in_=value("w_words")[:].rearrange("p n t -> p (n t)"))
@@ -359,18 +361,18 @@ def tile_groupedmanifoldhyperconnection_kernel(tc, x, gn, phi_bytes, phi_scale, 
             nc.tensor.matmul(value("qp", n)[:, cols], ident[:], q[:, cols], start=True, stop=True)
 
         def pre_prod(n, pair, lo, hi, engine):
-            src = xs[n][:, 2 * pair * D : (2 * pair + 2) * D].rearrange("p (a c t) -> p t a c", a=2 * G, t=T)
-            dst = value("pu", n, pair)[:].rearrange("p t r (g c) -> p t (r g) c", g=G)
+            src = xs[n][:, 2 * pair * D : (2 * pair + 2) * D].rearrange("p (a t c) -> p a t c", a=2 * G, t=T)
+            dst = value("pu", n, pair)[:].rearrange("p t r (g c) -> p (r g) t c", g=G)
             gate = gates_of(n, engine)[:, 2 * pair : 2 * pair + 2, :]
             if engine == "gpsimd":
-                weights = spread(spread(gate.rearrange("p r g -> p (r g)")[:, lo:hi], 2, C // T), 1, T)
-                nc.gpsimd.tensor_tensor(out=dst[:, :, lo:hi], in0=src[:, :, lo:hi], in1=weights, op=ALU.mult)
+                weights = spread(spread(gate.rearrange("p r g -> p (r g)")[:, lo:hi], 2, T), 3, C // T)
+                nc.gpsimd.tensor_tensor(out=dst[:, lo:hi], in0=src[:, lo:hi], in1=weights, op=ALU.mult)
             elif engine == "vector":
-                weights = spread(spread(gate[:, lo // G, :], 2, C // T), 1, T)
-                nc.vector.tensor_tensor(out=dst[:, :, lo:hi], in0=src[:, :, lo:hi], in1=weights, op=ALU.mult)
+                weights = spread(spread(gate[:, lo // G, :], 2, T), 3, C // T)
+                nc.vector.tensor_tensor(out=dst[:, lo:hi], in0=src[:, lo:hi], in1=weights, op=ALU.mult)
             else:
                 for a in range(lo, hi):
-                    nc.scalar.activation(dst[:, :, a], src[:, :, a], ACT.Copy, scale=gate[:, a // G, a % G : a % G + 1])
+                    nc.scalar.activation(dst[:, a], src[:, a], ACT.Copy, scale=gate[:, a // G, a % G : a % G + 1])
 
         def u_sum(n, plain):
             for r in range(R):
@@ -486,7 +488,7 @@ def tile_groupedmanifoldhyperconnection_kernel(tc, x, gn, phi_bytes, phi_scale, 
                 bias_turn: lambda: ([], [("bias_ps",)]),
                 bias_read: lambda: ([("bias_ps",)], [("bias",)]),
                 w_group: lambda: ([("w_raw",)], [("w_words",)]),
-                gf_half: lambda: ([], [("half_gf",)]),
+                gf_half: lambda: ([("bias_ps",)], [("half_gf",)]),
                 w_quant: lambda: ([("w_words",)], [("w_codes",)]),
                 x_turn: lambda: ([], [("xp", n, a[0])]),
                 x_gain: lambda: ([("xp", n, a[0])], [("xn", xb)]),
@@ -566,13 +568,13 @@ def tile_groupedmanifoldhyperconnection_kernel(tc, x, gn, phi_bytes, phi_scale, 
         def when(n, *steps):
             return list(steps) if 0 <= n < NT else []
 
-        G_FROM = [G, 4] + [HALF] * (NT - 3)
-        V_LOW = [HALF, HALF] + [6] * (NT - 4) + [HALF]
+        G_FROM = [G, 4] + [6] * (NT - 3)
+        V_LOW = [HALF, HALF] + [4] * (NT - 4) + [HALF]
         Q_COLS = [(G + HALF, 4 * G)] + [(2 * G, 4 * G)] * (NT - 1)
         M0, M1, M2, RELU, SQUARE = 4, 12, 22, 2, 9
         QUANT_AT = {2: 1}
         WARM = [(warm, m, 2) for m in range(5)]
-        PAIR = {(0, 0): (2, 0)}
+        PAIR = {(0, 0): (2, 0), (5, 0): (0, 1), (6, 0): (0, 1)}
         EXTRA_T = {0: [usum(5)], 1: [usum(7)]}
         EXTRA_V = {(0, 0): [(u_gain, 4)], (0, 1): [(u_gain, 6)], (0, 3): [unit(0, 1, HALF, G, V)], (1, 1): [(u_gain, 5)]}
         EXTRA_S = {1: pre_s(7, 1)}
@@ -594,13 +596,13 @@ def tile_groupedmanifoldhyperconnection_kernel(tc, x, gn, phi_bytes, phi_scale, 
         vector += [pre_v(6, 1, 1)]
 
         scalar += [(phi_widen, 0, S, 0, T), (phi_widen, 2, S, 0, T)] + [(phi_group, r, True, S) for r in range(R)]
-        scalar += [(bias_read,), (gate_tanh, 0), (w_group, 0, S), (gate_tanh, 1), (gf_half,)] + pre_s(0, 0, G) + [(w_group, 1, S), (logit_exp, 0), (logit_exp, 1)]
+        scalar += [(bias_read,), (gf_half,), (gate_tanh, 0), (w_group, 0, S), (gate_tanh, 1)] + pre_s(0, 0, G) + [(w_group, 1, S), (logit_exp, 0), (logit_exp, 1)]
         scalar += pre_s(0, 1, 0, G) + [(gate_tanh, 2)] + pre_s(0, 1, G) + [(logit_exp, 2)] + pre_s(1, 1) + [(gate_tanh, 3)] + pre_s(2, 1, 0, G)
         scalar += [(logit_exp, 3)] + pre_s(2, 1, G) + [(gate_tanh, 4), (logit_exp, 4), (gate_tanh, 5), (gate_one, 4), (logit_exp, 5)]
-        work = pre_s(3, 1) + pre_s(4, 1) + pre_s(5, 1)
+        work = pre_s(3, 1) + pre_s(4, 1) + pre_s(5, 1, G)
         scalar += deal(work, *inverse(0, 2, 0) + inverse(1, 0, 1) + inverse(1, 1, 7) + inverse(1, 2, 14) + inverse(0, 3, 17))
 
-        gpsimd += [pre_g(0, 0, 0, G), pre_g(1, 0), pre_g(2, 0), pre_g(4, 0), pre_g(3, 0), pre_g(5, 0), (sink_last, 0)]
+        gpsimd += [pre_g(0, 0, 0, G), pre_g(1, 0), pre_g(2, 0), pre_g(4, 0), pre_g(3, 0), pre_g(5, 0), pre_g(5, 1, 0, G), (sink_last, 0)]
 
         for k in range(NT - 1):
             near, far = k + 1, k + 2

@@ -35,6 +35,7 @@ U_BATCHES = ((0, 4), (4, 8))
 X_BATCHES = ((0, 1), (1, 2), (2, 4), (4, 6), (6, 7), (7, 8))
 OWN_GATES = 4
 WHOLE = 2
+ORDER = (2, 3, BRANCH, 0, 1)
 LATE_PRE = (4, 1)
 FLOPS = 2 * TOK * R * D * M + 2 * TOK * D * D
 
@@ -321,10 +322,10 @@ def tile_groupedmanifoldhyperconnection_kernel(tc, x, gn, phi_bytes, phi_scale, 
             for m in range(2):
                 nc.scalar.activation(value("co", b)[:, m, :], value("tl", b)[:, m, :], ACT.Exp, bias=bias[:, 1 + m : 2 + m])
 
-        def e_turn(n, plain):
+        def e_turn(n, lo, hi, plain):
             b, k = xb_of[n]
-            for m in range(2):
-                turn(value("ct", n)[:, m * P : (m + 1) * P], value("co", b)[:, m, k * P : (k + 1) * P], True, True, m >= 2 - plain)
+            for m in range(lo, hi):
+                turn(value("ct", n)[:, m * P : (m + 1) * P], value("co", b)[:, m, k * P : (k + 1) * P], True, True, plain)
 
         def e_of(n):
             return value("ct", n)[:].rearrange("p (g i j) -> p g i j", i=R, j=R)
@@ -436,13 +437,14 @@ def tile_groupedmanifoldhyperconnection_kernel(tc, x, gn, phi_bytes, phi_scale, 
                 multiply = nc.vector.tensor_tensor if engine == "vector" else nc.gpsimd.tensor_tensor
                 multiply(out=dst, in0=spread(src, 2, R), in1=spread(weight, 3, C), op=ALU.mult)
 
-        def y_sum(n, a, order, plain):
-            for m, j in enumerate(order):
+        def y_sum(n, a, lo, hi, plain):
+            for m in range(lo, hi):
+                j = ORDER[m]
                 for b in range(QUAD):
                     g = QUAD - 1 - b
                     src = term(n, j, QUAD * a, QUAD * (a + 1))[:, g].rearrange("p i c -> p (i c)")
                     first, last = m == 0 and b == 0, m == BRANCH and b == QUAD - 1
-                    turn(value("yt", n, a)[:, :, g, :], src, first, last, QUAD * m + b < plain[0] or QUAD * m + b >= QUAD * (BRANCH + 1) - plain[1])
+                    turn(value("yt", n, a)[:, :, g, :], src, first, last, QUAD * (m - lo) + b < plain[0] or QUAD * (hi - m) - b <= plain[1])
 
         def y_out(n, a):
             yo = value("yo", n, a)
@@ -519,9 +521,9 @@ def tile_groupedmanifoldhyperconnection_kernel(tc, x, gn, phi_bytes, phi_scale, 
                     [("f", n), ("gate", xb)] if a[0] == BRANCH else [("qp", n)] if a[3] == "vector" else [("q", n)],
                     [home(n, a[0], a[1])] + [("part", n, a[0], quad) for quad in range(a[1] // QUAD, (a[2] - 1) // QUAD + 1)],
                 ),
-                y_sum: lambda: (parts(n, range(BRANCH + 1), a[0]), [("yt", n, a[0])]),
-                y_add: lambda: (parts(n, a[1:3], a[0]), [("added", n, a[0])]),
-                y_add_out: lambda: (parts(n, a[1:3], a[0]) + [("added", n, a[0])], [("yo", n, a[0])]),
+                y_sum: lambda: (parts(n, ORDER[a[1] : a[2]], a[0]), [("yt", n, a[0])]),
+                y_add: lambda: (parts(n, a[1:3], a[0]), [("added", n)]),
+                y_add_out: lambda: (parts(n, a[1:3], a[0]) + [("added", n)], [("yo", n, a[0])]),
                 y_store: lambda: ([("yo", n, a[0])], []),
                 y_out: lambda: ([("yt", n, a[0])], [("yo", n, a[0])]),
             }
@@ -529,7 +531,6 @@ def tile_groupedmanifoldhyperconnection_kernel(tc, x, gn, phi_bytes, phi_scale, 
 
         V, S, GP = "vector", "scalar", "gpsimd"
         tensor, vector, scalar, gpsimd = [], [], [], []
-        ORDER = (2, 3, BRANCH, 0, 1)
 
         def turns(*ns):
             return [(x_turn, n, pair) for n in ns for pair in range(2)]
@@ -568,23 +569,21 @@ def tile_groupedmanifoldhyperconnection_kernel(tc, x, gn, phi_bytes, phi_scale, 
         def when(n, *steps):
             return list(steps) if 0 <= n < NT else []
 
-        G_FROM = [G, 4] + [6] * (NT - 3)
-        V_LOW = [HALF, HALF] + [4] * (NT - 4) + [HALF]
-        Q_COLS = [(G + HALF, 4 * G)] + [(2 * G, 4 * G)] * (NT - 1)
+        G_FROM = [HALF, 4] + [HALF] * (NT - 3)
+        V_LOW = [HALF] * 2 + [7] * (NT - 4) + [HALF]
+        Q_COLS = [(2 * G, 4 * G)] * NT
         M0, M1, M2, RELU, SQUARE = 4, 12, 22, 2, 9
         QUANT_AT = {2: 1}
-        WARM = [(warm, m, 2) for m in range(5)]
-        PAIR = {(0, 0): (2, 0), (5, 0): (0, 1), (6, 0): (0, 1)}
-        EXTRA_T = {0: [usum(5)], 1: [usum(7)]}
-        EXTRA_V = {(0, 0): [(u_gain, 4)], (0, 1): [(u_gain, 6)], (0, 3): [unit(0, 1, HALF, G, V)], (1, 1): [(u_gain, 5)]}
+        WARM = [(warm, m, 2) for m in range(4)]
+        EXTRA_T = {1: [usum(7)]}
+        EXTRA_V = {(0, 0): [(u_gain, 4)], (0, 1): [(u_gain, 5)], (0, 2): [(u_gain, 6)]}
         EXTRA_S = {1: pre_s(7, 1)}
-        EXTRA_G = {0: [pre_g(7, 0)]}
-        tensor += WARM[0:3] + turns(0) + WARM[3:4] + turns(1) + [(bias_turn,)] + WARM[4:5] + turns(2)
-        tensor += [(gate_mm, 0)] + turns(3) + [(gate_turn, 0, True), (gate_mm, 1)] + turns(4)
-        tensor += [(gate_turn, 1, True), (logit_mm, 0, 0, R), (logit_mm, 1, 0, R)] + turns(5) + [(e_turn, 0, 0), (gate_mm, 2), (logit_mm, 2, 0, R)]
+        tensor += WARM[0:2] + turns(0) + WARM[2:3] + turns(1) + [(bias_turn,)] + WARM[3:4]
+        tensor += [(gate_mm, 0)] + turns(2, 3) + [(gate_turn, 0, True), (gate_mm, 1)] + turns(4)
+        tensor += [(gate_turn, 1, False), (logit_mm, 0, 0, R), (logit_mm, 1, 0, R)] + turns(5) + [(e_turn, 0, 0, 2, False), (gate_mm, 2), (logit_mm, 2, 0, R)]
         tensor += turns(6) + [(gate_turn, 2, False)] + turns(7) + [(gate_mm, 3), (logit_mm, 3, 0, R), (gate_turn, 3, False), usum(0)]
-        tensor += [(gate_mm, 4), (logit_mm, 4, 0, R), (gate_mm, 5), (logit_mm, 5, 0, R), (e_turn, 1, 0), (gate_turn, 4, False), (gate_turn, 5, False), usum(1)]
-        tensor += [(e_turn, 2, 0), usum(2), usum(3, (2, 0)), usum(4), (branch_mm, 0), (q_to_psum, 0) + Q_COLS[0], (branch_mm, 1), usum(6)]
+        tensor += [(gate_mm, 4), (logit_mm, 4, 0, R), (gate_mm, 5), (logit_mm, 5, 0, R), (e_turn, 1, 0, 2, False), (gate_turn, 4, False), (gate_turn, 5, False), usum(1)]
+        tensor += [(e_turn, 2, 0, 2, False), usum(2), usum(3, (2, 0)), usum(4), (branch_mm, 0), (q_to_psum, 0) + Q_COLS[0], (branch_mm, 1), usum(5), usum(6)]
 
         vector += [(phi_widen, 1, V, 0, T), (phi_widen, 3, V, 0, T), (phi_group, 0, False, V), (phi_group, 1, False, V), (phi_group, 3, False, V)]
         vector += [(x_gain, 0, 0), (phi_group, 2, False, V), (x_gain, 0, 1), (gate_quant,), (x_quant, 0)]
@@ -592,40 +591,47 @@ def tile_groupedmanifoldhyperconnection_kernel(tc, x, gn, phi_bytes, phi_scale, 
         vector += gains(3) + [(x_quant, 2), (gate_copy, 1, V)] + gains(4, 5) + [(sink_sum, 0, 0), (x_quant, 3), (sink_recip, 0, 0), (gate_copy, 2, V)]
         vector += gains(6) + [(x_gain, 7, 0), (sink_scale, 0, 0), (x_gain, 7, 1), (x_quant, 4), (x_quant, 5), (w_quant,), (sink_sum, 0, 1), (gate_copy, 3, V)]
         vector += [(sink_recip, 0, 1), (u_gain, 0), (sink_scale, 0, 1), (sink_sum, 1, 0), (sink_sum, 0, 2), pre_v(6, 0, 0), (gate_copy, 5, V), pre_v(6, 0, 1), (sink_scale, 0, 2), (sink_scale, 1, 0)]
-        vector += [(u_gain, 1), (sink_sum, 1, 1), (u_gain, 2), (sink_scale, 1, 1), (gate_copy, 4, V), (sink_sum, 1, 2), pre_v(6, 1, 0), (u_gain, 3), (sink_sum, 0, 3), (u_quant, 0)]
+        vector += [(u_gain, 1), (sink_sum, 1, 1), (u_gain, 2), (gate_copy, 4, V), (sink_scale, 1, 1), (u_gain, 3), (sink_sum, 0, 3), (u_quant, 0), (sink_sum, 1, 2), pre_v(6, 1, 0)]
         vector += [pre_v(6, 1, 1)]
 
         scalar += [(phi_widen, 0, S, 0, T), (phi_widen, 2, S, 0, T)] + [(phi_group, r, True, S) for r in range(R)]
         scalar += [(bias_read,), (gf_half,), (gate_tanh, 0), (w_group, 0, S), (gate_tanh, 1)] + pre_s(0, 0, G) + [(w_group, 1, S), (logit_exp, 0), (logit_exp, 1)]
-        scalar += pre_s(0, 1, 0, G) + [(gate_tanh, 2)] + pre_s(0, 1, G) + [(logit_exp, 2)] + pre_s(1, 1) + [(gate_tanh, 3)] + pre_s(2, 1, 0, G)
-        scalar += [(logit_exp, 3)] + pre_s(2, 1, G) + [(gate_tanh, 4), (logit_exp, 4), (gate_tanh, 5), (gate_one, 4), (logit_exp, 5)]
-        work = pre_s(3, 1) + pre_s(4, 1) + pre_s(5, 1, G)
-        scalar += deal(work, *inverse(0, 2, 0) + inverse(1, 0, 1) + inverse(1, 1, 7) + inverse(1, 2, 14) + inverse(0, 3, 17))
+        scalar += pre_s(0, 1) + [(gate_tanh, 2)] + pre_s(1, 1, 0, G) + [(logit_exp, 2)] + pre_s(1, 1, G) + pre_s(2, 1, 0, G) + [(gate_tanh, 3)] + pre_s(2, 1, G)
+        scalar += [(logit_exp, 3)] + pre_s(3, 1, 0, 24) + [(gate_tanh, 4)] + pre_s(3, 1, 24) + [(logit_exp, 4), (gate_tanh, 5), (gate_one, 4), (logit_exp, 5)]
+        work = pre_s(4, 1) + pre_s(5, 1)
+        scalar += deal(work, *inverse(0, 2, 0) + inverse(1, 0, 1) + inverse(1, 1, 6) + inverse(0, 3, 12) + inverse(1, 2, 13))
 
-        gpsimd += [pre_g(0, 0, 0, G), pre_g(1, 0), pre_g(2, 0), pre_g(4, 0), pre_g(3, 0), pre_g(5, 0), pre_g(5, 1, 0, G), (sink_last, 0)]
+        gpsimd += [pre_g(0, 0, 0, G), pre_g(1, 0), pre_g(2, 0), pre_g(4, 0), pre_g(3, 0), pre_g(5, 0), pre_g(7, 0), (sink_last, 0)]
 
         for k in range(NT - 1):
             near, far = k + 1, k + 2
-            banks = [(y_sum, k, a, ORDER, PAIR.get((k, a), (0, 0))) for a in range(NQ)]
-            tensor += banks[:1] + when(k + 3, (e_turn, k + 3, 1)) + [(q_to_psum, near) + Q_COLS[near]] + when(far, (branch_mm, far)) + banks[1:2] + EXTRA_T.get(k, []) + banks[2:]
+            banks = [(y_sum, k, a, 0, len(ORDER), (0, 0)) for a in range(NQ)]
+            tensor += banks[:1] + when(k + 3, (e_turn, k + 3, 0, 1, False)) + [(y_sum, k, 1, 0, 1, (0, int(k + 3 >= NT)))] + when(far, (branch_mm, far))
+            tensor += when(k + 3, (e_turn, k + 3, 1, 2, True)) + [(q_to_psum, near) + Q_COLS[near], (y_sum, k, 1, 1, len(ORDER), (0, 0))]
+            tensor += EXTRA_T.get(k, []) + banks[2:]
             back = [when(k - 1, (y_out, k - 1, a)) + EXTRA_V.get((k, a), []) for a in range(NQ)]
+            first, then = [unit(k, 2, 0, HALF, V)], [unit(k, 3, 0, V_LOW[k], V)]
+            if k < 2:
+                first, then = [[unit(k, j, lo, lo + QUAD, V) for j in (2, 3)] for lo in (0, QUAD)]
+            if k == 1:
+                back = [back[0] + back[1], [], back[2], back[3]]
             last_sum = [(sink_sum, near, 3)]
-            vector += [(sink_scale, near, 2)] + back[0] + when(far, (sink_sum, far, 0)) + last_sum * (k not in QUANT_AT) + [unit(k, 2, 0, HALF, V)]
-            vector += when(far, (sink_scale, far, 0)) + [unit(k, 3, 0, V_LOW[k], V)] + when(far, (sink_sum, far, 1)) + back[1] + ([(u_gain, NT - 1)] + last_sum + [(u_quant, 1)]) * (k in QUANT_AT) + [unit(k, 2, HALF, G, V)]
+            vector += [(sink_scale, near, 2)] + back[0] + when(far, (sink_sum, far, 0)) + last_sum * (k not in QUANT_AT) + first
+            vector += when(far, (sink_scale, far, 0)) + back[1] + when(far, (sink_sum, far, 1)) + then + ([(u_gain, NT - 1)] + last_sum + [(u_quant, QUANT_AT.get(k))]) * (k in QUANT_AT) + [unit(k, 2, HALF, G, V)]
             vector += when(far, (sink_scale, far, 1)) + back[2] + when(far, (sink_sum, far, 2)) + [unit(k, 3, HALF, G, V)] + back[3]
             work = unit_s(k, 1, 0, QUAD) + unit_s(k, BRANCH, 0, HALF) + unit_s(k, 1, QUAD, min(G_FROM[k], HALF))
-            work = work + unit_s(k, 3, V_LOW[k], HALF) + unit_s(k, BRANCH, HALF, G) + EXTRA_S.get(k, [])
+            work = work + unit_s(k, 3, V_LOW[k], HALF) + EXTRA_S.get(k, []) + unit_s(k, BRANCH, HALF, G)
             marks = when(far, *inverse(far, 0, M0)) + inverse(near, 3, M0 + 2 if k not in QUANT_AT else M1 + 3) + [(RELU if k else SQUARE, (branch_relu, near)), (SQUARE if k else 2 * SQUARE, (branch_square, near))]
             marks = [(1, (branch_relu, 0)), (2, (branch_square, 0))] * (k == 0) + marks
-            marks = marks + when(far, *inverse(far, 1, M1) + inverse(far, 2, M2))
+            marks = marks + when(far, *inverse(far, 1, M1) + inverse(far, 2, M2 + len(work) - 25 - 2 * (k == 0)))
             scalar += deal(work, *marks)
             second = [unit(k, 1, G_FROM[k], G, GP)] * (G_FROM[k] < G)
-            gpsimd += [unit(k, 0, 0, G, GP)] + second * (k in QUANT_AT) + [(sink_last, near)] + second * (k not in QUANT_AT) + EXTRA_G.get(k, [])
+            gpsimd += ([unit(k, 0, 0, G, GP)] if k else [unit(k, 0, 0, QUAD, GP), unit(k, 0, QUAD, G, GP)]) + second * (k in QUANT_AT) + [(sink_last, near)] + second * (k not in QUANT_AT)
 
         k, last = NT - 1, NQ - 1
-        tensor += [(y_sum, k, a, ORDER, (0, 0)) for a in range(last)]
+        tensor += [(y_sum, k, a, 0, len(ORDER), (0, 0)) for a in range(last)]
         outs = [(y_out, k - 1, a) for a in range(NQ)] + [(y_out, k, a) for a in range(last)]
-        vector += [unit(k, 2, 0, HALF, V), outs[0], unit(k, 3, 0, HALF, V), outs[1], unit(k, 2, HALF, G, V), outs[2], unit(k, 3, HALF, G, V), outs[3]]
+        vector += [outs[0], unit(k, 2, 0, HALF, V), outs[1], unit(k, 3, 0, HALF, V), outs[2], unit(k, 2, HALF, G, V), unit(k, 3, HALF, G, V), outs[3]]
         vector += [outs[4], (y_add, k, last, 2, 3, V), outs[5], (y_add, k, last, 2, BRANCH, V), (y_add_out, k, last, 0, 2), (y_store, k, last), outs[6]]
         scalar += [s for a in range(NQ) for j in (BRANCH, 1)[: 1 + (a < last)] for s in unit_s(k, j, QUAD * a, QUAD * a + QUAD)]
         gpsimd += [unit(k, 0, 0, HALF, GP), unit(k, 0, HALF, G, GP), unit(k, 1, QUAD * last, G, GP), (y_add, k, last, 0, 1, GP)]

@@ -43,7 +43,6 @@ BANKS = {"four": 4, "b0": 1, "b1": 1, "b2": 1, "b3": 1}
 KINDS = {
     "wide": ([P, T, M], BF16, "yo", 4),
     "bias_ps": ([P, MT + T, 2], F32, "b2", 1),
-    "warm": ([P, 2, P], F32, "b0", 1),
     "gate_words": ([P, R, P, T], BF16, "late", 7),
     "logit_words": ([P, 2, 2 * P, T], BF16, "late", 7),
     "w_words": ([P, D, T], BF16, "late", 7),
@@ -188,9 +187,6 @@ def tile_groupedmanifoldhyperconnection_kernel(tc, x, gn, phi_bytes, phi_scale, 
 
         def turn(dst, src, start, stop, plain):
             nc.tensor.matmul(dst, src, ident[:], start=start, stop=stop, is_transpose=not plain)
-
-        def warm(m, width):
-            nc.tensor.matmul(value("warm")[:, 0:width], ident[:], spread(ident[:], 1, width), start=True, stop=True)
 
         def phi_widen(r, engine, lo, hi):
             for t in range(lo, hi):
@@ -482,7 +478,6 @@ def tile_groupedmanifoldhyperconnection_kernel(tc, x, gn, phi_bytes, phi_scale, 
         def uses(fn, n=0, *a):
             xb = xb_of[n][0]
             table = {
-                warm: lambda: ([], [("warm",)]),
                 phi_widen: lambda: ([], [("wide", n)]),
                 phi_group: lambda: ([("wide", n)], [("logit_words", n // 2) if a[0] else ("gate_words",)]),
                 gate_quant: lambda: ([("gate_words",)], [("gate_codes",)]),
@@ -574,11 +569,10 @@ def tile_groupedmanifoldhyperconnection_kernel(tc, x, gn, phi_bytes, phi_scale, 
         Q_COLS = [(2 * G, 4 * G)] * NT
         M0, M1, M2, RELU, SQUARE = 4, 12, 22, 2, 9
         QUANT_AT = {2: 1}
-        WARM = [(warm, m, 2) for m in range(4)]
         EXTRA_T = {1: [usum(7)]}
         EXTRA_V = {(0, 0): [(u_gain, 4)], (0, 1): [(u_gain, 5)], (0, 2): [(u_gain, 6)]}
         EXTRA_S = {1: pre_s(7, 1)}
-        tensor += WARM[0:2] + turns(0) + WARM[2:3] + turns(1) + [(bias_turn,)] + WARM[3:4]
+        tensor += turns(0) + turns(1) + [(bias_turn,)]
         tensor += [(gate_mm, 0)] + turns(2, 3) + [(gate_turn, 0, True), (gate_mm, 1)] + turns(4)
         tensor += [(gate_turn, 1, False), (logit_mm, 0, 0, R), (logit_mm, 1, 0, R)] + turns(5) + [(e_turn, 0, 0, 2, False), (gate_mm, 2), (logit_mm, 2, 0, R)]
         tensor += turns(6) + [(gate_turn, 2, False)] + turns(7) + [(gate_mm, 3), (logit_mm, 3, 0, R), (gate_turn, 3, False), usum(0)]

@@ -35,7 +35,7 @@ U_BATCHES = ((0, 4), (4, 8))
 X_BATCHES = ((0, 1), (1, 2), (2, 4), (4, 6), (6, 7), (7, 8))
 OWN_GATES = 4
 WHOLE = 2
-ORDER = (2, 3, BRANCH, 0, 1)
+ORDERS = ((2, 1, BRANCH, 3, 0), (2, BRANCH, 3, 0, 1), (2, 0, BRANCH, 3, 1), (2, 0, BRANCH, 3, 1))
 LATE_PRE = (4, 1)
 FLOPS = 2 * TOK * R * D * M + 2 * TOK * D * D
 
@@ -435,7 +435,7 @@ def tile_groupedmanifoldhyperconnection_kernel(tc, x, gn, phi_bytes, phi_scale, 
 
         def y_sum(n, a, lo, hi, plain):
             for m in range(lo, hi):
-                j = ORDER[m]
+                j = ORDERS[a][m]
                 for b in range(QUAD):
                     g = QUAD - 1 - b
                     src = term(n, j, QUAD * a, QUAD * (a + 1))[:, g].rearrange("p i c -> p (i c)")
@@ -516,7 +516,7 @@ def tile_groupedmanifoldhyperconnection_kernel(tc, x, gn, phi_bytes, phi_scale, 
                     [("f", n), ("gate", xb)] if a[0] == BRANCH else [("qp", n)] if a[3] == "vector" else [("q", n)],
                     [home(n, a[0], a[1])] + [("part", n, a[0], quad) for quad in range(a[1] // QUAD, (a[2] - 1) // QUAD + 1)],
                 ),
-                y_sum: lambda: (parts(n, ORDER[a[1] : a[2]], a[0]), [("yt", n, a[0])]),
+                y_sum: lambda: (parts(n, ORDERS[a[0]][a[1] : a[2]], a[0]), [("yt", n, a[0])]),
                 y_add: lambda: (parts(n, a[1:3], a[0]), [("added", n)]),
                 y_add_out: lambda: (parts(n, a[1:3], a[0]) + [("added", n)], [("yo", n, a[0])]),
                 y_store: lambda: ([("yo", n, a[0])], []),
@@ -564,51 +564,52 @@ def tile_groupedmanifoldhyperconnection_kernel(tc, x, gn, phi_bytes, phi_scale, 
         def when(n, *steps):
             return list(steps) if 0 <= n < NT else []
 
-        G_FROM = [HALF, 4] + [HALF] * (NT - 3)
-        V_LOW = [HALF] * 2 + [7] * (NT - 4) + [HALF]
-        Q_COLS = [(2 * G, 4 * G)] * NT
+        G_FROM = [G, 4] + [HALF] * (NT - 3)
+        V_LOW = [HALF, HALF] + [7] * (NT - 4) + [HALF]
+        Q_COLS = [(G + HALF, 4 * G)] + [(2 * G, 4 * G)] * (NT - 1)
         M0, M1, M2, RELU, SQUARE = 4, 12, 22, 2, 9
         QUANT_AT = {2: 1}
         EXTRA_T = {1: [usum(7)]}
-        EXTRA_V = {(0, 0): [(u_gain, 4)], (0, 1): [(u_gain, 5)], (0, 2): [(u_gain, 6)]}
+        EXTRA_V = {(0, 0): [(u_gain, 4)], (0, 2): [(u_gain, 6)], (0, 3): [(y_out, 0, 0), unit(0, 1, HALF, G, V)]}
         EXTRA_S = {1: pre_s(7, 1)}
         tensor += turns(0) + turns(1) + [(bias_turn,)]
         tensor += [(gate_mm, 0)] + turns(2, 3) + [(gate_turn, 0, True), (gate_mm, 1)] + turns(4)
         tensor += [(gate_turn, 1, False), (logit_mm, 0, 0, R), (logit_mm, 1, 0, R)] + turns(5) + [(e_turn, 0, 0, 2, False), (gate_mm, 2), (logit_mm, 2, 0, R)]
-        tensor += turns(6) + [(gate_turn, 2, False)] + turns(7) + [(gate_mm, 3), (logit_mm, 3, 0, R), (gate_turn, 3, False), usum(0)]
-        tensor += [(gate_mm, 4), (logit_mm, 4, 0, R), (gate_mm, 5), (logit_mm, 5, 0, R), (e_turn, 1, 0, 2, False), (gate_turn, 4, False), (gate_turn, 5, False), usum(1)]
-        tensor += [(e_turn, 2, 0, 2, False), usum(2), usum(3, (2, 0)), usum(4), (branch_mm, 0), (q_to_psum, 0) + Q_COLS[0], (branch_mm, 1), usum(5), usum(6)]
+        tensor += turns(6) + [(gate_turn, 2, False)] + turns(7) + [(gate_mm, 3), (logit_mm, 3, 0, R), (gate_turn, 3, False), usum(0), (e_turn, 1, 0, 2, False)]
+        tensor += [(gate_mm, 4), (logit_mm, 4, 0, R), (gate_mm, 5), (logit_mm, 5, 0, R), (gate_turn, 4, False), usum(1), (gate_turn, 5, False)]
+        tensor += [usum(2), (e_turn, 2, 0, 2, False), usum(3), usum(4), (branch_mm, 0), (q_to_psum, 0) + Q_COLS[0], (branch_mm, 1), usum(5, (1, 0)), usum(6)]
 
         vector += [(phi_widen, 1, V, 0, T), (phi_widen, 3, V, 0, T), (phi_group, 0, False, V), (phi_group, 1, False, V), (phi_group, 3, False, V)]
         vector += [(x_gain, 0, 0), (phi_group, 2, False, V), (x_gain, 0, 1), (gate_quant,), (x_quant, 0)]
         vector += gains(1) + [(logit_quant, 0), (x_quant, 1)] + gains(2) + [(logit_quant, 1), (gate_copy, 0, V)]
-        vector += gains(3) + [(x_quant, 2), (gate_copy, 1, V)] + gains(4, 5) + [(sink_sum, 0, 0), (x_quant, 3), (sink_recip, 0, 0), (gate_copy, 2, V)]
-        vector += gains(6) + [(x_gain, 7, 0), (sink_scale, 0, 0), (x_gain, 7, 1), (x_quant, 4), (x_quant, 5), (w_quant,), (sink_sum, 0, 1), (gate_copy, 3, V)]
-        vector += [(sink_recip, 0, 1), (u_gain, 0), (sink_scale, 0, 1), (sink_sum, 1, 0), (sink_sum, 0, 2), pre_v(6, 0, 0), (gate_copy, 5, V), pre_v(6, 0, 1), (sink_scale, 0, 2), (sink_scale, 1, 0)]
-        vector += [(u_gain, 1), (sink_sum, 1, 1), (u_gain, 2), (gate_copy, 4, V), (sink_scale, 1, 1), (u_gain, 3), (sink_sum, 0, 3), (u_quant, 0), (sink_sum, 1, 2), pre_v(6, 1, 0)]
-        vector += [pre_v(6, 1, 1)]
+        vector += gains(3) + [(x_quant, 2), (gate_copy, 1, V)] + gains(4, 5) + [(sink_sum, 0, 0), (x_quant, 3), (gate_copy, 2, V)]
+        vector += gains(6, 7) + [(x_quant, 4), (x_quant, 5), (w_quant,), (gate_copy, 3, V), (sink_recip, 0, 0), (u_gain, 0), (sink_scale, 0, 0), (sink_sum, 1, 0), (sink_sum, 0, 1)]
+        vector += [(sink_recip, 1, 0), (sink_recip, 0, 1), (sink_scale, 1, 0), (sink_scale, 0, 1), (sink_sum, 1, 1), (sink_sum, 0, 2), (gate_copy, 4, V), (u_gain, 1), (gate_copy, 5, V)]
+        vector += [(sink_scale, 0, 2), (u_gain, 2), (sink_scale, 1, 1), (u_gain, 3), (sink_sum, 0, 3), (u_quant, 0), (sink_sum, 1, 2), pre_v(6, 1, 0), pre_v(6, 1, 1)]
 
         scalar += [(phi_widen, 0, S, 0, T), (phi_widen, 2, S, 0, T)] + [(phi_group, r, True, S) for r in range(R)]
-        scalar += [(bias_read,), (gf_half,), (gate_tanh, 0), (w_group, 0, S), (gate_tanh, 1)] + pre_s(0, 0, G) + [(w_group, 1, S), (logit_exp, 0), (logit_exp, 1)]
-        scalar += pre_s(0, 1) + [(gate_tanh, 2)] + pre_s(1, 1, 0, G) + [(logit_exp, 2)] + pre_s(1, 1, G) + pre_s(2, 1, 0, G) + [(gate_tanh, 3)] + pre_s(2, 1, G)
-        scalar += [(logit_exp, 3)] + pre_s(3, 1, 0, 24) + [(gate_tanh, 4)] + pre_s(3, 1, 24) + [(logit_exp, 4), (gate_tanh, 5), (gate_one, 4), (logit_exp, 5)]
+        scalar += [(bias_read,), (gf_half,), (gate_tanh, 0), (w_group, 0, S), (w_group, 1, S), (gate_tanh, 1)] + pre_s(0, 0, G) + pre_s(0, 1, 0, G) + [(logit_exp, 0), (logit_exp, 1)]
+        scalar += pre_s(0, 1, G) + pre_s(1, 1, HALF, G) + [(gate_tanh, 2)] + pre_s(1, 1, G) + [(logit_exp, 2)] + pre_s(2, 1) + [(gate_tanh, 3)] + pre_s(3, 0, HALF)
+        scalar += [(logit_exp, 3)] + pre_s(3, 1, 0, 24) + [(gate_tanh, 4)] + pre_s(3, 1, 24) + [(logit_exp, 4), (gate_one, 4), (gate_tanh, 5), (logit_exp, 5)]
         work = pre_s(4, 1) + pre_s(5, 1)
-        scalar += deal(work, *inverse(0, 2, 0) + inverse(1, 0, 1) + inverse(1, 1, 6) + inverse(0, 3, 12) + inverse(1, 2, 13))
+        scalar += deal(work, *inverse(0, 2, 0) + inverse(1, 1, 1) + inverse(0, 3, 12) + inverse(1, 2, 14))
 
-        gpsimd += [pre_g(0, 0, 0, G), pre_g(1, 0), pre_g(2, 0), pre_g(4, 0), pre_g(3, 0), pre_g(5, 0), pre_g(7, 0), (sink_last, 0)]
+        gpsimd += [pre_g(0, 0, 0, G), pre_g(1, 0), pre_g(1, 1, 0, HALF), pre_g(2, 0), pre_g(3, 0, 0, HALF), pre_g(4, 0), pre_g(5, 0), pre_g(6, 0), (sink_last, 0)]
 
         for k in range(NT - 1):
             near, far = k + 1, k + 2
-            banks = [(y_sum, k, a, 0, len(ORDER), (0, 0)) for a in range(NQ)]
-            tensor += banks[:1] + when(k + 3, (e_turn, k + 3, 0, 1, False)) + [(y_sum, k, 1, 0, 1, (0, int(k + 3 >= NT)))] + when(far, (branch_mm, far))
-            tensor += when(k + 3, (e_turn, k + 3, 1, 2, True)) + [(q_to_psum, near) + Q_COLS[near], (y_sum, k, 1, 1, len(ORDER), (0, 0))]
+            banks = [(y_sum, k, a, 0, BRANCH + 1, (0, 0)) for a in range(NQ)]
+            tensor += [(q_to_psum, near) + Q_COLS[near]] * (near == NT - 1) + banks[:1] + when(k + 3, (e_turn, k + 3, 0, 1, False)) + [(y_sum, k, 1, 0, 1, (0, int(k + 3 == NT)))] + when(far, (branch_mm, far))
+            tensor += when(k + 3, (e_turn, k + 3, 1, 2, True)) + [(q_to_psum, near) + Q_COLS[near]] * (near < NT - 1) + [(y_sum, k, 1, 1, BRANCH + 1, (0, 0))]
             tensor += EXTRA_T.get(k, []) + banks[2:]
             back = [when(k - 1, (y_out, k - 1, a)) + EXTRA_V.get((k, a), []) for a in range(NQ)]
             first, then = [unit(k, 2, 0, HALF, V)], [unit(k, 3, 0, V_LOW[k], V)]
             if k < 2:
-                first, then = [[unit(k, j, lo, lo + QUAD, V) for j in (2, 3)] for lo in (0, QUAD)]
+                first, then = [unit(k, 2, 0, QUAD, V), unit(k, 3, 0, QUAD, V)], [unit(k, 2, QUAD, HALF, V), unit(k, 3, QUAD, V_LOW[k], V)]
+            if k == 0:
+                then = then + [(u_gain, 5)]
             if k == 1:
-                back = [back[0] + back[1], [], back[2], back[3]]
+                back = [back[1], [], back[2], back[3]]
             last_sum = [(sink_sum, near, 3)]
             vector += [(sink_scale, near, 2)] + back[0] + when(far, (sink_sum, far, 0)) + last_sum * (k not in QUANT_AT) + first
             vector += when(far, (sink_scale, far, 0)) + back[1] + when(far, (sink_sum, far, 1)) + then + ([(u_gain, NT - 1)] + last_sum + [(u_quant, QUANT_AT.get(k))]) * (k in QUANT_AT) + [unit(k, 2, HALF, G, V)]
@@ -617,13 +618,13 @@ def tile_groupedmanifoldhyperconnection_kernel(tc, x, gn, phi_bytes, phi_scale, 
             work = work + unit_s(k, 3, V_LOW[k], HALF) + EXTRA_S.get(k, []) + unit_s(k, BRANCH, HALF, G)
             marks = when(far, *inverse(far, 0, M0)) + inverse(near, 3, M0 + 2 if k not in QUANT_AT else M1 + 3) + [(RELU if k else SQUARE, (branch_relu, near)), (SQUARE if k else 2 * SQUARE, (branch_square, near))]
             marks = [(1, (branch_relu, 0)), (2, (branch_square, 0))] * (k == 0) + marks
-            marks = marks + when(far, *inverse(far, 1, M1) + inverse(far, 2, M2 + len(work) - 25 - 2 * (k == 0)))
+            marks = marks + when(far, *inverse(far, 1, M1) + inverse(far, 2, M2 + len(work) - 25))
             scalar += deal(work, *marks)
             second = [unit(k, 1, G_FROM[k], G, GP)] * (G_FROM[k] < G)
-            gpsimd += ([unit(k, 0, 0, G, GP)] if k else [unit(k, 0, 0, QUAD, GP), unit(k, 0, QUAD, G, GP)]) + second * (k in QUANT_AT) + [(sink_last, near)] + second * (k not in QUANT_AT)
+            gpsimd += ([unit(k, 0, 0, G, GP)] if k else [unit(k, 0, 0, QUAD, GP), unit(k, 0, QUAD, G, GP)]) + second * (k in QUANT_AT) + [(sink_last, near)] + second * (k not in QUANT_AT) + [pre_g(7, 0)] * (k == 0)
 
         k, last = NT - 1, NQ - 1
-        tensor += [(y_sum, k, a, 0, len(ORDER), (0, 0)) for a in range(last)]
+        tensor += [(y_sum, k, a, 0, BRANCH + 1, (0, 0)) for a in range(last)]
         outs = [(y_out, k - 1, a) for a in range(NQ)] + [(y_out, k, a) for a in range(last)]
         vector += [outs[0], unit(k, 2, 0, HALF, V), outs[1], unit(k, 3, 0, HALF, V), outs[2], unit(k, 2, HALF, G, V), unit(k, 3, HALF, G, V), outs[3]]
         vector += [outs[4], (y_add, k, last, 2, 3, V), outs[5], (y_add, k, last, 2, BRANCH, V), (y_add_out, k, last, 0, 2), (y_store, k, last), outs[6]]

@@ -35,6 +35,8 @@ U_BATCHES = ((0, 4), (4, 8))
 X_BATCHES = ((0, 1), (1, 2), (2, 4), (4, 6), (6, 7), (7, 8))
 OWN_GATES = 4
 WHOLE = 2
+TINY = 1e-30
+ADDED = ((2, 3),)
 ORDERS = ((2, 1, BRANCH, 3, 0), (2, BRANCH, 3, 0, 1), (2, 0, BRANCH, 3, 1), (2, 0, BRANCH, 3, 1))
 LATE_PRE = (4, 1)
 FLOPS = 2 * TOK * R * D * M + 2 * TOK * D * D
@@ -67,8 +69,8 @@ KINDS = {
     "pu": ([P, T, 2, P], F32, "prod", 3),
     "ut": ([P, T, P], F32, "four", 4),
     "h": ([P, D], F32, "four", 4),
-    "hr": ([P, D], F32, "hr", 1),
-    "f": ([P, D], F32, "f", 2),
+    "hr": ([P, D], F32, "hr", 2),
+    "post": ([P, 0], F32, "post", 2),
     "prod": ([P, HALF, R, C], F32, "prod", 3),
     "whole": ([P, G, R, C], F32, "whole", 2),
     "w_raw": ([P, T, D], BF16, "whole", 2),
@@ -81,6 +83,10 @@ def spread(ap, axis, n):
     shape = list(ap.shape)
     shape.insert(axis, n)
     return ap.unsqueeze(axis).to_broadcast(shape)
+
+
+def order_of(n, a):
+    return tuple(j for j in ORDERS[a] if j != 1 or (n, a) not in ADDED)
 
 
 def tag_of(key):
@@ -407,8 +413,15 @@ def tile_groupedmanifoldhyperconnection_kernel(tc, x, gn, phi_bytes, phi_scale, 
         def branch_relu(n):
             nc.scalar.activation(value("hr", n)[:], value("h", n)[:], ACT.Relu)
 
-        def branch_square(n):
-            nc.scalar.activation(value("f", n)[:], value("hr", n)[:], ACT.Square)
+        def post_root(b, step):
+            post = value("gate", b)[:].rearrange("p (m k g) -> p m k g", k=GATES, g=G)[:, :, R:GATES, :].rearrange("p m k g -> p m (k g)")
+            half = [value("post", b, s)[:].rearrange("p (m c) -> p m c", c=P)[:, :, 0 : R * G] for s in range(min(step + 1, 2))]
+            if step == 0:
+                nc.scalar.activation(half[0], post, ACT.Abs_reciprocal_sqrt, bias=TINY)
+            elif step == 1:
+                nc.scalar.activation(half[1], half[0], ACT.Square)
+            else:
+                nc.scalar.activation(post, half[1], ACT.Abs_reciprocal_sqrt)
 
         def term(n, j, lo, hi):
             if j < WHOLE:
@@ -416,7 +429,7 @@ def tile_groupedmanifoldhyperconnection_kernel(tc, x, gn, phi_bytes, phi_scale, 
             return value("prod", n, j, lo // HALF)[:, lo % HALF : lo % HALF + hi - lo]
 
         def product(n, j, lo, hi, engine):
-            src = xs[n][:, j * D : (j + 1) * D] if j < R else value("f", n)[:]
+            src = xs[n][:, j * D : (j + 1) * D] if j < R else value("hr", n)[:]
             src = src.rearrange("p (g c) -> p g c", g=G)[:, lo:hi]
             dst = term(n, j, lo, hi)
             if engine == "vector":
@@ -428,18 +441,18 @@ def tile_groupedmanifoldhyperconnection_kernel(tc, x, gn, phi_bytes, phi_scale, 
             if engine == "scalar":
                 for g in range(hi - lo):
                     for i in range(R):
-                        nc.scalar.activation(dst[:, g, i, :], src[:, g, :], ACT.Copy, scale=weight[:, g, i : i + 1])
+                        nc.scalar.activation(dst[:, g, i, :], src[:, g, :], ACT.Copy if j < R else ACT.Square, scale=weight[:, g, i : i + 1])
             else:
                 multiply = nc.vector.tensor_tensor if engine == "vector" else nc.gpsimd.tensor_tensor
                 multiply(out=dst, in0=spread(src, 2, R), in1=spread(weight, 3, C), op=ALU.mult)
 
         def y_sum(n, a, lo, hi, plain):
             for m in range(lo, hi):
-                j = ORDERS[a][m]
+                j = order_of(n, a)[m]
                 for b in range(QUAD):
                     g = QUAD - 1 - b
                     src = term(n, j, QUAD * a, QUAD * (a + 1))[:, g].rearrange("p i c -> p (i c)")
-                    first, last = m == 0 and b == 0, m == BRANCH and b == QUAD - 1
+                    first, last = m == 0 and b == 0, m == len(order_of(n, a)) - 1 and b == QUAD - 1
                     turn(value("yt", n, a)[:, :, g, :], src, first, last, QUAD * (m - lo) + b < plain[0] or QUAD * (hi - m) - b <= plain[1])
 
         def y_out(n, a):
@@ -511,14 +524,14 @@ def tile_groupedmanifoldhyperconnection_kernel(tc, x, gn, phi_bytes, phi_scale, 
                 u_quant: lambda: ([("u_words", n)], [("u_codes", n)]),
                 branch_mm: lambda: ([("u_codes", batch_of[n][0]), ("w_codes",)], [("h", n)]),
                 branch_relu: lambda: ([("h", n)], [("hr", n)]),
-                branch_square: lambda: ([("hr", n)], [("f", n)]),
+                post_root: lambda: ([("post", n, a[0] - 1) if a[0] else ("gate", n)], [("post", n, a[0]) if a[0] < 2 else ("rooted", n)]),
                 product: lambda: (
-                    [("f", n), ("gate", xb)] if a[0] == BRANCH else [("qp", n)] if a[3] == "vector" else [("q", n)],
+                    [("hr", n), ("rooted", xb), ("gate", xb)] if a[0] == BRANCH else [("qp", n)] if a[3] == "vector" else [("q", n)],
                     [home(n, a[0], a[1])] + [("part", n, a[0], quad) for quad in range(a[1] // QUAD, (a[2] - 1) // QUAD + 1)],
                 ),
-                y_sum: lambda: (parts(n, ORDERS[a[0]][a[1] : a[2]], a[0]), [("yt", n, a[0])]),
-                y_add: lambda: (parts(n, a[1:3], a[0]), [("added", n)]),
-                y_add_out: lambda: (parts(n, a[1:3], a[0]) + [("added", n)], [("yo", n, a[0])]),
+                y_sum: lambda: (parts(n, order_of(n, a[0])[a[1] : a[2]], a[0]) + [("added", n, a[0])], [("yt", n, a[0])]),
+                y_add: lambda: (parts(n, a[1:3], a[0]), [("added", n, a[0])]),
+                y_add_out: lambda: (parts(n, a[1:3], a[0]) + [("added", n, a[0])], [("yo", n, a[0])]),
                 y_store: lambda: ([("yo", n, a[0])], []),
                 y_out: lambda: ([("yt", n, a[0])], [("yo", n, a[0])]),
             }
@@ -561,13 +574,17 @@ def tile_groupedmanifoldhyperconnection_kernel(tc, x, gn, phi_bytes, phi_scale, 
         def inverse(n, step, place):
             return [(place, (sink_root, n, step)), (place + 1, (sink_inv, n, step))]
 
+        def roots(n, place):
+            b, m = xb_of[n]
+            return [(place + step, (post_root, b, step)) for step in range(3)] * (m == 0)
+
         def when(n, *steps):
             return list(steps) if 0 <= n < NT else []
 
         G_FROM = [G, 4] + [HALF] * (NT - 3)
-        V_LOW = [HALF, HALF] + [7] * (NT - 4) + [HALF]
+        V_LOW = [HALF, HALF] + [6] * (NT - 4) + [HALF]
         Q_COLS = [(G + HALF, 4 * G)] + [(2 * G, 4 * G)] * (NT - 1)
-        M0, M1, M2, RELU, SQUARE = 4, 12, 22, 2, 9
+        M0, M1, M2, RELU, ROOT = 4, 13, 22, 2, 9
         QUANT_AT = {2: 1}
         EXTRA_T = {1: [usum(7)]}
         EXTRA_V = {(0, 0): [(u_gain, 4)], (0, 2): [(u_gain, 6)], (0, 3): [(y_out, 0, 0), unit(0, 1, HALF, G, V)]}
@@ -575,30 +592,30 @@ def tile_groupedmanifoldhyperconnection_kernel(tc, x, gn, phi_bytes, phi_scale, 
         tensor += turns(0) + turns(1) + [(bias_turn,)]
         tensor += [(gate_mm, 0)] + turns(2, 3) + [(gate_turn, 0, True), (gate_mm, 1)] + turns(4)
         tensor += [(gate_turn, 1, False), (logit_mm, 0, 0, R), (logit_mm, 1, 0, R)] + turns(5) + [(e_turn, 0, 0, 2, False), (gate_mm, 2), (logit_mm, 2, 0, R)]
-        tensor += turns(6) + [(gate_turn, 2, False)] + turns(7) + [(gate_mm, 3), (logit_mm, 3, 0, R), (gate_turn, 3, False), usum(0), (e_turn, 1, 0, 2, False)]
-        tensor += [(gate_mm, 4), (logit_mm, 4, 0, R), (gate_mm, 5), (logit_mm, 5, 0, R), (gate_turn, 4, False), usum(1), (gate_turn, 5, False)]
-        tensor += [usum(2), (e_turn, 2, 0, 2, False), usum(3), usum(4), (branch_mm, 0), (q_to_psum, 0) + Q_COLS[0], (branch_mm, 1), usum(5, (1, 0)), usum(6)]
+        tensor += [(gate_turn, 2, False)] + turns(6, 7) + [(gate_mm, 3), (logit_mm, 3, 0, R), usum(0), (gate_turn, 3, False), usum(1), (e_turn, 1, 0, 2, False)]
+        tensor += [(gate_mm, 4), (logit_mm, 4, 0, R), (gate_mm, 5), (logit_mm, 5, 0, R), (gate_turn, 4, False), usum(2), (gate_turn, 5, False)]
+        tensor += [usum(3), (e_turn, 2, 0, 2, False), usum(4), (branch_mm, 0), (q_to_psum, 0) + Q_COLS[0], (branch_mm, 1), usum(5, (1, 0)), usum(6)]
 
         vector += [(phi_widen, 1, V, 0, T), (phi_widen, 3, V, 0, T), (phi_group, 0, False, V), (phi_group, 1, False, V), (phi_group, 3, False, V)]
         vector += [(x_gain, 0, 0), (phi_group, 2, False, V), (x_gain, 0, 1), (gate_quant,), (x_quant, 0)]
         vector += gains(1) + [(logit_quant, 0), (x_quant, 1)] + gains(2) + [(logit_quant, 1), (gate_copy, 0, V)]
         vector += gains(3) + [(x_quant, 2), (gate_copy, 1, V)] + gains(4, 5) + [(sink_sum, 0, 0), (x_quant, 3), (gate_copy, 2, V)]
         vector += gains(6, 7) + [(x_quant, 4), (x_quant, 5), (w_quant,), (gate_copy, 3, V), (sink_recip, 0, 0), (u_gain, 0), (sink_scale, 0, 0), (sink_sum, 1, 0), (sink_sum, 0, 1)]
-        vector += [(sink_recip, 1, 0), (sink_recip, 0, 1), (sink_scale, 1, 0), (sink_scale, 0, 1), (sink_sum, 1, 1), (sink_sum, 0, 2), (gate_copy, 4, V), (u_gain, 1), (gate_copy, 5, V)]
-        vector += [(sink_scale, 0, 2), (u_gain, 2), (sink_scale, 1, 1), (u_gain, 3), (sink_sum, 0, 3), (u_quant, 0), (sink_sum, 1, 2), pre_v(6, 1, 0), pre_v(6, 1, 1)]
+        vector += [(u_gain, 1), (sink_recip, 0, 1), (sink_recip, 1, 0), (sink_scale, 0, 1), (sink_scale, 1, 0), (sink_sum, 0, 2), (sink_sum, 1, 1), (gate_copy, 4, V), (u_gain, 2)]
+        vector += [(sink_scale, 0, 2), (gate_copy, 5, V), (sink_scale, 1, 1), (u_gain, 3), (sink_sum, 0, 3), (u_quant, 0), (sink_sum, 1, 2), pre_v(6, 1, 0), pre_v(6, 1, 1)]
 
         scalar += [(phi_widen, 0, S, 0, T), (phi_widen, 2, S, 0, T)] + [(phi_group, r, True, S) for r in range(R)]
         scalar += [(bias_read,), (gf_half,), (gate_tanh, 0), (w_group, 0, S), (w_group, 1, S), (gate_tanh, 1)] + pre_s(0, 0, G) + pre_s(0, 1, 0, G) + [(logit_exp, 0), (logit_exp, 1)]
         scalar += pre_s(0, 1, G) + pre_s(1, 1, HALF, G) + [(gate_tanh, 2)] + pre_s(1, 1, G) + [(logit_exp, 2)] + pre_s(2, 1) + [(gate_tanh, 3)] + pre_s(3, 0, HALF)
         scalar += [(logit_exp, 3)] + pre_s(3, 1, 0, 24) + [(gate_tanh, 4)] + pre_s(3, 1, 24) + [(logit_exp, 4), (gate_one, 4), (gate_tanh, 5), (logit_exp, 5)]
         work = pre_s(4, 1) + pre_s(5, 1)
-        scalar += deal(work, *inverse(0, 2, 0) + inverse(1, 1, 1) + inverse(0, 3, 12) + inverse(1, 2, 14))
+        scalar += deal(work, *inverse(0, 2, 0) + inverse(1, 1, 1) + roots(0, 3) + inverse(0, 3, 7) + inverse(1, 2, 9))
 
         gpsimd += [pre_g(0, 0, 0, G), pre_g(1, 0), pre_g(1, 1, 0, HALF), pre_g(2, 0), pre_g(3, 0, 0, HALF), pre_g(4, 0), pre_g(5, 0), pre_g(6, 0), (sink_last, 0)]
 
         for k in range(NT - 1):
             near, far = k + 1, k + 2
-            banks = [(y_sum, k, a, 0, BRANCH + 1, (0, 0)) for a in range(NQ)]
+            banks = [(y_sum, k, a, 0, len(order_of(k, a)), (0, 0)) for a in range(NQ)]
             tensor += [(q_to_psum, near) + Q_COLS[near]] * (near == NT - 1) + banks[:1] + when(k + 3, (e_turn, k + 3, 0, 1, False)) + [(y_sum, k, 1, 0, 1, (0, int(k + 3 == NT)))] + when(far, (branch_mm, far))
             tensor += when(k + 3, (e_turn, k + 3, 1, 2, True)) + [(q_to_psum, near) + Q_COLS[near]] * (near < NT - 1) + [(y_sum, k, 1, 1, BRANCH + 1, (0, 0))]
             tensor += EXTRA_T.get(k, []) + banks[2:]
@@ -616,20 +633,20 @@ def tile_groupedmanifoldhyperconnection_kernel(tc, x, gn, phi_bytes, phi_scale, 
             vector += when(far, (sink_scale, far, 1)) + back[2] + when(far, (sink_sum, far, 2)) + [unit(k, 3, HALF, G, V)] + back[3]
             work = unit_s(k, 1, 0, QUAD) + unit_s(k, BRANCH, 0, HALF) + unit_s(k, 1, QUAD, min(G_FROM[k], HALF))
             work = work + unit_s(k, 3, V_LOW[k], HALF) + EXTRA_S.get(k, []) + unit_s(k, BRANCH, HALF, G)
-            marks = when(far, *inverse(far, 0, M0)) + inverse(near, 3, M0 + 2 if k not in QUANT_AT else M1 + 3) + [(RELU if k else SQUARE, (branch_relu, near)), (SQUARE if k else 2 * SQUARE, (branch_square, near))]
-            marks = [(1, (branch_relu, 0)), (2, (branch_square, 0))] * (k == 0) + marks
+            marks = when(far, *inverse(far, 0, M0 if k else 2)) + inverse(near, 3, M0 + 2 if k not in QUANT_AT else M1 + 3) + [(RELU if k else ROOT - 1, (branch_relu, near))] + roots(near, ROOT)
+            marks = [(1, (branch_relu, 0))] * (k == 0) + marks
             marks = marks + when(far, *inverse(far, 1, M1) + inverse(far, 2, M2 + len(work) - 25))
             scalar += deal(work, *marks)
-            second = [unit(k, 1, G_FROM[k], G, GP)] * (G_FROM[k] < G)
+            second = [unit(k, 1, G_FROM[k], G, GP)] * (G_FROM[k] < G) + [(y_add, k, a, 0, 1, GP) for a in range(NQ) if (k, a) in ADDED]
             gpsimd += ([unit(k, 0, 0, G, GP)] if k else [unit(k, 0, 0, QUAD, GP), unit(k, 0, QUAD, G, GP)]) + second * (k in QUANT_AT) + [(sink_last, near)] + second * (k not in QUANT_AT) + [pre_g(7, 0)] * (k == 0)
 
         k, last = NT - 1, NQ - 1
-        tensor += [(y_sum, k, a, 0, BRANCH + 1, (0, 0)) for a in range(last)]
+        tensor += [(y_sum, k, a, 0, len(order_of(k, a)), (0, 0)) for a in range(last)]
         outs = [(y_out, k - 1, a) for a in range(NQ)] + [(y_out, k, a) for a in range(last)]
         vector += [outs[0], unit(k, 2, 0, HALF, V), outs[1], unit(k, 3, 0, HALF, V), outs[2], unit(k, 2, HALF, G, V), unit(k, 3, HALF, G, V), outs[3]]
         vector += [outs[4], (y_add, k, last, 2, 3, V), outs[5], (y_add, k, last, 2, BRANCH, V), (y_add_out, k, last, 0, 2), (y_store, k, last), outs[6]]
         scalar += [s for a in range(NQ) for j in (BRANCH, 1)[: 1 + (a < last)] for s in unit_s(k, j, QUAD * a, QUAD * a + QUAD)]
-        gpsimd += [unit(k, 0, 0, HALF, GP), unit(k, 0, HALF, G, GP), unit(k, 1, QUAD * last, G, GP), (y_add, k, last, 0, 1, GP)]
+        gpsimd += [unit(k, 0, 0, HALF, GP), unit(k, 0, HALF, G, GP), unit(k, 1, QUAD * last, G, GP), (y_add, k, last, 0, 1, GP)] + [(y_add, k, a, 0, 1, GP) for a in range(last) if (k, a) in ADDED]
 
         queues = (tensor, vector, scalar, gpsimd)
         steps = [s for queue in queues for s in queue]

@@ -594,7 +594,7 @@ def tile_groupedmanifoldhyperconnection_kernel(tc, x, gn, phi_bytes, phi_scale, 
         tensor += [(gate_turn, 1, False), (logit_mm, 0, 0, R), (logit_mm, 1, 0, R)] + turns(5) + [(e_turn, 0, 0, 2, False), (gate_mm, 2), (logit_mm, 2, 0, R)]
         tensor += [(gate_turn, 2, False)] + turns(6, 7) + [(gate_mm, 3), (logit_mm, 3, 0, R), usum(0), (gate_turn, 3, False), usum(1), (e_turn, 1, 0, 2, False)]
         tensor += [(gate_mm, 4), (logit_mm, 4, 0, R), (gate_mm, 5), (logit_mm, 5, 0, R), (gate_turn, 4, False), usum(2), (gate_turn, 5, False)]
-        tensor += [usum(3), (e_turn, 2, 0, 2, False), usum(4), (branch_mm, 0), (q_to_psum, 0) + Q_COLS[0], (branch_mm, 1), usum(5, (1, 0)), usum(6)]
+        tensor += [usum(3), (e_turn, 2, 0, 2, False), usum(4), (branch_mm, 0), (q_to_psum, 0) + Q_COLS[0], (branch_mm, 1), usum(5), usum(6)]
 
         vector += [(phi_widen, 1, V, 0, T), (phi_widen, 3, V, 0, T), (phi_group, 0, False, V), (phi_group, 1, False, V), (phi_group, 3, False, V)]
         vector += [(x_gain, 0, 0), (phi_group, 2, False, V), (x_gain, 0, 1), (gate_quant,), (x_quant, 0)]
@@ -616,8 +616,8 @@ def tile_groupedmanifoldhyperconnection_kernel(tc, x, gn, phi_bytes, phi_scale, 
         for k in range(NT - 1):
             near, far = k + 1, k + 2
             banks = [(y_sum, k, a, 0, len(order_of(k, a)), (0, 0)) for a in range(NQ)]
-            tensor += [(q_to_psum, near) + Q_COLS[near]] * (near == NT - 1) + banks[:1] + when(k + 3, (e_turn, k + 3, 0, 1, False)) + [(y_sum, k, 1, 0, 1, (0, int(k + 3 == NT)))] + when(far, (branch_mm, far))
-            tensor += when(k + 3, (e_turn, k + 3, 1, 2, True)) + [(q_to_psum, near) + Q_COLS[near]] * (near < NT - 1) + [(y_sum, k, 1, 1, BRANCH + 1, (0, 0))]
+            tensor += [(q_to_psum, near) + Q_COLS[near]] * (near == NT - 1) + banks[:1] + when(k + 3, (e_turn, k + 3, 0, 2, False)) + [(y_sum, k, 1, 0, 1, (0, 0))] + when(far, (branch_mm, far))
+            tensor += [(q_to_psum, near) + Q_COLS[near]] * (near < NT - 1) + [(y_sum, k, 1, 1, BRANCH + 1, (0, 0))]
             tensor += EXTRA_T.get(k, []) + banks[2:]
             back = [when(k - 1, (y_out, k - 1, a)) + EXTRA_V.get((k, a), []) for a in range(NQ)]
             first, then = [unit(k, 2, 0, HALF, V)], [unit(k, 3, 0, V_LOW[k], V)]

from contextlib import ExitStack

import concourse.mybir as mybir
from concourse.masks import make_identity

F32 = mybir.dt.float32
BF16 = mybir.dt.bfloat16
U32 = mybir.dt.uint32
U8 = mybir.dt.uint8
FP8 = mybir.dt.float8_e4m3fn
FP8X4 = mybir.dt.float8_e4m3fn_x4
ACT = mybir.ActivationFunctionType
ALU = mybir.AluOpType
AX = mybir.AxisListType

P = 128
T = 4
R = 4
D = 512
G = 16
C = 32
GATES = 2 * R
LOGITS = R * R
KC = GATES + LOGITS
M = G * KC
MT = M // P
TOK = 1024
NT = TOK // P
TB = P // C
QUAD = 4
NQ = G // QUAD
BRANCH = R
HALF = G // 2
U_BATCHES = ((0, 4), (4, 8))
X_BATCHES = ((0, 1), (1, 2), (2, 4), (4, 6), (6, 7), (7, 8))
OWN_GATES = 4
WHOLE = 2
TINY = 1e-30
ADDED = ((2, 3),)
ORDERS = ((2, 1, BRANCH, 3, 0), (2, BRANCH, 3, 0, 1), (2, 0, BRANCH, 3, 1), (2, 0, BRANCH, 3, 1))
LATE_PRE = (4, 1)
FLOPS = 2 * TOK * R * D * M + 2 * TOK * D * D

BANKS = {"four": 4, "b0": 1, "b1": 1, "b2": 1, "b3": 1}
KINDS = {
    "wide": ([P, T, M], BF16, "yo", 4),
    "bias_ps": ([P, MT + T, 2], F32, "b2", 1),
    "gate_words": ([P, R, P, T], BF16, "late", 7),
    "logit_words": ([P, 2, 2 * P, T], BF16, "late", 7),
    "w_words": ([P, D, T], BF16, "late", 7),
    "xp": ([P, 2, 2, P], F32, "four", 4),
    "xn": ([P, R, 0, T], BF16, "xn", 2),
    "xc": ([P, R, 0], U32, "xc", 3),
    "xs": ([P, R, 0], U8, "xs", 3),
    "tg": ([P, 0], F32, "b0", 1),
    "tl": ([P, 2, 0], F32, "b1", 1),
    "th": ([P, 0], F32, "th", 2),
    "th1": ([P, 0], F32, "th1", 1),
    "gt": ([P, 0], F32, "b2", 1),
    "gate": ([P, 0], F32, "gate", len(X_BATCHES)),
    "co": ([P, 2, 0], F32, "co", len(X_BATCHES)),
    "ct": ([P, 2 * P], F32, "b0", 1),
    "qp": ([P, 2 * P], F32, "b3", 1),
    "sums": ([P, G, R], F32, "sums", 3),
    "root": ([P, G, R], F32, "root", 2),
    "factor": ([P, G, R], F32, "factor", 3),
    "scaled": ([P, G, R, R], F32, "scaled", 3),
    "q": ([P, R, G, R], F32, "q", 3),
    "pu": ([P, T, 2, P], F32, "prod", 3),
    "ut": ([P, T, P], F32, "four", 4),
    "h": ([P, D], F32, "four", 4),
    "hr": ([P, D], F32, "hr", 2),
    "post": ([P, 0], F32, "post", 2),
    "prod": ([P, HALF, R, C], F32, "prod", 3),
    "whole": ([P, G, R, C], F32, "whole", 2),
    "w_raw": ([P, T, D], BF16, "whole", 2),
    "yt": ([P, TB, QUAD, C], F32, "four", 4),
    "yo": ([P, D], F32, "yo", 4),
}


def spread(ap, axis, n):
    shape = list(ap.shape)
    shape.insert(axis, n)
    return ap.unsqueeze(axis).to_broadcast(shape)


def order_of(n, a):
    return tuple(j for j in ORDERS[a] if j != 1 or (n, a) not in ADDED)


def tag_of(key):
    tag = KINDS[key[0]][2]
    if key[0] == "ct":
        return ("b0", "b1")[key[1] % 2] if key[1] else "b3"
    if key[0] == "qp":
        return ("b3", "b2")[key[1] % 2]
    if key in (("tl", 1), ("xp", 2, 1)):
        return "b3"
    if key in (("tl", 4), ("tl", 5), ("gt", 5)):
        return "four"
    if key == ("xp", 2, 0):
        return "b1"
    if key[0] == "pu" and key[1:] >= LATE_PRE:
        return "late"
    if key[0] == "pu":
        return "prod%d" % (2 + (2 * key[1] + key[2]) % 3)
    if tag == "whole":
        return "whole%d" % (key[2] if key[1:] else 0)
    return "prod%d" % key[2] if tag == "prod" else tag


def bufs_of(key):
    return 7 if tag_of(key) == "late" else BANKS.get(tag_of(key), KINDS[key[0]][3])


def tile_groupedmanifoldhyperconnection_kernel(tc, x, gn, phi_bytes, phi_scale, bm, gf, w, out):
    nc = tc.nc
    x_rows = x.rearrange("b s r d -> (b s) (r d)")
    out_view = out.rearrange("b (n tb t) i (q c) -> (b n) i q t tb c", tb=TB, t=C, q=NQ)
    out_rows = out.rearrange("b s i (q c) -> (b s) i q c", q=NQ)
    with ExitStack() as ctx:
        keep = ctx.enter_context(tc.tile_pool(name="keep", bufs=1))
        sb = ctx.enter_context(tc.tile_pool(name="sb", bufs=2))
        ps = ctx.enter_context(tc.psum_pool(name="ps", bufs=1))
        ctx.enter_context(tc.manual_schedule())

        xb_of = {n: (b, n - lo) for b, (lo, hi) in enumerate(X_BATCHES) for n in range(lo, hi)}

        tiles = dict()

        def value(*key):
            if key not in tiles:
                shape, dtype, tag, bufs = KINDS[key[0]]
                if 0 in shape:
                    lo, hi = X_BATCHES[key[1]]
                    shape = [size or (hi - lo) * P for size in shape]
                if tag in BANKS:
                    tiles[key] = ps.tile(shape, dtype, name=tag_of(key), bufs=bufs_of(key))
                else:
                    tiles[key] = sb.tile(shape, dtype, name=tag_of(key), bufs=bufs_of(key), align_bytes=64)
            return tiles[key]

        ident = keep.tile([P, P], F32)
        bm_row = keep.tile([P, M + D], BF16)
        nc.vector.memset(bm_row[:], 0.0)
        ones = keep.tile([P, 2], BF16)
        nc.vector.memset(ones[:], 1.0)
        make_identity(nc, ident[:])

        scale = keep.tile([P, R, T], F32)
        phi_view = phi_bytes.rearrange("(r p t) n -> r p t n", p=P, t=T)
        phi_raw = [keep.tile([P, T, M], U8, name="phb%d" % r) for r in range(R)]
        xs = [keep.tile([P, R * D], BF16, name="x%d" % n) for n in range(NT)]
        gn_k = keep.tile([P, R, T], BF16)

        def load_x(n, lo, hi):
            nc.sync.dma_start(out=xs[n][:, lo * D : hi * D], in_=x_rows[n * P : (n + 1) * P, lo * D : hi * D])

        nc.sync.dma_start(out=scale[:], in_=phi_scale.rearrange("(r p t) o -> p r (t o)", p=P, t=T))
        for r in range(R):
            nc.sync.dma_start(out=phi_raw[r][:], in_=phi_view[r])
        load_x(0, 0, 2)
        nc.sync.dma_start(out=gn_k[:], in_=gn.rearrange("(r p t) -> p r t", p=P, t=T))
        load_x(0, 2, 4)
        load_x(1, 0, R)
        bm_groups = bm.rearrange("(o g k) -> o g k", o=1, g=G)
        nc.sync.dma_start(out=bm_row[0:1, 0:P].rearrange("p (g k) -> p g k", g=G), in_=bm_groups[:, :, 0:GATES])
        nc.sync.dma_start(out=bm_row[0:1, P:M].rearrange("p (g k) -> p g k", g=G), in_=bm_groups[:, :, GATES:KC])
        gf_dst = bm_row[0:1, M : M + D].rearrange("p (t g c) -> p t g c", t=T, g=G)
        nc.sync.dma_start(out=gf_dst, in_=gf.rearrange("(o g t c) -> o t g c", o=1, g=G, t=T))
        load_x(2, 0, R)
        load_x(3, 0, R)
        w_rows = w.rearrange("(g t c) n -> t g c n", g=G, t=T)
        for t in range(T):
            nc.sync.dma_start(out=value("w_raw")[:, t, :], in_=w_rows[t])
        for n in range(4, NT):
            load_x(n, 0, R)

        gate_codes = keep.tile([P, R, P], U32, align_bytes=64)
        gate_scales = keep.tile([P, R, P], U8, align_bytes=64)
        logit_codes = keep.tile([P, R, 2 * P], U32, align_bytes=64)
        logit_scales = keep.tile([P, R, 2 * P], U8, align_bytes=64)
        bias = keep.tile([P, MT], F32)
        half_bias = keep.tile([P, 1], F32)
        half_gf = keep.tile([P, T], F32)
        w_codes = keep.tile([P, D], U32, align_bytes=64)
        w_scales = keep.tile([P, D], U8, align_bytes=64)
        u_words = [keep.tile([P, hi - lo, P, T], BF16, name="uw%d" % lo, align_bytes=64) for lo, hi in U_BATCHES]
        u_codes = [keep.tile([P, hi - lo, P], U32, name="uc%d" % lo, align_bytes=64) for lo, hi in U_BATCHES]
        u_scales = [keep.tile([P, hi - lo, P], U8, name="us%d" % lo, align_bytes=64) for lo, hi in U_BATCHES]
        batch_of = {n: (b, n - lo) for b, (lo, hi) in enumerate(U_BATCHES) for n in range(lo, hi)}

        def turn(dst, src, start, stop, plain):
            nc.tensor.matmul(dst, src, ident[:], start=start, stop=stop, is_transpose=not plain)

        def phi_widen(r, engine, lo, hi):
            for t in range(lo, hi):
                src = phi_raw[r][:, t, :].bitcast(FP8)
                if engine == "vector":
                    nc.vector.tensor_scalar(value("wide", r)[:, t, :], src, scale[:, r, t : t + 1], None, op0=ALU.mult)
                else:
                    nc.scalar.activation(value("wide", r)[:, t, :], src, ACT.Copy, scale=scale[:, r, t : t + 1])

        def phi_group(r, logits, engine):
            lo, hi = (GATES, KC) if logits else (0, GATES)
            dst = value("logit_words", r // 2)[:, r % 2] if logits else value("gate_words")[:, r]
            src = value("wide", r)[:].rearrange("p t (g k) -> p g t k", g=G)[:, :, :, lo:hi]
            copy = nc.vector.tensor_copy if engine == "vector" else nc.scalar.copy
            copy(out=dst.rearrange("p (g a i) t -> p g a t i", g=G, i=4), in_=src.rearrange("p g t (a i) -> p g a t i", i=4))

        def gate_quant():
            nc.vector.quantize_mx(
                out=gate_codes[:].rearrange("p r n -> p (r n)").bitcast(FP8X4),
                scales=gate_scales[:].rearrange("p r n -> p (r n)"),
                in_=value("gate_words")[:].rearrange("p r n t -> p (r n t)"),
            )

        def logit_quant(h):
            nc.vector.quantize_mx(
                out=logit_codes[:, 2 * h : 2 * h + 2].rearrange("p r n -> p (r n)").bitcast(FP8X4),
                scales=logit_scales[:, 2 * h : 2 * h + 2].rearrange("p r n -> p (r n)"),
                in_=value("logit_words", h)[:].rearrange("p r n t -> p (r n t)"),
            )

        def bias_turn():
            for m in range(MT + T):
                nc.tensor.matmul(value("bias_ps")[:, m, :], bm_row[:, m * P : (m + 1) * P], ones[:], start=True, stop=True)

        def bias_read():
            nc.scalar.copy(out=bias[:], in_=value("bias_ps")[:, 0:MT, 0])
            nc.scalar.activation(half_bias[:], value("bias_ps")[:, 0, 0:1], ACT.Copy, scale=0.5)

        def w_group(half, engine):
            cols = slice(half * D // 2, (half + 1) * D // 2)
            copy = nc.vector.tensor_copy if engine == "vector" else nc.scalar.copy
            copy(
                out=value("w_words")[:, cols, :].rearrange("p (c i) t -> p c t i", i=4),
                in_=value("w_raw")[:, :, cols].rearrange("p t (c i) -> p c t i", i=4),
            )

        def gf_half():
            nc.scalar.activation(half_gf[:], value("bias_ps")[:, MT:, 0], ACT.Copy, scale=0.5)

        def w_quant():
            nc.vector.quantize_mx(out=w_codes[:].bitcast(FP8X4), scales=w_scales[:], in_=value("w_words")[:].rearrange("p n t -> p (n t)"))

        def x_turn(n, pair):
            words = xs[n][:].bitcast(F32)
            for rr in range(2):
                r = 2 * pair + rr
                for u in range(2):
                    nc.tensor.transpose(value("xp", n, pair)[:, u, rr, :], words[:, 256 * r + u : 256 * (r + 1) : 2], ident[:])

        def x_gain(n, pair):
            b, m = xb_of[n]
            turned = value("xp", n, pair)[:].rearrange("p u r s -> p (u r s)").bitcast(BF16)
            dst = value("xn", b)[:, 2 * pair : 2 * pair + 2, m * P : (m + 1) * P, :]
            nc.vector.tensor_tensor(
                out=dst.rearrange("p r s (u e) -> p r s u e", e=2),
                in0=turned.rearrange("p (u r s e) -> p r s u e", u=2, r=2, e=2),
                in1=spread(gn_k[:, 2 * pair : 2 * pair + 2, :].rearrange("p r (u e) -> p r u e", e=2), 2, P),
                op=ALU.mult,
            )

        def x_quant(b):
            nc.vector.quantize_mx(
                out=value("xc", b)[:].rearrange("p r s -> p (r s)").bitcast(FP8X4),
                scales=value("xs", b)[:].rearrange("p r s -> p (r s)"),
                in_=value("xn", b)[:].rearrange("p r s t -> p (r s t)"),
            )

        def coef_pass(b, dst, codes, scales, r, start, stop):
            nc.tensor.matmul_mx(
                out=dst,
                lhsT=codes.bitcast(FP8X4),
                lhsT_scale=scales,
                rhs=value("xc", b)[:, r, :].bitcast(FP8X4),
                rhs_scale=value("xs", b)[:, r, :],
                start=start,
                stop=stop,
            )

        def gate_mm(b):
            for r in range(R):
                coef_pass(b, value("tg", b)[:], gate_codes[:, r, :], gate_scales[:, r, :], r, r == 0, r == R - 1)

        def logit_mm(b, lo, hi):
            for r in range(lo, hi):
                for m in range(2):
                    cols = slice(m * P, (m + 1) * P)
                    first, last = r == 0 and m == 0, r == R - 1 and m == 1
                    coef_pass(b, value("tl", b)[:, m, :], logit_codes[:, r, cols], logit_scales[:, r, cols], r, first, last)

        def gate_tanh(b):
            nc.scalar.activation(value("th", b)[:], value("tg", b)[:], ACT.Tanh, bias=half_bias[:], scale=0.5)

        def gate_one(b):
            nc.scalar.activation(value("th1", b)[:], value("th", b)[:], ACT.Identity, bias=1.0)

        def gate_turn(b, plain):
            lo, hi = X_BATCHES[b]
            for m in range(hi - lo):
                cols = slice(m * P, (m + 1) * P)
                turn(value("gt", b)[:, cols], value("th1" if b == OWN_GATES else "th", b)[:, cols], True, True, plain)

        def gate_copy(b, engine):
            dst = value("gate", b)[:].rearrange("p (m k g) -> p m k g", k=GATES, g=G)
            src = value("gt", b)[:].rearrange("p (m g k) -> p m k g", k=GATES, g=G)
            if b == OWN_GATES:
                nc.vector.tensor_copy(out=dst, in_=src)
            elif engine == "vector":
                nc.vector.tensor_scalar(dst, src, 1.0, None, op0=ALU.add)
            else:
                nc.scalar.activation(dst, src, ACT.Identity, bias=1.0)

        def gates_of(n, engine):
            b, m = xb_of[n]
            if engine == "vector":
                return value("gt", b)[:, m * P : (m + 1) * P].rearrange("p (g k) -> p k g", k=GATES)
            return value("gate", b)[:, m * P : (m + 1) * P].rearrange("p (k g) -> p k g", k=GATES)

        def logit_exp(b):
            for m in range(2):
                nc.scalar.activation(value("co", b)[:, m, :], value("tl", b)[:, m, :], ACT.Exp, bias=bias[:, 1 + m : 2 + m])

        def e_turn(n, lo, hi, plain):
            b, k = xb_of[n]
            for m in range(lo, hi):
                turn(value("ct", n)[:, m * P : (m + 1) * P], value("co", b)[:, m, k * P : (k + 1) * P], True, True, plain)

        def e_of(n):
            return value("ct", n)[:].rearrange("p (g i j) -> p g i j", i=R, j=R)

        def sink_sum(n, step):
            src = value("scaled", n, step - 1)[:] if step else e_of(n)
            nc.vector.tensor_reduce(value("sums", n, step)[:], src, axis=AX.X, op=ALU.add)

        def sink_root(n, step):
            nc.scalar.activation(value("root", n, step)[:], value("sums", n, step)[:], ACT.Abs_reciprocal_sqrt)

        def sink_inv(n, step):
            nc.scalar.activation(value("factor", n, step)[:], value("root", n, step)[:], ACT.Square)

        def sink_recip(n, step):
            nc.vector.reciprocal(value("factor", n, step)[:], value("sums", n, step)[:])

        def sink_scale(n, step):
            e = e_of(n).rearrange("p g i j -> p g j i") if step % 2 == 0 else e_of(n)
            factor = spread(value("factor", n, step)[:], 2, R)
            nc.vector.tensor_tensor(out=value("scaled", n, step)[:], in0=e, in1=factor, op=ALU.mult)

        def sink_last(n):
            nc.gpsimd.tensor_tensor(
                out=value("q", n)[:].rearrange("p j g i -> p g j i"),
                in0=value("scaled", n, 2)[:],
                in1=spread(value("factor", n, 3)[:], 3, R),
                op=ALU.mult,
            )

        def q_to_psum(n, lo, hi):
            q = value("q", n)[:].rearrange("p j g i -> p (j g i)")
            cols = slice(lo * R, hi * R)
            nc.tensor.matmul(value("qp", n)[:, cols], ident[:], q[:, cols], start=True, stop=True)

        def pre_prod(n, pair, lo, hi, engine):
            src = xs[n][:, 2 * pair * D : (2 * pair + 2) * D].rearrange("p (a t c) -> p a t c", a=2 * G, t=T)
            dst = value("pu", n, pair)[:].rearrange("p t r (g c) -> p (r g) t c", g=G)
            gate = gates_of(n, engine)[:, 2 * pair : 2 * pair + 2, :]
            if engine == "gpsimd":
                weights = spread(spread(gate.rearrange("p r g -> p (r g)")[:, lo:hi], 2, T), 3, C // T)
                nc.gpsimd.tensor_tensor(out=dst[:, lo:hi], in0=src[:, lo:hi], in1=weights, op=ALU.mult)
            elif engine == "vector":
                weights = spread(spread(gate[:, lo // G, :], 2, T), 3, C // T)
                nc.vector.tensor_tensor(out=dst[:, lo:hi], in0=src[:, lo:hi], in1=weights, op=ALU.mult)
            else:
                for a in range(lo, hi):
                    nc.scalar.activation(dst[:, a], src[:, a], ACT.Copy, scale=gate[:, a // G, a % G : a % G + 1])

        def u_sum(n, plain):
            for r in range(R):
                for t in range(T):
                    first, last = r == 0 and t == 0, r == R - 1 and t == T - 1
                    src = value("pu", n, r // 2)[:, t, r % 2, :]
                    turn(value("ut", n)[:, t, :], src, first, last, T * r + t < plain[0] or T * r + t >= R * T - plain[1])

        def u_gain(n):
            nc.vector.tensor_tensor(
                out=u_words[batch_of[n][0]][:, batch_of[n][1]],
                in0=value("ut", n)[:].rearrange("p t s -> p s t"),
                in1=spread(half_gf[:], 1, P),
                op=ALU.mult,
            )

        def u_quant(b):
            nc.vector.quantize_mx(
                out=u_codes[b][:].rearrange("p n s -> p (n s)").bitcast(FP8X4),
                scales=u_scales[b][:].rearrange("p n s -> p (n s)"),
                in_=u_words[b][:].rearrange("p n s t -> p (n s t)"),
            )

        def branch_mm(n):
            nc.tensor.matmul_mx(
                out=value("h", n)[:],
                lhsT=u_codes[batch_of[n][0]][:, batch_of[n][1]].bitcast(FP8X4),
                lhsT_scale=u_scales[batch_of[n][0]][:, batch_of[n][1]],
                rhs=w_codes[:].bitcast(FP8X4),
                rhs_scale=w_scales[:],
                start=True,
                stop=True,
            )

        def branch_relu(n):
            nc.scalar.activation(value("hr", n)[:], value("h", n)[:], ACT.Relu)

        def post_root(b, step):
            post = value("gate", b)[:].rearrange("p (m k g) -> p m k g", k=GATES, g=G)[:, :, R:GATES, :].rearrange("p m k g -> p m (k g)")
            half = [value("post", b, s)[:].rearrange("p (m c) -> p m c", c=P)[:, :, 0 : R * G] for s in range(min(step + 1, 2))]
            if step == 0:
                nc.scalar.activation(half[0], post, ACT.Abs_reciprocal_sqrt, bias=TINY)
            elif step == 1:
                nc.scalar.activation(half[1], half[0], ACT.Square)
            else:
                nc.scalar.activation(post, half[1], ACT.Abs_reciprocal_sqrt)

        def term(n, j, lo, hi):
            if j < WHOLE:
                return value("whole", n, j)[:, lo:hi]
            return value("prod", n, j, lo // HALF)[:, lo % HALF : lo % HALF + hi - lo]

        def product(n, j, lo, hi, engine):
            src = xs[n][:, j * D : (j + 1) * D] if j < R else value("hr", n)[:]
            src = src.rearrange("p (g c) -> p g c", g=G)[:, lo:hi]
            dst = term(n, j, lo, hi)
            if engine == "vector":
                weight = value("qp", n)[:].rearrange("p (j g i) -> p j g i", j=R, i=R)[:, j, lo:hi, :]
            elif j < R:
                weight = value("q", n)[:, j, lo:hi, :]
            else:
                weight = gates_of(n, engine)[:, R:GATES, lo:hi].rearrange("p i g -> p g i")
            if engine == "scalar":
                for g in range(hi - lo):
                    for i in range(R):
                        nc.scalar.activation(dst[:, g, i, :], src[:, g, :], ACT.Copy if j < R else ACT.Square, scale=weight[:, g, i : i + 1])
            else:
                multiply = nc.vector.tensor_tensor if engine == "vector" else nc.gpsimd.tensor_tensor
                multiply(out=dst, in0=spread(src, 2, R), in1=spread(weight, 3, C), op=ALU.mult)

        def y_sum(n, a, lo, hi, plain):
            for m in range(lo, hi):
                j = order_of(n, a)[m]
                for b in range(QUAD):
                    g = QUAD - 1 - b
                    src = term(n, j, QUAD * a, QUAD * (a + 1))[:, g].rearrange("p i c -> p (i c)")
                    first, last = m == 0 and b == 0, m == len(order_of(n, a)) - 1 and b == QUAD - 1
                    turn(value("yt", n, a)[:, :, g, :], src, first, last, QUAD * (m - lo) + b < plain[0] or QUAD * (hi - m) - b <= plain[1])

        def y_out(n, a):
            yo = value("yo", n, a)
            nc.vector.transpose(yo[:], value("yt", n, a)[:].rearrange("p tb b t -> p (tb b t)"))
            for i in range(R):
                nc.sync.dma_start(
                    out=out_view[n, i, a], in_=yo[C * i : C * (i + 1), :].rearrange("p (tb c) -> p tb c", tb=TB)
                )

        def y_add(n, a, into, other, engine):
            dst = term(n, into, QUAD * a, QUAD * (a + 1)).rearrange("p g i c -> p (g i c)")
            src = term(n, other, QUAD * a, QUAD * (a + 1)).rearrange("p g i c -> p (g i c)")
            add = nc.vector.tensor_tensor if engine == "vector" else nc.gpsimd.tensor_tensor
            add(out=dst, in0=dst, in1=src, op=ALU.add)

        def y_add_out(n, a, one, other):
            yo = value("yo", n, a)[:].rearrange("p (i g c) -> p i g c", i=R, g=QUAD)
            nc.vector.tensor_tensor(
                out=yo,
                in0=term(n, one, QUAD * a, QUAD * (a + 1)).rearrange("p g i c -> p i g c"),
                in1=term(n, other, QUAD * a, QUAD * (a + 1)).rearrange("p g i c -> p i g c"),
                op=ALU.add,
            )

        def y_store(n, a):
            yo = value("yo", n, a)[:].rearrange("p (i c) -> p i c", i=R)
            nc.sync.dma_start(out=out_rows[n * P : (n + 1) * P, :, a, :], in_=yo)

        def home(n, j, group):
            return ("whole", n, j) if j < WHOLE else ("prod", n, j, group // HALF)

        def parts(n, terms, quad):
            return [("part", n, j, quad) for j in terms] + [("held",) + home(n, j, QUAD * quad) for j in terms]

        def uses(fn, n=0, *a):
            xb = xb_of[n][0]
            table = {
                phi_widen: lambda: ([], [("wide", n)]),
                phi_group: lambda: ([("wide", n)], [("logit_words", n // 2) if a[0] else ("gate_words",)]),
                gate_quant: lambda: ([("gate_words",)], [("gate_codes",)]),
                logit_quant: lambda: ([("logit_words", n)], [("logit_codes", n)]),
                bias_turn: lambda: ([], [("bias_ps",)]),
                bias_read: lambda: ([("bias_ps",)], [("bias",)]),
                w_group: lambda: ([("w_raw",)], [("w_words",)]),
                gf_half: lambda: ([("bias_ps",)], [("half_gf",)]),
                w_quant: lambda: ([("w_words",)], [("w_codes",)]),
                x_turn: lambda: ([], [("xp", n, a[0])]),
                x_gain: lambda: ([("xp", n, a[0])], [("xn", xb)]),
                x_quant: lambda: ([("xn", n)], [("xc", n), ("xs", n)]),
                gate_mm: lambda: ([("xc", n), ("xs", n), ("gate_codes",)], [("tg", n)]),
                logit_mm: lambda: ([("xc", n), ("xs", n)] + [("logit_codes", r // 2) for r in range(*a)], [("tl", n)]),
                gate_tanh: lambda: ([("tg", n), ("bias",)], [("th", n)]),
                gate_one: lambda: ([("th", n)], [("th1", n)]),
                gate_turn: lambda: ([("th1" if n == OWN_GATES else "th", n)], [("gt", n)]),
                gate_copy: lambda: ([("gt", n)], [("gate", n)]),
                logit_exp: lambda: ([("tl", n), ("bias",)], [("co", n)]),
                e_turn: lambda: ([("co", xb)], [("ct", n)]),
                sink_sum: lambda: ([("scaled", n, a[0] - 1) if a[0] else ("ct", n)], [("sums", n, a[0])]),
                sink_root: lambda: ([("sums", n, a[0])], [("root", n, a[0])]),
                sink_inv: lambda: ([("root", n, a[0])], [("factor", n, a[0])]),
                sink_recip: lambda: ([("sums", n, a[0])], [("factor", n, a[0])]),
                sink_scale: lambda: ([("ct", n), ("factor", n, a[0])], [("scaled", n, a[0])]),
                sink_last: lambda: ([("scaled", n, 2), ("factor", n, 3)], [("q", n)]),
                q_to_psum: lambda: ([("q", n)], [("qp", n)]),
                pre_prod: lambda: ([("gt" if a[3] == "vector" else "gate", xb)], [("pu", n, a[0])]),
                u_sum: lambda: ([("pu", n, pair) for pair in range(2)], [("ut", n)]),
                u_gain: lambda: ([("ut", n), ("half_gf",)], [("u_words", batch_of[n][0])]),
                u_quant: lambda: ([("u_words", n)], [("u_codes", n)]),
                branch_mm: lambda: ([("u_codes", batch_of[n][0]), ("w_codes",)], [("h", n)]),
                branch_relu: lambda: ([("h", n)], [("hr", n)]),
                post_root: lambda: ([("post", n, a[0] - 1) if a[0] else ("gate", n)], [("post", n, a[0]) if a[0] < 2 else ("rooted", n)]),
                product: lambda: (
                    [("hr", n), ("rooted", xb), ("gate", xb)] if a[0] == BRANCH else [("qp", n)] if a[3] == "vector" else [("q", n)],
                    [home(n, a[0], a[1])] + [("part", n, a[0], quad) for quad in range(a[1] // QUAD, (a[2] - 1) // QUAD + 1)],
                ),
                y_sum: lambda: (parts(n, order_of(n, a[0])[a[1] : a[2]], a[0]) + [("added", n, a[0])], [("yt", n, a[0])]),
                y_add: lambda: (parts(n, a[1:3], a[0]), [("added", n, a[0])]),
                y_add_out: lambda: (parts(n, a[1:3], a[0]) + [("added", n, a[0])], [("yo", n, a[0])]),
                y_store: lambda: ([("yo", n, a[0])], []),
                y_out: lambda: ([("yt", n, a[0])], [("yo", n, a[0])]),
            }
            return table[fn]()

        V, S, GP = "vector", "scalar", "gpsimd"
        tensor, vector, scalar, gpsimd = [], [], [], []

        def turns(*ns):
            return [(x_turn, n, pair) for n in ns for pair in range(2)]

        def gains(*ns):
            return [(x_gain, n, pair) for n in ns for pair in range(2)]

        def pre_g(n, pair, lo=0, hi=2 * G):
            return (pre_prod, n, pair, lo, hi, GP)

        def pre_v(n, pair, r):
            return (pre_prod, n, pair, r * G, (r + 1) * G, V)

        def pre_s(n, pair, lo=0, hi=2 * G):
            return [(pre_prod, n, pair, a, min(a + QUAD, hi), S) for a in range(lo, hi, QUAD)]

        def usum(n, plain=(0, 0)):
            return (u_sum, n, plain)

        def unit(n, j, lo, hi, engine):
            return (product, n, j, lo, hi, engine)

        def unit_s(n, j, lo, hi):
            return [unit(n, j, g, g + 1, S) for g in range(lo, hi)]

        def deal(work, *marks):
            merged = []
            for m, entry in enumerate(work + [None]):
                merged.extend(step for place, step in marks if min(place, len(work)) == m)
                merged.extend([entry] if entry else [])
            return merged

        def inverse(n, step, place):
            return [(place, (sink_root, n, step)), (place + 1, (sink_inv, n, step))]

        def roots(n, place):
            b, m = xb_of[n]
            return [(place + step, (post_root, b, step)) for step in range(3)] * (m == 0)

        def when(n, *steps):
            return list(steps) if 0 <= n < NT else []

        G_FROM = [G, 4] + [HALF] * (NT - 3)
        V_LOW = [HALF, HALF] + [6] * (NT - 4) + [HALF]
        Q_COLS = [(G + HALF, 4 * G)] + [(2 * G, 4 * G)] * (NT - 1)
        M0, M1, M2, RELU, ROOT = 4, 13, 22, 2, 9
        QUANT_AT = {2: 1}
        EXTRA_T = {1: [usum(7)]}
        EXTRA_V = {(0, 0): [(u_gain, 4)], (0, 2): [(u_gain, 6)], (0, 3): [(y_out, 0, 0), unit(0, 1, HALF, G, V)]}
        EXTRA_S = {1: pre_s(7, 1)}
        tensor += turns(0) + turns(1) + [(bias_turn,)]
        tensor += [(gate_mm, 0)] + turns(2, 3) + [(gate_turn, 0, True), (gate_mm, 1)] + turns(4)
        tensor += [(gate_turn, 1, False), (logit_mm, 0, 0, R), (logit_mm, 1, 0, R)] + turns(5) + [(e_turn, 0, 0, 2, False), (gate_mm, 2), (logit_mm, 2, 0, R)]
        tensor += [(gate_turn, 2, False)] + turns(6, 7) + [(gate_mm, 3), (logit_mm, 3, 0, R), usum(0), (gate_turn, 3, False), usum(1), (e_turn, 1, 0, 2, False)]
        tensor += [(gate_mm, 4), (logit_mm, 4, 0, R), (gate_mm, 5), (logit_mm, 5, 0, R), (gate_turn, 4, False), usum(2), (gate_turn, 5, False)]
        tensor += [usum(3), (e_turn, 2, 0, 2, False), usum(4), (branch_mm, 0), (q_to_psum, 0) + Q_COLS[0], (branch_mm, 1), usum(5), usum(6)]

        vector += [(phi_widen, 1, V, 0, T), (phi_widen, 3, V, 0, T), (phi_group, 0, False, V), (phi_group, 1, False, V), (phi_group, 3, False, V)]
        vector += [(x_gain, 0, 0), (phi_group, 2, False, V), (x_gain, 0, 1), (gate_quant,), (x_quant, 0)]
        vector += gains(1) + [(logit_quant, 0), (x_quant, 1)] + gains(2) + [(logit_quant, 1), (gate_copy, 0, V)]
        vector += gains(3) + [(x_quant, 2), (gate_copy, 1, V)] + gains(4, 5) + [(sink_sum, 0, 0), (x_quant, 3), (gate_copy, 2, V)]
        vector += gains(6, 7) + [(x_quant, 4), (x_quant, 5), (w_quant,), (gate_copy, 3, V), (sink_recip, 0, 0), (u_gain, 0), (sink_scale, 0, 0), (sink_sum, 1, 0), (sink_sum, 0, 1)]
        vector += [(u_gain, 1), (sink_recip, 0, 1), (sink_recip, 1, 0), (sink_scale, 0, 1), (sink_scale, 1, 0), (sink_sum, 0, 2), (sink_sum, 1, 1), (gate_copy, 4, V), (u_gain, 2)]
        vector += [(sink_scale, 0, 2), (gate_copy, 5, V), (sink_scale, 1, 1), (u_gain, 3), (sink_sum, 0, 3), (u_quant, 0), (sink_sum, 1, 2), pre_v(6, 1, 0), pre_v(6, 1, 1)]

        scalar += [(phi_widen, 0, S, 0, T), (phi_widen, 2, S, 0, T)] + [(phi_group, r, True, S) for r in range(R)]
        scalar += [(bias_read,), (gf_half,), (gate_tanh, 0), (w_group, 0, S), (w_group, 1, S), (gate_tanh, 1)] + pre_s(0, 0, G) + pre_s(0, 1, 0, G) + [(logit_exp, 0), (logit_exp, 1)]
        scalar += pre_s(0, 1, G) + pre_s(1, 1, HALF, G) + [(gate_tanh, 2)] + pre_s(1, 1, G) + [(logit_exp, 2)] + pre_s(2, 1) + [(gate_tanh, 3)] + pre_s(3, 0, HALF)
        scalar += [(logit_exp, 3)] + pre_s(3, 1, 0, 24) + [(gate_tanh, 4)] + pre_s(3, 1, 24) + [(logit_exp, 4), (gate_one, 4), (gate_tanh, 5), (logit_exp, 5)]
        work = pre_s(4, 1) + pre_s(5, 1)
        scalar += deal(work, *inverse(0, 2, 0) + inverse(1, 1, 1) + roots(0, 3) + inverse(0, 3, 7) + inverse(1, 2, 9))

        gpsimd += [pre_g(0, 0, 0, G), pre_g(1, 0), pre_g(1, 1, 0, HALF), pre_g(2, 0), pre_g(3, 0, 0, HALF), pre_g(4, 0), pre_g(5, 0), pre_g(6, 0), (sink_last, 0)]

        for k in range(NT - 1):
            near, far = k + 1, k + 2
            banks = [(y_sum, k, a, 0, len(order_of(k, a)), (0, 0)) for a in range(NQ)]
            tensor += [(q_to_psum, near) + Q_COLS[near]] * (near == NT - 1) + banks[:1] + when(k + 3, (e_turn, k + 3, 0, 2, False)) + [(y_sum, k, 1, 0, 1, (0, 0))] + when(far, (branch_mm, far))
            tensor += [(q_to_psum, near) + Q_COLS[near]] * (near < NT - 1) + [(y_sum, k, 1, 1, BRANCH + 1, (0, 0))]
            tensor += EXTRA_T.get(k, []) + banks[2:]
            back = [when(k - 1, (y_out, k - 1, a)) + EXTRA_V.get((k, a), []) for a in range(NQ)]
            first, then = [unit(k, 2, 0, HALF, V)], [unit(k, 3, 0, V_LOW[k], V)]
            if k < 2:
                first, then = [unit(k, 2, 0, QUAD, V), unit(k, 3, 0, QUAD, V)], [unit(k, 2, QUAD, HALF, V), unit(k, 3, QUAD, V_LOW[k], V)]
            if k == 0:
                then = then + [(u_gain, 5)]
            if k == 1:
                back = [back[1], [], back[2], back[3]]
            last_sum = [(sink_sum, near, 3)]
            vector += [(sink_scale, near, 2)] + back[0] + when(far, (sink_sum, far, 0)) + last_sum * (k not in QUANT_AT) + first
            vector += when(far, (sink_scale, far, 0)) + back[1] + when(far, (sink_sum, far, 1)) + then + ([(u_gain, NT - 1)] + last_sum + [(u_quant, QUANT_AT.get(k))]) * (k in QUANT_AT) + [unit(k, 2, HALF, G, V)]
            vector += when(far, (sink_scale, far, 1)) + back[2] + when(far, (sink_sum, far, 2)) + [unit(k, 3, HALF, G, V)] + back[3]
            work = unit_s(k, 1, 0, QUAD) + unit_s(k, BRANCH, 0, HALF) + unit_s(k, 1, QUAD, min(G_FROM[k], HALF))
            work = work + unit_s(k, 3, V_LOW[k], HALF) + EXTRA_S.get(k, []) + unit_s(k, BRANCH, HALF, G)
            marks = when(far, *inverse(far, 0, M0 if k else 2)) + inverse(near, 3, M0 + 2 if k not in QUANT_AT else M1 + 3) + [(RELU if k else ROOT - 1, (branch_relu, near))] + roots(near, ROOT)
            marks = [(1, (branch_relu, 0))] * (k == 0) + marks
            marks = marks + when(far, *inverse(far, 1, M1) + inverse(far, 2, M2 + len(work) - 25))
            scalar += deal(work, *marks)
            second = [unit(k, 1, G_FROM[k], G, GP)] * (G_FROM[k] < G) + [(y_add, k, a, 0, 1, GP) for a in range(NQ) if (k, a) in ADDED]
            gpsimd += ([unit(k, 0, 0, G, GP)] if k else [unit(k, 0, 0, QUAD, GP), unit(k, 0, QUAD, G, GP)]) + second * (k in QUANT_AT) + [(sink_last, near)] + second * (k not in QUANT_AT) + [pre_g(7, 0)] * (k == 0)

        k, last = NT - 1, NQ - 1
        tensor += [(y_sum, k, a, 0, len(order_of(k, a)), (0, 0)) for a in range(last)]
        outs = [(y_out, k - 1, a) for a in range(NQ)] + [(y_out, k, a) for a in range(last)]
        vector += [outs[0], unit(k, 2, 0, HALF, V), outs[1], unit(k, 3, 0, HALF, V), outs[2], unit(k, 2, HALF, G, V), unit(k, 3, HALF, G, V), outs[3]]
        vector += [outs[4], (y_add, k, last, 2, 3, V), outs[5], (y_add, k, last, 2, BRANCH, V), (y_add_out, k, last, 0, 2), (y_store, k, last), outs[6]]
        scalar += [s for a in range(NQ) for j in (BRANCH, 1)[: 1 + (a < last)] for s in unit_s(k, j, QUAD * a, QUAD * a + QUAD)]
        gpsimd += [unit(k, 0, 0, HALF, GP), unit(k, 0, HALF, G, GP), unit(k, 1, QUAD * last, G, GP), (y_add, k, last, 0, 1, GP)] + [(y_add, k, a, 0, 1, GP) for a in range(last) if (k, a) in ADDED]

        queues = (tensor, vector, scalar, gpsimd)
        steps = [s for queue in queues for s in queue]
        assert len(set(steps)) == len(steps)
        writers, users = dict(), dict()
        for s in steps:
            reads, writes = uses(*s)
            for key in writes:
                writers.setdefault(key, []).append(s)
            for key in reads + writes:
                users.setdefault(key[1:] if key[0] == "held" else key, []).append(s)
        done, taken = set(), {"whole0": [("w_raw",)]}

        def ready(s):
            reads, writes = uses(*s)
            if not all(t in done for key in reads for t in writers.get(key, [])):
                return False
            for key in writes:
                if key[0] in KINDS and key not in tiles:
                    older, bufs = taken.setdefault(tag_of(key), []), bufs_of(key)
                    if len(older) >= bufs and not all(t in done for t in users[older[-bufs]]):
                        return False
            return True

        pos = [0] * len(queues)
        while len(done) < len(steps):
            count = len(done)
            for e, queue in enumerate(queues):
                if pos[e] < len(queue) and ready(queue[pos[e]]):
                    s = queue[pos[e]]
                    for key in uses(*s)[1]:
                        if key[0] in KINDS and key not in tiles:
                            taken[tag_of(key)].append(key)
                    s[0](*s[1:])
                    done.add(s)
                    pos[e] = pos[e] + 1
            assert len(done) > count, [(q[p][0], q[p][1:]) for q, p in zip(queues, pos) if p < len(q)]
